import numpy as np, ml_dtypes
CORES = [13,21,141,149]
N = 4
BF = ml_dtypes.bfloat16
M, L, S, E, G0, T, Q, W = 1744, 192, 64, 4, 2, 4, 560, 1952
LV = [235, 436, 604, 405]
def forest(rng, lean):
    sn = np.full((16, M), M); fa = rng.integers(0, M, M); gn = np.zeros(M, np.int64)
    o = 64 + rng.permutation(M - 64); cur = np.arange(64); at = 0
    for i, n in enumerate(LV):
        nxt = o[at:at + n]; at += n
        share = 0.9 if i == 0 else 0.45 + 0.3 * rng.random()
        fert = rng.permutation(cur)[:max(n // 16 + 1, int(len(cur) * share))]
        key = rng.random((len(fert), 16)) * np.exp2(lean * rng.random((len(fert), 1)))
        pk = np.argsort(key.reshape(-1))[:n]; dad = fert[pk >> 4]
        sn[pk & 15, dad] = nxt; fa[nxt] = dad; gn[nxt] = i + 1; cur = nxt
    return sn, fa, gn
def woods(rng, lean):
    v = [forest(rng, lean) for _ in range(8 * N)]
    return np.stack([a[0] for a in v]).reshape(N, 8, 16, M), np.stack([a[1] for a in v]).reshape(N, 8, M), np.stack([a[2] for a in v]).reshape(N, 8, M)
def pack(x, w, sn, fa, gn):
    return {"x": np.ascontiguousarray(x.reshape(N, 128, M)).astype(np.float32).astype(BF), "w": np.ascontiguousarray(w.reshape(N, 128, 1)).astype(np.float32).astype(BF),
            "sn": np.ascontiguousarray(sn.reshape(N, 128, M)).astype(np.int32), "fa": fa.astype(np.int32), "gn": gn.astype(np.int32)}
def few(rng, sn, fa, gn, n):
    if n: sn[:, 64] = M; sn[:, M - 1] = M
    z = int(rng.integers(0, 64)); sn[:, z] = M
    empty = np.all(sn == M, axis=0); gn[empty] = np.minimum(gn[empty], G0 - 1)
    if n:
        o = np.flatnonzero(empty); o = rng.permutation(o[(o > 64) & (o < M - 1)])[:n - 2]
        o = np.concatenate([np.array([64, M - 1]), o]); fa[o] = z; gn[o] = G0 + rng.integers(0, 2, len(o))
def ladders(rng, sn, fa, gn):
    U = (E - 2) // 2 + 1; B = 2 * U + 4; nb = (M - 64) // B
    sn[:] = M; gn[:] = 0; fa[:] = rng.integers(0, 64, M)
    k = (64 + rng.permutation(M - 64))[:nb * B].reshape(nb, B); u = rng.integers(0, U + 1, nb); a = rng.integers(0, 16, nb)
    for j in range(U + 1):
        m = j <= u; up = k[m, j]; so = k[m, 1 + j]
        sn[a[m] if j == 0 else rng.integers(0, 16, len(up)), up] = so; fa[so] = up
    a = (a + 1 + rng.integers(0, 15, nb)) & 15
    for j in range(U + 2):
        m = j <= u + 1; up = k[m, 0 if j == 0 else U + 1 + j]; so = k[m, U + 2 + j]
        sn[a[m] if j == 0 else rng.integers(0, 16, len(up)), up] = so; fa[so] = up
    gn[k[np.arange(nb), 1 + u]] = G0 + rng.integers(0, 2, nb)
    sn[:4, :64] = rng.choice(k[:, 0], (4, 64))
def guests(rng, x, sn, fa, gn):
    n = S - int(rng.integers(0, 4)); z = int(rng.integers(1, 64)); o = 64 + rng.permutation(M - 64)
    last = M - 16 - np.arange(n); o = np.concatenate([last, o[~np.isin(o, last)]])
    s, p, q, y, h, r, u, v = o[:8 * n].reshape(8, n); h = np.sort(h)
    x[:] = rng.integers(0, 256, (16, M)); sn[:] = M; fa[:] = rng.integers(0, M, M); gn[:] = rng.integers(0, G0, M)
    deck = [np.arange(64)] + np.array_split(o[8 * n:], E)
    for a, b in zip(deck[:-1], deck[1:]):
        m = rng.random((16, len(a))) < 0.3; m[rng.integers(0, 16, len(a)), np.arange(len(a))] = True
        sn[:, a] = np.where(m, rng.choice(b, (16, len(a))), M); fa[b] = rng.choice(a, len(b))
    sn[:, z] = M
    for top, one, two in ((p, q, y), (y, h, r), (r, s, u)):
        i = rng.integers(0, 16, n); j = (i + rng.integers(1, 16, n)) & 15
        sn[i, top] = one; sn[j, top] = two; fa[one] = top; fa[two] = top
    sn[rng.integers(0, 16, n), s] = v; fa[v] = s; fa[h] = z; gn[q] = G0; gn[h] = G0
    x[:, h] = x[:, q]; x[:, r] = 255 - x[:, q]; x[:, u] = 255 - x[:, q]
    x[:, s] = x[:, q]; x[:8, s] = x[:8, s] ^ rng.integers(0, 2, (8, n))
def doubles(rng, o, x, sn, fa, gn, nought):
    n = len(o) // 8; p, g, y, z, v, u, a, b = o[:8 * n].reshape(8, n)
    h = 1 + rng.permutation(31)[:n]
    if nought: h[0] = 0
    sn[:, o] = M; sn[:, h] = M; fa[h] = p; fa[p] = g; gn[h] = G0
    up = np.arange(n) % 2 == 1; top = np.where(up, g, p); low = np.where(up, p, h); k = np.argsort(rng.random((n, 16)), axis=1).T
    sn[k[0], top] = low; sn[k[1], top] = low; sn[np.minimum(k[2], k[3]), top] = z; sn[np.maximum(k[2], k[3]), top] = y
    sn[k[4][up], p[up]] = h[up]; sn[k[5][up], p[up]] = h[up]
    sn[k[6], y] = v; sn[k[7], z] = u; sn[k[8], v] = a; sn[k[9], u] = b
    end = 255 * rng.integers(0, 2, (16, n)); m = rng.integers(0, 64, (16, n)) * ((np.arange(n) // 2) % 2)
    one = np.zeros((16, n), np.int64); one[rng.integers(0, 16, n), np.arange(n)] = 1
    x[:, h] = end; x[:, p] = end; x[:, z] = np.abs(255 - end - m); x[:, y] = np.abs(255 - end - m - one)
    return h
def setup_inputs(rng):
    sn, fa, gn = woods(rng, 3.0)
    return pack(rng.integers(0, 256, (N, 8, 16, M)), rng.integers(0, 16, (N, 8, 16, 1)), sn, fa, gn)
def setup_inputs_again(rng):
    sn, fa, gn = woods(rng, 2.0); base = rng.choice(np.array([0, 7, 130, 254]), (N, 8, 1, 1))
    x = base + np.where(rng.random((N, 8, 1, M)) < 0.75, rng.integers(0, 2, (N, 8, 1, M)), rng.integers(0, 2, (N, 8, 16, M)))
    for g in rng.permutation(8)[:4]:
        for q in range(N): guests(rng, x[q, g], sn[q, g], fa[q, g], gn[q, g])
    return pack(x, rng.integers(0, 16, (N, 8, 16, 1)), sn, fa, gn)
def setup_inputs_corners(rng):
    sn, fa, gn = woods(rng, 3.0)
    for q in range(N):
        for g, kind in enumerate(rng.permutation(8)):
            s, f_, n_ = sn[q, g], fa[q, g], gn[q, g]
            if kind < 6: few(rng, s, f_, n_, (S, S + 1, S - 1, L, L + 1, 0)[int(kind)])
            elif kind == 6:
                half = rng.permutation(M)[:M // 2]; s[:] = M; s[:, half] = rng.integers(0, M, (16, len(half)))
                f_[:] = rng.choice(half, M); n_[:] = rng.integers(0, E + 1, M)
            else: ladders(rng, s, f_, n_)
    return pack(rng.integers(0, 256, (N, 8, 16, M)), rng.integers(0, 16, (N, 8, 16, 1)), sn, fa, gn)
def setup_inputs_ends(rng):
    w = 15 * rng.integers(0, 2, (N, 8, 16, 1))
    for q in range(N):
        full, none = rng.permutation(8)[:2]
        if q == N - 1: full, none = 7, 0
        w[q, full] = 15; w[q, none] = 0
    x = 255 * np.where(rng.random((N, 8, 1, M)) < 0.6, rng.integers(0, 2, (N, 8, 1, M)), rng.integers(0, 2, (N, 8, 16, M))); x[..., 0] = 0; x[..., M - 1] = 255
    gn = E * rng.integers(0, 2, (N, 8, M)); sn = np.full((N, 8, 16, M), M)
    fa = np.where(rng.random((N, 8, M)) < 0.68, (M - 1) * rng.integers(0, 2, (N, 8, M)), rng.integers(0, M, (N, 8, M)))
    for q in range(N):
        for g in range(8):
            fer = rng.random(M) < 0.45; fer[:64] = True; fer[M - 1] = g % 2 == 0; fc = np.flatnonzero(fer)
            u = rng.random(M); m = rng.random((16, M)) < 0.3; m[:, u < 0.25] = False; m[15, u < 0.25] = True; m[:, u > 0.9] = True
            v = np.where(rng.random((16, M)) < 0.75, rng.choice(fc, (16, M)), rng.integers(0, M, (16, M)))
            v = np.where(rng.random((16, M)) < 0.12, (M - 1) * rng.integers(0, 2, (16, M)), v)
            sn[q, g] = np.where(m & fer, v, M); sn[q, g, 15, 0] = 0
            if g % 2 == 0:
                far = fc[np.all(x[q, g][:, fc] == 255, axis=0)]; sn[q, g, :, M - 1] = rng.choice(far, 16)
            else: gn[q, g, M - 1] = E; fa[q, g, M - 1] = rng.choice(fc)
    return pack(x, w, sn, fa, gn)
def setup_inputs_loops(rng):
    fa = rng.integers(0, M, (N, 8, M)); fa = np.where(rng.random((N, 8, M)) < 0.05, np.arange(M), fa)
    gn = rng.integers(0, E + 1, (N, 8, M)); sn = np.full((N, 8, 16, M), M); x = rng.integers(0, 256, (N, 8, 16, M))
    for q in range(N):
        for g in range(8):
            m = rng.random((16, M)) < rng.choice(np.array([0.0, 0.0, 0.06, 0.4, 1.0]), M)
            v = rng.integers(0, M, (16, M))
            if g % 2: v = rng.choice(rng.permutation(M)[:200], (16, M))
            v = np.where(rng.random((16, M)) < 0.03, np.arange(M), v); s = np.where(m, v, M)
            far = 64 + rng.permutation(M - 64); o = far[:192]; a, b, h = o[:64], o[64:128], o[128:]
            s[:, o] = M; s[5, a] = b; s[9, b] = h; s[11, b[:20]] = h[:20]; fa[q, g, h] = a; gn[q, g, h] = G0
            e = doubles(rng, far[192:384], x[q, g], s, fa[q, g], gn[q, g], g % 2 == 0)
            if g % 2:
                s[:, 32:64] = M; s[3, 32:64] = rng.choice(a, 32); s[:, 0] = M; fa[q, g, 0] = e[0]; gn[q, g, 0] = G0
            sn[q, g] = s
    return pack(x, rng.integers(0, 16, (N, 8, 16, 1)), sn, fa, gn)
def setup_inputs_spread(rng):
    sn, fa, gn = woods(rng, 9.0)
    x = (rng.random((N, 8, 16, M)) * np.exp2(8 * rng.random((N, 8, 1, M))) * (rng.random((N, 8, 1, M)) > 0.0625)).astype(np.int64)
    w = (rng.random((N, 8, 16, 1)) * np.exp2(4 * rng.random((N, 8, 16, 1)))).astype(np.int64)
    return pack(np.minimum(x, 255), np.minimum(w, 15), sn, fa, gn)
def check_inputs(d):
    bad = []
    for k, lo, hi in (("x", 0, 255), ("w", 0, 15), ("sn", 0, M), ("fa", 0, M - 1), ("gn", 0, E)):
        v = np.asarray(d[k]).astype(np.float64)
        if not (np.min(v) >= lo and np.max(v) <= hi): bad.append("range of " + k)
        elif np.any(v != np.floor(v)): bad.append("whole numbers in " + k)
    return bad
def narrow(tab, ix):
    return np.take_along_axis(tab, ix, 2)
def broad(tab, ix):
    return np.take_along_axis(tab, ix[:, :, None, :], 3)
def reference(x, w, sn, fa, gn):
    X = np.zeros((N, 8, 16, W), np.int32); X[..., :M] = x.astype(np.float32).reshape(N, 8, 16, M)
    SN = np.full((N, 8, 16, W), M, np.int64); SN[..., :M] = sn.reshape(N, 8, 16, M)
    F1 = np.zeros((N, 8, W), np.int64); F1[..., :M] = fa; F2 = F1.copy()
    GN = np.zeros((N, 8, W), np.int64); GN[..., :M] = gn
    wt = w.astype(np.float32).astype(np.int32).reshape(N, 8, 16, 1)
    ship_x = np.zeros((N, 8, 16, S), np.int32); ship_d = np.zeros((N, 8, S), np.int64); ship_h = np.full((N, 8, S), M)
    own = np.arange(L + S) < L; lower = np.tri(L, k=-1).astype(bool)
    for t in range(T):
        f = (F1 if t % 2 == 0 else F2).copy()
        order = (np.arange(W) + t * Q) % W
        ok = (np.all(SN == M, axis=2) & (GN >= G0))[..., order]; place = np.add.accumulate(ok.astype(np.int64), axis=2) - ok
        i, j, k = np.nonzero(ok & (place < L)); h = np.full((N, 8, L), M); h[i, j, place[i, j, k]] = order[k]
        xh = broad(X, h); ax = np.roll(ship_x, t, axis=0)
        xl = np.concatenate([xh, ax], axis=3); real = h != M
        live = np.concatenate([real, np.roll(ship_h, t, axis=0) != M], axis=2)
        c = np.concatenate([narrow(f, h), np.add.reduce(wt * ax, axis=2).astype(np.int64) & 63], axis=2); p = c.copy()
        b = np.concatenate([h, np.full((N, 8, S), M)], axis=2); up_n = np.ones((N, 8, L + S), np.int64)
        d = np.concatenate([np.full((N, 8, L), 2), np.roll(ship_d, t, axis=0)], axis=2)
        y = np.full((N, 8, L + S), M); s = y.copy(); a = np.zeros((N, 8, L + S), np.int64); found = np.zeros((N, 8, L + S), bool)
        for e in range(E):
            sons = broad(SN, c)
            can = (sons != M) & (sons != b[:, :, None, :])
            xs = broad(X, np.ascontiguousarray(sons.transpose(0, 1, 3, 2)).reshape(N, 8, -1)).reshape(N, 8, 16, L + S, 16)
            score = np.add.reduce(np.abs(xs - xl[..., None]), axis=2)
            best = np.argmin(np.where(can.transpose(0, 1, 3, 2), score, 2 ** 20), axis=3)
            son = np.take_along_axis(sons, best[:, :, None, :], 2)[:, :, 0]; some = np.any(can, axis=2)
            down = live & some; fail = live & ~some & (~own | (p < 64)); up = live & ~some & ~fail
            y = np.where(down, c, y); s = np.where(down, son, s); a = np.where(down, best, a); d = np.where(down, d - 1, d)
            hit = down & (d == 0); found = found | hit; live = live & ~fail & ~hit
            fp = narrow(f, p); up_n = np.where(up, up_n + 1, up_n); d = np.where(up, up_n + 1, d)
            b = np.where(up, p, np.where(down, M, b)); c = np.where(up, fp, np.where(down, son, c)); p = np.where(up, fp, p)
        fo, yo, so, ao = found[..., :L], y[..., :L], s[..., :L], a[..., :L]
        same = (yo[..., :, None] == yo[..., None, :]) | (so[..., :, None] == so[..., None, :])
        go = fo & ~np.any(same & fo[..., None, :] & lower, axis=3)
        several = np.add.reduce((broad(SN, yo) != M).astype(np.int64), axis=2) > 1
        mixed = (broad(X, so) + xh) >> 1
        back_x = np.roll(broad(X, s[..., L:]), -t, axis=0); back = np.roll(found[..., L:], -t, axis=0)
        lost = real & ~fo; place = np.add.accumulate(lost.astype(np.int64), axis=2) - lost; age = narrow(GN, h)
        i, j, k = np.nonzero(go); hh, yy, ss, aa = h[i, j, k], yo[i, j, k], so[i, j, k], ao[i, j, k]; m = several[i, j, k]
        SN[i, j, 0, hh] = ss; F2[i, j, ss] = hh; X[i, j, :, ss] = mixed[i, j, :, k]
        SN[i[m], j[m], aa[m], yy[m]] = M; F1[i[m], j[m], ss[m]] = hh[m]
        i, j, k = np.nonzero(back); hh = ship_h[i, j, k]; nc = M + 16 + S * (t - 1) + k
        X[i, j, :, nc] = back_x[i, j, :, k]; F1[i, j, nc] = hh; F2[i, j, nc] = hh; GN[i, j, nc] = GN[i, j, hh] + 1; SN[i, j, t, hh] = nc
        i, j, k = np.nonzero(lost & (place < S)); pl = place[i, j, k]
        ship_x = np.zeros((N, 8, 16, S), np.int32); ship_d = np.zeros((N, 8, S), np.int64); ship_h = np.full((N, 8, S), M)
        ship_x[i, j, :, pl] = xh[i, j, :, k]; ship_d[i, j, pl] = age[i, j, k]; ship_h[i, j, pl] = h[i, j, k]
    return {"xo": X.reshape(N, 128, W).astype(np.float32).astype(BF), "fo": F1.astype(np.float32), "f2o": F2.astype(np.float32)}

@@ -1,0 +1,800 @@
+from concourse.mybir import AluOpType as OP, ActivationFunctionType as AF
+
+M, W, L, S, T_, Q = 1744, 1952, 192, 64, 4, 560
+BK = 2176
+WT = BK + W + 32
+HWN = W + L
+TB = W
+BIG = 512.0
+SW_ = 68
+NENG = 8
+NV = {"A0": 48, "A1": 48, "A2": 64, "AB": 48}
+
+SCRATCH = {}
+PLACE = {}
+HALF = set()
+BANKS = set("k%d" % i for i in range(8))
+POOL = {"float32": ["poolf", 0], "float16": ["poole", 0], "bfloat16": ["poolh", 0], "int32": ["pooli", 0], "uint16": ["poolu", 0]}
+
+
+def _b(kind, dtype, **kw):
+    for n, w in kw.items():
+        if dtype in ("bfloat16", "uint16", "float16"):
+            HALF.add(n)
+        if kind == "psum" or n[:2] in ("ms", "bs", "ls", "mr", "br", "lr"):
+            SCRATCH[n] = (kind, [128, w], dtype)
+        else:
+            p = POOL[dtype]
+            PLACE[n] = (p[0], p[1], w)
+            p[1] += (w + 15) // 16 * 16
+            SCRATCH[p[0]] = (kind, [128, p[1]], dtype)
+
+
+_b("sbuf", "float32", SN=WT, F1=W + L, F2=W + L, GH=W, H=L, TMP=L, RW=L, P0=L, P1=L, SA=L, HG=L, RMOD=384, DIAG=L, LTM=384, RS0=384, RST=96, D15=L, OF=128, I3=384, SW=512,
+   R16=1, PBF=2, M0=1, E0=1, TRL=12, TR4=48, COLC=64, ZER=122, HW12=12, P0W=12, U2=24, ND=12, WALL=36, KALL=24, D1=24, YS=24, KF=12, AW=12, FND=24, YT=24, BS0=384, SCB=384,
+   BSA=L, FR=L, FRS=L, SR=L, SRS=L, FL4=48, Z4=48, Z5=48, SY=L, DD=L, VH=L, VY=L, XG=L, LOF=12,
+   CS=12, DA=12, DB=12, RT=S, RTS=S, RTB=S, RTSB=S, FDW=4, RZ=4, RV=S, RV2=S, RVB=S, RV2B=S, FD=S, GENM=12, LB3=12, LBT=12,
+   LFF=128, LG=128, G2K=128, MTC=8, MKEEP=384)
+for _n in ("A0", "A1", "A2", "AB"):
+    _b("sbuf", "float32", **{"SF" + _n: 64, "MM" + _n: 64, "IM" + _n: 64, "NI" + _n: 64, "ZZ" + _n: 64})
+    _b("sbuf", "float16", **{"RR" + _n: 64})
+_b("sbuf", "float16", SWH=512, ONESH=128, DX=384, FGF=M, LF=128, IDH=128, NIDH=128, S0=L, S1=L)
+_b("sbuf", "bfloat16", IDK=128, NIDK=128, UR=L, EC=1056, EZ=1056)
+_b("sbuf", "float32", UD=L, SROW=L)
+SCRATCH["gnd"] = ("dram", [8, Q * 3 + W], "int32")
+_b("sbuf", "float32", HWIN=HWN, D=W, R122=1, POS=122, GTH=488, NOK=122, C1=122)
+_b("sbuf", "bfloat16", NINC=122, IDB=128, NIDB=128)
+_b("sbuf", "int32", GTI=488, PAD=208)
+_b("sbuf", "uint16", OFF16=122)
+_b("sbuf", "bfloat16", X=WT, ANE=W, SEL=2048, WSEL=2048, ONES=128, ONESB=128, TRI=128, TRMO=128, SLR=128, XL=L, XR=3072,
+   XRB=1024, UA=3072, UB=1024, EQ0=L, EM0=L, EQ1=L, EDM=384, EE=2112, EMY=L, AX=L, LO=12, WC=1, TMPB=128,
+   FGB=M, LGB=128, VH8=W, VL8=W)
+_b("sbuf", "int32", SNI=M, FGI=M, PI=1, PI2=1, LKI=64, KI=12, KI2=12, HI4=4, HI4B=4, HIR=S, HIR2=S,
+   CI=4, CI2=4, XI=L)
+_b("sbuf", "uint16", H16=L, HL=12, P0L=12, P1L=12, SA16=L, S16B=64, S16A=L, LA=12, LB=12, LK=64, BL=4,
+   YR16=384, YL=12, SL=12, L4=48, LO16=12, RL16=4, BF16=4)
+_b("psum", "float32", k0=512, k1=512, k2=512, k3=512, k4=512, k5=512, k6=512, k7=512)
+for _t in range(3):
+    _b("sbuf", "bfloat16", **{"ms%d" % _t: 384, "bs%d" % _t: SW_, "ls%d" % _t: SW_, "mr%d" % (_t + 1): S, "br%d" % (_t + 1): S, "lr%d" % (_t + 1): S})
+    _b("sbuf", "float32", **{"HGS%d" % _t: 384, "HROW%d" % _t: S, "GHN%d" % _t: S, "HSW%d" % _t: 4})
+    _b("sbuf", "uint16", **{"HS%d" % _t: 4})
+
+MSGS = [("s", 0), ("r", 1), ("s", 1), ("r", 2), ("s", 2), ("r", 3)]
+SEMAPHORES = ["qv", "qs", "qt", "qg", "lo"] + ["d%d" % i for i in range(24)] + ["x%s%d" % m for m in MSGS] + ["a%s%d" % m for m in MSGS]
+
+
+def goal(T, rank, kind, t):
+    return T.cores[(rank + 1 + t) % 4] if kind == "s" else T.cores[(rank - t) % 4]
+
+
+def via(topo, src, dst):
+    if topo.may_write(src, dst):
+        return None
+    c = [k for k in topo.cores_of(src) if k != src and topo.may_write(k, dst)]
+    near = [k for k in c if topo.die(k) == topo.die(src)]
+    return (near + c)[0]
+
+
+def send(g, topo, src, dst, out, in_, rsem, lsem):
+    rid, pid = topo.addr(dst, src)
+    mask = sum(1 << e for e in topo.engines(src, dst)[:NENG])
+    g.remote_dma(out, in_, rsem, lsem, pid, rid, mask)
+
+
+def hand_on(g, core, T, topo):
+    n = 0
+    for kind, t in MSGS:
+        for r in range(len(T.cores)):
+            dst = goal(T, r, kind, t)
+            if via(topo, T.cores[r], dst) == core:
+                k = "%s%d" % (kind, t)
+                g.wait_ge(T.sem["x" + k], NENG)
+                send(g, topo, core, dst, T["l" + k][:], T["b" + k][:], T.sem["a" + k], T.sem.lo)
+                n += NENG
+    if n:
+        g.wait_ge(T.sem.lo, n)
+
+
+def rank_program(g, core, T, topo):
+    rank = T.rank_of(core)
+    if rank is None:
+        hand_on(g, core, T, topo)
+        return
+
+    queue = {"v": g.vector, "s": g.scalar, "t": g.tensor, "g": g, "y": g.sync}
+    count = {"qv": 0, "qs": 0, "qt": 0, "qg": 0}
+    known = {e: {} for e in queue}
+    clock = {}
+    wr, rd = {}, {}
+    dsem = [0]
+    total = {}
+    WAKE, CY = 0.1, 0.00083
+    free = {e: 0.0 for e in queue}
+    when = {}
+    tape = [None]
+
+    def deps(e, reads, writes):
+        w = {}
+
+        def want(sem, val):
+            if known[e].get(sem, 0) < val and w.get(sem, 0) < val:
+                w[sem] = val
+        for isw, lst in ((0, reads), (1, writes)):
+            for n, lo, hi in lst:
+                ps = n in BANKS
+                for lo2, hi2, e2, sem, val in wr.get(n, ()):
+                    if ps and e2 != e or lo < hi2 and lo2 < hi:
+                        if not (e == "t" and e2 == "t" and ps):
+                            want(sem, val)
+                if isw or ps:
+                    for (e2, lo2, hi2), (sem, val) in rd.get(n, {}).items():
+                        if ps and e2 != e or (isw and lo < hi2 and lo2 < hi):
+                            want(sem, val)
+        return w
+
+    def need(e, reads, writes):
+        w = deps(e, reads, writes)
+        for sem in w:
+            free[e] = max(free[e], when.get((sem, w[sem]), 0) + WAKE)
+        for sem in sorted(w):
+            if known[e].get(sem, 0) >= w[sem]:
+                continue
+            queue[e].wait_ge(T.sem[sem], w[sem])
+            known[e][sem] = w[sem]
+            for s2, v2 in clock.get((sem, w[sem]), {}).items():
+                if known[e].get(s2, 0) < v2:
+                    known[e][s2] = v2
+
+    def note(e, sem, val, reads, writes):
+        c = dict(known[e])
+        if sem[0] == "q":
+            for s2, v2 in clock.get((sem, val - 1), {}).items():
+                if c.get(s2, 0) < v2:
+                    c[s2] = v2
+        c[sem] = val
+        clock[(sem, val)] = c
+        total[sem] = max(total.get(sem, 0), val)
+        for n, lo, hi in writes:
+            wr[n] = [x for x in wr.get(n, []) if not (lo <= x[0] and x[1] <= hi)] + [(lo, hi, e, sem, val)]
+            rd[n] = {k: x for k, x in rd.get(n, {}).items() if not (lo <= k[1] and k[2] <= hi)}
+        for n, lo, hi in reads:
+            rd.setdefault(n, {})[(e, lo, hi)] = (sem, val)
+
+    def flat(xs):
+        r = []
+        for x in xs:
+            if x is not None and not isinstance(x, (int, float)):
+                r += [x[0:3]] if len(x) == 4 else [x[0][0:3], x[1][0:3]]
+        return r
+
+    def ap(x):
+        return x if x is None or isinstance(x, (int, float)) else x[3] if len(x) == 4 else x[2]
+
+    def emit(e, call, reads, writes, us):
+        if tape[0] is not None:
+            tape[0].append((e, call, flat(reads), flat(writes), us))
+        else:
+            issue(e, call, flat(reads), flat(writes), us)
+
+    def issue(e, call, reads, writes, us):
+        need(e, reads, writes)
+        free[e] += us
+        if writes:
+            sem = "q" + e
+            count[sem] += 1
+            call().then_inc(T.sem[sem], 1)
+            when[(sem, count[sem])] = free[e]
+            note(e, sem, count[sem], reads, writes)
+        else:
+            call()
+
+    def record(gen):
+        tape[0] = []
+        for _ in gen:
+            pass
+        r = tape[0]
+        tape[0] = None
+        return r
+
+    def merge(streams):
+        pos = {n: 0 for n in streams}
+        done = set()
+        while len(done) < len(streams):
+            best = None
+            for n in streams:
+                if n in done or any(p not in done for p in streams[n][1]):
+                    continue
+                if pos[n] == len(streams[n][2]):
+                    done.add(n)
+                    best = None
+                    break
+                e, call, reads, writes, us = streams[n][2][pos[n]]
+                st = free[e]
+                w = deps(e, reads, writes)
+                for sem in w:
+                    st = max(st, when.get((sem, w[sem]), 0) + WAKE)
+                key = (round(st / 0.04), streams[n][0], st)
+                if best is None or key < best[0]:
+                    best = (key, n)
+            if best is not None:
+                n = best[1]
+                issue(*streams[n][2][pos[n]])
+                pos[n] += 1
+
+    def size(x):
+        return x[3].shape[1] if len(x) == 4 else 16 * x[1][3].shape[1]
+
+    def two(*xs):
+        return all(len(x) == 4 and (x[0] in HALF) for x in xs)
+
+    def dma(e, out, in_):
+        reads, writes = flat([in_]), flat([out])
+        need(e, reads, writes)
+        sem = "d%d" % dsem[0]
+        dsem[0] += 1
+        queue[e].dma_start(ap(out), ap(in_)).then_inc(T.sem[sem], 16)
+        free[e] += 0.1
+        when[(sem, 16)] = free[e] + (6.0 if out[0] in ("SNI", "X") else 3.0)
+        note(e, sem, 16, reads, writes)
+
+    def v(name, lo=0, hi=None, st=1, p=None):
+        buf, o, w = PLACE[name] if name in PLACE else (name, 0, SCRATCH[name][1][1])
+        t = T[buf]
+        if hi is None:
+            hi = w
+        ps = slice(None) if p is None else slice(*p)
+        return (name, lo, hi, t[ps, o + lo:o + hi] if st == 1 else t[ps, o + lo:o + hi:st])
+
+    def at(win, off):
+        return (win, off, win[3].indirect(off[3]))
+
+    def tc(out, in_):
+        sc, ga = len(out) == 3, len(in_) == 3
+        emit("v", lambda: g.vector.tensor_copy(ap(out), ap(in_)), [in_] + ([out[1]] if sc else []), [out[0] if sc else out],
+             0.05 + 3.8 * CY * size(out) if sc else 0.05 + 1.5 * CY * size(in_) if ga else CY * max(64, size(out) * (0.5 if two(out, in_) else 1)))
+
+    def tt(out, a, b, op):
+        emit("v", lambda: g.vector.tensor_tensor(ap(out), ap(a), ap(b), op), [a, b], [out],
+             0.05 + 1.5 * CY * size(a) if len(a) == 3 else CY * max(64, size(out) * (1 if a[0] in BANKS or b[0] in BANKS else 2)))
+
+    def ts(out, a, s1, op0, s2=None, op1=None):
+        us = CY * max(64, size(out) * (0.5 if two(out, a) else 1))
+        if op1 is None:
+            emit("v", lambda: g.vector.tensor_scalar(ap(out), ap(a), ap(s1), None, op0), [a, s1], [out], us)
+        else:
+            emit("v", lambda: g.vector.tensor_scalar(ap(out), ap(a), ap(s1), ap(s2), op0, op1), [a, s1, s2], [out], us)
+
+    def scan(out, d0, d1, op0, op1, init=0.0):
+        emit("v", lambda: g.vector.tensor_tensor_scan(ap(out), ap(d0), ap(d1), init, op0, op1), [d0, d1], [out], CY * max(64, size(out)))
+
+    def turn(out, in_):
+        emit("v", lambda: g.vector.transpose(ap(out), ap(in_)), [in_], [out], CY * max(64, size(out)))
+
+    def fill(out, c):
+        emit("v", lambda: g.vector.memset(ap(out), c), [], [out], CY * max(64, size(out)))
+
+    def act(out, in_, func=AF.Copy, bias=0.0, scale=1.0):
+        us = 0.065 + 1.5 * CY * size(out) if len(in_) == 3 else CY * max(64, size(out))
+        if bias != 0.0 or scale != 1.0:
+            emit("s", lambda: g.scalar.activation(ap(out), ap(in_), func, bias=ap(bias), scale=scale), [in_, bias], [out], us)
+        else:
+            emit("s", lambda: g.scalar.activation(ap(out), ap(in_), func), [in_], [out], us)
+
+    def mm(out, lhsT, rhs, start, stop):
+        emit("t", lambda: g.tensor.matmul(ap(out), ap(lhsT), ap(rhs), start, stop), [lhsT, rhs], [out], CY * max(64, size(out)) * (1 if two(lhsT) else 4))
+
+    def iota(out, pattern, base, cm, small=False):
+        us = 0.15 + 2 * CY * size(out)
+        if small:
+            emit("g", lambda: g.iota(ap(out), pattern, base, cm, allow_small_or_imprecise_dtypes=True), [], [out], us)
+        else:
+            emit("g", lambda: g.iota(ap(out), pattern, base, cm), [], [out], us)
+
+    def pick(out, in_, pattern, op, base, cm):
+        emit("g", lambda: g.affine_select(ap(out), ap(in_), pattern, op, 0.0, base, cm), [in_], [out], 0.17 + 2 * CY * size(out))
+
+    add, sub, mul, eq, ne = OP.add, OP.subtract, OP.mult, OP.is_equal, OP.not_equal
+    ge, gt, lt = OP.is_ge, OP.is_gt, OP.is_lt
+
+    half = M // 2
+    dma("s", ("gnd", 0, M, T.gnd[:, 0:M]), ("gn", 0, M, T.gn[:]))
+    dma("s", ("gnd", W, Q * 3 + W, T.gnd[:, W:Q * 3 + W]), ("gn", 0, Q * 3, T.gn[:, 0:Q * 3]))
+    dma("y", v("SNI", 0, half), ("sn", 0, half, T.sn[:, 0:half]))
+    dma("y", v("SNI", half, M), ("sn", half, M, T.sn[:, half:M]))
+    dma("s", v("FGI", 0, M, p=(0, 8)), ("fa", 0, M, T.fa[:]))
+    dma("s", v("FGI", 0, M, p=(8, 16)), ("gn", 0, M, T.gn[:]))
+    dma("y", v("X", 0, M), ("x", 0, M, T.x[:]))
+    dma("y", v("WC"), ("w", 0, 1, T.w[:]))
+
+    fill(v("PAD", 0, 16), 0)
+    fill(v("PAD", 16, 208), 2)
+    dma("s", ("gnd", M, W, T.gnd[:, M:W]), v("PAD", p=(0, 8)))
+    for t in range(T_):
+        dma("s", v("GTI", 122 * t, 122 * (t + 1)), ("gnd", Q * t, Q * t + W, T.gnd[:, Q * t:Q * t + W]))
+
+    iota(v("PI"), [[1, 1]], 0, 1)
+    fill(v("ONES"), 1.0)
+    pick(v("TMPB"), v("ONES"), [[-16, 8], [0, 16]], ge, 0, 1)
+    pick(v("ONESB"), v("TMPB"), [[16, 8], [0, 16]], ge, 15, -1)
+    pick(v("TRI"), v("ONESB"), [[1, 128]], ge, -1, -1)
+    iota(v("RMOD"), [[0, 24], [1, 16]], 0, 0, True)
+    iota(v("POS"), [[1, 122]], 0, 0, True)
+    iota(v("D"), [[1, 122], [122, 16]], 0, 0, True)
+    ts(v("PI2"), v("PI"), 15, OP.bitwise_and)
+    tc(v("R16"), v("PI2"))
+    ts(v("PI2"), v("PI"), 4, OP.logical_shift_right, 1, OP.bitwise_and)
+    tc(v("PBF", 1, 2), v("PI2"))
+    ts(v("PBF", 0, 1), v("PBF", 1, 2), -1.0, mul, 1.0, add)
+    R16 = v("R16")
+    POSB, CQB, DIAGB = v("k4", 256, 378), v("k4", 384, 506), v("k3", 256, 448)
+    ts(v("R122"), R16, 122.0, mul)
+    ts(POSB, v("POS"), v("R122"), add)
+    ts(CQB, POSB, -1.0, mul, float(HWN), add)
+    fill(v("ZER"), 0.0)
+    fill(v("SEL"), 0.0)
+    for s in range(16):
+        ts(v("SEL", s * 128 + s, (s + 1) * 128, 16), v("ONESB", s, 128, 16), 16.0, mul)
+    fill(v("SN", M, 1760), float(M))
+    fill(v("SN", 1760, W), 0.0)
+    fill(v("SN", W, WT), float(M))
+    tc(v("SN", 0, half), v("SNI", 0, half))
+    tc(v("SN", half, M), v("SNI", half, M))
+    ts(v("GTH"), v("GTI"), 2, ge, -1.0, add)
+    iota(v("SLR"), [[0, 8], [1, 16]], 0, 0, True)
+    fill(v("OF"), 1.0)
+    for i, base in enumerate((0, 16, -16)):
+        pick(v("I3", 128 * i, 128 * (i + 1)), v("OF"), [[-1, 128]], eq, base, 1)
+    fill(v("G2K"), 2048.0)
+    pick(v("LG", p=(0, 16)), v("G2K", p=(0, 16)), [[1, 8], [0, 16]], eq, 8, -1)
+    pick(v("LFF", p=(0, 16)), v("OF", p=(0, 16)), [[1, 8], [0, 16]], eq, 0, -1)
+    iota(v("TRL"), [[16, 12]], L, 0, True)
+    iota(v("TR4"), [[0, 4], [16, 12]], TB, 0, True)
+    iota(v("LKI"), [[1, 64]], 0, 0)
+    iota(v("COLC"), [[1, 64]], 1760, 0, True)
+    iota(v("VH8", p=(0, 1)), [[8, W // 8], [0, 8]], 0, 0, True)
+    iota(v("VL8", p=(0, 1)), [[0, W // 8], [1, 8]], 0, 0, True)
+
+    def constants_late():
+        tc(v("FGF", p=(0, 16)), v("FGI", p=(0, 16)))
+        tc(v("LF", p=(0, 16)), v("LFF", p=(0, 16)))
+        ts(v("DIAG"), v("RMOD", 0, L), R16, eq)
+        ts(DIAGB, v("RMOD", 0, L), R16, eq)
+        ts(v("RS0"), v("RMOD"), 0.0, ne)
+        ts(v("RST"), v("RMOD", 0, 96), 0.0, eq, float(2 ** 20), mul)
+        fill(v("F1", M, 1760), float(M))
+        fill(v("F1", 1760, W + L), 0.0)
+        fill(v("F2", M, 1760), float(M))
+        fill(v("F2", 1760, W + L), 0.0)
+        fill(v("GH", M, W), 0.0)
+        fill(v("X", M, WT), BIG)
+        fill(v("X", 1760, W), 0.0)
+        w = M // 4
+        for j in range(4):
+            a, b = j * w, (j + 1) * w
+            k = "k%d" % (2 * (j % 2))
+            mm(v(k, 0, w), v("LF", p=(0, 16)), v("FGF", a, b, p=(0, 16)), True, True)
+            act(v("F1", a, b), v(k, 0, w))
+        for e in range(2):
+            for y in range(2):
+                i = 0 if e == y else 1 if y else 2
+                ts(v("SW", 128 * (2 * e + y), 128 * (2 * e + y + 1)), v("I3", 128 * i, 128 * (i + 1)), v("PBF", e, e + 1), mul)
+        tc(v("SWH"), v("SW"))
+        act(v("IDB"), v("I3", 0, 128))
+        act(v("NIDB"), v("I3", 0, 128), scale=-1.0)
+        act(v("IDK"), v("I3", 0, 128), scale=float(BK))
+        act(v("NIDK"), v("I3", 0, 128), scale=-float(BK))
+        tc(v("IDH"), v("I3", 0, 128))
+        ts(v("NIDH"), v("I3", 0, 128), -1.0, mul)
+        ts(v("TRL"), v("TRL"), R16, add)
+        ts(v("TR4"), v("TR4"), R16, add)
+        yield
+
+    def constants_last():
+        tc(v("FGB", p=(0, 16)), v("FGI", p=(0, 16)))
+        tc(v("LGB", p=(0, 16)), v("LG", p=(0, 16)))
+        act(v("F2", 0, M), v("F1", 0, M))
+        w = M // 4
+        for j in range(4):
+            a, b = j * w, (j + 1) * w
+            k = "k2"
+            mm(v(k, 0, w), v("LGB", p=(0, 16)), v("FGB", a, b, p=(0, 16)), True, False)
+            mm(v(k, 0, w), v("ONES", p=(0, 1)), v("VH8", a, b, p=(0, 1)), False, False)
+            mm(v(k, 0, w), v("ONES", p=(0, 1)), v("VL8", a, b, p=(0, 1)), False, True)
+            act(v("GH", a, b), v(k, 0, w))
+        ts(v("LTM"), v("RMOD"), R16, gt)
+        ts(v("D15"), v("DIAG"), -998.5, mul, 1000.0, add)
+        ts(v("M0"), R16, 0.0, eq)
+        ts(v("E0"), R16, 0.0, ne, float(M + 1), mul)
+        ts(v("E0"), v("E0"), -1.0, add)
+        for t in range(1, 4):
+            ts(v("MTC", t, t + 1), R16, float(t), eq)
+            ts(v("MTC", 4 + t, 5 + t), R16, float(t), ne)
+        tc(v("ONESH"), v("ONESB"))
+        tt(v("TRMO"), v("TRI"), v("ONESB"), sub)
+        ts(v("WSEL"), v("SEL"), v("WC"), mul, 0.0625, mul)
+        fill(v("BS0"), 0.0)
+        fill(v("BSA"), 0.0)
+        tc(v("LK"), v("LKI"))
+        yield
+
+    def narrow(src, n, tmp="TMP", res="RW"):
+        tt(v(tmp, 0, n), src, v("DIAG", 0, n) if src[0] in BANKS else v("k3", 256, 256 + n), mul)
+        scan(v(res, 0, n), v("RS0", 0, n), v(tmp, 0, n), mul, add)
+        return v(res, 15, n, 16)
+
+    def lanes1(t):
+        c = W // 4
+        st = Q * t
+        segs = [(a, a + c) for a in range(0, W, c)]
+        k0 = st // c
+        fill(v("HWIN", 0, L), float(M))
+        for a, b in segs[k0:] + segs[:k0]:
+            act(v("ANE", a, b), v("SN", a, b), AF.Abs, -float(M))
+        for m in range(16):
+            a = st + 122 * m
+            parts = [(a, a + 122)] if a + 122 <= W or a >= W else [(a, W), (W, a + 122)]
+            for x, y in parts:
+                mm(v("k6", x - a, y - a), v("SEL", 128 * m, 128 * (m + 1)), v("ANE", x % W, x % W + y - x), m == 0, m == 15)
+        tt(v("NOK"), v("k6", 0, 122), v("GTH", 122 * t, 122 * (t + 1)), gt)
+        scan(v("NINC"), v("NOK"), v("ZER"), add, add)
+        mm(v("k7", 0, 1), v("TRI"), v("NINC", 121, 122), True, True)
+        tt(v("C1"), v("NOK"), CQB, mul)
+        tt(v("k3", 0, 122), v("C1"), POSB, add)
+        tt(v("C1"), v("k3", 0, 122), v("NINC"), sub)
+        ts(v("OFF16"), v("C1"), v("k7", 0, 1), sub)
+        tc(at(v("HWIN"), v("OFF16")), v("D"))
+        if t < 3:
+            iota(v("D"), [[1, 122], [122, 16]], Q * (t + 1), 0, True)
+        yield
+
+    def lanes2(t):
+        if t:
+            ts(v("k4", 0, L), v("HWIN", 0, L), float(W), ge, -float(W), mul)
+            tt(v("H"), v("k4", 0, L), v("HWIN", 0, L), add)
+        else:
+            tc(v("H"), v("HWIN", 0, L))
+        F = "F1" if t % 2 == 0 else "F2"
+        tab = v("SN")
+        r = narrow(v("H"), L)
+        tc(v("HL"), r)
+        tc(v("P0"), at(v(F, 0, W), v("HL")))
+        tc(v("H16"), v("H"))
+        act(v("HW12"), r)
+        act(v("XR", 0, 1536), at(v("X"), v("H16", 0, 96)))
+        act(v("XR", 1536, 3072), at(v("X"), v("H16", 96, 192)))
+        r = narrow(v("P0"), L)
+        tc(v("P0L"), r)
+        act(v("P0W"), r)
+        tc(v("S0"), at(tab, v("P0L")))
+        tc(v("P1"), at(v(F, 0, W), v("P0L")))
+        tt(v("EQ0"), v("S0"), v("H"), eq)
+        ts(v("EM0"), v("S0"), float(M), eq)
+        mm(v("k6", 0, L), v("ONESB"), v("EQ0"), True, False)
+        mm(v("k6", 0, L), v("ONESB"), v("EM0"), False, True)
+        W0, WD = v("k6", 256, 448), v("k7", 256, 448)
+        mm(W0, v("IDH"), v("S0"), True, False)
+        mm(W0, v("IDK"), v("EQ0"), False, True)
+        mm(WD, v("NIDH"), v("S0"), True, False)
+        mm(WD, v("NIDK"), v("EQ0"), False, False)
+        r = narrow(v("P1"), L)
+        tc(v("P1L"), r)
+        tc(v("S1"), at(tab, v("P1L")))
+        mm(WD, v("IDH"), v("S1"), False, False)
+        ts(v("UR"), v("k6", 0, L), 16.0, ge)
+        tt(v("EQ1"), v("S1"), v("P0"), eq)
+        mm(WD, v("IDK"), v("EQ1"), False, True)
+        tt(v("UD"), WD, v("UR"), mul)
+        tt(v("SA"), W0, v("UD"), add)
+        tc(v("SA16"), v("SA"))
+        yield
+
+    def own_flags(t):
+        act(v("XL"), at(v("X"), v("HL")))
+        for r in range(16):
+            mm(v("k6", 448, 460), v("SEL", 128 * r, 128 * (r + 1)), v("UR", r, L, 16), r == 0, r == 15)
+        if t < 3:
+            act(v("HG"), at(v("GH"), v("HL")))
+        act(v("U2", 0, 12), v("k6", 448, 460), scale=1.0 / 256)
+        act(v("U2", 12, 24), v("k6", 448, 460), scale=1.0 / 256)
+        ts(v("ND"), v("P0W"), 64.0, lt)
+        tt(v("ND"), v("ND"), v("U2", 0, 12), mul)
+        ts(v("ND"), v("ND"), -1.0, mul, 1.0, add)
+        act(v("Z4", 0, 12), v("HW12"))
+        if t < 3:
+            ts(v("LOF"), v("HW12"), float(M), ne)
+            fill(v("ms%d" % t, 0, 384), 0.0)
+            fill(v("HGS%d" % t, 0, 384), 0.0)
+        yield
+
+    def down(tag, nq, idx, son, offl, xr, u, u0, lst, keep=None):
+        n = nq * 16
+        kb, vb, vo = {"A0": ("k0", "k3", 0), "A1": ("k1", "k3", 128), "A2": ("k7", "k4", 0), "AB": ("k2", "k5", 0)}[tag]
+        nv = NV[tag]
+        if nv < n:
+            us, dif = v(u, u0 + 16 * nv, u0 + 16 * n), v(kb, 128, 128 + 16 * (n - nv))
+            act(us, at(v("X"), v(idx, offl + nv, offl + n)))
+            mm(dif, v("NIDB"), v(xr, u0 + 16 * nv, u0 + 16 * n), True, False)
+            mm(dif, v("IDB"), us, False, True)
+        ux = v(u, u0, u0 + 16 * nv)
+        tt(ux, at(v("X"), v(idx, offl, offl + nv)), v(xr, u0, u0 + 16 * nv), sub)
+        if nv < n:
+            act(us, dif, AF.Abs)
+        act(ux, ux, AF.Abs)
+        for s in range(16):
+            mm(v(kb, 0, n), v("SEL", 128 * s, 128 * (s + 1)), v(u, u0 + s, u0 + 16 * n, 16), s == 0, False)
+        mm(v(kb, 0, n), v("SLR", p=(0, 1)), v("ONES", 0, n, p=(0, 1)), False, True)
+        SP, KP = v(vb, vo, vo + n), v(vb, vo + n, vo + 2 * n)
+        turn(SP, son)
+        turn(KP, v(kb, 0, n))
+        im, ni, zz, rr = [v(x + tag, 0, n) for x in ("IM", "NI", "ZZ", "RR")]
+        mm_ = v("MM" + tag, 0, n) if keep is None else v("MKEEP", keep, keep + n)
+        scan(mm_, v("RST", 0, n), KP, add, OP.min, float(2 ** 20))
+        tt(im, mm_, KP, eq)
+        tt(ni, mm_, KP, ne)
+        tt(zz, im, SP, mul)
+        scan(rr, ni, zz, mul, add)
+        for e in range(2):
+            for y in range(2):
+                mm(v(kb, 64 + e, 64 + nq, 2), v("SWH", 128 * (2 * e + y), 128 * (2 * e + y + 1)), v("RR" + tag, 15 + 16 * y, n, 32), y == 0, y == 1)
+        lst(v(kb, 64, 64 + nq))
+
+    def own(h):
+        tag, o, lo = "A%d" % h, 4 * h, 64 * h
+
+        def after(step, name):
+            def f(x):
+                if step < 2:
+                    tc(v(name, o, o + 4), x)
+                act(v("WALL", 12 * step + o, 12 * step + o + 4), x)
+            return f
+        down(tag, 4, "SA16", v("SA", lo, lo + 64), lo, "XR", "UA", 16 * lo, after(0, "LA"))
+        for step, prev, name in ((1, "LA", "LB"), (2, "LB", "")):
+            tc(v("S16A", lo, lo + 64), at(v("SN"), v(prev, o, o + 4)))
+            act(v("SF" + tag), at(v("SN"), v(prev, o, o + 4)))
+            down(tag, 4, "S16A", v("SF" + tag), lo, "XR", "UA", 16 * lo, after(step, name), keep=192 * (step - 1) + lo)
+        yield
+
+    def arrivals(t):
+        ls = "ls%d" % (t - 1)
+        for r in range(16):
+            mm(v("k2", 0, 4), v("WSEL", 128 * r, 128 * (r + 1)), v(ls, r, S, 16), r == 0, r == 15)
+        act(v("XRB"), at(v(ls, 0, S), v("LK")))
+        tc(v("CI"), v("k2", 0, 4))
+        for d in range(3):
+            ts(v("GENM", 4 * d, 4 * d + 4), v(ls, S, SW_), float(d + 2), eq)
+        ts(v("CI2"), v("CI"), 63, OP.bitwise_and)
+        tc(v("BL"), v("CI2"))
+        for e in range(4):
+            tc(v("S16B"), at(v("SN"), v("BL")))
+            act(v("SFAB"), at(v("SN"), v("BL")))
+
+            def f(x):
+                if e < 3:
+                    tc(v("BL"), x)
+                if e:
+                    act(v("LB3", 4 * (e - 1), 4 * e), x)
+            down("AB", 4, "S16B", v("SFAB"), 0, "XRB", "UB", 0, f)
+        ts(v("LBT"), v("LB3"), -float(M), add)
+        tt(v("LB3"), v("LBT"), v("GENM"), mul)
+        tt(v("LBT", 0, 4), v("LB3", 0, 4), v("LB3", 4, 8), add)
+        tt(v("LBT", 4, 8), v("LBT", 0, 4), v("LB3", 8, 12), add)
+        ts(v("BF16"), v("LBT", 4, 8), float(M), add)
+        tc(v("mr%d" % t), at(v("X"), v("BF16")))
+        ship("r", t, v("mr%d" % t))
+        yield
+
+    sent = [0]
+
+    def ship(kind, t, src):
+        k = "%s%d" % (kind, t)
+        dst = goal(T, rank, kind, t)
+        mid = via(topo, core, dst)
+
+        def call():
+            if mid is None:
+                send(g, topo, core, dst, T["l" + k][:], src[3], T.sem["a" + k], T.sem.lo)
+            else:
+                send(g, topo, core, mid, T["b" + k][:], src[3], T.sem["x" + k], T.sem.lo)
+            sent[0] += NENG
+            when[("a" + k, NENG)] = free["g"] + 10.0
+        emit("g", call, [src], [], 1.0)
+
+    def found(t):
+        tt(v("D1"), v("WALL", 12, 36), v("WALL", 0, 24), sub)
+        tt(v("YT"), v("D1"), v("U2"), mul)
+        tt(v("YS"), v("YT"), v("WALL", 0, 24), add)
+        ts(v("YT", 0, 12), v("YS", 12, 24), float(M), ne)
+        tt(v("FND", 0, 12), v("YT", 0, 12), v("ND"), mul)
+        tt(v("FND", 12, 24), v("YT", 0, 12), v("ND"), mul)
+        if t < 3:
+            tt(v("LOF"), v("LOF"), v("FND", 0, 12), sub)
+            act(v("LO"), v("LOF"))
+            mm(v("k0", 256, 268), v("ONESB"), v("LO"), True, True)
+            mm(v("k0", 272, 284), v("TRMO"), v("LO"), True, True)
+        yield
+
+    def adopt(t):
+        ts(v("D1"), v("YS"), 1.0, add)
+        tc(v("YL"), v("YS", 0, 12))
+        tt(v("BS0", 0, 384, 16), v("D1"), v("FND"), mul)
+        tc(v("SL"), v("YS", 12, 24))
+        scan(v("SCB"), v("RS0"), v("BS0"), mul, add)
+        tt(v("DX", 0, L), v("SCB", 0, L), DIAGB, mul)
+        mm(v("k7", 0, L), v("ONESH"), v("DX", 0, L), True, True)
+        tt(v("DX", L, 384), v("SCB", L, 384), DIAGB, mul)
+        mm(v("k7", L, 384), v("ONESH"), v("DX", L, 384), True, True)
+        tc(v("SY"), at(v("SN"), v("YL")))
+        act(v("Z4", 12, 24), v("YS", 12, 24))
+        act(v("Z4", 24, 36), v("YS", 0, 12))
+        act(v("Z4", 36, 48), v("YS", 12, 24))
+        ts(v("EMY"), v("SY"), float(M), ne)
+        mm(v("k1", 0, L), v("ONESB"), v("EMY"), True, True)
+        tt(v("Z5"), v("Z4"), v("TR4"), sub)
+        act(v("SROW"), v("k7", L, 384))
+        o = 0
+        for q in range(11):
+            n = (11 - q) * 16
+            act(v("EZ", o, o + n), v("SROW", L - n, L), AF.Abs, bias=v("BS0", L + 16 * q, L + 16 * q + 1), scale=-1.0)
+            o += n
+        act(v("EC"), v("EZ"), AF.Relu, bias=1.0, scale=-1.0)
+        tc(v("YR16", 0, L), v("k7", 0, L))
+        tt(v("k5", 128, 512), v("SCB"), v("k7", 0, 384), eq)
+        tt(v("EDM"), v("k5", 128, 512), v("LTM"), mul)
+        mm(v("k6", 0, L), v("ONESB"), v("EDM", 0, L), True, False)
+        mm(v("k6", 0, L), v("ONESB"), v("EDM", L, 384), False, False)
+        o = 0
+        for q in range(11):
+            n = (11 - q) * 16
+            ts(v("EE", o, o + n), v("YR16", L - n, L), v("BS0", 16 * q, 16 * q + 1), eq)
+            mm(v("k6", L - n, L), v("ONESB"), v("EE", o, o + n), False, False)
+            o += n
+        o = 0
+        for q in range(11):
+            n = (11 - q) * 16
+            mm(v("k6", L - n, L), v("ONESB"), v("EC", o, o + n), False, q == 10)
+            o += n
+        tt(v("SR"), v("D15"), v("k1", 0, L), lt)
+        scan(v("SRS"), v("RS0", 0, L), v("SR"), mul, add)
+        tt(v("FR"), v("DIAG"), v("k6", 0, L), gt)
+        scan(v("FRS"), v("RS0", 0, L), v("FR"), mul, add)
+        tt(v("FL4", 0, 12), v("FRS", 15, L, 16), v("FND", 0, 12), mul)
+        tt(v("FL4", 12, 24), v("FRS", 15, L, 16), v("FND", 0, 12), mul)
+        tt(v("FL4", 24, 36), v("SRS", 15, L, 16), v("FL4", 0, 12), mul)
+        tt(v("FL4", 36, 48), v("SRS", 15, L, 16), v("FL4", 0, 12), mul)
+        tt(v("Z4"), v("Z5"), v("FL4"), mul)
+        tt(v("Z5"), v("Z4"), v("TR4"), add)
+        tc(v("L4"), v("Z5"))
+        yield
+
+    def slots(t):
+        for e in range(2):
+            for y in range(2):
+                mm(v("k2", 256 + e, 280, 2), v("SW", 128 * (2 * e + y), 128 * (2 * e + y + 1)), v("MKEEP", 15 + 16 * y, 384, 32), y == 0, y == 1)
+        act(v("KALL"), v("k2", 256, 280))
+        tt(v("KF"), v("KALL", 12, 24), v("KALL", 0, 12), sub)
+        tt(v("AW"), v("KF"), v("U2", 0, 12), mul)
+        tt(v("KF"), v("AW"), v("KALL", 0, 12), add)
+        tc(v("KI"), v("KF"))
+        ts(v("KI2"), v("KI"), 15, OP.bitwise_and)
+        tc(v("BSA", 0, L, 16), v("KI2"))
+        scan(v("k4", 0, L), v("RS0", 0, L), v("BSA"), mul, add)
+        tt(v("AX"), v("k4", 0, L), v("DIAG"), mul)
+        mm(v("k0", 0, L), v("ONESB"), v("AX"), True, True)
+        yield
+
+    def change_sons(t):
+        ts(v("VH"), v("k7", L, 384), v("M0"), mul, v("E0"), add)
+        ts(v("DD"), v("SY"), -1.0, mul, float(M), add)
+        ts(v("k1", 0, L), v("k0", 0, L), R16, eq)
+        tc(at(v("SN", 0, W + L), v("L4", 0, 12)), v("VH"))
+        tt(v("k3", 0, L), v("DD"), v("k1", 0, L), mul)
+        tt(v("VY"), v("k3", 0, L), v("SY"), add)
+        tc(at(v("SN", 0, W + L), v("L4", 24, 36)), v("VY"))
+        yield
+
+    def sending(t):
+        ms, hg = "ms%d" % t, "HGS%d" % t
+        scan(v("CS"), v("k0", 256, 268), v("ZER", 0, 12), add, add)
+        tt(v("DA"), v("CS"), v("k0", 272, 284), add)
+        tt(v("DB"), v("DA"), v("TRL"), sub)
+        tt(v("DA"), v("DB"), v("LOF"), mul)
+        tt(v("DB"), v("DA"), v("TRL"), add)
+        tc(v("LO16"), v("DB"))
+        tc(at(v(hg), v("LO16")), v("HG"))
+        tc(at(v(ms), v("LO16")), v("XL"))
+        r = narrow(v(hg, 0, S), S, "RT", "RTS")
+        tc(v("HI4"), r)
+        ts(v("HI4B"), v("HI4"), 11, OP.logical_shift_right)
+        tc(v(ms, S, SW_), v("HI4B"))
+        ship("s", t, v(ms, 0, SW_))
+        ts(v("HI4B"), v("HI4"), 2047, OP.bitwise_and)
+        tc(v("HSW%d" % t), v("HI4B"))
+        tc(v("HS%d" % t), v("HI4B"))
+        yield
+
+    def change_rest(t):
+        tt(v("XG"), at(v("X"), v("SL")), v("XL"), add)
+        ts(v("XG"), v("XG"), 0.5, sub, 0.5, mul)
+        tc(v("XI"), v("XG"))
+        tc(at(v("X", 0, W + L), v("L4", 12, 24)), v("XI"))
+        tc(at(v("F2"), v("L4", 12, 24)), v("H"))
+        tc(at(v("F1"), v("L4", 36, 48)), v("H"))
+        yield
+
+    def guests(t):
+        if t >= 1:
+            lr, a = "lr%d" % t, 1760 + S * (t - 1)
+            tt(v("X", a, a + S), v(lr), v("FD"), mul)
+            tt(v("F1", a, a + S), v("HROW%d" % (t - 1)), v("FD"), mul)
+            tt(v("F2", a, a + S), v("HROW%d" % (t - 1)), v("FD"), mul)
+            if t < 3:
+                tc(v("GH", a, a + S), v("GHN%d" % (t - 1)))
+        yield
+
+    def note_sent(t):
+        hg = "HGS%d" % t
+        tc(v("HIR"), v(hg, 0, S))
+        ts(v("HIR2"), v("HIR"), 2047, OP.bitwise_and)
+        tc(v("HROW%d" % t), v("HIR2"))
+        tt(v("RV"), v(hg, 0, S), v("HROW%d" % t), sub)
+        ts(v("RV2"), v("RV"), 2048.0 + S * t, add)
+        tt(v("GHN%d" % t), v("RV2"), v("COLC"), add)
+        yield
+
+    def returns(t):
+        lr, a = "lr%d" % t, 1760 + S * (t - 1)
+        hw, hs = "HSW%d" % (t - 1), "HS%d" % (t - 1)
+        ts(v("FD"), v(lr), 256.0, lt)
+        if t < 3:
+            r = narrow(v("FD"), S, "RTB", "RTSB")
+            tt(v("RZ"), v(hw), v("TR4", 0, 4), sub)
+            tc(v("RVB"), at(v("SN", 0, W), v(hs)))
+            tt(v("FDW"), v("RZ"), r, mul)
+            ts(v("RV2B"), v("RVB"), v("MTC", 4 + t, 5 + t), mul)
+            tt(v("RZ"), v("FDW"), v("TR4", 0, 4), add)
+            ts(v("RTB"), v("COLC"), float(S * (t - 1)), add, v("MTC", t, t + 1), mul)
+            tc(v("RL16"), v("RZ"))
+            tt(v("RVB"), v("RV2B"), v("RTB"), add)
+            ts(v("SN", a, a + S), v(lr), 256.0, lt, float(M), mul)
+            tc(at(v("SN", 0, W + L), v("RL16")), v("RVB"))
+        yield
+
+    for kind, t in MSGS:
+        k = "%s%d" % (kind, t)
+        wr["l" + k] = [(0, 1 << 20, "remote", "a" + k, NENG)]
+        total["a" + k] = NENG
+    st = {"late": (3, [], record(constants_late()))}
+    for t in range(T_):
+        p, last = "%d" % t, "%d" % (t - 1)
+        st["lanes1" + p] = (1, ["returns" + last] if t else [], record(lanes1(t)))
+        st["lanes2" + p] = (1, ["lanes1" + p] + (["rest" + last, "guests" + last, "sending" + last] if t else ["late"]), record(lanes2(t)))
+        if t:
+            st["arrivals" + p] = (2, ["rest" + last, "guests" + last, "returns" + last], record(arrivals(t)))
+        else:
+            st["last"] = (6, ["lanes2" + p], record(constants_last()))
+        st["own0" + p] = (2, ["lanes2" + p], record(own(0)))
+        st["own1" + p] = (3, ["lanes2" + p], record(own(1)))
+        st["own2" + p] = (4, ["lanes2" + p], record(own(2)))
+        st["flags" + p] = (4, ["lanes2" + p, "last"], record(own_flags(t)))
+        st["found" + p] = (1, ["own0" + p, "own1" + p, "own2" + p, "flags" + p], record(found(t)))
+        st["adopt" + p] = (1, ["found" + p], record(adopt(t)))
+        over = ["adopt" + p] + (["arrivals" + p] if t else [])
+        if t < 3:
+            st["slots" + p] = (2, ["found" + p] + (["arrivals" + p] if t else []), record(slots(t)))
+            st["sending" + p] = (0, ["found" + p], record(sending(t)))
+            st["sons" + p] = (1, over + ["slots" + p], record(change_sons(t)))
+            st["noted" + p] = (5, ["sending" + p], record(note_sent(t)))
+        st["returns" + p] = (4, (["sons" + p] if t < 3 else over) + (["noted" + last] if t else []), record(returns(t)) if t else [])
+        st["rest" + p] = (4, over, record(change_rest(t)))
+        st["guests" + p] = (4, ["rest" + p, "returns" + p], record(guests(t)))
+    merge(st)
+
+    fill(v("F1", M, 1760), 0.0)
+    fill(v("F2", M, 1760), 0.0)
+    fill(v("X", M, 1760), 0.0)
+    dma("s", ("fo", 0, W, T.fo[:]), v("F1", 0, W, p=(0, 128, 16)))
+    dma("y", ("xo", 0, W, T.xo[:]), v("X", 0, W))
+    dma("s", ("f2o", 0, W, T.f2o[:]), v("F2", 0, W, p=(0, 128, 16)))
+    for sem in sorted(total):
+        g.wait_ge(T.sem[sem], total[sem])
+    g.wait_ge(T.sem.lo, sent[0])

@@ -1,20 +1,26 @@
 from concourse.mybir import AluOpType as OP, ActivationFunctionType as AF
 
 M, W, L, S, T_, Q = 1744, 1952, 192, 64, 4, 560
+NB = W // 16
+RW = M // 16
 BK = 2176
 WT = BK + W + 32
-HWN = W + L
 TB = W
 BIG = 512.0
+KS = 8192.0
+PO = 2048.0
 SW_ = 68
 NENG = 8
-NV = {"A0": 48, "A1": 48, "A2": 64, "AB": 48}
+NV = {"A0": 44, "A1": 44, "A2": 44, "AB": 32}
+BANK = {"A0": ("k0",), "A1": ("k1",), "A2": ("k7",), "AB": ("k2", "k5")}
+PARTS = ("A0", "A1", "A2", "AB")
 
 SCRATCH = {}
 PLACE = {}
 HALF = set()
 BANKS = set("k%d" % i for i in range(8))
 POOL = {"float32": ["poolf", 0], "float16": ["poole", 0], "bfloat16": ["poolh", 0], "int32": ["pooli", 0], "uint16": ["poolu", 0]}
+ORDER = []
 
 
 def _b(kind, dtype, **kw):
@@ -30,33 +36,29 @@ def _b(kind, dtype, **kw):
             SCRATCH[p[0]] = (kind, [128, p[1]], dtype)
 
 
-_b("sbuf", "float32", SN=WT, F1=W + L, F2=W + L, GH=W, H=L, TMP=L, RW=L, P0=L, P1=L, SA=L, HG=L, RMOD=384, DIAG=L, LTM=384, RS0=384, RST=96, D15=L, OF=128, I3=384, SW=512,
-   R16=1, PBF=2, M0=1, E0=1, TRL=12, TR4=48, COLC=64, ZER=122, HW12=12, P0W=12, U2=24, ND=12, WALL=36, KALL=24, D1=24, YS=24, KF=12, AW=12, FND=24, YT=24, BS0=384, SCB=384,
-   BSA=L, FR=L, FRS=L, SR=L, SRS=L, FL4=48, Z4=48, Z5=48, SY=L, DD=L, VH=L, VY=L, XG=L, LOF=12,
-   CS=12, DA=12, DB=12, RT=S, RTS=S, RTB=S, RTSB=S, FDW=4, RZ=4, RV=S, RV2=S, RVB=S, RV2B=S, FD=S, GENM=12, LB3=12, LBT=12,
-   LFF=128, LG=128, G2K=128, MTC=8, MKEEP=384)
-for _n in ("A0", "A1", "A2", "AB"):
-    _b("sbuf", "float32", **{"SF" + _n: 64, "MM" + _n: 64, "IM" + _n: 64, "NI" + _n: 64, "ZZ" + _n: 64})
+_b("sbuf", "float32", SN=WT, F1=W + L, F2=W + L, H=L, P0=L, S0=L, S1=L, SA=L, UD=L, RMOD=384, DIAG=L, D15=L, DTH=S, OF=128, I3=384,
+   R16=1, PBF=2, M0=1, E0=1, MK=16, TRL=12, TR4=48, TRM=12, TRN=12, LANB=12, LANE=L, CT3=192, ZER=128, RST=64, CB=128, CT=128, NBS=12,
+   U=12, NU=12, UP=12, CA=12, CC=12, BASE=12, W1=12, W2=12, D1=12, YP=12, T1=12, NF=12, LOF=12, LOT=12, BS0=384, SCB=384,
+   Z4=48, Z5=48, ZT=24, SY=L, MS=L, VT=L, VH=L, CS=12, DA=12, DB=12, RZ=4, RY=4, RVB=S, FD=S, GENM=12, LB3=12, LBT=12, RS3=12, MTC=8,
+   HZ=12)
+for _n in PARTS:
+    _b("sbuf", "float32", **{"SF" + _n: 64, "MM" + _n: 64, "DD" + _n: 64, "EE" + _n: 64})
     _b("sbuf", "float16", **{"RR" + _n: 64})
-_b("sbuf", "float16", SWH=512, ONESH=128, DX=384, FGF=M, LF=128, IDH=128, NIDH=128, S0=L, S1=L)
-_b("sbuf", "bfloat16", IDK=128, NIDK=128, UR=L, EC=1056, EZ=1056)
-_b("sbuf", "float32", UD=L, SROW=L)
-SCRATCH["gnd"] = ("dram", [8, Q * 3 + W], "int32")
-_b("sbuf", "float32", HWIN=HWN, D=W, R122=1, POS=122, GTH=488, NOK=122, C1=122)
-_b("sbuf", "bfloat16", NINC=122, IDB=128, NIDB=128)
-_b("sbuf", "int32", GTI=488, PAD=208)
-_b("sbuf", "uint16", OFF16=122)
-_b("sbuf", "bfloat16", X=WT, ANE=W, SEL=2048, WSEL=2048, ONES=128, ONESB=128, TRI=128, TRMO=128, SLR=128, XL=L, XR=3072,
-   XRB=1024, UA=3072, UB=1024, EQ0=L, EM0=L, EQ1=L, EDM=384, EE=2112, EMY=L, AX=L, LO=12, WC=1, TMPB=128,
-   FGB=M, LGB=128, VH8=W, VL8=W)
-_b("sbuf", "int32", SNI=M, FGI=M, PI=1, PI2=1, LKI=64, KI=12, KI2=12, HI4=4, HI4B=4, HIR=S, HIR2=S,
-   CI=4, CI2=4, XI=L)
-_b("sbuf", "uint16", H16=L, HL=12, P0L=12, P1L=12, SA16=L, S16B=64, S16A=L, LA=12, LB=12, LK=64, BL=4,
-   YR16=384, YL=12, SL=12, L4=48, LO16=12, RL16=4, BF16=4)
+    _b("sbuf", "bfloat16", **{"XT" + _n: 128, "XR" + _n: 1024, "UU" + _n: 1024})
+    _b("sbuf", "uint16", **{"IX" + _n: 64, "LL" + _n: 4})
+_b("sbuf", "float16", SWH=512, ONESH=128, DX=384, YR=384, PICK=2048, IDH=128, FAS=RW, GNS=RW, RRS=RW, NTRL=12, POR=128, ONR=384,
+   TMP=L, RWH=L, RWP=L, RWQ=L, TMG=S, RWG=S)
+_b("sbuf", "bfloat16", X=WT, GN=W, RM=W + L, ANE=M, SEL=2048, WSEL=2048, REP=1024, ONES=L, ONESB=128, NONESB=128, TRI=128, TRMO=128, TIMO=128,
+   SLR=128, XL=L, XS=L, IDB=128, NIDB=128, IDK=128, NIDK=128, ID16=128, IDHALF=128, QRT=128, TMPB=128, WC=1, RS0=384,
+   OKB=128, OK=128, JK=12 * 128, BT=512, FLG=L, BR=L, EQ0=L, EQ1=L, A0N=L, NE0=L, UR=L, ED=384, EQ=2112, NFR=L, GO=L, FR=L, FRS=L,
+   AY=L, EMY=L, SR=L, SRS=L, EQS=L, LO=12, GNR=S, TMR=S, RWR=S)
+_b("sbuf", "int32", SNI=M, FAI=RW, GNI=RW, PI=1, PI2=1, CI=4, CI2=4, XI=L)
+_b("sbuf", "uint16", BL=12, HL=12, HLT=12, P0L=12, P1L=12, SA16=L, YL=12, SL=12, L4=48, LO16=12, RL16=4, BF16=4)
 _b("psum", "float32", k0=512, k1=512, k2=512, k3=512, k4=512, k5=512, k6=512, k7=512)
 for _t in range(3):
-    _b("sbuf", "bfloat16", **{"ms%d" % _t: 384, "bs%d" % _t: SW_, "ls%d" % _t: SW_, "mr%d" % (_t + 1): S, "br%d" % (_t + 1): S, "lr%d" % (_t + 1): S})
-    _b("sbuf", "float32", **{"HGS%d" % _t: 384, "HROW%d" % _t: S, "GHN%d" % _t: S, "HSW%d" % _t: 4})
+    _b("sbuf", "bfloat16", **{"ms%d" % _t: SW_, "bs%d" % _t: SW_, "ls%d" % _t: SW_, "mr%d" % (_t + 1): S, "br%d" % (_t + 1): S, "lr%d" % (_t + 1): S})
+    _b("sbuf", "float32", **{"HR%d" % _t: 384})
+    _b("sbuf", "float16", **{"HW%d" % _t: S})
     _b("sbuf", "uint16", **{"HS%d" % _t: 4})
 
 MSGS = [("s", 0), ("r", 1), ("s", 1), ("r", 2), ("s", 2), ("r", 3)]
@@ -95,6 +97,91 @@ def hand_on(g, core, T, topo):
         g.wait_ge(T.sem.lo, n)
 
 
+HOP, CY, GA, SC = 0.16, 0.00087, 1.56, 3.8
+
+
+def plan(ops):
+    n = len(ops)
+    pred = [set() for _ in ops]
+    wr, rd, tlast = {}, {}, {}
+    for i, (e, kind, call, reads, writes, us, dur) in enumerate(ops):
+        for nm, lo, hi in reads + writes:
+            pred[i].update(j for lo2, hi2, j in wr.get(nm, ()) if lo < hi2 and lo2 < hi)
+        for nm, lo, hi in writes:
+            pred[i].update(j for lo2, hi2, j in rd.get(nm, ()) if lo < hi2 and lo2 < hi)
+            if e == "t":
+                if nm in tlast:
+                    pred[i].add(tlast[nm])
+                tlast[nm] = i
+        for nm, lo, hi in writes:
+            wr[nm] = [x for x in wr.get(nm, ()) if not (lo <= x[0] and x[1] <= hi)] + [(lo, hi, i)]
+            rd[nm] = [x for x in rd.get(nm, ()) if not (lo <= x[0] and x[1] <= hi)]
+        for nm, lo, hi in reads:
+            rd.setdefault(nm, []).append((lo, hi, i))
+        pred[i].discard(i)
+    succ = [[] for _ in ops]
+    for i in range(n):
+        for j in pred[i]:
+            succ[j].append(i)
+
+    def hop(a, b):
+        return 0.0 if ops[a][0] == ops[b][0] == "t" else HOP
+    rest = [0.0] * n
+    for i in range(n - 1, -1, -1):
+        rest[i] = ops[i][6] + max([hop(i, j) + rest[j] for j in succ[i]], default=0.0)
+    banks = [set(x[0] for x in o[3] + o[4] if x[0] in BANKS) for o in ops]
+    left = [len(p) for p in pred]
+    ready = [0.0] * n
+    free = {e: 0.0 for e in "vstgy"}
+    used = {}
+    cand = {e: [] for e in free}
+    for i in range(n):
+        if not left[i]:
+            cand[ops[i][0]].append(i)
+    order = []
+
+    def start(i):
+        e = ops[i][0]
+        s = max(free[e], ready[i])
+        for b in banks[i]:
+            for e2, t in used.get(b, {}).items():
+                if e2 != e:
+                    s = max(s, t + HOP)
+        return s
+    while len(order) < n:
+        st = {e: [(start(i), i) for i in cand[e]] for e in cand if cand[e]}
+        e = min(st, key=lambda k: min(st[k])[0])
+        t0 = min(st[e])[0]
+        near = sorted((x for x in st[e] if x[0] <= t0 + 0.7), key=lambda x: -rest[x[1]])[:10]
+        first = min(st[e], key=lambda x: (round(x[0] / 0.02), -rest[x[1]]))
+        if first not in near:
+            near.append(first)
+        best = None
+        for s, i in near:
+            b, t = s + rest[i], s + ops[i][5]
+            for s2, j in near:
+                if j != i:
+                    t = max(t, s2)
+                    b = max(b, t + rest[j])
+                    t += ops[j][5]
+            key = (round(b / 0.03), round(s / 0.02), -rest[i])
+            if best is None or key < best[0]:
+                best = (key, s, i)
+        s, i = best[1], best[2]
+        cand[e].remove(i)
+        order.append(i)
+        free[e] = s + ops[i][5]
+        end = s + ops[i][6]
+        for b in banks[i]:
+            used.setdefault(b, {})[e] = end
+        for j in succ[i]:
+            ready[j] = max(ready[j], end + hop(i, j))
+            left[j] -= 1
+            if not left[j]:
+                cand[ops[j][0]].append(j)
+    return order
+
+
 def rank_program(g, core, T, topo):
     rank = T.rank_of(core)
     if rank is None:
@@ -108,12 +195,9 @@ def rank_program(g, core, T, topo):
     wr, rd = {}, {}
     dsem = [0]
     total = {}
-    WAKE, CY = 0.1, 0.00083
-    free = {e: 0.0 for e in queue}
-    when = {}
-    tape = [None]
+    ops = []
 
-    def deps(e, reads, writes):
+    def need(e, reads, writes):
         w = {}
 
         def want(sem, val):
@@ -130,12 +214,6 @@ def rank_program(g, core, T, topo):
                     for (e2, lo2, hi2), (sem, val) in rd.get(n, {}).items():
                         if ps and e2 != e or (isw and lo < hi2 and lo2 < hi):
                             want(sem, val)
-        return w
-
-    def need(e, reads, writes):
-        w = deps(e, reads, writes)
-        for sem in w:
-            free[e] = max(free[e], when.get((sem, w[sem]), 0) + WAKE)
         for sem in sorted(w):
             if known[e].get(sem, 0) >= w[sem]:
                 continue
@@ -160,6 +238,26 @@ def rank_program(g, core, T, topo):
         for n, lo, hi in reads:
             rd.setdefault(n, {})[(e, lo, hi)] = (sem, val)
 
+    def issue(e, kind, call, reads, writes, us, dur):
+        if kind == "r":
+            need(e, reads, [])
+            call()
+            n = writes[0][0]
+            wr[n] = [(0, 1 << 20, "remote", "a" + n[1:], NENG)]
+            total["a" + n[1:]] = NENG
+            return
+        need(e, reads, writes)
+        if kind == "d":
+            sem = "d%d" % dsem[0]
+            dsem[0] += 1
+            call().then_inc(T.sem[sem], 16)
+            note(e, sem, 16, reads, writes)
+        else:
+            sem = "q" + e
+            count[sem] += 1
+            call().then_inc(T.sem[sem], 1)
+            note(e, sem, count[sem], reads, writes)
+
     def flat(xs):
         r = []
         for x in xs:
@@ -170,56 +268,8 @@ def rank_program(g, core, T, topo):
     def ap(x):
         return x if x is None or isinstance(x, (int, float)) else x[3] if len(x) == 4 else x[2]
 
-    def emit(e, call, reads, writes, us):
-        if tape[0] is not None:
-            tape[0].append((e, call, flat(reads), flat(writes), us))
-        else:
-            issue(e, call, flat(reads), flat(writes), us)
-
-    def issue(e, call, reads, writes, us):
-        need(e, reads, writes)
-        free[e] += us
-        if writes:
-            sem = "q" + e
-            count[sem] += 1
-            call().then_inc(T.sem[sem], 1)
-            when[(sem, count[sem])] = free[e]
-            note(e, sem, count[sem], reads, writes)
-        else:
-            call()
-
-    def record(gen):
-        tape[0] = []
-        for _ in gen:
-            pass
-        r = tape[0]
-        tape[0] = None
-        return r
-
-    def merge(streams):
-        pos = {n: 0 for n in streams}
-        done = set()
-        while len(done) < len(streams):
-            best = None
-            for n in streams:
-                if n in done or any(p not in done for p in streams[n][1]):
-                    continue
-                if pos[n] == len(streams[n][2]):
-                    done.add(n)
-                    best = None
-                    break
-                e, call, reads, writes, us = streams[n][2][pos[n]]
-                st = free[e]
-                w = deps(e, reads, writes)
-                for sem in w:
-                    st = max(st, when.get((sem, w[sem]), 0) + WAKE)
-                key = (round(st / 0.04), streams[n][0], st)
-                if best is None or key < best[0]:
-                    best = (key, n)
-            if best is not None:
-                n = best[1]
-                issue(*streams[n][2][pos[n]])
-                pos[n] += 1
+    def emit(e, call, reads, writes, us, kind="c", dur=None):
+        ops.append((e, kind, call, flat(reads), flat(writes), us, us if dur is None else dur))
 
     def size(x):
         return x[3].shape[1] if len(x) == 4 else 16 * x[1][3].shape[1]
@@ -227,15 +277,8 @@ def rank_program(g, core, T, topo):
     def two(*xs):
         return all(len(x) == 4 and (x[0] in HALF) for x in xs)
 
-    def dma(e, out, in_):
-        reads, writes = flat([in_]), flat([out])
-        need(e, reads, writes)
-        sem = "d%d" % dsem[0]
-        dsem[0] += 1
-        queue[e].dma_start(ap(out), ap(in_)).then_inc(T.sem[sem], 16)
-        free[e] += 0.1
-        when[(sem, 16)] = free[e] + (6.0 if out[0] in ("SNI", "X") else 3.0)
-        note(e, sem, 16, reads, writes)
+    def dma(e, out, in_, dur):
+        emit(e, lambda: queue[e].dma_start(ap(out), ap(in_)), [in_], [out], 0.07, "d", dur)
 
     def v(name, lo=0, hi=None, st=1, p=None):
         buf, o, w = PLACE[name] if name in PLACE else (name, 0, SCRATCH[name][1][1])
@@ -248,340 +291,357 @@ def rank_program(g, core, T, topo):
     def at(win, off):
         return (win, off, win[3].indirect(off[3]))
 
+    def vec(call, out, ins, rate):
+        if len(out) == 3:
+            emit("v", call, ins + [out[1]], [out[0]], 0.05 + SC * CY * size(out))
+        elif len(ins[0]) == 3:
+            emit("v", call, ins, [out], 0.05 + GA * CY * size(out))
+        else:
+            emit("v", call, ins, [out], CY * max(64, size(out) * rate))
+
     def tc(out, in_):
-        sc, ga = len(out) == 3, len(in_) == 3
-        emit("v", lambda: g.vector.tensor_copy(ap(out), ap(in_)), [in_] + ([out[1]] if sc else []), [out[0] if sc else out],
-             0.05 + 3.8 * CY * size(out) if sc else 0.05 + 1.5 * CY * size(in_) if ga else CY * max(64, size(out) * (0.5 if two(out, in_) else 1)))
+        vec(lambda: g.vector.tensor_copy(ap(out), ap(in_)), out, [in_], 0.5 if two(out, in_) else 1)
 
     def tt(out, a, b, op):
-        emit("v", lambda: g.vector.tensor_tensor(ap(out), ap(a), ap(b), op), [a, b], [out],
-             0.05 + 1.5 * CY * size(a) if len(a) == 3 else CY * max(64, size(out) * (1 if a[0] in BANKS or b[0] in BANKS else 2)))
+        vec(lambda: g.vector.tensor_tensor(ap(out), ap(a), ap(b), op), out, [a, b], 1 if a[0] in BANKS or b[0] in BANKS else 2)
 
     def ts(out, a, s1, op0, s2=None, op1=None):
-        us = CY * max(64, size(out) * (0.5 if two(out, a) else 1))
+        rate = 0.5 if two(out, a) else 1
         if op1 is None:
-            emit("v", lambda: g.vector.tensor_scalar(ap(out), ap(a), ap(s1), None, op0), [a, s1], [out], us)
+            vec(lambda: g.vector.tensor_scalar(ap(out), ap(a), ap(s1), None, op0), out, [a, s1], rate)
         else:
-            emit("v", lambda: g.vector.tensor_scalar(ap(out), ap(a), ap(s1), ap(s2), op0, op1), [a, s1, s2], [out], us)
+            vec(lambda: g.vector.tensor_scalar(ap(out), ap(a), ap(s1), ap(s2), op0, op1), out, [a, s1, s2], rate)
 
     def scan(out, d0, d1, op0, op1, init=0.0):
-        emit("v", lambda: g.vector.tensor_tensor_scan(ap(out), ap(d0), ap(d1), init, op0, op1), [d0, d1], [out], CY * max(64, size(out)))
+        vec(lambda: g.vector.tensor_tensor_scan(ap(out), ap(d0), ap(d1), init, op0, op1), out, [d0, d1], 0.5 if two(out, d0, d1) else 1)
 
     def turn(out, in_):
-        emit("v", lambda: g.vector.transpose(ap(out), ap(in_)), [in_], [out], CY * max(64, size(out)))
+        vec(lambda: g.vector.transpose(ap(out), ap(in_)), out, [in_], 1)
 
     def fill(out, c):
-        emit("v", lambda: g.vector.memset(ap(out), c), [], [out], CY * max(64, size(out)))
+        emit("v", lambda: g.vector.memset(ap(out), c), [], [out], CY * max(64, size(out) * (0.5 if two(out) else 1)))
 
-    def act(out, in_, func=AF.Copy, bias=0.0, scale=1.0):
-        us = 0.065 + 1.5 * CY * size(out) if len(in_) == 3 else CY * max(64, size(out))
-        if bias != 0.0 or scale != 1.0:
-            emit("s", lambda: g.scalar.activation(ap(out), ap(in_), func, bias=ap(bias), scale=scale), [in_, bias], [out], us)
-        else:
-            emit("s", lambda: g.scalar.activation(ap(out), ap(in_), func), [in_], [out], us)
+    def act(out, in_, func=AF.Copy, bias=0.0, scale=1.0, acc=None):
+        us = 0.065 + GA * CY * size(out) if len(in_) == 3 else CY * max(64, size(out))
+        kw = {}
+        if bias != 0.0:
+            kw["bias"] = ap(bias)
+            if func == AF.Copy:
+                func = AF.Identity
+        if scale != 1.0:
+            kw["scale"] = ap(scale)
+        if acc is not None:
+            kw["accum_out"] = ap(acc)
+            us += 0.02
+        emit("s", lambda: g.scalar.activation(ap(out), ap(in_), func, **kw), [in_, bias, scale], [out, acc], us)
 
     def mm(out, lhsT, rhs, start, stop):
-        emit("t", lambda: g.tensor.matmul(ap(out), ap(lhsT), ap(rhs), start, stop), [lhsT, rhs], [out], CY * max(64, size(out)) * (1 if two(lhsT) else 4))
+        emit("t", lambda: g.tensor.matmul(ap(out), ap(lhsT), ap(rhs), start, stop), [lhsT, rhs], [out],
+             CY * max(min(64, size(lhsT)), size(out)) * (1 if two(lhsT) else 4))
 
-    def iota(out, pattern, base, cm, small=False):
+    def iota(out, pattern, base, cm, after=None):
         us = 0.15 + 2 * CY * size(out)
-        if small:
-            emit("g", lambda: g.iota(ap(out), pattern, base, cm, allow_small_or_imprecise_dtypes=True), [], [out], us)
-        else:
+        if out[0] == "PI":
             emit("g", lambda: g.iota(ap(out), pattern, base, cm), [], [out], us)
+        else:
+            emit("g", lambda: g.iota(ap(out), pattern, base, cm, allow_small_or_imprecise_dtypes=True), [after], [out], us)
 
     def pick(out, in_, pattern, op, base, cm):
         emit("g", lambda: g.affine_select(ap(out), ap(in_), pattern, op, 0.0, base, cm), [in_], [out], 0.17 + 2 * CY * size(out))
 
     add, sub, mul, eq, ne = OP.add, OP.subtract, OP.mult, OP.is_equal, OP.not_equal
-    ge, gt, lt = OP.is_ge, OP.is_gt, OP.is_lt
+    ge, gt, lt, le = OP.is_ge, OP.is_gt, OP.is_lt, OP.is_le
+    SELW = 16 * KS
 
-    half = M // 2
-    dma("s", ("gnd", 0, M, T.gnd[:, 0:M]), ("gn", 0, M, T.gn[:]))
-    dma("s", ("gnd", W, Q * 3 + W, T.gnd[:, W:Q * 3 + W]), ("gn", 0, Q * 3, T.gn[:, 0:Q * 3]))
-    dma("y", v("SNI", 0, half), ("sn", 0, half, T.sn[:, 0:half]))
-    dma("y", v("SNI", half, M), ("sn", half, M, T.sn[:, half:M]))
-    dma("s", v("FGI", 0, M, p=(0, 8)), ("fa", 0, M, T.fa[:]))
-    dma("s", v("FGI", 0, M, p=(8, 16)), ("gn", 0, M, T.gn[:]))
-    dma("y", v("X", 0, M), ("x", 0, M, T.x[:]))
-    dma("y", v("WC"), ("w", 0, 1, T.w[:]))
+    C4 = M // 4
+    dma("s", v("GNI"), ("gn", 0, M, T.gn[:]), 2.5)
+    for j in range(4):
+        dma("y", v("SNI", j * C4, (j + 1) * C4), ("sn", j * C4, (j + 1) * C4, T.sn[:, j * C4:(j + 1) * C4]), 3.5 + j)
+    dma("s", v("FAI"), ("fa", 0, M, T.fa[:]), 2.5)
+    dma("y", v("X", 0, M), ("x", 0, M, T.x[:]), 8.0)
+    dma("s", v("WC"), ("w", 0, 1, T.w[:]), 3.0)
 
-    fill(v("PAD", 0, 16), 0)
-    fill(v("PAD", 16, 208), 2)
-    dma("s", ("gnd", M, W, T.gnd[:, M:W]), v("PAD", p=(0, 8)))
-    for t in range(T_):
-        dma("s", v("GTI", 122 * t, 122 * (t + 1)), ("gnd", Q * t, Q * t + W, T.gnd[:, Q * t:Q * t + W]))
-
+    R16 = v("R16")
+    DIAGB = v("k3", 0, L)
     iota(v("PI"), [[1, 1]], 0, 1)
     fill(v("ONES"), 1.0)
-    pick(v("TMPB"), v("ONES"), [[-16, 8], [0, 16]], ge, 0, 1)
+    fill(v("OF"), 1.0)
+    pick(v("TMPB"), v("ONES", 0, 128), [[-16, 8], [0, 16]], ge, 0, 1)
     pick(v("ONESB"), v("TMPB"), [[16, 8], [0, 16]], ge, 15, -1)
-    pick(v("TRI"), v("ONESB"), [[1, 128]], ge, -1, -1)
-    iota(v("RMOD"), [[0, 24], [1, 16]], 0, 0, True)
-    iota(v("POS"), [[1, 122]], 0, 0, True)
-    iota(v("D"), [[1, 122], [122, 16]], 0, 0, True)
+    iota(v("RMOD"), [[0, 24], [1, 16]], 0, 0)
     ts(v("PI2"), v("PI"), 15, OP.bitwise_and)
-    tc(v("R16"), v("PI2"))
+    tc(R16, v("PI2"))
+    ts(v("MK"), v("RMOD", 0, 16), R16, eq)
+    for m in range(16):
+        ts(v("PICK", 128 * m, 128 * (m + 1)), v("ONESB"), v("MK", m, m + 1), mul)
+    fill(v("SEL"), 0.0)
+    for s in range(16):
+        ts(v("SEL", s * 128 + s, (s + 1) * 128, 16), v("ONESB", s, 128, 16), SELW, mul)
+    pick(v("TRI"), v("ONESB"), [[1, 128]], ge, -1, -1)
+    pick(v("TIMO"), v("ONESB"), [[-1, 128]], ge, -1, 1)
+    ts(v("TIMO"), v("TIMO"), -1.0, mul)
+    fill(v("ZER"), 0.0)
+    fill(v("CT", NB, 128), 9999.0)
+    fill(v("OKB", RW, 128), 0.0)
+    iota(v("LANB"), [[16, 12]], 0, 0)
+    ts(v("LANB"), v("LANB"), R16, add, 0.5, add)
+    iota(v("LANE"), [[1, L]], 0, 0)
+    for i, base in enumerate((0, 16, -16)):
+        pick(v("I3", 128 * i, 128 * (i + 1)), v("OF"), [[-1, 128]], eq, base, 1)
+    ID = v("I3", 0, 128)
+    for nm, c in (("IDB", 1.0), ("NIDB", -1.0), ("IDK", float(BK)), ("NIDK", -float(BK)), ("ID16", 16.0), ("IDHALF", 0.5)):
+        act(v(nm), ID, scale=c)
+    act(v("OF"), ID, scale=-1.0)
+    NID = v("OF")
+    for t in range(T_):
+        a = Q * t // 16
+        iota(v("BT", 128 * t, 128 * t + NB - a), [[1, NB - a]], a, 0)
+        if a:
+            iota(v("BT", 128 * t + NB - a, 128 * t + NB), [[1, a]], 0, 0)
+        iota(v("BT", 128 * t + NB, 128 * t + 128), [[0, 128 - NB]], RW, 0)
+    iota(v("SN", M, WT), [[0, WT - M]], M, 0, v("I3"))
+    fill(v("SN", M + 1, M + 2), float(M + 2))
+
+    ts(v("RRS"), v("GNI"), 2, ge, float(M + 1), mul)
+    ts(v("RRS"), v("RRS"), -1.0, add)
+
+    def spread(src, j, k):
+        for m in range(4 * j, 4 * j + 4):
+            mm(v(k, (m % 4) * RW, (m % 4 + 1) * RW), v("PICK", 128 * m, 128 * (m + 1)), v(src), True, True)
+        return v(k, 0, C4)
+    for j in range(4):
+        tt(v("ANE", j * C4, (j + 1) * C4), v("SNI", j * C4, (j + 1) * C4), spread("RRS", j, ("k0", "k1")[j % 2]), ne)
+    for a, b in ((0, 54), (54, RW)):
+        for r in range(16):
+            mm(v("k6", a, b), v("SEL", 128 * r, 128 * (r + 1)), v("ANE", 16 * a + r, 16 * b, 16), r == 0, r == 15)
+    ts(v("OKB", 0, RW), v("k6", 0, RW), 0.0, eq)
+    tc(v("FAS"), v("FAI"))
+    tc(v("GNS"), v("GNI"))
+    for j in range(4):
+        act(v("F1", j * C4, (j + 1) * C4), spread("FAS", j, ("k2", "k5")[j % 2]))
+        tc(v("SN", j * C4, (j + 1) * C4), v("SNI", j * C4, (j + 1) * C4))
+    ts(v("DIAG"), v("RMOD", 0, L), R16, eq)
+    ts(DIAGB, v("RMOD", 0, L), R16, eq)
+    ts(v("RS0"), v("RMOD"), 0.0, ne)
+    ts(v("RST"), v("RMOD", 0, 64), 0.0, eq, float(2 ** 31), mul)
+    for f in ("F1", "F2"):
+        fill(v(f, M, 1760), float(M + 1))
+        fill(v(f, 1760, W + L), 0.0)
+    fill(v("X", M, WT), BIG)
     ts(v("PI2"), v("PI"), 4, OP.logical_shift_right, 1, OP.bitwise_and)
     tc(v("PBF", 1, 2), v("PI2"))
     ts(v("PBF", 0, 1), v("PBF", 1, 2), -1.0, mul, 1.0, add)
-    R16 = v("R16")
-    POSB, CQB, DIAGB = v("k4", 256, 378), v("k4", 384, 506), v("k3", 256, 448)
-    ts(v("R122"), R16, 122.0, mul)
-    ts(POSB, v("POS"), v("R122"), add)
-    ts(CQB, POSB, -1.0, mul, float(HWN), add)
-    fill(v("ZER"), 0.0)
-    fill(v("SEL"), 0.0)
-    for s in range(16):
-        ts(v("SEL", s * 128 + s, (s + 1) * 128, 16), v("ONESB", s, 128, 16), 16.0, mul)
-    fill(v("SN", M, 1760), float(M))
-    fill(v("SN", 1760, W), 0.0)
-    fill(v("SN", W, WT), float(M))
-    tc(v("SN", 0, half), v("SNI", 0, half))
-    tc(v("SN", half, M), v("SNI", half, M))
-    ts(v("GTH"), v("GTI"), 2, ge, -1.0, add)
-    iota(v("SLR"), [[0, 8], [1, 16]], 0, 0, True)
-    fill(v("OF"), 1.0)
-    for i, base in enumerate((0, 16, -16)):
-        pick(v("I3", 128 * i, 128 * (i + 1)), v("OF"), [[-1, 128]], eq, base, 1)
-    fill(v("G2K"), 2048.0)
-    pick(v("LG", p=(0, 16)), v("G2K", p=(0, 16)), [[1, 8], [0, 16]], eq, 8, -1)
-    pick(v("LFF", p=(0, 16)), v("OF", p=(0, 16)), [[1, 8], [0, 16]], eq, 0, -1)
-    iota(v("TRL"), [[16, 12]], L, 0, True)
-    iota(v("TR4"), [[0, 4], [16, 12]], TB, 0, True)
-    iota(v("LKI"), [[1, 64]], 0, 0)
-    iota(v("COLC"), [[1, 64]], 1760, 0, True)
-    iota(v("VH8", p=(0, 1)), [[8, W // 8], [0, 8]], 0, 0, True)
-    iota(v("VL8", p=(0, 1)), [[0, W // 8], [1, 8]], 0, 0, True)
+    for e in range(2):
+        for y in range(2):
+            i = 0 if e == y else 1 if y else 2
+            ts(v("SWH", 128 * (2 * e + y), 128 * (2 * e + y + 1)), v("I3", 128 * i, 128 * (i + 1)), v("PBF", e, e + 1), mul)
+    iota(v("SLR", p=(0, 1)), [[0, 8], [int(KS), 16]], 0, 0)
+    iota(v("REP", p=(0, 64)), [[-1, 64], [0, 16]], 0, 1, v("I3"))
+    ts(v("REP", p=(0, 64)), v("REP", p=(0, 64)), 0.0, eq)
+    act(v("NONESB"), v("ONESB"), scale=-1.0)
+    iota(v("TRL"), [[16, 12]], L, 0)
+    iota(v("TR4"), [[0, 4], [16, 12]], TB, 0)
+    iota(v("CT3"), [[1, 192]], 1760, 0)
+    ts(v("TRL"), v("TRL"), R16, add)
+    ts(v("NTRL"), v("TRL"), -1.0, mul)
+    ts(v("TR4"), v("TR4"), R16, add)
+    ts(v("TRM"), v("TR4", 0, 12), -PO, add)
+    ts(v("TRN"), v("TR4", 0, 12), 1 - PO, add)
+    tc(v("IDH"), ID)
+    for j in range(4):
+        act(v("GN", j * C4, (j + 1) * C4), spread("GNS", j, ("k2", "k5")[j % 2]))
+    fill(v("GN", M, W), 0.0)
+    act(v("F2", 0, M), v("F1", 0, M))
+    fill(v("RM"), 0.0)
+    ts(v("D15"), v("DIAG"), -998.5, mul, 1000.0, add)
+    ts(v("DTH"), v("DIAG", 0, S), -745.0, mul, 1000.0, add)
+    ts(v("M0"), R16, 0.0, eq)
+    ts(v("E0"), R16, 0.0, ne, float(M), mul)
+    for t in range(1, 3):
+        ts(v("MTC", t, t + 1), R16, float(t), eq)
+        ts(v("MTC", 4 + t, 5 + t), R16, float(t), ne)
+        ts(v("CT3", S * (t - 1), S * t), v("CT3", S * (t - 1), S * t), v("MTC", t, t + 1), mul)
+    tc(v("ONESH"), v("ONESB"))
+    fill(v("POR", p=(0, 1)), PO)
+    fill(v("ONR", p=(0, 1)), 1.0)
+    fill(v("QRT", p=(0, 1)), -0.25)
+    tt(v("TRMO"), v("TRI"), v("ONESB"), sub)
+    ts(v("WSEL"), v("SEL"), v("WC"), mul, 1.0 / SELW, mul)
+    ts(v("BS0"), v("RMOD"), 1.0, sub, R16, eq)
+    ts(v("BS0"), v("BS0"), PO, mul)
+    fill(v("RS3"), 1.0)
+    fill(v("RS3", 0, 12, 3), 0.0)
 
-    def constants_late():
-        tc(v("FGF", p=(0, 16)), v("FGI", p=(0, 16)))
-        tc(v("LF", p=(0, 16)), v("LFF", p=(0, 16)))
-        ts(v("DIAG"), v("RMOD", 0, L), R16, eq)
-        ts(DIAGB, v("RMOD", 0, L), R16, eq)
-        ts(v("RS0"), v("RMOD"), 0.0, ne)
-        ts(v("RST"), v("RMOD", 0, 96), 0.0, eq, float(2 ** 20), mul)
-        fill(v("F1", M, 1760), float(M))
-        fill(v("F1", 1760, W + L), 0.0)
-        fill(v("F2", M, 1760), float(M))
-        fill(v("F2", 1760, W + L), 0.0)
-        fill(v("GH", M, W), 0.0)
-        fill(v("X", M, WT), BIG)
-        fill(v("X", 1760, W), 0.0)
-        w = M // 4
-        for j in range(4):
-            a, b = j * w, (j + 1) * w
-            k = "k%d" % (2 * (j % 2))
-            mm(v(k, 0, w), v("LF", p=(0, 16)), v("FGF", a, b, p=(0, 16)), True, True)
-            act(v("F1", a, b), v(k, 0, w))
-        for e in range(2):
-            for y in range(2):
-                i = 0 if e == y else 1 if y else 2
-                ts(v("SW", 128 * (2 * e + y), 128 * (2 * e + y + 1)), v("I3", 128 * i, 128 * (i + 1)), v("PBF", e, e + 1), mul)
-        tc(v("SWH"), v("SW"))
-        act(v("IDB"), v("I3", 0, 128))
-        act(v("NIDB"), v("I3", 0, 128), scale=-1.0)
-        act(v("IDK"), v("I3", 0, 128), scale=float(BK))
-        act(v("NIDK"), v("I3", 0, 128), scale=-float(BK))
-        tc(v("IDH"), v("I3", 0, 128))
-        ts(v("NIDH"), v("I3", 0, 128), -1.0, mul)
-        ts(v("TRL"), v("TRL"), R16, add)
-        ts(v("TR4"), v("TR4"), R16, add)
-        yield
-
-    def constants_last():
-        tc(v("FGB", p=(0, 16)), v("FGI", p=(0, 16)))
-        tc(v("LGB", p=(0, 16)), v("LG", p=(0, 16)))
-        act(v("F2", 0, M), v("F1", 0, M))
-        w = M // 4
-        for j in range(4):
-            a, b = j * w, (j + 1) * w
-            k = "k2"
-            mm(v(k, 0, w), v("LGB", p=(0, 16)), v("FGB", a, b, p=(0, 16)), True, False)
-            mm(v(k, 0, w), v("ONES", p=(0, 1)), v("VH8", a, b, p=(0, 1)), False, False)
-            mm(v(k, 0, w), v("ONES", p=(0, 1)), v("VL8", a, b, p=(0, 1)), False, True)
-            act(v("GH", a, b), v(k, 0, w))
-        ts(v("LTM"), v("RMOD"), R16, gt)
-        ts(v("D15"), v("DIAG"), -998.5, mul, 1000.0, add)
-        ts(v("M0"), R16, 0.0, eq)
-        ts(v("E0"), R16, 0.0, ne, float(M + 1), mul)
-        ts(v("E0"), v("E0"), -1.0, add)
-        for t in range(1, 4):
-            ts(v("MTC", t, t + 1), R16, float(t), eq)
-            ts(v("MTC", 4 + t, 5 + t), R16, float(t), ne)
-        tc(v("ONESH"), v("ONESB"))
-        tt(v("TRMO"), v("TRI"), v("ONESB"), sub)
-        ts(v("WSEL"), v("SEL"), v("WC"), mul, 0.0625, mul)
-        fill(v("BS0"), 0.0)
-        fill(v("BSA"), 0.0)
-        tc(v("LK"), v("LKI"))
-        yield
-
-    def narrow(src, n, tmp="TMP", res="RW"):
-        tt(v(tmp, 0, n), src, v("DIAG", 0, n) if src[0] in BANKS else v("k3", 256, 256 + n), mul)
-        scan(v(res, 0, n), v("RS0", 0, n), v(tmp, 0, n), mul, add)
+    def listed(res, masked):
+        n = size(masked)
+        scan(v(res, 0, n), v("RS0", 0, n), masked, mul, add)
         return v(res, 15, n, 16)
 
-    def lanes1(t):
-        c = W // 4
-        st = Q * t
-        segs = [(a, a + c) for a in range(0, W, c)]
-        k0 = st // c
-        fill(v("HWIN", 0, L), float(M))
-        for a, b in segs[k0:] + segs[:k0]:
-            act(v("ANE", a, b), v("SN", a, b), AF.Abs, -float(M))
-        for m in range(16):
-            a = st + 122 * m
-            parts = [(a, a + 122)] if a + 122 <= W or a >= W else [(a, W), (W, a + 122)]
-            for x, y in parts:
-                mm(v("k6", x - a, y - a), v("SEL", 128 * m, 128 * (m + 1)), v("ANE", x % W, x % W + y - x), m == 0, m == 15)
-        tt(v("NOK"), v("k6", 0, 122), v("GTH", 122 * t, 122 * (t + 1)), gt)
-        scan(v("NINC"), v("NOK"), v("ZER"), add, add)
-        mm(v("k7", 0, 1), v("TRI"), v("NINC", 121, 122), True, True)
-        tt(v("C1"), v("NOK"), CQB, mul)
-        tt(v("k3", 0, 122), v("C1"), POSB, add)
-        tt(v("C1"), v("k3", 0, 122), v("NINC"), sub)
-        ts(v("OFF16"), v("C1"), v("k7", 0, 1), sub)
-        tc(at(v("HWIN"), v("OFF16")), v("D"))
-        if t < 3:
-            iota(v("D"), [[1, 122], [122, 16]], Q * (t + 1), 0, True)
-        yield
+    def numbers(tag, src):
+        k = BANK[tag][0]
+        mm(v(k, 128, 256, p=(0, 64)), src, v("IDB"), True, True)
+        act(v("XT" + tag, p=(0, 64)), v(k, 128, 256, p=(0, 64)))
+        for a in range(0, 16 * NV[tag], 384):
+            b = min(a + 384, 16 * NV[tag])
+            mm(v(k, 128, 128 + b - a), v("XT" + tag, p=(0, 64)), v("REP", a, b, p=(0, 64)), True, True)
+            act(v("XR" + tag, a, b), v(k, 128, 128 + b - a))
 
-    def lanes2(t):
+    def lanes(t):
+        ok = v("OKB", 0, NB)
         if t:
-            ts(v("k4", 0, L), v("HWIN", 0, L), float(W), ge, -float(W), mul)
-            tt(v("H"), v("k4", 0, L), v("HWIN", 0, L), add)
-        else:
-            tc(v("H"), v("HWIN", 0, L))
-        F = "F1" if t % 2 == 0 else "F2"
+            a = Q * t // 16
+            for r in range(16):
+                mm(v("k6", 0, NB), v("SEL", 128 * r, 128 * (r + 1)), v("RM", r, W, 16), r == 0, r == 15)
+            tt(v("OK", 0, NB - a), v("OKB", a, NB), v("k6", a, NB), gt)
+            tt(v("OK", NB - a, NB), v("OKB", 0, a), v("k6", 0, a), gt)
+            ok = v("OK", 0, NB)
+        mm(v("k6", 128, 128 + NB), v("ONESB"), ok, True, True)
+        mm(v("k6", 256, 256 + NB), v("TIMO"), ok, True, True)
+        scan(v("CB", 0, NB), v("k6", 128, 128 + NB), v("ZER", 0, NB), add, add)
+        tt(v("CT", 0, NB), v("k6", 256, 256 + NB), v("CB", 0, NB), add)
+        for q in range(12):
+            act(v("JK", 128 * q, 128 * q + NB), v("CB", 0, NB), AF.Sign, v("LANB", q, q + 1), -1.0, v("NBS", q, q + 1))
+        ts(v("BL"), v("NBS"), 0.5, mul, NB / 2, add)
+        tt(v("FLG"), at(v("CT"), v("BL")), v("LANE"), le)
+        act(v("BR"), at(v("BT", 128 * t, 128 * t + 128), v("BL")))
+        HP = v("k6", 0, L)
+        mm(HP, v("ID16"), v("BR"), True, False)
+        mm(HP, v("ONESB"), v("FLG"), False, True)
+        tt(v("TMP"), HP, v("DIAG"), mul)
+        act(v("H"), HP)
+        hw = listed("RWH", v("TMP"))
+        tc(v("HL"), hw)
+        F = v("F1" if t % 2 == 0 else "F2", 0, W)
         tab = v("SN")
-        r = narrow(v("H"), L)
-        tc(v("HL"), r)
-        tc(v("P0"), at(v(F, 0, W), v("HL")))
-        tc(v("H16"), v("H"))
-        act(v("HW12"), r)
-        act(v("XR", 0, 1536), at(v("X"), v("H16", 0, 96)))
-        act(v("XR", 1536, 3072), at(v("X"), v("H16", 96, 192)))
-        r = narrow(v("P0"), L)
-        tc(v("P0L"), r)
-        act(v("P0W"), r)
-        tc(v("S0"), at(tab, v("P0L")))
-        tc(v("P1"), at(v(F, 0, W), v("P0L")))
-        tt(v("EQ0"), v("S0"), v("H"), eq)
-        ts(v("EM0"), v("S0"), float(M), eq)
-        mm(v("k6", 0, L), v("ONESB"), v("EQ0"), True, False)
-        mm(v("k6", 0, L), v("ONESB"), v("EM0"), False, True)
-        W0, WD = v("k6", 256, 448), v("k7", 256, 448)
-        mm(W0, v("IDH"), v("S0"), True, False)
+        tt(v("TMP"), at(F, v("HL")), v("DIAG"), mul)
+        act(v("XL"), at(v("X"), v("HL")))
+        act(v("P0"), at(F, v("HL")))
+        pw = listed("RWP", v("TMP"))
+        tc(v("P0L"), pw)
+        for h in range(3):
+            numbers("A%d" % h, v("XL", 64 * h, 64 * h + 64))
+        tt(v("TMP"), at(F, v("P0L")), v("DIAG"), mul)
+        tc(v("P1L"), listed("RWQ", v("TMP")))
+        tt(v("EQ0"), at(tab, v("P0L")), v("H"), eq)
+        act(v("S0"), at(tab, v("P0L")))
+        act(v("A0N"), v("S0"), AF.Abs, -float(M))
+        act(v("NE0"), v("A0N"), AF.Sign)
+        KK, W0, WD = v("k6", 256, 448), v("k5", 0, L), v("k5", 256, 448)
+        mm(KK, v("ONESB"), v("EQ0"), True, False)
+        mm(KK, v("NONESB"), v("NE0"), False, True)
+        act(v("UR"), KK, AF.Relu, 1.0)
+        mm(W0, ID, v("S0"), True, False)
         mm(W0, v("IDK"), v("EQ0"), False, True)
-        mm(WD, v("NIDH"), v("S0"), True, False)
+        mm(WD, NID, v("S0"), True, False)
         mm(WD, v("NIDK"), v("EQ0"), False, False)
-        r = narrow(v("P1"), L)
-        tc(v("P1L"), r)
-        tc(v("S1"), at(tab, v("P1L")))
-        mm(WD, v("IDH"), v("S1"), False, False)
-        ts(v("UR"), v("k6", 0, L), 16.0, ge)
-        tt(v("EQ1"), v("S1"), v("P0"), eq)
+        act(v("S1"), at(tab, v("P1L")))
+        tt(v("EQ1"), at(tab, v("P1L")), v("P0"), eq)
+        mm(WD, ID, v("S1"), False, False)
         mm(WD, v("IDK"), v("EQ1"), False, True)
         tt(v("UD"), WD, v("UR"), mul)
         tt(v("SA"), W0, v("UD"), add)
         tc(v("SA16"), v("SA"))
-        yield
-
-    def own_flags(t):
-        act(v("XL"), at(v("X"), v("HL")))
         for r in range(16):
             mm(v("k6", 448, 460), v("SEL", 128 * r, 128 * (r + 1)), v("UR", r, L, 16), r == 0, r == 15)
+        act(v("U"), v("k6", 448, 460), scale=1.0 / (16 * SELW))
+        act(v("NU"), v("U"), AF.Identity, 1.0, -1.0)
+        ts(v("CA"), pw, 64.0, ge)
+        tt(v("UP"), v("CA"), v("U"), mul)
+        act(v("CA"), v("U"), scale=M - PO)
+        act(v("CC"), v("UP"), scale=float(M))
+        tt(v("CC"), v("CA"), v("CC"), sub)
+        tt(v("Z5", 0, 12), hw, v("TR4", 0, 12), sub)
         if t < 3:
-            act(v("HG"), at(v("GH"), v("HL")))
-        act(v("U2", 0, 12), v("k6", 448, 460), scale=1.0 / 256)
-        act(v("U2", 12, 24), v("k6", 448, 460), scale=1.0 / 256)
-        ts(v("ND"), v("P0W"), 64.0, lt)
-        tt(v("ND"), v("ND"), v("U2", 0, 12), mul)
-        ts(v("ND"), v("ND"), -1.0, mul, 1.0, add)
-        act(v("Z4", 0, 12), v("HW12"))
-        if t < 3:
-            ts(v("LOF"), v("HW12"), float(M), ne)
-            fill(v("ms%d" % t, 0, 384), 0.0)
-            fill(v("HGS%d" % t, 0, 384), 0.0)
-        yield
+            ts(v("LOF"), hw, float(M), ne)
+            tt(v("HZ"), v("Z5", 0, 12), v("LOF"), mul)
+            tt(v("HZ"), v("HZ"), v("TR4", 0, 12), add)
+            tc(v("HLT"), v("HZ"))
+            fill(v("HR%d" % t, 0, 384), float(M))
 
-    def down(tag, nq, idx, son, offl, xr, u, u0, lst, keep=None):
-        n = nq * 16
-        kb, vb, vo = {"A0": ("k0", "k3", 0), "A1": ("k1", "k3", 128), "A2": ("k7", "k4", 0), "AB": ("k2", "k5", 0)}[tag]
-        nv = NV[tag]
-        if nv < n:
-            us, dif = v(u, u0 + 16 * nv, u0 + 16 * n), v(kb, 128, 128 + 16 * (n - nv))
-            act(us, at(v("X"), v(idx, offl + nv, offl + n)))
-            mm(dif, v("NIDB"), v(xr, u0 + 16 * nv, u0 + 16 * n), True, False)
-            mm(dif, v("IDB"), us, False, True)
-        ux = v(u, u0, u0 + 16 * nv)
-        tt(ux, at(v("X"), v(idx, offl, offl + nv)), v(xr, u0, u0 + 16 * nv), sub)
-        if nv < n:
+    def down(tag, idx, son):
+        n, nv, kb = 64, NV[tag], BANK[tag][0]
+        u, xr = "UU" + tag, "XR" + tag
+        a, difs = nv, []
+        for k in BANK[tag]:
+            o = 128 if k == kb else 0
+            b = min(n, a + (512 - o) // 16)
+            if a < b:
+                us, dif = v(u, 16 * a, 16 * b), v(k, o, o + 16 * (b - a))
+                mm(dif, v("XT" + tag, p=(0, 64)), v("REP", 16 * a, 16 * b, p=(0, 64)), True, False)
+                act(us, at(v("X"), idx(a, b)))
+                mm(dif, v("NIDB"), us, False, True)
+                difs.append((us, dif))
+            a = b
+        if nv:
+            ux = v(u, 0, 16 * nv)
+            tt(ux, at(v("X"), idx(0, nv)), v(xr, 0, 16 * nv), sub)
+            act(ux, ux, AF.Abs)
+        for us, dif in difs:
             act(us, dif, AF.Abs)
-        act(ux, ux, AF.Abs)
+        mm(v(kb, 0, n), v("SLR", p=(0, 1)), v("ONES", 0, n, p=(0, 1)), True, False)
         for s in range(16):
-            mm(v(kb, 0, n), v("SEL", 128 * s, 128 * (s + 1)), v(u, u0 + s, u0 + 16 * n, 16), s == 0, False)
-        mm(v(kb, 0, n), v("SLR", p=(0, 1)), v("ONES", 0, n, p=(0, 1)), False, True)
-        SP, KP = v(vb, vo, vo + n), v(vb, vo + n, vo + 2 * n)
+            mm(v(kb, 0, n), v("SEL", 128 * s, 128 * (s + 1)), v(u, s, 16 * n, 16), False, s == 15)
+        vo = 128 * PARTS.index(tag)
+        SP, KP = v("k4", vo, vo + n), v("k4", vo + n, vo + 2 * n)
         turn(SP, son)
         turn(KP, v(kb, 0, n))
-        im, ni, zz, rr = [v(x + tag, 0, n) for x in ("IM", "NI", "ZZ", "RR")]
-        mm_ = v("MM" + tag, 0, n) if keep is None else v("MKEEP", keep, keep + n)
-        scan(mm_, v("RST", 0, n), KP, add, OP.min, float(2 ** 20))
-        tt(im, mm_, KP, eq)
-        tt(ni, mm_, KP, ne)
-        tt(zz, im, SP, mul)
-        scan(rr, ni, zz, mul, add)
+        low, dd, ee, rr = [v(x + tag) for x in ("MM", "DD", "EE", "RR")]
+        scan(low, v("RST"), KP, add, OP.min, float(2 ** 31))
+        tt(dd, KP, low, sub)
+        tt(ee, SP, dd, sub)
+        scan(rr, dd, ee, OP.min, OP.max)
         for e in range(2):
             for y in range(2):
-                mm(v(kb, 64 + e, 64 + nq, 2), v("SWH", 128 * (2 * e + y), 128 * (2 * e + y + 1)), v("RR" + tag, 15 + 16 * y, n, 32), y == 0, y == 1)
-        lst(v(kb, 64, 64 + nq))
+                mm(v(kb, 64 + e, 68, 2), v("SWH", 128 * (2 * e + y), 128 * (2 * e + y + 1)), v("RR" + tag, 15 + 16 * y, n, 32), y == 0, y == 1)
+        return v(kb, 64, 68)
 
-    def own(h):
-        tag, o, lo = "A%d" % h, 4 * h, 64 * h
+    def step(tag):
+        tc(v("IX" + tag), at(v("SN"), v("LL" + tag)))
+        act(v("SF" + tag), at(v("SN"), v("LL" + tag)))
+        return down(tag, lambda a, b: v("IX" + tag, a, b), v("SF" + tag))
 
-        def after(step, name):
-            def f(x):
-                if step < 2:
-                    tc(v(name, o, o + 4), x)
-                act(v("WALL", 12 * step + o, 12 * step + o + 4), x)
-            return f
-        down(tag, 4, "SA16", v("SA", lo, lo + 64), lo, "XR", "UA", 16 * lo, after(0, "LA"))
-        for step, prev, name in ((1, "LA", "LB"), (2, "LB", "")):
-            tc(v("S16A", lo, lo + 64), at(v("SN"), v(prev, o, o + 4)))
-            act(v("SF" + tag), at(v("SN"), v(prev, o, o + 4)))
-            down(tag, 4, "S16A", v("SF" + tag), lo, "XR", "UA", 16 * lo, after(step, name), keep=192 * (step - 1) + lo)
-        yield
+    def own():
+        for h in range(3):
+            tag, o, lo = "A%d" % h, 4 * h, 64 * h
+            x = down(tag, lambda a, b: v("SA16", lo + a, lo + b), v("SA", lo, lo + 64))
+            tc(v("LL" + tag), x)
+            act(v("W1", o, o + 4), x, bias=-PO)
+            x = step(tag)
+            tc(v("LL" + tag), x)
+            act(v("W2", o, o + 4), x, bias=-PO)
+        tt(v("D1"), v("W2"), v("W1"), sub)
+        tt(v("D1"), v("D1"), v("U"), mul)
+        tt(v("D1"), v("D1"), v("W1"), add)
+        ts(v("YP"), v("D1"), 1.0, add)
+        tt(v("BASE"), v("W2"), v("NU"), mul)
+        tt(v("BASE"), v("BASE"), v("CC"), add)
+        for h in range(3):
+            o = 4 * h
+            x = step("A%d" % h)
+            tt(v("T1", o, o + 4), x, v("UP", o, o + 4), mul)
+            tt(v("BS0", L + 16 * o, L + 16 * o + 64, 16), v("T1", o, o + 4), v("BASE", o, o + 4), add)
 
     def arrivals(t):
         ls = "ls%d" % (t - 1)
         for r in range(16):
             mm(v("k2", 0, 4), v("WSEL", 128 * r, 128 * (r + 1)), v(ls, r, S, 16), r == 0, r == 15)
-        act(v("XRB"), at(v(ls, 0, S), v("LK")))
         tc(v("CI"), v("k2", 0, 4))
+        numbers("AB", v(ls, 0, S))
         for d in range(3):
-            ts(v("GENM", 4 * d, 4 * d + 4), v(ls, S, SW_), float(d + 2), eq)
+            ts(v("GENM", d, 12, 3), v(ls, S, SW_), float(d + 2), eq)
         ts(v("CI2"), v("CI"), 63, OP.bitwise_and)
-        tc(v("BL"), v("CI2"))
+        tc(v("LLAB"), v("CI2"))
         for e in range(4):
-            tc(v("S16B"), at(v("SN"), v("BL")))
-            act(v("SFAB"), at(v("SN"), v("BL")))
-
-            def f(x):
-                if e < 3:
-                    tc(v("BL"), x)
-                if e:
-                    act(v("LB3", 4 * (e - 1), 4 * e), x)
-            down("AB", 4, "S16B", v("SFAB"), 0, "XRB", "UB", 0, f)
-        ts(v("LBT"), v("LB3"), -float(M), add)
-        tt(v("LB3"), v("LBT"), v("GENM"), mul)
-        tt(v("LBT", 0, 4), v("LB3", 0, 4), v("LB3", 4, 8), add)
-        tt(v("LBT", 4, 8), v("LBT", 0, 4), v("LB3", 8, 12), add)
-        ts(v("BF16"), v("LBT", 4, 8), float(M), add)
-        tc(v("mr%d" % t), at(v("X"), v("BF16")))
+            x = step("AB")
+            if e < 3:
+                tc(v("LLAB"), x)
+            if e:
+                act(v("LB3", e - 1, 12, 3), x, bias=-float(M))
+        tt(v("LBT"), v("LB3"), v("GENM"), mul)
+        scan(v("LB3"), v("RS3"), v("LBT"), mul, add)
+        ts(v("BF16"), v("LB3", 2, 12, 3), float(M), add)
+        act(v("mr%d" % t), at(v("X"), v("BF16")))
         ship("r", t, v("mr%d" % t))
-        yield
 
     sent = [0]
 
@@ -596,205 +656,146 @@ def rank_program(g, core, T, topo):
             else:
                 send(g, topo, core, mid, T["b" + k][:], src[3], T.sem["x" + k], T.sem.lo)
             sent[0] += NENG
-            when[("a" + k, NENG)] = free["g"] + 10.0
-        emit("g", call, [src], [], 1.0)
-
-    def found(t):
-        tt(v("D1"), v("WALL", 12, 36), v("WALL", 0, 24), sub)
-        tt(v("YT"), v("D1"), v("U2"), mul)
-        tt(v("YS"), v("YT"), v("WALL", 0, 24), add)
-        ts(v("YT", 0, 12), v("YS", 12, 24), float(M), ne)
-        tt(v("FND", 0, 12), v("YT", 0, 12), v("ND"), mul)
-        tt(v("FND", 12, 24), v("YT", 0, 12), v("ND"), mul)
-        if t < 3:
-            tt(v("LOF"), v("LOF"), v("FND", 0, 12), sub)
-            act(v("LO"), v("LOF"))
-            mm(v("k0", 256, 268), v("ONESB"), v("LO"), True, True)
-            mm(v("k0", 272, 284), v("TRMO"), v("LO"), True, True)
-        yield
+        emit("g", call, [src], [v("l" + k)], 1.0, "r", 14.0 if k == "s0" else 9.0)
 
     def adopt(t):
-        ts(v("D1"), v("YS"), 1.0, add)
-        tc(v("YL"), v("YS", 0, 12))
-        tt(v("BS0", 0, 384, 16), v("D1"), v("FND"), mul)
-        tc(v("SL"), v("YS", 12, 24))
+        sp, yp = v("BS0", L, 384, 16), v("BS0", 0, L, 16)
+        ts(v("NF"), sp, M - PO, ne, -2 * PO, mul)
+        tt(yp, v("YP"), v("NF"), OP.max)
         scan(v("SCB"), v("RS0"), v("BS0"), mul, add)
-        tt(v("DX", 0, L), v("SCB", 0, L), DIAGB, mul)
-        mm(v("k7", 0, L), v("ONESH"), v("DX", 0, L), True, True)
-        tt(v("DX", L, 384), v("SCB", L, 384), DIAGB, mul)
-        mm(v("k7", L, 384), v("ONESH"), v("DX", L, 384), True, True)
-        tc(v("SY"), at(v("SN"), v("YL")))
-        act(v("Z4", 12, 24), v("YS", 12, 24))
-        act(v("Z4", 24, 36), v("YS", 0, 12))
-        act(v("Z4", 36, 48), v("YS", 12, 24))
-        ts(v("EMY"), v("SY"), float(M), ne)
-        mm(v("k1", 0, L), v("ONESB"), v("EMY"), True, True)
-        tt(v("Z5"), v("Z4"), v("TR4"), sub)
-        act(v("SROW"), v("k7", L, 384))
+        ts(v("SL"), sp, PO, add)
+        YROW, SROW, CNT = v("k7", 0, L), v("k1", 0, L), v("k6", 0, L)
+        for o, row in ((0, YROW), (L, SROW)):
+            mm(row, v("POR", p=(0, 1)), v("ONR", 0, L, p=(0, 1)), True, False)
+            tt(v("DX", o, o + L), v("SCB", o, o + L), DIAGB, mul)
+            mm(row, v("ONESH"), v("DX", o, o + L), False, True)
+            tc(v("YR", o, o + L), row)
+            tt(v("ED", o, o + L), v("SCB", o, o + L), row, eq)
+        act(v("NFR"), YROW, AF.Relu, 1.0 - PO)
+        mm(CNT, v("ONESB"), v("NFR"), True, False)
+        mm(CNT, v("ONESB"), v("ED", 0, L), False, False)
+        mm(CNT, v("ONESB"), v("ED", L, 384), False, False)
         o = 0
-        for q in range(11):
-            n = (11 - q) * 16
-            act(v("EZ", o, o + n), v("SROW", L - n, L), AF.Abs, bias=v("BS0", L + 16 * q, L + 16 * q + 1), scale=-1.0)
-            o += n
-        act(v("EC"), v("EZ"), AF.Relu, bias=1.0, scale=-1.0)
-        tc(v("YR16", 0, L), v("k7", 0, L))
-        tt(v("k5", 128, 512), v("SCB"), v("k7", 0, 384), eq)
-        tt(v("EDM"), v("k5", 128, 512), v("LTM"), mul)
-        mm(v("k6", 0, L), v("ONESB"), v("EDM", 0, L), True, False)
-        mm(v("k6", 0, L), v("ONESB"), v("EDM", L, 384), False, False)
-        o = 0
-        for q in range(11):
-            n = (11 - q) * 16
-            ts(v("EE", o, o + n), v("YR16", L - n, L), v("BS0", 16 * q, 16 * q + 1), eq)
-            mm(v("k6", L - n, L), v("ONESB"), v("EE", o, o + n), False, False)
-            o += n
-        o = 0
-        for q in range(11):
-            n = (11 - q) * 16
-            mm(v("k6", L - n, L), v("ONESB"), v("EC", o, o + n), False, q == 10)
-            o += n
-        tt(v("SR"), v("D15"), v("k1", 0, L), lt)
-        scan(v("SRS"), v("RS0", 0, L), v("SR"), mul, add)
-        tt(v("FR"), v("DIAG"), v("k6", 0, L), gt)
-        scan(v("FRS"), v("RS0", 0, L), v("FR"), mul, add)
-        tt(v("FL4", 0, 12), v("FRS", 15, L, 16), v("FND", 0, 12), mul)
-        tt(v("FL4", 12, 24), v("FRS", 15, L, 16), v("FND", 0, 12), mul)
-        tt(v("FL4", 24, 36), v("SRS", 15, L, 16), v("FL4", 0, 12), mul)
-        tt(v("FL4", 36, 48), v("SRS", 15, L, 16), v("FL4", 0, 12), mul)
-        tt(v("Z4"), v("Z5"), v("FL4"), mul)
-        tt(v("Z5"), v("Z4"), v("TR4"), add)
-        tc(v("L4"), v("Z5"))
-        yield
-
-    def slots(t):
-        for e in range(2):
-            for y in range(2):
-                mm(v("k2", 256 + e, 280, 2), v("SW", 128 * (2 * e + y), 128 * (2 * e + y + 1)), v("MKEEP", 15 + 16 * y, 384, 32), y == 0, y == 1)
-        act(v("KALL"), v("k2", 256, 280))
-        tt(v("KF"), v("KALL", 12, 24), v("KALL", 0, 12), sub)
-        tt(v("AW"), v("KF"), v("U2", 0, 12), mul)
-        tt(v("KF"), v("AW"), v("KALL", 0, 12), add)
-        tc(v("KI"), v("KF"))
-        ts(v("KI2"), v("KI"), 15, OP.bitwise_and)
-        tc(v("BSA", 0, L, 16), v("KI2"))
-        scan(v("k4", 0, L), v("RS0", 0, L), v("BSA"), mul, add)
-        tt(v("AX"), v("k4", 0, L), v("DIAG"), mul)
-        mm(v("k0", 0, L), v("ONESB"), v("AX"), True, True)
-        yield
-
-    def change_sons(t):
-        ts(v("VH"), v("k7", L, 384), v("M0"), mul, v("E0"), add)
-        ts(v("DD"), v("SY"), -1.0, mul, float(M), add)
-        ts(v("k1", 0, L), v("k0", 0, L), R16, eq)
-        tc(at(v("SN", 0, W + L), v("L4", 0, 12)), v("VH"))
-        tt(v("k3", 0, L), v("DD"), v("k1", 0, L), mul)
-        tt(v("VY"), v("k3", 0, L), v("SY"), add)
-        tc(at(v("SN", 0, W + L), v("L4", 24, 36)), v("VY"))
-        yield
+        for lo in (0, L):
+            for q in range(11):
+                n = (11 - q) * 16
+                ts(v("EQ", o, o + n), v("YR", lo + L - n, lo + L), PO, sub, v("BS0", lo + 16 * q, lo + 16 * q + 1), eq)
+                mm(v("k6", L - n, L), v("ONESB"), v("EQ", o, o + n), False, lo == L and q == 10)
+                o += n
+        act(v("XS"), at(v("X"), v("SL")))
+        XG = v("k0", 0, L)
+        mm(XG, v("QRT", p=(0, 1)), v("ONES", 0, L, p=(0, 1)), True, False)
+        mm(XG, v("IDHALF"), v("XL"), False, False)
+        mm(XG, v("IDHALF"), v("XS"), False, True)
+        tc(v("XI"), XG)
+        ts(v("YL"), yp, PO - 1, add)
+        act(v("SY"), at(v("SN"), v("YL")))
+        act(v("AY"), v("SY"), AF.Abs, -float(M))
+        act(v("EMY"), v("AY"), AF.Sign)
+        mm(v("k0", 256, 448), v("ONESB"), v("EMY"), True, True)
+        tt(v("SR"), v("D15"), v("k0", 256, 448), lt)
+        sev = listed("SRS", v("SR"))
+        tt(v("Z5", 12, 24), sp, v("TRM"), sub)
+        tt(v("Z5", 36, 48), v("Z5", 12, 24), sev, mul)
+        if t < 3:
+            tt(v("ZT", 0, 12), yp, v("TRN"), sub)
+            tt(v("Z5", 24, 36), v("ZT", 0, 12), sev, mul)
+            act(v("GO"), CNT, AF.Relu, 1.0, -1.0)
+            tc(at(v("RM"), v("HLT")), v("GO"))
+            tt(v("EQS"), at(v("SN"), v("YL")), v("YR", L, 384), eq)
+            mm(v("k2", 0, L), v("TRI"), v("EQS"), True, True)
+            act(v("MS"), SROW, AF.Identity, float(M), -1.0)
+            tt(v("FR"), v("EQS"), v("k2", 0, L), gt)
+            tc(v("k3", 256, 448), v("FR"))
+            tt(v("VT"), v("k3", 256, 448), v("MS"), mul)
+            act(v("VH"), SROW, AF.Identity, v("E0"), v("M0"))
+        tt(v("FR"), v("DIAG"), CNT, gt)
+        go = listed("FRS", v("FR"))
+        keep = range(4) if t < 3 else (1, 3)
+        for j in keep:
+            tt(v("Z4", 12 * j, 12 * j + 12), v("Z5", 12 * j, 12 * j + 12), go, mul)
+        if t < 3:
+            tt(v("Z4"), v("Z4"), v("TR4"), add)
+            tc(v("L4"), v("Z4"))
+        else:
+            for j in keep:
+                tt(v("Z4", 12 * j, 12 * j + 12), v("Z4", 12 * j, 12 * j + 12), v("TR4", 0, 12), add)
+                tc(v("L4", 12 * j, 12 * j + 12), v("Z4", 12 * j, 12 * j + 12))
 
     def sending(t):
-        ms, hg = "ms%d" % t, "HGS%d" % t
-        scan(v("CS"), v("k0", 256, 268), v("ZER", 0, 12), add, add)
-        tt(v("DA"), v("CS"), v("k0", 272, 284), add)
-        tt(v("DB"), v("DA"), v("TRL"), sub)
-        tt(v("DA"), v("DB"), v("LOF"), mul)
-        tt(v("DB"), v("DA"), v("TRL"), add)
-        tc(v("LO16"), v("DB"))
-        tc(at(v(hg), v("LO16")), v("HG"))
-        tc(at(v(ms), v("LO16")), v("XL"))
-        r = narrow(v(hg, 0, S), S, "RT", "RTS")
-        tc(v("HI4"), r)
-        ts(v("HI4B"), v("HI4"), 11, OP.logical_shift_right)
-        tc(v(ms, S, SW_), v("HI4B"))
-        ship("s", t, v(ms, 0, SW_))
-        ts(v("HI4B"), v("HI4"), 2047, OP.bitwise_and)
-        tc(v("HSW%d" % t), v("HI4B"))
-        tc(v("HS%d" % t), v("HI4B"))
-        yield
+        ms, hr, hs = "ms%d" % t, "HR%d" % t, v("HS%d" % t)
+        ts(v("LOT"), v("BS0", L, 384, 16), M - PO, eq)
+        tt(v("LO"), v("LOT"), v("LOF"), mul)
+        mm(v("k5", 0, 12), v("ONESB"), v("LO"), True, True)
+        mm(v("k5", 16, 28), v("IDH"), v("NTRL"), True, False)
+        mm(v("k5", 16, 28), v("TRMO"), v("LO"), False, True)
+        scan(v("CS"), v("k5", 0, 12), v("ZER", 0, 12), add, add)
+        tt(v("DA"), v("CS"), v("k5", 16, 28), add)
+        tt(v("DB"), v("DA"), v("LO"), mul)
+        tt(v("DA"), v("DB"), v("TRL"), add)
+        tc(v("LO16"), v("DA"))
+        tc(at(v(hr), v("LO16")), v("H"))
+        tt(v("TMG"), v(hr, 0, S), v("k3", 0, S), mul)
+        tc(hs, listed("HW%d" % t, v("TMG")))
+        act(v(ms, 0, S), at(v("X"), hs))
+        tt(v("TMG"), at(v("GN"), hs), v("DIAG", 0, S), mul)
+        tc(v(ms, S, SW_), listed("RWG", v("TMG")))
+        ship("s", t, v(ms))
+        if t == 0:
+            act(v("GNR"), at(v("GN"), hs), AF.Identity, 1.0)
+            act(v("GN", 1760, 1760 + S), v("GNR"))
 
-    def change_rest(t):
-        tt(v("XG"), at(v("X"), v("SL")), v("XL"), add)
-        ts(v("XG"), v("XG"), 0.5, sub, 0.5, mul)
-        tc(v("XI"), v("XG"))
-        tc(at(v("X", 0, W + L), v("L4", 12, 24)), v("XI"))
+    def returned(t):
+        lr, a = v("lr%d" % t), 1760 + S * (t - 1)
+        ts(v("FD"), lr, 256.0, lt)
+        if t < 3:
+            tt(v("TMR"), lr, v("DTH"), gt)
+            nf = listed("RWR", v("TMR"))
+            act(v("OKB", a // 16, a // 16 + 4), nf, AF.Identity, 1.0, -1.0)
+            tt(v("RZ"), nf, v("TR4", 0, 4), mul)
+            tt(v("RY"), v("RZ"), v("HW%d" % (t - 1), 15, S, 16), OP.max)
+            tc(v("RL16"), v("RY"))
+
+    def changes(t):
+        wide = W + L
+        if 0 < t < 3:
+            tc(at(v("RM"), v("RL16")), v("ONES", 0, S))
+        tc(at(v("X", 0, wide), v("L4", 12, 24)), v("XI"))
         tc(at(v("F2"), v("L4", 12, 24)), v("H"))
         tc(at(v("F1"), v("L4", 36, 48)), v("H"))
-        yield
-
-    def guests(t):
-        if t >= 1:
-            lr, a = "lr%d" % t, 1760 + S * (t - 1)
-            tt(v("X", a, a + S), v(lr), v("FD"), mul)
-            tt(v("F1", a, a + S), v("HROW%d" % (t - 1)), v("FD"), mul)
-            tt(v("F2", a, a + S), v("HROW%d" % (t - 1)), v("FD"), mul)
-            if t < 3:
-                tc(v("GH", a, a + S), v("GHN%d" % (t - 1)))
-        yield
-
-    def note_sent(t):
-        hg = "HGS%d" % t
-        tc(v("HIR"), v(hg, 0, S))
-        ts(v("HIR2"), v("HIR"), 2047, OP.bitwise_and)
-        tc(v("HROW%d" % t), v("HIR2"))
-        tt(v("RV"), v(hg, 0, S), v("HROW%d" % t), sub)
-        ts(v("RV2"), v("RV"), 2048.0 + S * t, add)
-        tt(v("GHN%d" % t), v("RV2"), v("COLC"), add)
-        yield
-
-    def returns(t):
-        lr, a = "lr%d" % t, 1760 + S * (t - 1)
-        hw, hs = "HSW%d" % (t - 1), "HS%d" % (t - 1)
-        ts(v("FD"), v(lr), 256.0, lt)
         if t < 3:
-            r = narrow(v("FD"), S, "RTB", "RTSB")
-            tt(v("RZ"), v(hw), v("TR4", 0, 4), sub)
-            tc(v("RVB"), at(v("SN", 0, W), v(hs)))
-            tt(v("FDW"), v("RZ"), r, mul)
-            ts(v("RV2B"), v("RVB"), v("MTC", 4 + t, 5 + t), mul)
-            tt(v("RZ"), v("FDW"), v("TR4", 0, 4), add)
-            ts(v("RTB"), v("COLC"), float(S * (t - 1)), add, v("MTC", t, t + 1), mul)
-            tc(v("RL16"), v("RZ"))
-            tt(v("RVB"), v("RV2B"), v("RTB"), add)
-            ts(v("SN", a, a + S), v(lr), 256.0, lt, float(M), mul)
-            tc(at(v("SN", 0, W + L), v("RL16")), v("RVB"))
-        yield
-
-    for kind, t in MSGS:
-        k = "%s%d" % (kind, t)
-        wr["l" + k] = [(0, 1 << 20, "remote", "a" + k, NENG)]
-        total["a" + k] = NENG
-    st = {"late": (3, [], record(constants_late()))}
-    for t in range(T_):
-        p, last = "%d" % t, "%d" % (t - 1)
-        st["lanes1" + p] = (1, ["returns" + last] if t else [], record(lanes1(t)))
-        st["lanes2" + p] = (1, ["lanes1" + p] + (["rest" + last, "guests" + last, "sending" + last] if t else ["late"]), record(lanes2(t)))
+            tc(at(v("SN", 0, wide), v("L4", 0, 12)), v("VH"))
+            tt(at(v("SN", 0, wide), v("L4", 24, 36)), v("SY"), v("VT"), add)
         if t:
-            st["arrivals" + p] = (2, ["rest" + last, "guests" + last, "returns" + last], record(arrivals(t)))
-        else:
-            st["last"] = (6, ["lanes2" + p], record(constants_last()))
-        st["own0" + p] = (2, ["lanes2" + p], record(own(0)))
-        st["own1" + p] = (3, ["lanes2" + p], record(own(1)))
-        st["own2" + p] = (4, ["lanes2" + p], record(own(2)))
-        st["flags" + p] = (4, ["lanes2" + p, "last"], record(own_flags(t)))
-        st["found" + p] = (1, ["own0" + p, "own1" + p, "own2" + p, "flags" + p], record(found(t)))
-        st["adopt" + p] = (1, ["found" + p], record(adopt(t)))
-        over = ["adopt" + p] + (["arrivals" + p] if t else [])
-        if t < 3:
-            st["slots" + p] = (2, ["found" + p] + (["arrivals" + p] if t else []), record(slots(t)))
-            st["sending" + p] = (0, ["found" + p], record(sending(t)))
-            st["sons" + p] = (1, over + ["slots" + p], record(change_sons(t)))
-            st["noted" + p] = (5, ["sending" + p], record(note_sent(t)))
-        st["returns" + p] = (4, (["sons" + p] if t < 3 else over) + (["noted" + last] if t else []), record(returns(t)) if t else [])
-        st["rest" + p] = (4, over, record(change_rest(t)))
-        st["guests" + p] = (4, ["rest" + p, "returns" + p], record(guests(t)))
-    merge(st)
+            lr, a, hr = v("lr%d" % t), 1760 + S * (t - 1), v("HR%d" % (t - 1), 0, S)
+            if t < 3:
+                act(v("RVB"), at(v("SN", 0, W), v("HS%d" % (t - 1))), scale=v("MTC", 4 + t, 5 + t))
+                tt(at(v("SN", 0, wide), v("RL16")), v("RVB"), v("CT3", S * (t - 1), S * t), add)
+            tt(v("X", a, a + S), lr, v("FD"), mul)
+            tt(v("F1", a, a + S), hr, v("FD"), mul)
+            tt(v("F2", a, a + S), hr, v("FD"), mul)
 
-    fill(v("F1", M, 1760), 0.0)
-    fill(v("F2", M, 1760), 0.0)
-    fill(v("X", M, 1760), 0.0)
-    dma("s", ("fo", 0, W, T.fo[:]), v("F1", 0, W, p=(0, 128, 16)))
-    dma("y", ("xo", 0, W, T.xo[:]), v("X", 0, W))
-    dma("s", ("f2o", 0, W, T.f2o[:]), v("F2", 0, W, p=(0, 128, 16)))
+    for t in range(T_):
+        lanes(t)
+        if t:
+            arrivals(t)
+        own()
+        if t < 3:
+            sending(t)
+        if t:
+            returned(t)
+        adopt(t)
+        changes(t)
+    for f in ("X", "F1", "F2"):
+        fill(v(f, M, 1760), 0.0)
+    dma("y", ("xo", 0, W, T.xo[:]), v("X", 0, W), 4.5)
+    dma("s", ("fo", 0, W, T.fo[:]), v("F1", 0, W, p=(0, 128, 16)), 2.5)
+    dma("s", ("f2o", 0, W, T.f2o[:]), v("F2", 0, W, p=(0, 128, 16)), 2.5)
+
+    if not ORDER:
+        ORDER.extend(plan(ops))
+    for i in ORDER:
+        issue(*ops[i])
     for sem in sorted(total):
         g.wait_ge(T.sem[sem], total[sem])
     g.wait_ge(T.sem.lo, sent[0])

@@ -9,10 +9,13 @@ TB = W
 BIG = 512.0
 KS = 8192.0
 PO = 2048.0
-SW_ = 68
+ROUND = 1.5 * 2 ** 23
+SW_ = 128
 NENG = 8
-NV = {"A0": 44, "A1": 44, "A2": 44, "AB": 32}
-BANK = {"A0": ("k0",), "A1": ("k1",), "A2": ("k7",), "AB": ("k2", "k5")}
+NV = {"A0": 44, "A1": 44, "A2": 44, "AB": 40}
+BANK = {"A0": ("k0",), "A1": ("k1",), "A2": ("k7",), "AB": ("k2",)}
+CH = ((0, 64), (64, 128), (128, 192))
+TURN = Q // 16
 PARTS = ("A0", "A1", "A2", "AB")
 
 SCRATCH = {}
@@ -36,28 +39,28 @@ def _b(kind, dtype, **kw):
             SCRATCH[p[0]] = (kind, [128, p[1]], dtype)
 
 
-_b("sbuf", "float32", SN=WT, F1=W + L, F2=W + L, H=L, P0=L, S0=L, S1=L, SA=L, UD=L, RMOD=384, DIAG=L, D15=L, DTH=S, OF=128, I3=384,
-   R16=1, PBF=2, M0=1, E0=1, MK=16, TRL=12, TR4=48, TRM=12, TRN=12, LANB=12, LANE=L, CT3=192, ZER=128, RST=64, CB=128, CT=128, NBS=12,
-   U=12, NU=12, UP=12, CA=12, CC=12, BASE=12, W1=12, W2=12, D1=12, YP=12, T1=12, NF=12, LOF=12, LOT=12, BS0=384, SCB=384,
-   Z4=48, Z5=48, ZT=24, SY=L, MS=L, VT=L, VH=L, CS=12, DA=12, DB=12, RZ=4, RY=4, RVB=S, FD=S, GENM=12, LB3=12, LBT=12, RS3=12, MTC=8,
-   HZ=12)
+_b("sbuf", "float32", SN=WT, F1=W + L, F2=W + L, H=L + 16, P0=L, S0=L, S1=L, SA=L, UD=L, RMOD=384, DIAG=L, D15=L, DTH=S, OF=128, I3=384,
+   R16=1, PBF=2, M0=1, E0=1, MK=16, TR4=48, TRM=12, TRN=12, LANB=12, LANE=L, CT3=192, ZER=128, RST=64, CB=128, CT=128, NBS=12,
+   U=12, NU=12, UP=12, CA=12, CC=12, BASE=12, W1=12, W2=12, D1=12, T1=12, NF=12, BS0=384, SCB=384,
+   Z4=48, Z5=48, ZT=24, SY=L, MS=L, VT=L, VH=L, RZ=4, RY=4, RVB=S, FD=S, GENM=12, LB3=12, LBT=12, RS3=12, MTC=8,
+   TMC=S, RWC=S, NR16=1, NR17=1, NLS=4, CTS=128, AA=128, AB=128, R2=128, XJ=L)
 for _n in PARTS:
     _b("sbuf", "float32", **{"SF" + _n: 64, "MM" + _n: 64, "DD" + _n: 64, "EE" + _n: 64})
     _b("sbuf", "float16", **{"RR" + _n: 64})
     _b("sbuf", "bfloat16", **{"XT" + _n: 128, "XR" + _n: 1024, "UU" + _n: 1024})
     _b("sbuf", "uint16", **{"IX" + _n: 64, "LL" + _n: 4})
-_b("sbuf", "float16", SWH=512, ONESH=128, DX=384, YR=384, PICK=2048, IDH=128, FAS=RW, GNS=RW, RRS=RW, NTRL=12, POR=128, ONR=384,
-   TMP=L, RWH=L, RWP=L, RWQ=L, TMG=S, RWG=S)
-_b("sbuf", "bfloat16", X=WT, GN=W, RM=W + L, ANE=M, SEL=2048, WSEL=2048, REP=1024, ONES=L, ONESB=128, NONESB=128, TRI=128, TRMO=128, TIMO=128,
-   SLR=128, XL=L, XS=L, IDB=128, NIDB=128, IDK=128, NIDK=128, ID16=128, IDHALF=128, QRT=128, TMPB=128, WC=1, RS0=384,
-   OKB=128, OK=128, JK=12 * 128, BT=512, FLG=L, BR=L, EQ0=L, EQ1=L, A0N=L, NE0=L, UR=L, ED=384, EQ=2112, NFR=L, GO=L, FR=L, FRS=L,
-   AY=L, EMY=L, SR=L, SRS=L, EQS=L, LO=12, GNR=S, TMR=S, RWR=S)
-_b("sbuf", "int32", SNI=M, FAI=RW, GNI=RW, PI=1, PI2=1, CI=4, CI2=4, XI=L)
-_b("sbuf", "uint16", BL=12, HL=12, HLT=12, P0L=12, P1L=12, SA16=L, YL=12, SL=12, L4=48, LO16=12, RL16=4, BF16=4)
+_b("sbuf", "float16", SWH=512, ONESH=128, DX=384, YR=384, PICK=2048, FAS=RW, GNS=RW, RRS=RW, YP=12, TMI=128,
+   RWI=128, POR=128, ONR=384, TMP=L, RWH=L, RWP=L, RWQ=L, TMG=S, TMH=S, RWG=S)
+_b("sbuf", "bfloat16", X=WT, GN=W, RM=W + L, ANE=M, SEL=2048, WONE=128, REP=1024, ONES=L, ONESB=128, NONESB=128, TRI=128, TIMO=128,
+   SLR=128, XL=L + 16, GL=L + 16, ZEH=L, JL=4 * L, XJB=L, XS=L, IDB=128, NIDB=128, IDK=128, NIDK=128, ID16=128, IDHALF=128, QRT=128, QRZ=128, TMPB=128, WC=1, RS0=384,
+   OK=128, OH=L, NOH=L, VAL=L, GG=L, CUM=L, JK=12 * 128, BT=512, FLG=L, BR=L, EQ0=L, EQ1=L, A0N=L, NE0=L, UR=L, ED=384, EQ=2112, NFR=L, FR=L, FRS=L,
+   AY=L, EMY=L, SR=L, SRS=L, EQS=L, TMR=S, RWR=S)
+_b("sbuf", "int32", SNI=M, FAI=RW, GNI=RW, PI=1, PI2=1, CI=4, CI2=4)
+_b("sbuf", "uint16", BL=12, HL=12, IDX=8, P0L=12, P1L=12, SA16=L, YL=12, SL=12, L4=48, LI=4, RL16=4, BF16=4)
 _b("psum", "float32", k0=512, k1=512, k2=512, k3=512, k4=512, k5=512, k6=512, k7=512)
 for _t in range(3):
     _b("sbuf", "bfloat16", **{"ms%d" % _t: SW_, "bs%d" % _t: SW_, "ls%d" % _t: SW_, "mr%d" % (_t + 1): S, "br%d" % (_t + 1): S, "lr%d" % (_t + 1): S})
-    _b("sbuf", "float32", **{"HR%d" % _t: 384})
+    _b("sbuf", "float32", **{"HR%d" % _t: S})
     _b("sbuf", "float16", **{"HW%d" % _t: S})
     _b("sbuf", "uint16", **{"HS%d" % _t: 4})
 
@@ -97,7 +100,32 @@ def hand_on(g, core, T, topo):
         g.wait_ge(T.sem.lo, n)
 
 
-HOP, CY, GA, SC = 0.16, 0.00087, 1.56, 3.8
+HOP, CY, GA, SC = 0.16, 0.00095, 1.56, 3.8
+
+
+FAR = {"s0": 10.0, "r1": 7.0, "s1": 4.5, "r2": 4.5, "s2": 7.0, "r3": 7.0}
+LEAD = {"A0": 4.0, "A1": 2.0, "A2": 0.0, "AB": 2.0}
+ROWS = ("FLG", "BR", "TMP", "H", "RWH", "XL", "P0", "RWP", "RWQ", "EQ0", "S0", "A0N", "NE0", "UR", "S1", "EQ1", "UD", "SA", "SA16")
+
+
+def lead(x):
+    nm, lo, hi = x
+    if nm[-2:] in LEAD:
+        return LEAD[nm[-2:]]
+    if nm == "k4":
+        return LEAD[PARTS[lo // 128]]
+    if nm in ROWS:
+        return LEAD[PARTS[lo // 64]]
+    if nm in ("BL", "HL", "P0L", "P1L", "NBS"):
+        return LEAD[PARTS[lo // 4]]
+    for p in PARTS:
+        if nm in BANK[p]:
+            return LEAD[p]
+    return 0.0
+
+
+PASSES, SHAKE = 600, 0.5
+ENDS = []
 
 
 def plan(ops):
@@ -126,60 +154,78 @@ def plan(ops):
 
     def hop(a, b):
         return 0.0 if ops[a][0] == ops[b][0] == "t" else HOP
+    banks = [set(x[0] for x in o[3] + o[4] if x[0] in BANKS) for o in ops]
+
+    def first(l, t, k):
+        a, b = 0, len(l)
+        while a < b:
+            m = (a + b) // 2
+            if l[m][k] <= t:
+                a = m + 1
+            else:
+                b = m
+        return a
+
+    def place(seq, before, back):
+        at, busy = [0.0] * n, {}
+        for i in seq:
+            e, us, dur = ops[i][0], ops[i][5], ops[i][6]
+            s = max([at[j] + ops[j][6] + hop(i, j) for j in before[i]], default=0.0)
+            off = dur - us if back else 0.0
+            moved = True
+            while moved:
+                moved = False
+                for r, pad in [(e, 0.0)] + [(b, HOP) for b in banks[i]]:
+                    l = busy.get(r, ())
+                    for x, y, e2 in l[max(first(l, s + off - pad, 1) - 3, 0):]:
+                        if x >= s + off + us + pad:
+                            break
+                        if (not pad or e2 != e) and y + pad > s + off + 1e-9:
+                            s = y + pad - off
+                            moved = True
+            at[i] = s
+            for r in [e] + list(banks[i]):
+                l = busy.setdefault(r, [])
+                l.insert(first(l, s + off, 0), (s + off, s + off + us, e))
+        return at
+
+    def sorted_by(key, before, after):
+        left = [len(p) for p in before]
+        free = sorted((key[i], i) for i in range(n) if not left[i])
+        seq = []
+        while free:
+            i = free.pop(0)[1]
+            seq.append(i)
+            for j in after[i]:
+                left[j] -= 1
+                if not left[j]:
+                    free.insert(first(free, key[j], 0), (key[j], j))
+        return seq
     rest = [0.0] * n
     for i in range(n - 1, -1, -1):
         rest[i] = ops[i][6] + max([hop(i, j) + rest[j] for j in succ[i]], default=0.0)
-    banks = [set(x[0] for x in o[3] + o[4] if x[0] in BANKS) for o in ops]
-    left = [len(p) for p in pred]
-    ready = [0.0] * n
-    free = {e: 0.0 for e in "vstgy"}
-    used = {}
-    cand = {e: [] for e in free}
-    for i in range(n):
-        if not left[i]:
-            cand[ops[i][0]].append(i)
-    order = []
+    key = [-rest[i] - max(lead(x) for x in ops[i][4]) for i in range(n)]
+    best = None
+    ENDS.append(round(max(rest), 1))
+    dice = [1]
 
-    def start(i):
-        e = ops[i][0]
-        s = max(free[e], ready[i])
-        for b in banks[i]:
-            for e2, t in used.get(b, {}).items():
-                if e2 != e:
-                    s = max(s, t + HOP)
-        return s
-    while len(order) < n:
-        st = {e: [(start(i), i) for i in cand[e]] for e in cand if cand[e]}
-        e = min(st, key=lambda k: min(st[k])[0])
-        t0 = min(st[e])[0]
-        near = sorted((x for x in st[e] if x[0] <= t0 + 0.7), key=lambda x: -rest[x[1]])[:10]
-        first = min(st[e], key=lambda x: (round(x[0] / 0.02), -rest[x[1]]))
-        if first not in near:
-            near.append(first)
-        best = None
-        for s, i in near:
-            b, t = s + rest[i], s + ops[i][5]
-            for s2, j in near:
-                if j != i:
-                    t = max(t, s2)
-                    b = max(b, t + rest[j])
-                    t += ops[j][5]
-            key = (round(b / 0.03), round(s / 0.02), -rest[i])
-            if best is None or key < best[0]:
-                best = (key, s, i)
-        s, i = best[1], best[2]
-        cand[e].remove(i)
-        order.append(i)
-        free[e] = s + ops[i][5]
-        end = s + ops[i][6]
-        for b in banks[i]:
-            used.setdefault(b, {})[e] = end
-        for j in succ[i]:
-            ready[j] = max(ready[j], end + hop(i, j))
-            left[j] -= 1
-            if not left[j]:
-                cand[ops[j][0]].append(j)
-    return order
+    def die():
+        dice[0] = (dice[0] * 1103515245 + 12345) % 2 ** 31
+        return dice[0] / 2 ** 31
+    for k in range(PASSES):
+        if k >= 3:
+            mid, wide = die() * best[0], 5 + 30 * die()
+            key = [t + (SHAKE * (2 * die() - 1) if abs(t - mid) < wide else 0.0) for t in best[1]]
+        at = place(sorted_by(key, pred, succ), pred, False)
+        bk = place(sorted_by([-at[i] - ops[i][6] for i in range(n)], succ, pred), succ, True)
+        at = place(sorted_by([-bk[i] - ops[i][6] for i in range(n)], pred, succ), pred, False)
+        end = max(at[i] + ops[i][6] for i in range(n))
+        if best is None or end <= best[0] + 0.03:
+            best = (min(end, best[0]) if best else end, at)
+        key = at
+    ENDS.append(round(best[0], 1))
+    loads = [i for i in range(n) if ops[i][1] == "o"]
+    return loads + [i for i in sorted_by(best[1], pred, succ) if ops[i][1] != "o"]
 
 
 def rank_program(g, core, T, topo):
@@ -247,7 +293,7 @@ def rank_program(g, core, T, topo):
             total["a" + n[1:]] = NENG
             return
         need(e, reads, writes)
-        if kind == "d":
+        if kind in "do":
             sem = "d%d" % dsem[0]
             dsem[0] += 1
             call().then_inc(T.sem[sem], 16)
@@ -271,14 +317,23 @@ def rank_program(g, core, T, topo):
     def emit(e, call, reads, writes, us, kind="c", dur=None):
         ops.append((e, kind, call, flat(reads), flat(writes), us, us if dur is None else dur))
 
+    def joined(n):
+        part = ops[-n:]
+        del ops[-n:]
+
+        def call():
+            return [o[2]() for o in part][-1]
+        us = sum(o[5] for o in part)
+        ops.append((part[0][0], "c", call, sum((o[3] for o in part), []), sum((o[4] for o in part), []), us, us))
+
     def size(x):
         return x[3].shape[1] if len(x) == 4 else 16 * x[1][3].shape[1]
 
     def two(*xs):
         return all(len(x) == 4 and (x[0] in HALF) for x in xs)
 
-    def dma(e, out, in_, dur):
-        emit(e, lambda: queue[e].dma_start(ap(out), ap(in_)), [in_], [out], 0.07, "d", dur)
+    def dma(e, out, in_, dur, turn=None):
+        emit(e, lambda: queue[e].dma_start(ap(out), ap(in_)), [in_], [out], 0.07, "o" if turn else "d", dur)
 
     def v(name, lo=0, hi=None, st=1, p=None):
         buf, o, w = PLACE[name] if name in PLACE else (name, 0, SCRATCH[name][1][1])
@@ -337,7 +392,7 @@ def rank_program(g, core, T, topo):
 
     def mm(out, lhsT, rhs, start, stop):
         emit("t", lambda: g.tensor.matmul(ap(out), ap(lhsT), ap(rhs), start, stop), [lhsT, rhs], [out],
-             CY * max(min(64, size(lhsT)), size(out)) * (1 if two(lhsT) else 4))
+             CY * max(min(64, size(lhsT)), size(out)) * (0.5 if two(lhsT) else 2))
 
     def iota(out, pattern, base, cm, after=None):
         us = 0.15 + 2 * CY * size(out)
@@ -354,12 +409,13 @@ def rank_program(g, core, T, topo):
     SELW = 16 * KS
 
     C4 = M // 4
-    dma("s", v("GNI"), ("gn", 0, M, T.gn[:]), 2.5)
+    turns = ("y", 0, 1, None)
+    dma("s", v("GNI"), ("gn", 0, M, T.gn[:]), 2.2)
     for j in range(4):
-        dma("y", v("SNI", j * C4, (j + 1) * C4), ("sn", j * C4, (j + 1) * C4, T.sn[:, j * C4:(j + 1) * C4]), 3.5 + j)
-    dma("s", v("FAI"), ("fa", 0, M, T.fa[:]), 2.5)
-    dma("y", v("X", 0, M), ("x", 0, M, T.x[:]), 8.0)
-    dma("s", v("WC"), ("w", 0, 1, T.w[:]), 3.0)
+        dma("y", v("SNI", j * C4, (j + 1) * C4), ("sn", j * C4, (j + 1) * C4, T.sn[:, j * C4:(j + 1) * C4]), 3.2 + 1.1 * j, turns)
+    dma("y", v("FAI"), ("fa", 0, M, T.fa[:]), 7.0, turns)
+    dma("y", v("X", 0, M), ("x", 0, M, T.x[:]), 8.5, turns)
+    dma("y", v("WC"), ("w", 0, 1, T.w[:]), 9.0, turns)
 
     R16 = v("R16")
     DIAGB = v("k3", 0, L)
@@ -376,13 +432,15 @@ def rank_program(g, core, T, topo):
         ts(v("PICK", 128 * m, 128 * (m + 1)), v("ONESB"), v("MK", m, m + 1), mul)
     fill(v("SEL"), 0.0)
     for s in range(16):
-        ts(v("SEL", s * 128 + s, (s + 1) * 128, 16), v("ONESB", s, 128, 16), SELW, mul)
+        act(v("SEL", s * 128 + s, (s + 1) * 128, 16), v("ONESB", s, 128, 16), scale=SELW)
+    act(v("NONESB"), v("ONESB"), scale=-1.0)
     pick(v("TRI"), v("ONESB"), [[1, 128]], ge, -1, -1)
-    pick(v("TIMO"), v("ONESB"), [[-1, 128]], ge, -1, 1)
-    ts(v("TIMO"), v("TIMO"), -1.0, mul)
+    pick(v("TIMO"), v("NONESB"), [[-1, 128]], ge, -1, 1)
+    ts(v("NR16"), R16, -1.0, mul)
+    ts(v("NR17"), R16, -1.0, mul, -1.0, add)
     fill(v("ZER"), 0.0)
     fill(v("CT", NB, 128), 9999.0)
-    fill(v("OKB", RW, 128), 0.0)
+    fill(v("OK", RW, 128), 0.0)
     iota(v("LANB"), [[16, 12]], 0, 0)
     ts(v("LANB"), v("LANB"), R16, add, 0.5, add)
     iota(v("LANE"), [[1, L]], 0, 0)
@@ -405,6 +463,11 @@ def rank_program(g, core, T, topo):
     ts(v("RRS"), v("GNI"), 2, ge, float(M + 1), mul)
     ts(v("RRS"), v("RRS"), -1.0, add)
 
+    def sixteen(out, sel, src, a, b):
+        for r in range(16):
+            mm(out, v(sel, 128 * r, 128 * (r + 1)), v(src, a + r, b, 16), r == 0, r == 15)
+        joined(16)
+
     def spread(src, j, k):
         for m in range(4 * j, 4 * j + 4):
             mm(v(k, (m % 4) * RW, (m % 4 + 1) * RW), v("PICK", 128 * m, 128 * (m + 1)), v(src), True, True)
@@ -412,21 +475,20 @@ def rank_program(g, core, T, topo):
     for j in range(4):
         tt(v("ANE", j * C4, (j + 1) * C4), v("SNI", j * C4, (j + 1) * C4), spread("RRS", j, ("k0", "k1")[j % 2]), ne)
     for a, b in ((0, 54), (54, RW)):
-        for r in range(16):
-            mm(v("k6", a, b), v("SEL", 128 * r, 128 * (r + 1)), v("ANE", 16 * a + r, 16 * b, 16), r == 0, r == 15)
-    ts(v("OKB", 0, RW), v("k6", 0, RW), 0.0, eq)
+        sixteen(v("k6", a, b), "SEL", "ANE", 16 * a, 16 * b)
+    ts(v("OK", 0, RW), v("k6", 0, RW), 0.0, eq)
     tc(v("FAS"), v("FAI"))
     tc(v("GNS"), v("GNI"))
     for j in range(4):
         act(v("F1", j * C4, (j + 1) * C4), spread("FAS", j, ("k2", "k5")[j % 2]))
         tc(v("SN", j * C4, (j + 1) * C4), v("SNI", j * C4, (j + 1) * C4))
-    ts(v("DIAG"), v("RMOD", 0, L), R16, eq)
-    ts(DIAGB, v("RMOD", 0, L), R16, eq)
-    ts(v("RS0"), v("RMOD"), 0.0, ne)
-    ts(v("RST"), v("RMOD", 0, 64), 0.0, eq, float(2 ** 31), mul)
-    for f in ("F1", "F2"):
-        fill(v(f, M, 1760), float(M + 1))
-        fill(v(f, 1760, W + L), 0.0)
+    act(v("D15"), v("RMOD", 0, L), AF.Abs, v("NR16"))
+    act(v("DIAG"), v("D15"), AF.Relu, 1.0, -1.0)
+    act(DIAGB, v("D15"), AF.Relu, 1.0, -1.0)
+    act(v("RS0"), v("RMOD"), AF.Sign)
+    act(v("RST"), v("RMOD", 0, 64), AF.Relu, float(2 ** 31), -float(2 ** 31))
+    fill(v("F1", M, 1760), float(M + 1))
+    act(v("F1", 1760, W + L), v("RMOD"), scale=0.0)
     fill(v("X", M, WT), BIG)
     ts(v("PI2"), v("PI"), 4, OP.logical_shift_right, 1, OP.bitwise_and)
     tc(v("PBF", 1, 2), v("PI2"))
@@ -438,23 +500,24 @@ def rank_program(g, core, T, topo):
     iota(v("SLR", p=(0, 1)), [[0, 8], [int(KS), 16]], 0, 0)
     iota(v("REP", p=(0, 64)), [[-1, 64], [0, 16]], 0, 1, v("I3"))
     ts(v("REP", p=(0, 64)), v("REP", p=(0, 64)), 0.0, eq)
-    act(v("NONESB"), v("ONESB"), scale=-1.0)
-    iota(v("TRL"), [[16, 12]], L, 0)
     iota(v("TR4"), [[0, 4], [16, 12]], TB, 0)
     iota(v("CT3"), [[1, 192]], 1760, 0)
-    ts(v("TRL"), v("TRL"), R16, add)
-    ts(v("NTRL"), v("TRL"), -1.0, mul)
+    for nm in ("AA", "AB", "R2"):
+        fill(v(nm, NB, 128), 0.0)
+    fill(v("ZEH"), 0.0)
+    for nm, c in (("H", float(M)), ("XL", BIG), ("GL", 0.0)):
+        fill(v(nm, L, L + 16), c)
+    fill(v("QRZ", p=(0, 1)), 0.0)
     ts(v("TR4"), v("TR4"), R16, add)
     ts(v("TRM"), v("TR4", 0, 12), -PO, add)
     ts(v("TRN"), v("TR4", 0, 12), 1 - PO, add)
-    tc(v("IDH"), ID)
     for j in range(4):
         act(v("GN", j * C4, (j + 1) * C4), spread("GNS", j, ("k2", "k5")[j % 2]))
     fill(v("GN", M, W), 0.0)
-    act(v("F2", 0, M), v("F1", 0, M))
-    fill(v("RM"), 0.0)
-    ts(v("D15"), v("DIAG"), -998.5, mul, 1000.0, add)
-    ts(v("DTH"), v("DIAG", 0, S), -745.0, mul, 1000.0, add)
+    dma("y", v("F2"), v("F1"), 5.0)
+    iota(v("RM"), [[0, W + L]], 0, 0, v("REP"))
+    act(v("D15"), v("DIAG"), AF.Identity, 1000.0, -998.5)
+    act(v("DTH"), v("DIAG", 0, S), AF.Identity, 1000.0, -745.0)
     ts(v("M0"), R16, 0.0, eq)
     ts(v("E0"), R16, 0.0, ne, float(M), mul)
     for t in range(1, 3):
@@ -465,17 +528,16 @@ def rank_program(g, core, T, topo):
     fill(v("POR", p=(0, 1)), PO)
     fill(v("ONR", p=(0, 1)), 1.0)
     fill(v("QRT", p=(0, 1)), -0.25)
-    tt(v("TRMO"), v("TRI"), v("ONESB"), sub)
-    ts(v("WSEL"), v("SEL"), v("WC"), mul, 1.0 / SELW, mul)
-    ts(v("BS0"), v("RMOD"), 1.0, sub, R16, eq)
-    ts(v("BS0"), v("BS0"), PO, mul)
+    ts(v("WONE"), v("ONESB"), v("WC"), mul)
+    act(v("SCB"), v("RMOD"), AF.Abs, v("NR17"))
+    act(v("BS0"), v("SCB"), AF.Relu, PO, -PO)
     fill(v("RS3"), 1.0)
     fill(v("RS3", 0, 12, 3), 0.0)
 
     def listed(res, masked):
-        n = size(masked)
-        scan(v(res, 0, n), v("RS0", 0, n), masked, mul, add)
-        return v(res, 15, n, 16)
+        a, b = masked[1:3]
+        scan(v(res, a, b), v("RS0", a, b), masked, mul, add)
+        return v(res, a + 15, b, 16)
 
     def numbers(tag, src):
         k = BANK[tag][0]
@@ -487,62 +549,61 @@ def rank_program(g, core, T, topo):
             act(v("XR" + tag, a, b), v(k, 128, 128 + b - a))
 
     def lanes(t):
-        ok = v("OKB", 0, NB)
-        if t:
-            a = Q * t // 16
-            for r in range(16):
-                mm(v("k6", 0, NB), v("SEL", 128 * r, 128 * (r + 1)), v("RM", r, W, 16), r == 0, r == 15)
-            tt(v("OK", 0, NB - a), v("OKB", a, NB), v("k6", a, NB), gt)
-            tt(v("OK", NB - a, NB), v("OKB", 0, a), v("k6", 0, a), gt)
-            ok = v("OK", 0, NB)
+        ok = v("OK", 0, NB)
         mm(v("k6", 128, 128 + NB), v("ONESB"), ok, True, True)
         mm(v("k6", 256, 256 + NB), v("TIMO"), ok, True, True)
         scan(v("CB", 0, NB), v("k6", 128, 128 + NB), v("ZER", 0, NB), add, add)
         tt(v("CT", 0, NB), v("k6", 256, 256 + NB), v("CB", 0, NB), add)
         for q in range(12):
             act(v("JK", 128 * q, 128 * q + NB), v("CB", 0, NB), AF.Sign, v("LANB", q, q + 1), -1.0, v("NBS", q, q + 1))
-        ts(v("BL"), v("NBS"), 0.5, mul, NB / 2, add)
-        tt(v("FLG"), at(v("CT"), v("BL")), v("LANE"), le)
-        act(v("BR"), at(v("BT", 128 * t, 128 * t + 128), v("BL")))
-        HP = v("k6", 0, L)
-        mm(HP, v("ID16"), v("BR"), True, False)
-        mm(HP, v("ONESB"), v("FLG"), False, True)
-        tt(v("TMP"), HP, v("DIAG"), mul)
-        act(v("H"), HP)
-        hw = listed("RWH", v("TMP"))
-        tc(v("HL"), hw)
         F = v("F1" if t % 2 == 0 else "F2", 0, W)
         tab = v("SN")
-        tt(v("TMP"), at(F, v("HL")), v("DIAG"), mul)
-        act(v("XL"), at(v("X"), v("HL")))
-        act(v("P0"), at(F, v("HL")))
-        pw = listed("RWP", v("TMP"))
-        tc(v("P0L"), pw)
-        for h in range(3):
-            numbers("A%d" % h, v("XL", 64 * h, 64 * h + 64))
-        tt(v("TMP"), at(F, v("P0L")), v("DIAG"), mul)
-        tc(v("P1L"), listed("RWQ", v("TMP")))
-        tt(v("EQ0"), at(tab, v("P0L")), v("H"), eq)
-        act(v("S0"), at(tab, v("P0L")))
-        act(v("A0N"), v("S0"), AF.Abs, -float(M))
-        act(v("NE0"), v("A0N"), AF.Sign)
-        KK, W0, WD = v("k6", 256, 448), v("k5", 0, L), v("k5", 256, 448)
-        mm(KK, v("ONESB"), v("EQ0"), True, False)
-        mm(KK, v("NONESB"), v("NE0"), False, True)
-        act(v("UR"), KK, AF.Relu, 1.0)
-        mm(W0, ID, v("S0"), True, False)
-        mm(W0, v("IDK"), v("EQ0"), False, True)
-        mm(WD, NID, v("S0"), True, False)
-        mm(WD, v("NIDK"), v("EQ0"), False, False)
-        act(v("S1"), at(tab, v("P1L")))
-        tt(v("EQ1"), at(tab, v("P1L")), v("P0"), eq)
-        mm(WD, ID, v("S1"), False, False)
-        mm(WD, v("IDK"), v("EQ1"), False, True)
-        tt(v("UD"), WD, v("UR"), mul)
-        tt(v("SA"), W0, v("UD"), add)
-        tc(v("SA16"), v("SA"))
-        for r in range(16):
-            mm(v("k6", 448, 460), v("SEL", 128 * r, 128 * (r + 1)), v("UR", r, L, 16), r == 0, r == 15)
+
+        def first(a, b):
+            r, l = (lambda n: v(n, a, b)), (lambda n: v(n, a // 16, b // 16))
+            ts(l("BL"), l("NBS"), 0.5, mul, NB / 2, add)
+            tt(r("FLG"), at(v("CT"), l("BL")), r("LANE"), le)
+            act(r("BR"), at(v("BT", 128 * t, 128 * t + 128), l("BL")))
+            mm(r("k6"), v("ID16"), r("BR"), True, False)
+            mm(r("k6"), v("ONESB"), r("FLG"), False, True)
+            tt(r("TMP"), r("k6"), r("DIAG"), mul)
+            act(r("H"), r("k6"))
+            tc(l("HL"), listed("RWH", r("TMP")))
+            tt(r("TMP"), at(F, l("HL")), r("DIAG"), mul)
+            act(r("XL"), at(v("X"), l("HL")))
+            act(r("P0"), at(F, l("HL")))
+            tc(l("P0L"), listed("RWP", r("TMP")))
+            for h in range(a // 64, b // 64):
+                numbers("A%d" % h, v("XL", 64 * h, 64 * h + 64))
+
+        def second(a, b):
+            r, l = (lambda n: v(n, a, b)), (lambda n: v(n, a // 16, b // 16))
+            tt(r("TMP"), at(F, l("P0L")), r("DIAG"), mul)
+            tc(l("P1L"), listed("RWQ", r("TMP")))
+            tt(r("EQ0"), at(tab, l("P0L")), r("H"), eq)
+            act(r("S0"), at(tab, l("P0L")))
+            act(r("A0N"), r("S0"), AF.Abs, -float(M))
+            act(r("NE0"), r("A0N"), AF.Sign)
+            KK, W0, WD = v("k6", L + a, L + b), r("k5"), v("k5", L + a, L + b)
+            mm(KK, v("ONESB"), r("EQ0"), True, False)
+            mm(KK, v("NONESB"), r("NE0"), False, True)
+            act(r("UR"), KK, AF.Relu, 1.0)
+            mm(W0, ID, r("S0"), True, False)
+            mm(W0, v("IDK"), r("EQ0"), False, True)
+            mm(WD, NID, r("S0"), True, False)
+            mm(WD, v("NIDK"), r("EQ0"), False, False)
+            act(r("S1"), at(tab, l("P1L")))
+            tt(r("EQ1"), at(tab, l("P1L")), r("P0"), eq)
+            mm(WD, ID, r("S1"), False, False)
+            mm(WD, v("IDK"), r("EQ1"), False, True)
+            tt(r("UD"), WD, r("UR"), mul)
+            tt(r("SA"), W0, r("UD"), add)
+            tc(r("SA16"), r("SA"))
+        for stage in (first, second):
+            for a, b in CH:
+                stage(a, b)
+        hw, pw = v("RWH", 15, L, 16), v("RWP", 15, L, 16)
+        sixteen(v("k6", 448, 460), "SEL", "UR", 0, L)
         act(v("U"), v("k6", 448, 460), scale=1.0 / (16 * SELW))
         act(v("NU"), v("U"), AF.Identity, 1.0, -1.0)
         ts(v("CA"), pw, 64.0, ge)
@@ -552,18 +613,22 @@ def rank_program(g, core, T, topo):
         tt(v("CC"), v("CA"), v("CC"), sub)
         tt(v("Z5", 0, 12), hw, v("TR4", 0, 12), sub)
         if t < 3:
-            ts(v("LOF"), hw, float(M), ne)
-            tt(v("HZ"), v("Z5", 0, 12), v("LOF"), mul)
-            tt(v("HZ"), v("HZ"), v("TR4", 0, 12), add)
-            tc(v("HLT"), v("HZ"))
-            fill(v("HR%d" % t, 0, 384), float(M))
+            mm(v("k5", 0, L), v("ONESB"), v("FLG"), True, True)
+            ts(v("OH"), v("k5", 0, L), R16, eq)
+            act(v("NOH"), v("OH"), AF.Identity, 1.0, -1.0)
+            act(v("CTS", 0, NB), v("CT", 0, NB), scale=1.0 / (L + 0.5))
+            for x, y, n in ((0, TURN, NB - TURN), (NB - TURN, 0, TURN)):
+                act(v("R2", x, x + n), v("CB", y, y + n), AF.Relu, float(L), -1.0)
+                tt(v("AA", x, x + n), v("OK", y, y + n), v("CTS", y, y + n), mul)
+            tt(v("TMI"), v("R2"), v("k3", 0, 128), mul)
+            ts(v("IDX"), listed("RWI", v("TMI")), -1.0, mul, L - 1.0, add)
 
     def down(tag, idx, son):
         n, nv, kb = 64, NV[tag], BANK[tag][0]
         u, xr = "UU" + tag, "XR" + tag
         a, difs = nv, []
         for k in BANK[tag]:
-            o = 128 if k == kb else 0
+            o = 64 if k == kb else 0
             b = min(n, a + (512 - o) // 16)
             if a < b:
                 us, dif = v(u, 16 * a, 16 * b), v(k, o, o + 16 * (b - a))
@@ -581,6 +646,7 @@ def rank_program(g, core, T, topo):
         mm(v(kb, 0, n), v("SLR", p=(0, 1)), v("ONES", 0, n, p=(0, 1)), True, False)
         for s in range(16):
             mm(v(kb, 0, n), v("SEL", 128 * s, 128 * (s + 1)), v(u, s, 16 * n, 16), False, s == 15)
+        joined(17)
         vo = 128 * PARTS.index(tag)
         SP, KP = v("k4", vo, vo + n), v("k4", vo + n, vo + 2 * n)
         turn(SP, son)
@@ -592,15 +658,16 @@ def rank_program(g, core, T, topo):
         scan(rr, dd, ee, OP.min, OP.max)
         for e in range(2):
             for y in range(2):
-                mm(v(kb, 64 + e, 68, 2), v("SWH", 128 * (2 * e + y), 128 * (2 * e + y + 1)), v("RR" + tag, 15 + 16 * y, n, 32), y == 0, y == 1)
-        return v(kb, 64, 68)
+                mm(v(kb, e, 4, 2), v("SWH", 128 * (2 * e + y), 128 * (2 * e + y + 1)), v("RR" + tag, 15 + 16 * y, n, 32), y == 0, y == 1)
+        joined(4)
+        return v(kb, 0, 4)
 
     def step(tag):
         tc(v("IX" + tag), at(v("SN"), v("LL" + tag)))
         act(v("SF" + tag), at(v("SN"), v("LL" + tag)))
         return down(tag, lambda a, b: v("IX" + tag, a, b), v("SF" + tag))
 
-    def own():
+    def own(t):
         for h in range(3):
             tag, o, lo = "A%d" % h, 4 * h, 64 * h
             x = down(tag, lambda a, b: v("SA16", lo + a, lo + b), v("SA", lo, lo + 64))
@@ -613,6 +680,7 @@ def rank_program(g, core, T, topo):
         tt(v("D1"), v("D1"), v("U"), mul)
         tt(v("D1"), v("D1"), v("W1"), add)
         ts(v("YP"), v("D1"), 1.0, add)
+        early(t)
         tt(v("BASE"), v("W2"), v("NU"), mul)
         tt(v("BASE"), v("BASE"), v("CC"), add)
         for h in range(3):
@@ -623,12 +691,14 @@ def rank_program(g, core, T, topo):
 
     def arrivals(t):
         ls = "ls%d" % (t - 1)
-        for r in range(16):
-            mm(v("k2", 0, 4), v("WSEL", 128 * r, 128 * (r + 1)), v(ls, r, S, 16), r == 0, r == 15)
-        tc(v("CI"), v("k2", 0, 4))
+        mm(v("k2", 0, S), v("WONE"), v(ls, 0, S), True, True)
+        tt(v("TMC"), v("k2", 0, S), v("DIAG", 0, S), mul)
+        tc(v("CI"), listed("RWC", v("TMC")))
         numbers("AB", v(ls, 0, S))
+        tt(v("TMG"), v(ls, S, SW_), v("k3", 0, S), mul)
+        gen = listed("RWG", v("TMG"))
         for d in range(3):
-            ts(v("GENM", d, 12, 3), v(ls, S, SW_), float(d + 2), eq)
+            ts(v("GENM", d, 12, 3), gen, float(d + 2), eq)
         ts(v("CI2"), v("CI"), 63, OP.bitwise_and)
         tc(v("LLAB"), v("CI2"))
         for e in range(4):
@@ -656,57 +726,68 @@ def rank_program(g, core, T, topo):
             else:
                 send(g, topo, core, mid, T["b" + k][:], src[3], T.sem["x" + k], T.sem.lo)
             sent[0] += NENG
-        emit("g", call, [src], [v("l" + k)], 1.0, "r", 14.0 if k == "s0" else 9.0)
+        emit("g", call, [src], [v("l" + k)], 1.0, "r", FAR[k])
 
-    def adopt(t):
-        sp, yp = v("BS0", L, 384, 16), v("BS0", 0, L, 16)
-        ts(v("NF"), sp, M - PO, ne, -2 * PO, mul)
-        tt(yp, v("YP"), v("NF"), OP.max)
-        scan(v("SCB"), v("RS0"), v("BS0"), mul, add)
-        ts(v("SL"), sp, PO, add)
-        YROW, SROW, CNT = v("k7", 0, L), v("k1", 0, L), v("k6", 0, L)
-        for o, row in ((0, YROW), (L, SROW)):
-            mm(row, v("POR", p=(0, 1)), v("ONR", 0, L, p=(0, 1)), True, False)
-            tt(v("DX", o, o + L), v("SCB", o, o + L), DIAGB, mul)
-            mm(row, v("ONESH"), v("DX", o, o + L), False, True)
-            tc(v("YR", o, o + L), row)
-            tt(v("ED", o, o + L), v("SCB", o, o + L), row, eq)
-        act(v("NFR"), YROW, AF.Relu, 1.0 - PO)
-        mm(CNT, v("ONESB"), v("NFR"), True, False)
-        mm(CNT, v("ONESB"), v("ED", 0, L), False, False)
-        mm(CNT, v("ONESB"), v("ED", L, 384), False, False)
-        o = 0
-        for lo in (0, L):
-            for q in range(11):
-                n = (11 - q) * 16
-                ts(v("EQ", o, o + n), v("YR", lo + L - n, lo + L), PO, sub, v("BS0", lo + 16 * q, lo + 16 * q + 1), eq)
-                mm(v("k6", L - n, L), v("ONESB"), v("EQ", o, o + n), False, lo == L and q == 10)
-                o += n
-        act(v("XS"), at(v("X"), v("SL")))
-        XG = v("k0", 0, L)
-        mm(XG, v("QRT", p=(0, 1)), v("ONES", 0, L, p=(0, 1)), True, False)
-        mm(XG, v("IDHALF"), v("XL"), False, False)
-        mm(XG, v("IDHALF"), v("XS"), False, True)
-        tc(v("XI"), XG)
-        ts(v("YL"), yp, PO - 1, add)
+    YROW, SROW, CNT = v("k5", 0, L), v("k1", 0, L), v("k6", 0, L)
+
+    def early(t):
+        mm(YROW, v("POR", p=(0, 1)), v("ONR", 0, L, p=(0, 1)), True, False)
+        for r in range(16):
+            mm(v("k5", r, L, 16), v("PICK", 128 * r, 128 * (r + 1)), v("YP"), False, r == 15)
+        joined(17)
+        tc(v("YR", 0, L), YROW)
+        ts(v("YL"), v("YP"), PO - 1, add)
         act(v("SY"), at(v("SN"), v("YL")))
         act(v("AY"), v("SY"), AF.Abs, -float(M))
         act(v("EMY"), v("AY"), AF.Sign)
-        mm(v("k0", 256, 448), v("ONESB"), v("EMY"), True, True)
-        tt(v("SR"), v("D15"), v("k0", 256, 448), lt)
+        mm(v("k6", 256, 448), v("ONESB"), v("EMY"), True, True)
+        tt(v("SR"), v("D15"), v("k6", 256, 448), lt)
         sev = listed("SRS", v("SR"))
-        tt(v("Z5", 12, 24), sp, v("TRM"), sub)
-        tt(v("Z5", 36, 48), v("Z5", 12, 24), sev, mul)
         if t < 3:
-            tt(v("ZT", 0, 12), yp, v("TRN"), sub)
+            tt(v("ZT", 0, 12), v("YP"), v("TRN"), sub)
             tt(v("Z5", 24, 36), v("ZT", 0, 12), sev, mul)
-            act(v("GO"), CNT, AF.Relu, 1.0, -1.0)
-            tc(at(v("RM"), v("HLT")), v("GO"))
+        mm(CNT, v("QRZ", p=(0, 1)), v("ONES", 0, L, p=(0, 1)), True, False)
+
+    def adopt(t):
+        sp, yp = v("BS0", L, 384, 16), v("BS0", 0, L, 16)
+        scan(v("SCB", L, 384), v("RS0", 0, L), v("BS0", L, 384), mul, add)
+        mm(SROW, v("POR", p=(0, 1)), v("ONR", 0, L, p=(0, 1)), True, False)
+        tt(v("DX", 0, L), v("SCB", L, 384), DIAGB, mul)
+        mm(SROW, v("ONESH"), v("DX", 0, L), False, True)
+        tc(v("YR", L, 384), SROW)
+        ts(v("NF"), sp, M - PO, ne, -2 * PO, mul)
+        tt(yp, v("YP"), v("NF"), OP.max)
+        scan(v("SCB", 0, L), v("RS0", 0, L), v("BS0", 0, L), mul, add)
+        ts(v("SL"), sp, PO, add)
+        o = 0
+        for lo, whole in ((0, YROW), (L, SROW)):
+            for q in range(11):
+                n = (11 - q) * 16
+                ts(v("EQ", o, o + n), v("YR", lo + L - n, lo + L), PO, sub, v("BS0", lo + 16 * q, lo + 16 * q + 1), eq)
+                mm(v("k6", L - n, L), v("ONESB"), v("EQ", o, o + n), False, False)
+                o += n
+            tt(v("ED", lo, lo + L), v("SCB", lo, lo + L), whole, eq)
+            mm(CNT, v("ONESB"), v("ED", lo, lo + L), False, False)
+        ts(v("NFR"), v("YR", L, 384), float(M), eq)
+        mm(CNT, v("ONESB"), v("NFR"), False, True)
+        if t < 3:
+            tt(v("VAL"), v("OH"), CNT, gt)
+            scan(v("GG"), v("NOH"), v("VAL"), mul, add)
+            tt(v("OK"), at(v("GG"), v("IDX")), v("AB" if t else "AA"), lt)
+        act(v("XS"), at(v("X"), v("SL")))
+        XG = v("k0", 0, L)
+        mm(XG, v("QRT", p=(0, 1)), v("ONES", 0, L, p=(0, 1)), True, False)
+        mm(XG, v("IDHALF"), v("XL", 0, L), False, False)
+        mm(XG, v("IDHALF"), v("XS"), False, True)
+        act(v("XJ"), XG, bias=ROUND)
+        act(v("XJB"), v("XJ"), bias=-ROUND)
+        tt(v("Z5", 12, 24), sp, v("TRM"), sub)
+        tt(v("Z5", 36, 48), v("Z5", 12, 24), v("SRS", 15, L, 16), mul)
+        if t < 3:
             tt(v("EQS"), at(v("SN"), v("YL")), v("YR", L, 384), eq)
-            mm(v("k2", 0, L), v("TRI"), v("EQS"), True, True)
+            mm(v("k7", 0, L), v("TRI"), v("EQS"), True, True)
             act(v("MS"), SROW, AF.Identity, float(M), -1.0)
-            tt(v("FR"), v("EQS"), v("k2", 0, L), gt)
-            tc(v("k3", 256, 448), v("FR"))
+            tt(v("k3", 256, 448), v("EQS"), v("k7", 0, L), gt)
             tt(v("VT"), v("k3", 256, 448), v("MS"), mul)
             act(v("VH"), SROW, AF.Identity, v("E0"), v("M0"))
         tt(v("FR"), v("DIAG"), CNT, gt)
@@ -724,26 +805,19 @@ def rank_program(g, core, T, topo):
 
     def sending(t):
         ms, hr, hs = "ms%d" % t, "HR%d" % t, v("HS%d" % t)
-        ts(v("LOT"), v("BS0", L, 384, 16), M - PO, eq)
-        tt(v("LO"), v("LOT"), v("LOF"), mul)
-        mm(v("k5", 0, 12), v("ONESB"), v("LO"), True, True)
-        mm(v("k5", 16, 28), v("IDH"), v("NTRL"), True, False)
-        mm(v("k5", 16, 28), v("TRMO"), v("LO"), False, True)
-        scan(v("CS"), v("k5", 0, 12), v("ZER", 0, 12), add, add)
-        tt(v("DA"), v("CS"), v("k5", 16, 28), add)
-        tt(v("DB"), v("DA"), v("LO"), mul)
-        tt(v("DA"), v("DB"), v("TRL"), add)
-        tc(v("LO16"), v("DA"))
-        tc(at(v(hr), v("LO16")), v("H"))
-        tt(v("TMG"), v(hr, 0, S), v("k3", 0, S), mul)
-        tc(hs, listed("HW%d" % t, v("TMG")))
-        act(v(ms, 0, S), at(v("X"), hs))
-        tt(v("TMG"), at(v("GN"), hs), v("DIAG", 0, S), mul)
-        tc(v(ms, S, SW_), listed("RWG", v("TMG")))
+        act(v("GL", 0, L), at(v("GN"), v("HL")))
+        scan(v("CUM"), v("NFR"), v("ZEH"), add, add)
+        for q in range(4):
+            act(v("JL", L * q, L * q + L), v("CUM"), AF.Sign, v("LANB", q, q + 1), -1.0, v("NLS", q, q + 1))
+        ts(v("LI"), v("NLS"), 0.5, mul, L / 2, add)
+        act(v(ms, 0, S), at(v("XL"), v("LI")))
+        act(v(ms, S, SW_), at(v("GL"), v("LI")))
         ship("s", t, v(ms))
+        act(v(hr), at(v("H"), v("LI")))
+        tt(v("TMH"), v(hr), v("k3", 0, S), mul)
+        tc(hs, listed("HW%d" % t, v("TMH")))
         if t == 0:
-            act(v("GNR"), at(v("GN"), hs), AF.Identity, 1.0)
-            act(v("GN", 1760, 1760 + S), v("GNR"))
+            act(v("GN", 1760, 1760 + S), v(ms, S, SW_), AF.Identity, 1.0)
 
     def returned(t):
         lr, a = v("lr%d" % t), 1760 + S * (t - 1)
@@ -751,43 +825,47 @@ def rank_program(g, core, T, topo):
         if t < 3:
             tt(v("TMR"), lr, v("DTH"), gt)
             nf = listed("RWR", v("TMR"))
-            act(v("OKB", a // 16, a // 16 + 4), nf, AF.Identity, 1.0, -1.0)
             tt(v("RZ"), nf, v("TR4", 0, 4), mul)
             tt(v("RY"), v("RZ"), v("HW%d" % (t - 1), 15, S, 16), OP.max)
             tc(v("RL16"), v("RY"))
+            tc(at(v("RM"), v("RL16")), v("ONES", 0, S))
+            sixteen(v("k2", 0, NB), "SEL", "RM", 0, W)
+            x = TURN * (t + 1)
+            tt(v("AB", 0, NB - x), v("AA", 0, NB - x), v("k2", x, NB), sub)
+            tt(v("AB", NB - x, NB), v("AA", NB - x, NB), v("k2", 0, x), sub)
+            act(v("AB", a // 16 - x, a // 16 - x + 4), nf, AF.Identity, 2.0, -2.0)
 
     def changes(t):
         wide = W + L
-        if 0 < t < 3:
-            tc(at(v("RM"), v("RL16")), v("ONES", 0, S))
-        tc(at(v("X", 0, wide), v("L4", 12, 24)), v("XI"))
-        tc(at(v("F2"), v("L4", 12, 24)), v("H"))
-        tc(at(v("F1"), v("L4", 36, 48)), v("H"))
-        if t < 3:
-            tc(at(v("SN", 0, wide), v("L4", 0, 12)), v("VH"))
-            tt(at(v("SN", 0, wide), v("L4", 24, 36)), v("SY"), v("VT"), add)
         if t:
-            lr, a, hr = v("lr%d" % t), 1760 + S * (t - 1), v("HR%d" % (t - 1), 0, S)
-            if t < 3:
-                act(v("RVB"), at(v("SN", 0, W), v("HS%d" % (t - 1))), scale=v("MTC", 4 + t, 5 + t))
-                tt(at(v("SN", 0, wide), v("RL16")), v("RVB"), v("CT3", S * (t - 1), S * t), add)
+            lr, a, hr = v("lr%d" % t), 1760 + S * (t - 1), v("HR%d" % (t - 1))
             tt(v("X", a, a + S), lr, v("FD"), mul)
             tt(v("F1", a, a + S), hr, v("FD"), mul)
             tt(v("F2", a, a + S), hr, v("FD"), mul)
+        if t == 3:
+            for f in ("X", "F1", "F2"):
+                fill(v(f, M, 1760), 0.0)
+        tc(at(v("X", 0, wide), v("L4", 12, 24)), v("XJB"))
+        tc(at(v("F2"), v("L4", 12, 24)), v("H", 0, L))
+        tc(at(v("F1"), v("L4", 36, 48)), v("H", 0, L))
+        if t < 3:
+            tc(at(v("SN", 0, wide), v("L4", 0, 12)), v("VH"))
+            tt(at(v("SN", 0, wide), v("L4", 24, 36)), v("SY"), v("VT"), add)
+        if 0 < t < 3:
+            act(v("RVB"), at(v("SN", 0, W), v("HS%d" % (t - 1))), scale=v("MTC", 4 + t, 5 + t))
+            tt(at(v("SN", 0, wide), v("RL16")), v("RVB"), v("CT3", S * (t - 1), S * t), add)
 
     for t in range(T_):
         lanes(t)
         if t:
             arrivals(t)
-        own()
-        if t < 3:
-            sending(t)
+        own(t)
         if t:
             returned(t)
         adopt(t)
+        if t < 3:
+            sending(t)
         changes(t)
-    for f in ("X", "F1", "F2"):
-        fill(v(f, M, 1760), 0.0)
     dma("y", ("xo", 0, W, T.xo[:]), v("X", 0, W), 4.5)
     dma("s", ("fo", 0, W, T.fo[:]), v("F1", 0, W, p=(0, 128, 16)), 2.5)
     dma("s", ("f2o", 0, W, T.f2o[:]), v("F2", 0, W, p=(0, 128, 16)), 2.5)

@@ -10,11 +10,18 @@ BIG = 512.0
 KS = 8192.0
 PO = 2048.0
 ROUND = 1.5 * 2 ** 23
-SW_ = 128
-NENG = 8
-NV = {"A0": 44, "A1": 44, "A2": 44, "AB": 40}
+LW = L + 16
+NV = {"A0": 40, "A1": 40, "A2": 40, "AB": 40}
 BANK = {"A0": ("k0",), "A1": ("k1",), "A2": ("k7",), "AB": ("k2",)}
-CH = ((0, 64), (64, 128), (128, 192))
+CH = ((0, 64), (64, 192))
+SLOW = ()
+YS = (4, 4, 4, 3)
+
+
+def HALVES(n):
+    return ((0, 28), (28, n))
+
+
 TURN = Q // 16
 PARTS = ("A0", "A1", "A2", "AB")
 
@@ -30,7 +37,7 @@ def _b(kind, dtype, **kw):
     for n, w in kw.items():
         if dtype in ("bfloat16", "uint16", "float16"):
             HALF.add(n)
-        if kind == "psum" or n[:2] in ("ms", "bs", "ls", "mr", "br", "lr"):
+        if kind == "psum" or n[:2] in ("me", "be", "le", "ms", "bs", "ls", "mr", "br", "lr"):
             SCRATCH[n] = (kind, [128, w], dtype)
         else:
             p = POOL[dtype]
@@ -39,37 +46,38 @@ def _b(kind, dtype, **kw):
             SCRATCH[p[0]] = (kind, [128, p[1]], dtype)
 
 
-_b("sbuf", "float32", SN=WT, F1=W + L, F2=W + L, H=L + 16, P0=L, S0=L, S1=L, SA=L, UD=L, RMOD=384, DIAG=L, D15=L, DTH=S, OF=128, I3=384,
+_b("sbuf", "float32", SN=WT, F1=W + L, F2=W + L, H=L + 16, P0=L, S0=L, S1=L, UD=L, SA=L, YW=L, RMOD=384, DIAG=L, D15=L, DTH=S, OF=128, I3=384,
    R16=1, PBF=2, M0=1, E0=1, MK=16, TR4=48, TRM=12, TRN=12, LANB=12, LANE=L, CT3=192, ZER=128, RST=64, CB=128, CT=128, NBS=12,
    U=12, NU=12, UP=12, CA=12, CC=12, BASE=12, W1=12, W2=12, D1=12, T1=12, NF=12, BS0=384, SCB=384,
-   Z4=48, Z5=48, ZT=24, SY=L, MS=L, VT=L, VH=L, RZ=4, RY=4, RVB=S, FD=S, GENM=12, LB3=12, LBT=12, RS3=12, MTC=8,
-   TMC=S, RWC=S, NR16=1, NR17=1, NLS=4, CTS=128, AA=128, AB=128, R2=128, XJ=L)
+   Z4=48, Z5=48, ZT=24, SY=L, MS=L, VT=L, VH=L, RZ=4, RVB=S, RVD=S, GENM=12, LB3=12, LBT=12, RS3=12, MTC=8,
+   TMC=S, RWC=S, NR16=1, NR17=1, NLS=4, CTS=128, AA=128, AB=128, XJ=L)
 for _n in PARTS:
-    _b("sbuf", "float32", **{"SF" + _n: 64, "MM" + _n: 64, "DD" + _n: 64, "EE" + _n: 64})
+    _b("sbuf", "float32", **{"MM" + _n: 64, "DD" + _n: 64, "EE" + _n: 64, "SF" + _n: 64})
     _b("sbuf", "float16", **{"RR" + _n: 64})
     _b("sbuf", "bfloat16", **{"XT" + _n: 128, "XR" + _n: 1024, "UU" + _n: 1024})
     _b("sbuf", "uint16", **{"IX" + _n: 64, "LL" + _n: 4})
-_b("sbuf", "float16", SWH=512, ONESH=128, DX=384, YR=384, PICK=2048, FAS=RW, GNS=RW, RRS=RW, YP=12, TMI=128,
-   RWI=128, POR=128, ONR=384, TMP=L, RWH=L, RWP=L, RWQ=L, TMG=S, TMH=S, RWG=S)
-_b("sbuf", "bfloat16", X=WT, GN=W, RM=W + L, ANE=M, SEL=2048, WONE=128, REP=1024, ONES=L, ONESB=128, NONESB=128, TRI=128, TIMO=128,
-   SLR=128, XL=L + 16, GL=L + 16, ZEH=L, JL=4 * L, XJB=L, XS=L, IDB=128, NIDB=128, IDK=128, NIDK=128, ID16=128, IDHALF=128, QRT=128, QRZ=128, TMPB=128, WC=1, RS0=384,
+_b("sbuf", "float16", SWH=512, ONESH=128, DX=384, YR=384, PICK=2048, FAS=RW, GNS=RW, RRS=RW, YP=12, NFL=12,
+   POR=128, ONR=384, TMP=L, RWH=L, RWP=L, RWQ=L, TMH=S, HW=S)
+_b("sbuf", "bfloat16", X=WT, GN=W, RM=W + L, ANE=M, SELP=16, SEL=2048, SELD=2048, R2=128, SEV=12, EY=1056, WONE=128, REP=1024, ONES=L, ONESB=128, NONESB=128, TRI=128, TIMO=128,
+   SLR=128, ZEH=L, JL=4 * L, XJB=L, XS=L, IDB=128, NIDB=128, IDK=128, NIDK=128, ID16=128, IDHALF=128, QRT=128, QRZ=128, TMPB=128, WC=1, RS0=384,
    OK=128, OH=L, NOH=L, VAL=L, GG=L, CUM=L, JK=12 * 128, BT=512, FLG=L, BR=L, EQ0=L, EQ1=L, A0N=L, NE0=L, UR=L, ED=384, EQ=2112, NFR=L, FR=L, FRS=L,
-   AY=L, EMY=L, SR=L, SRS=L, EQS=L, TMR=S, RWR=S)
+   AY=L, EMY=L, SR=L, SRS=L, EQS=L, FD=S, XN=S)
 _b("sbuf", "int32", SNI=M, FAI=RW, GNI=RW, PI=1, PI2=1, CI=4, CI2=4)
 _b("sbuf", "uint16", BL=12, HL=12, IDX=8, P0L=12, P1L=12, SA16=L, YL=12, SL=12, L4=48, LI=4, RL16=4, BF16=4)
 _b("psum", "float32", k0=512, k1=512, k2=512, k3=512, k4=512, k5=512, k6=512, k7=512)
 for _t in range(3):
-    _b("sbuf", "bfloat16", **{"ms%d" % _t: SW_, "bs%d" % _t: SW_, "ls%d" % _t: SW_, "mr%d" % (_t + 1): S, "br%d" % (_t + 1): S, "lr%d" % (_t + 1): S})
+    _b("sbuf", "uint16", **{"ms%d" % _t: 4, "bs%d" % _t: 4, "ls%d" % _t: 4})
+    _b("sbuf", "bfloat16", **{"me%d" % _t: 2 * LW, "be%d" % _t: 2 * LW, "le%d" % _t: 2 * LW, "mr%d" % (_t + 1): S, "br%d" % (_t + 1): S, "lr%d" % (_t + 1): S})
     _b("sbuf", "float32", **{"HR%d" % _t: S})
-    _b("sbuf", "float16", **{"HW%d" % _t: S})
-    _b("sbuf", "uint16", **{"HS%d" % _t: 4})
+    _b("sbuf", "uint16", **{"HT%d" % _t: 4})
 
-MSGS = [("s", 0), ("r", 1), ("s", 1), ("r", 2), ("s", 2), ("r", 3)]
+_b("sbuf", "bfloat16", me3=LW, AX=2 * S)
+MSGS = [("e", 0), ("s", 0), ("e", 1), ("r", 1), ("s", 1), ("e", 2), ("r", 2), ("s", 2), ("r", 3)]
 SEMAPHORES = ["qv", "qs", "qt", "qg", "lo"] + ["d%d" % i for i in range(24)] + ["x%s%d" % m for m in MSGS] + ["a%s%d" % m for m in MSGS]
 
 
 def goal(T, rank, kind, t):
-    return T.cores[(rank + 1 + t) % 4] if kind == "s" else T.cores[(rank - t) % 4]
+    return T.cores[(rank + 1 + t) % 4] if kind != "r" else T.cores[(rank - t) % 4]
 
 
 def via(topo, src, dst):
@@ -82,8 +90,8 @@ def via(topo, src, dst):
 
 def send(g, topo, src, dst, out, in_, rsem, lsem):
     rid, pid = topo.addr(dst, src)
-    mask = sum(1 << e for e in topo.engines(src, dst)[:NENG])
-    g.remote_dma(out, in_, rsem, lsem, pid, rid, mask)
+    g.remote_dma(out, in_, rsem, lsem, pid, rid, topo.mask(src, dst))
+    return len(topo.engines(src, dst))
 
 
 def hand_on(g, core, T, topo):
@@ -93,18 +101,17 @@ def hand_on(g, core, T, topo):
             dst = goal(T, r, kind, t)
             if via(topo, T.cores[r], dst) == core:
                 k = "%s%d" % (kind, t)
-                g.wait_ge(T.sem["x" + k], NENG)
-                send(g, topo, core, dst, T["l" + k][:], T["b" + k][:], T.sem["a" + k], T.sem.lo)
-                n += NENG
+                g.wait_ge(T.sem["x" + k], len(topo.engines(T.cores[r], core)))
+                n += send(g, topo, core, dst, T["l" + k][:], T["b" + k][:], T.sem["a" + k], T.sem.lo)
     if n:
         g.wait_ge(T.sem.lo, n)
 
 
-HOP, CY, GA, SC = 0.16, 0.00095, 1.56, 3.8
+HOP, CY, GA, SC = 0.2, 0.00097, 1.56, 3.8
 
 
-FAR = {"s0": 10.0, "r1": 7.0, "s1": 4.5, "r2": 4.5, "s2": 7.0, "r3": 7.0}
-LEAD = {"A0": 4.0, "A1": 2.0, "A2": 0.0, "AB": 2.0}
+FAR = {"e0": 28.0, "e1": 26.0, "e2": 26.0, "s0": 9.5, "r1": 9.5, "s1": 5.5, "r2": 5.5, "s2": 9.5, "r3": 9.5}
+LEAD = {"A0": 4.0, "A1": 2.0, "A2": 0.1, "AB": 2.1}
 ROWS = ("FLG", "BR", "TMP", "H", "RWH", "XL", "P0", "RWP", "RWQ", "EQ0", "S0", "A0N", "NE0", "UR", "S1", "EQ1", "UD", "SA", "SA16")
 
 
@@ -112,9 +119,7 @@ def lead(x):
     nm, lo, hi = x
     if nm[-2:] in LEAD:
         return LEAD[nm[-2:]]
-    if nm == "k4":
-        return LEAD[PARTS[lo // 128]]
-    if nm in ROWS:
+    if nm in ROWS or nm[:2] == "me" and lo < L:
         return LEAD[PARTS[lo // 64]]
     if nm in ("BL", "HL", "P0L", "P1L", "NBS"):
         return LEAD[PARTS[lo // 4]]
@@ -124,7 +129,9 @@ def lead(x):
     return 0.0
 
 
-PASSES, SHAKE = 600, 0.5
+PASSES, SHAKE = 900, 0.5
+SPARE = 0.15
+PE = 0.6
 ENDS = []
 
 
@@ -156,6 +163,17 @@ def plan(ops):
         return 0.0 if ops[a][0] == ops[b][0] == "t" else HOP
     banks = [set(x[0] for x in o[3] + o[4] if x[0] in BANKS) for o in ops]
 
+    uses = [[(ops[i][0], 0.0)] + [(b, HOP) for b in sorted(banks[i])] for i in range(n)]
+    dur = [o[6] for o in ops]
+    lag = [[[(j, dur[j] + hop(i, j)) for j in sorted(x[i])] for i in range(n)] for x in (pred, succ)]
+    far = [i for i in range(n) if ops[i][1] == "r" and ops[i][4][0][0][:2] != "le"]
+
+    def stretch(i, d):
+        dur[i] += d
+        for x, y in ((0, succ), (1, pred)):
+            for j in y[i]:
+                lag[x][j] = [(k, t + d if k == i else t) for k, t in lag[x][j]]
+
     def first(l, t, k):
         a, b = 0, len(l)
         while a < b:
@@ -167,26 +185,38 @@ def plan(ops):
         return a
 
     def place(seq, before, back):
-        at, busy = [0.0] * n, {}
+        at, gaps = [0.0] * n, lag[back]
+        busy = {r: [] for r in list("vstgy") + list(BANKS)}
         for i in seq:
-            e, us, dur = ops[i][0], ops[i][5], ops[i][6]
-            s = max([at[j] + ops[j][6] + hop(i, j) for j in before[i]], default=0.0)
-            off = dur - us if back else 0.0
+            e, us = ops[i][0], ops[i][5]
+            s = 0.0
+            for j, d in gaps[i]:
+                if at[j] + d > s:
+                    s = at[j] + d
+            off = dur[i] - us if back else 0.0
+            s += off
             moved = True
             while moved:
                 moved = False
-                for r, pad in [(e, 0.0)] + [(b, HOP) for b in banks[i]]:
-                    l = busy.get(r, ())
-                    for x, y, e2 in l[max(first(l, s + off - pad, 1) - 3, 0):]:
-                        if x >= s + off + us + pad:
+                for r, pad in uses[i]:
+                    l = busy[r]
+                    k = len(l)
+                    while k and l[k - 1][1] + pad > s + 1e-9:
+                        k -= 1
+                    for k in range(k, len(l)):
+                        x, y, e2 = l[k]
+                        if x >= s + us + pad:
                             break
-                        if (not pad or e2 != e) and y + pad > s + off + 1e-9:
-                            s = y + pad - off
-                            moved = True
-            at[i] = s
-            for r in [e] + list(banks[i]):
-                l = busy.setdefault(r, [])
-                l.insert(first(l, s + off, 0), (s + off, s + off + us, e))
+                        if (not pad or e2 != e) and y + pad > s + 1e-9:
+                            s = y + pad
+                            moved = len(uses[i]) > 1
+            at[i] = s - off
+            for r, pad in uses[i]:
+                l = busy[r]
+                k = len(l)
+                while k and l[k - 1][0] > s:
+                    k -= 1
+                l.insert(k, (s, s + us, e))
         return at
 
     def sorted_by(key, before, after):
@@ -204,7 +234,8 @@ def plan(ops):
     rest = [0.0] * n
     for i in range(n - 1, -1, -1):
         rest[i] = ops[i][6] + max([hop(i, j) + rest[j] for j in succ[i]], default=0.0)
-    key = [-rest[i] - max(lead(x) for x in ops[i][4]) for i in range(n)]
+    part = [max(lead(x) for x in ops[i][4]) for i in range(n)]
+    key = [-rest[i] - part[i] for i in range(n)]
     best = None
     ENDS.append(round(max(rest), 1))
     dice = [1]
@@ -215,15 +246,29 @@ def plan(ops):
     for k in range(PASSES):
         if k >= 3:
             mid, wide = die() * best[0], 5 + 30 * die()
-            key = [t + (SHAKE * (2 * die() - 1) if abs(t - mid) < wide else 0.0) for t in best[1]]
+            if k % 2:
+                move = {x: 4 * SHAKE * (2 * die() - 1) for x in sorted(set(part))}
+                key = [t + (move[part[i]] + 0.1 * die() if abs(t - mid) < wide else 0.0) for i, t in enumerate(best[1])]
+            else:
+                key = [t + (SHAKE * (2 * die() - 1) if abs(t - mid) < wide else 0.0) for t in best[1]]
+        late = far[k // 8 % len(far)] if k % 8 == 7 and 3 * k > PASSES else None
+        if late is not None:
+            key = best[1]
+            stretch(late, 1.0)
         at = place(sorted_by(key, pred, succ), pred, False)
-        bk = place(sorted_by([-at[i] - ops[i][6] for i in range(n)], succ, pred), succ, True)
-        at = place(sorted_by([-bk[i] - ops[i][6] for i in range(n)], pred, succ), pred, False)
-        end = max(at[i] + ops[i][6] for i in range(n))
-        if best is None or end <= best[0] + 0.03:
+        bk = place(sorted_by([-at[i] - dur[i] for i in range(n)], succ, pred), succ, True)
+        at = place(sorted_by([-bk[i] - dur[i] for i in range(n)], pred, succ), pred, False)
+        end = max(at[i] + dur[i] for i in range(n))
+        if late is not None:
+            if end <= best[0] + SPARE:
+                best = (end, at)
+            else:
+                stretch(late, -1.0)
+        elif best is None or end <= best[0] + 0.03:
             best = (min(end, best[0]) if best else end, at)
         key = at
     ENDS.append(round(best[0], 1))
+    ENDS.append([dur[i] for i in far])
     loads = [i for i in range(n) if ops[i][1] == "o"]
     return loads + [i for i in sorted_by(best[1], pred, succ) if ops[i][1] != "o"]
 
@@ -242,6 +287,10 @@ def rank_program(g, core, T, topo):
     dsem = [0]
     total = {}
     ops = []
+    landed = {}
+    for kind, t in MSGS:
+        src = [c for r, c in enumerate(T.cores) if goal(T, r, kind, t) == core][0]
+        landed["%s%d" % (kind, t)] = len(topo.engines(via(topo, src, core) or src, core))
 
     def need(e, reads, writes):
         w = {}
@@ -289,8 +338,8 @@ def rank_program(g, core, T, topo):
             need(e, reads, [])
             call()
             n = writes[0][0]
-            wr[n] = [(0, 1 << 20, "remote", "a" + n[1:], NENG)]
-            total["a" + n[1:]] = NENG
+            wr[n] = [(0, 1 << 20, "remote", "a" + n[1:], landed[n[1:]])]
+            total["a" + n[1:]] = landed[n[1:]]
             return
         need(e, reads, writes)
         if kind in "do":
@@ -392,7 +441,7 @@ def rank_program(g, core, T, topo):
 
     def mm(out, lhsT, rhs, start, stop):
         emit("t", lambda: g.tensor.matmul(ap(out), ap(lhsT), ap(rhs), start, stop), [lhsT, rhs], [out],
-             CY * max(min(64, size(lhsT)), size(out)) * (0.5 if two(lhsT) else 2))
+             CY * max(min(64, size(lhsT)), size(out)) * (PE if two(lhsT) else 4 * PE))
 
     def iota(out, pattern, base, cm, after=None):
         us = 0.15 + 2 * CY * size(out)
@@ -410,10 +459,10 @@ def rank_program(g, core, T, topo):
 
     C4 = M // 4
     turns = ("y", 0, 1, None)
-    dma("s", v("GNI"), ("gn", 0, M, T.gn[:]), 2.2)
+    dma("s", v("GNI"), ("gn", 0, M, T.gn[:]), 2.2, turns)
     for j in range(4):
-        dma("y", v("SNI", j * C4, (j + 1) * C4), ("sn", j * C4, (j + 1) * C4, T.sn[:, j * C4:(j + 1) * C4]), 3.2 + 1.1 * j, turns)
-    dma("y", v("FAI"), ("fa", 0, M, T.fa[:]), 7.0, turns)
+        dma("y", v("SNI", j * C4, (j + 1) * C4), ("sn", j * C4, (j + 1) * C4, T.sn[:, j * C4:(j + 1) * C4]), 3.5 + 1.1 * j, turns)
+    dma("s", v("FAI"), ("fa", 0, M, T.fa[:]), 3.5, turns)
     dma("y", v("X", 0, M), ("x", 0, M, T.x[:]), 8.5, turns)
     dma("y", v("WC"), ("w", 0, 1, T.w[:]), 9.0, turns)
 
@@ -486,7 +535,6 @@ def rank_program(g, core, T, topo):
     act(v("DIAG"), v("D15"), AF.Relu, 1.0, -1.0)
     act(DIAGB, v("D15"), AF.Relu, 1.0, -1.0)
     act(v("RS0"), v("RMOD"), AF.Sign)
-    act(v("RST"), v("RMOD", 0, 64), AF.Relu, float(2 ** 31), -float(2 ** 31))
     fill(v("F1", M, 1760), float(M + 1))
     act(v("F1", 1760, W + L), v("RMOD"), scale=0.0)
     fill(v("X", M, WT), BIG)
@@ -497,16 +545,24 @@ def rank_program(g, core, T, topo):
         for y in range(2):
             i = 0 if e == y else 1 if y else 2
             ts(v("SWH", 128 * (2 * e + y), 128 * (2 * e + y + 1)), v("I3", 128 * i, 128 * (i + 1)), v("PBF", e, e + 1), mul)
-    iota(v("SLR", p=(0, 1)), [[0, 8], [int(KS), 16]], 0, 0)
+    fill(v("SLR", p=(0, 1)), KS)
+    fill(v("SLR", 0, 128, 16, p=(0, 1)), -float(2 ** 32))
+    for j in range(4):
+        a = 512 * j
+        mm(v("k7"), v("IDB"), v("SEL", a, a + 512), True, False)
+        mm(v("k7", 0 if j else 1, 512), v("NIDB"), v("SEL", a - 1 if j else 0, a + 511), False, True)
+        act(v("SELD", a, a + 512), v("k7"))
     iota(v("REP", p=(0, 64)), [[-1, 64], [0, 16]], 0, 1, v("I3"))
     ts(v("REP", p=(0, 64)), v("REP", p=(0, 64)), 0.0, eq)
     iota(v("TR4"), [[0, 4], [16, 12]], TB, 0)
-    iota(v("CT3"), [[1, 192]], 1760, 0)
+    iota(v("CT3"), [[1, 192]], 1760 - M, 0)
     for nm in ("AA", "AB", "R2"):
         fill(v(nm, NB, 128), 0.0)
     fill(v("ZEH"), 0.0)
-    for nm, c in (("H", float(M)), ("XL", BIG), ("GL", 0.0)):
-        fill(v(nm, L, L + 16), c)
+    fill(v("H", L, LW), float(M))
+    for t in range(3):
+        act(v("me%d" % t, L, LW), v("ONES", 0, 16))
+        act(v("me%d" % t, LW + L, 2 * LW), v("ONES", 0, 16), scale=0.0)
     fill(v("QRZ", p=(0, 1)), 0.0)
     ts(v("TR4"), v("TR4"), R16, add)
     ts(v("TRM"), v("TR4", 0, 12), -PO, add)
@@ -516,13 +572,10 @@ def rank_program(g, core, T, topo):
     fill(v("GN", M, W), 0.0)
     dma("y", v("F2"), v("F1"), 5.0)
     iota(v("RM"), [[0, W + L]], 0, 0, v("REP"))
-    act(v("D15"), v("DIAG"), AF.Identity, 1000.0, -998.5)
-    act(v("DTH"), v("DIAG", 0, S), AF.Identity, 1000.0, -745.0)
     ts(v("M0"), R16, 0.0, eq)
     ts(v("E0"), R16, 0.0, ne, float(M), mul)
     for t in range(1, 3):
         ts(v("MTC", t, t + 1), R16, float(t), eq)
-        ts(v("MTC", 4 + t, 5 + t), R16, float(t), ne)
         ts(v("CT3", S * (t - 1), S * t), v("CT3", S * (t - 1), S * t), v("MTC", t, t + 1), mul)
     tc(v("ONESH"), v("ONESB"))
     fill(v("POR", p=(0, 1)), PO)
@@ -543,6 +596,10 @@ def rank_program(g, core, T, topo):
         k = BANK[tag][0]
         mm(v(k, 128, 256, p=(0, 64)), src, v("IDB"), True, True)
         act(v("XT" + tag, p=(0, 64)), v(k, 128, 256, p=(0, 64)))
+        if tag in SLOW:
+            for s in range(16):
+                pick(v("XR" + tag, s, 16 * NV[tag], 16), v(src[0], src[1], src[1] + NV[tag]), [[0, NV[tag]]], ge, 0, 0)
+            return
         for a in range(0, 16 * NV[tag], 384):
             b = min(a + 384, 16 * NV[tag])
             mm(v(k, 128, 128 + b - a), v("XT" + tag, p=(0, 64)), v("REP", a, b, p=(0, 64)), True, True)
@@ -570,11 +627,11 @@ def rank_program(g, core, T, topo):
             act(r("H"), r("k6"))
             tc(l("HL"), listed("RWH", r("TMP")))
             tt(r("TMP"), at(F, l("HL")), r("DIAG"), mul)
-            act(r("XL"), at(v("X"), l("HL")))
+            act(r("me%d" % t), at(v("X"), l("HL")))
             act(r("P0"), at(F, l("HL")))
             tc(l("P0L"), listed("RWP", r("TMP")))
             for h in range(a // 64, b // 64):
-                numbers("A%d" % h, v("XL", 64 * h, 64 * h + 64))
+                numbers("A%d" % h, v("me%d" % t, 64 * h, 64 * h + 64))
 
         def second(a, b):
             r, l = (lambda n: v(n, a, b)), (lambda n: v(n, a // 16, b // 16))
@@ -613,6 +670,8 @@ def rank_program(g, core, T, topo):
         tt(v("CC"), v("CA"), v("CC"), sub)
         tt(v("Z5", 0, 12), hw, v("TR4", 0, 12), sub)
         if t < 3:
+            act(v("me%d" % t, LW, LW + L), at(v("GN"), v("HL")))
+            ship("e", t, v("me%d" % t))
             mm(v("k5", 0, L), v("ONESB"), v("FLG"), True, True)
             ts(v("OH"), v("k5", 0, L), R16, eq)
             act(v("NOH"), v("OH"), AF.Identity, 1.0, -1.0)
@@ -620,40 +679,30 @@ def rank_program(g, core, T, topo):
             for x, y, n in ((0, TURN, NB - TURN), (NB - TURN, 0, TURN)):
                 act(v("R2", x, x + n), v("CB", y, y + n), AF.Relu, float(L), -1.0)
                 tt(v("AA", x, x + n), v("OK", y, y + n), v("CTS", y, y + n), mul)
-            tt(v("TMI"), v("R2"), v("k3", 0, 128), mul)
-            ts(v("IDX"), listed("RWI", v("TMI")), -1.0, mul, L - 1.0, add)
+            sixteen(v("k6", 464, 472), "SEL", "R2", 0, 128)
+            ts(v("IDX"), v("k6", 464, 472), -1.0 / (16 * SELW), mul, L - 1.0, add)
 
     def down(tag, idx, son):
         n, nv, kb = 64, NV[tag], BANK[tag][0]
         u, xr = "UU" + tag, "XR" + tag
-        a, difs = nv, []
-        for k in BANK[tag]:
-            o = 64 if k == kb else 0
-            b = min(n, a + (512 - o) // 16)
-            if a < b:
-                us, dif = v(u, 16 * a, 16 * b), v(k, o, o + 16 * (b - a))
-                mm(dif, v("XT" + tag, p=(0, 64)), v("REP", 16 * a, 16 * b, p=(0, 64)), True, False)
-                act(us, at(v("X"), idx(a, b)))
-                mm(dif, v("NIDB"), us, False, True)
-                difs.append((us, dif))
-            a = b
-        if nv:
-            ux = v(u, 0, 16 * nv)
-            tt(ux, at(v("X"), idx(0, nv)), v(xr, 0, 16 * nv), sub)
+        SP = v("k3", 256 + n * PARTS.index(tag), 256 + n * PARTS.index(tag) + n)
+        turn(SP, son)
+        us, dif = v(u, 16 * nv, 16 * n), v(kb, n, n + 16 * (n - nv))
+        mm(dif, v("XT" + tag, p=(0, 64)), v("REP", 16 * nv, 16 * n, p=(0, 64)), True, False)
+        act(us, at(v("X"), idx(nv, n)))
+        mm(dif, v("NIDB"), us, False, True)
+        for a, b in HALVES(nv):
+            ux = v(u, 16 * a, 16 * b)
+            tt(ux, at(v("X"), idx(a, b)), v(xr, 16 * a, 16 * b), sub)
             act(ux, ux, AF.Abs)
-        for us, dif in difs:
-            act(us, dif, AF.Abs)
+        act(us, dif, AF.Abs)
         mm(v(kb, 0, n), v("SLR", p=(0, 1)), v("ONES", 0, n, p=(0, 1)), True, False)
         for s in range(16):
-            mm(v(kb, 0, n), v("SEL", 128 * s, 128 * (s + 1)), v(u, s, 16 * n, 16), False, s == 15)
+            mm(v(kb, 0, n), v("SELD", 128 * s, 128 * (s + 1)), v(u, s, 16 * n, 16), False, s == 15)
         joined(17)
-        vo = 128 * PARTS.index(tag)
-        SP, KP = v("k4", vo, vo + n), v("k4", vo + n, vo + 2 * n)
-        turn(SP, son)
-        turn(KP, v(kb, 0, n))
-        low, dd, ee, rr = [v(x + tag) for x in ("MM", "DD", "EE", "RR")]
-        scan(low, v("RST"), KP, add, OP.min, float(2 ** 31))
-        tt(dd, KP, low, sub)
+        kp, dd, ee, rr = [v(x + tag) for x in ("MM", "DD", "EE", "RR")]
+        turn(kp, v(kb, 0, n))
+        scan(dd, kp, v("ZER", 0, n), add, OP.max)
         tt(ee, SP, dd, sub)
         scan(rr, dd, ee, OP.min, OP.max)
         for e in range(2):
@@ -664,7 +713,7 @@ def rank_program(g, core, T, topo):
 
     def step(tag):
         tc(v("IX" + tag), at(v("SN"), v("LL" + tag)))
-        act(v("SF" + tag), at(v("SN"), v("LL" + tag)))
+        tc(v("SF" + tag), v("IX" + tag))
         return down(tag, lambda a, b: v("IX" + tag, a, b), v("SF" + tag))
 
     def own(t):
@@ -680,25 +729,26 @@ def rank_program(g, core, T, topo):
         tt(v("D1"), v("D1"), v("U"), mul)
         tt(v("D1"), v("D1"), v("W1"), add)
         ts(v("YP"), v("D1"), 1.0, add)
+        last = [step("A%d" % h) for h in range(3)]
         early(t)
         tt(v("BASE"), v("W2"), v("NU"), mul)
         tt(v("BASE"), v("BASE"), v("CC"), add)
         for h in range(3):
-            o = 4 * h
-            x = step("A%d" % h)
+            o, x = 4 * h, last[h]
             tt(v("T1", o, o + 4), x, v("UP", o, o + 4), mul)
             tt(v("BS0", L + 16 * o, L + 16 * o + 64, 16), v("T1", o, o + 4), v("BASE", o, o + 4), add)
 
     def arrivals(t):
-        ls = "ls%d" % (t - 1)
+        ls = "AX"
+        act(v(ls, 0, S), at(v("le%d" % (t - 1), 0, LW), v("ls%d" % (t - 1))))
+        act(v(ls, S, 2 * S), at(v("le%d" % (t - 1), LW, 2 * LW), v("ls%d" % (t - 1))))
         mm(v("k2", 0, S), v("WONE"), v(ls, 0, S), True, True)
         tt(v("TMC"), v("k2", 0, S), v("DIAG", 0, S), mul)
         tc(v("CI"), listed("RWC", v("TMC")))
         numbers("AB", v(ls, 0, S))
-        tt(v("TMG"), v(ls, S, SW_), v("k3", 0, S), mul)
-        gen = listed("RWG", v("TMG"))
+        sixteen(v("k4", 16, 20), "SEL", ls, S, 2 * S)
         for d in range(3):
-            ts(v("GENM", d, 12, 3), gen, float(d + 2), eq)
+            ts(v("GENM", d, 12, 3), v("k4", 16, 20), (d + 2) * 16 * SELW, eq)
         ts(v("CI2"), v("CI"), 63, OP.bitwise_and)
         tc(v("LLAB"), v("CI2"))
         for e in range(4):
@@ -722,10 +772,9 @@ def rank_program(g, core, T, topo):
 
         def call():
             if mid is None:
-                send(g, topo, core, dst, T["l" + k][:], src[3], T.sem["a" + k], T.sem.lo)
+                sent[0] += send(g, topo, core, dst, T["l" + k][:], src[3], T.sem["a" + k], T.sem.lo)
             else:
-                send(g, topo, core, mid, T["b" + k][:], src[3], T.sem["x" + k], T.sem.lo)
-            sent[0] += NENG
+                sent[0] += send(g, topo, core, mid, T["b" + k][:], src[3], T.sem["x" + k], T.sem.lo)
         emit("g", call, [src], [v("l" + k)], 1.0, "r", FAR[k])
 
     YROW, SROW, CNT = v("k5", 0, L), v("k1", 0, L), v("k6", 0, L)
@@ -735,14 +784,16 @@ def rank_program(g, core, T, topo):
         for r in range(16):
             mm(v("k5", r, L, 16), v("PICK", 128 * r, 128 * (r + 1)), v("YP"), False, r == 15)
         joined(17)
-        tc(v("YR", 0, L), YROW)
+        if YS[t] < 11:
+            tc(v("YR", 16 * YS[t] + 16, L), v("k5", 16 * YS[t] + 16, L))
+        act(v("YW"), YROW, bias=-PO)
         ts(v("YL"), v("YP"), PO - 1, add)
         act(v("SY"), at(v("SN"), v("YL")))
         act(v("AY"), v("SY"), AF.Abs, -float(M))
         act(v("EMY"), v("AY"), AF.Sign)
-        mm(v("k6", 256, 448), v("ONESB"), v("EMY"), True, True)
-        tt(v("SR"), v("D15"), v("k6", 256, 448), lt)
-        sev = listed("SRS", v("SR"))
+        sixteen(v("k4", 32, 44), "SEL", "EMY", 0, L)
+        sev = v("SEV")
+        ts(sev, v("k4", 32, 44), 1.5 * SELW, gt)
         if t < 3:
             tt(v("ZT", 0, 12), v("YP"), v("TRN"), sub)
             tt(v("Z5", 24, 36), v("ZT", 0, 12), sev, mul)
@@ -759,16 +810,33 @@ def rank_program(g, core, T, topo):
         tt(yp, v("YP"), v("NF"), OP.max)
         scan(v("SCB", 0, L), v("RS0", 0, L), v("BS0", 0, L), mul, add)
         ts(v("SL"), sp, PO, add)
-        o = 0
+        if t < 3:
+            ts(v("NFL"), sp, M - PO, eq)
+            sending(t)
+        cuts = [(q, sum((11 - j) * 16 for j in range(q)), (11 - q) * 16) for q in range(11)]
+        for q, o, n in cuts:
+            ts(v("EQ", o, o + n), v("YR", 2 * L - n, 2 * L), PO, sub, v("BS0", L + 16 * q, L + 16 * q + 1), eq)
+            mm(v("k6", L - n, L), v("ONESB"), v("EQ", o, o + n), False, False)
         for lo, whole in ((0, YROW), (L, SROW)):
-            for q in range(11):
-                n = (11 - q) * 16
-                ts(v("EQ", o, o + n), v("YR", lo + L - n, lo + L), PO, sub, v("BS0", lo + 16 * q, lo + 16 * q + 1), eq)
-                mm(v("k6", L - n, L), v("ONESB"), v("EQ", o, o + n), False, False)
-                o += n
             tt(v("ED", lo, lo + L), v("SCB", lo, lo + L), whole, eq)
             mm(CNT, v("ONESB"), v("ED", lo, lo + L), False, False)
-        ts(v("NFR"), v("YR", L, 384), float(M), eq)
+        ys = YS[t]
+        for q, o, n in cuts[ys:]:
+            ts(v("EY", o, o + n), v("YR", L - n, L), PO, sub, v("BS0", 16 * q, 16 * q + 1), eq)
+            mm(v("k6", L - n, L), v("ONESB"), v("EY", o, o + n), False, False)
+        for part in (cuts[:min(ys, 2)], cuts[2:min(ys, 5)], cuts[5:ys]):
+            if not part:
+                continue
+            for q, o, n in part:
+                act(v("EY", o, o + n), v("YW", L - n, L), AF.Abs, v("BS0", 16 * q, 16 * q + 1), -1.0)
+            a, b = part[0][1], part[-1][1] + part[-1][2]
+            act(v("EY", a, b), v("EY", a, b), AF.Relu, 1.0, -1.0)
+            for q, o, n in part:
+                mm(v("k6", L - n, L), v("ONESB"), v("EY", o, o + n), False, False)
+            joined(len(part))
+        act(v("MS"), SROW, AF.Identity, float(M), -1.0)
+        act(v("AY"), v("MS"), AF.Abs)
+        act(v("NFR"), v("AY"), AF.Relu, 1.0, -1.0)
         mm(CNT, v("ONESB"), v("NFR"), False, True)
         if t < 3:
             tt(v("VAL"), v("OH"), CNT, gt)
@@ -777,18 +845,17 @@ def rank_program(g, core, T, topo):
         act(v("XS"), at(v("X"), v("SL")))
         XG = v("k0", 0, L)
         mm(XG, v("QRT", p=(0, 1)), v("ONES", 0, L, p=(0, 1)), True, False)
-        mm(XG, v("IDHALF"), v("XL", 0, L), False, False)
+        mm(XG, v("IDHALF"), v("me%d" % t, 0, L), False, False)
         mm(XG, v("IDHALF"), v("XS"), False, True)
         act(v("XJ"), XG, bias=ROUND)
         act(v("XJB"), v("XJ"), bias=-ROUND)
         tt(v("Z5", 12, 24), sp, v("TRM"), sub)
-        tt(v("Z5", 36, 48), v("Z5", 12, 24), v("SRS", 15, L, 16), mul)
+        tt(v("Z5", 36, 48), v("Z5", 12, 24), v("SEV"), mul)
         if t < 3:
             tt(v("EQS"), at(v("SN"), v("YL")), v("YR", L, 384), eq)
             mm(v("k7", 0, L), v("TRI"), v("EQS"), True, True)
-            act(v("MS"), SROW, AF.Identity, float(M), -1.0)
-            tt(v("k3", 256, 448), v("EQS"), v("k7", 0, L), gt)
-            tt(v("VT"), v("k3", 256, 448), v("MS"), mul)
+            tt(v("k2", 256, 448), v("EQS"), v("k7", 0, L), gt)
+            tt(v("VT"), v("k2", 256, 448), v("MS"), mul)
             act(v("VH"), SROW, AF.Identity, v("E0"), v("M0"))
         tt(v("FR"), v("DIAG"), CNT, gt)
         go = listed("FRS", v("FR"))
@@ -804,44 +871,53 @@ def rank_program(g, core, T, topo):
                 tc(v("L4", 12 * j, 12 * j + 12), v("Z4", 12 * j, 12 * j + 12))
 
     def sending(t):
-        ms, hr, hs = "ms%d" % t, "HR%d" % t, v("HS%d" % t)
-        act(v("GL", 0, L), at(v("GN"), v("HL")))
-        scan(v("CUM"), v("NFR"), v("ZEH"), add, add)
+        ms, hr = "ms%d" % t, "HR%d" % t
+        for r in range(16):
+            mm(v("k7", 256 + r, 256 + L, 16), v("PICK", 128 * r, 128 * (r + 1)), v("NFL"), True, True)
+        joined(16)
+        scan(v("CUM"), v("k7", 256, 256 + L), v("ZEH"), add, add)
         for q in range(4):
             act(v("JL", L * q, L * q + L), v("CUM"), AF.Sign, v("LANB", q, q + 1), -1.0, v("NLS", q, q + 1))
-        ts(v("LI"), v("NLS"), 0.5, mul, L / 2, add)
-        act(v(ms, 0, S), at(v("XL"), v("LI")))
-        act(v(ms, S, SW_), at(v("GL"), v("LI")))
+        ts(v(ms), v("NLS"), 0.5, mul, L / 2, add)
         ship("s", t, v(ms))
-        act(v(hr), at(v("H"), v("LI")))
-        tt(v("TMH"), v(hr), v("k3", 0, S), mul)
-        tc(hs, listed("HW%d" % t, v("TMH")))
+        act(v(hr), at(v("H"), v(ms)))
+        if t < 2:
+            tt(v("TMH"), v(hr), v("k3", 0, S), mul)
+            hw = listed("HW", v("TMH"))
+            ts(v("RZ"), hw, float(M), eq)
+            tt(v("RZ"), v("RZ"), v("TR4", 0, 4), mul)
+            tt(v("RZ"), v("RZ"), hw, OP.max)
+            tc(v("HT%d" % t), v("RZ"))
         if t == 0:
-            act(v("GN", 1760, 1760 + S), v(ms, S, SW_), AF.Identity, 1.0)
+            act(v("GN", 1760, 1760 + S), at(v("me0", LW, 2 * LW), v(ms)), AF.Identity, 1.0)
 
     def returned(t):
         lr, a = v("lr%d" % t), 1760 + S * (t - 1)
         ts(v("FD"), lr, 256.0, lt)
         if t < 3:
-            tt(v("TMR"), lr, v("DTH"), gt)
-            nf = listed("RWR", v("TMR"))
-            tt(v("RZ"), nf, v("TR4", 0, 4), mul)
-            tt(v("RY"), v("RZ"), v("HW%d" % (t - 1), 15, S, 16), OP.max)
-            tc(v("RL16"), v("RY"))
-            tc(at(v("RM"), v("RL16")), v("ONES", 0, S))
+            tc(at(v("RM"), v("HT%d" % (t - 1))), v("FD"))
+            sixteen(v("k2", 128, 132), "SEL", "FD", 0, S)
             sixteen(v("k2", 0, NB), "SEL", "RM", 0, W)
+            tt(v("RVD"), v("FD"), v("CT3", S * (t - 1), S * t), mul)
             x = TURN * (t + 1)
             tt(v("AB", 0, NB - x), v("AA", 0, NB - x), v("k2", x, NB), sub)
             tt(v("AB", NB - x, NB), v("AA", NB - x, NB), v("k2", 0, x), sub)
-            act(v("AB", a // 16 - x, a // 16 - x + 4), nf, AF.Identity, 2.0, -2.0)
+            act(v("AB", a // 16 - x, a // 16 - x + 4), v("k2", 128, 132), scale=2.0 / (16 * SELW))
 
     def changes(t):
         wide = W + L
         if t:
             lr, a, hr = v("lr%d" % t), 1760 + S * (t - 1), v("HR%d" % (t - 1))
-            tt(v("X", a, a + S), lr, v("FD"), mul)
-            tt(v("F1", a, a + S), hr, v("FD"), mul)
-            tt(v("F2", a, a + S), hr, v("FD"), mul)
+            if t < 3:
+                tt(v("X", a, a + S), lr, v("FD"), mul)
+                tt(v("F1", a, a + S), hr, v("FD"), mul)
+                tt(v("F2", a, a + S), hr, v("FD"), mul)
+            else:
+                tt(v("XN"), lr, v("FD"), mul)
+                tt(v("RVB"), hr, v("FD"), mul)
+                dma("y", ("xo", a, W, T.xo[:, a:W]), v("XN"), 2.5)
+                dma("y", ("fo", a, W, T.fo[:, a:W]), v("RVB", p=(0, 128, 16)), 2.2)
+                dma("y", ("f2o", a, W, T.f2o[:, a:W]), v("RVB", p=(0, 128, 16)), 2.2)
         if t == 3:
             for f in ("X", "F1", "F2"):
                 fill(v(f, M, 1760), 0.0)
@@ -852,8 +928,8 @@ def rank_program(g, core, T, topo):
             tc(at(v("SN", 0, wide), v("L4", 0, 12)), v("VH"))
             tt(at(v("SN", 0, wide), v("L4", 24, 36)), v("SY"), v("VT"), add)
         if 0 < t < 3:
-            act(v("RVB"), at(v("SN", 0, W), v("HS%d" % (t - 1))), scale=v("MTC", 4 + t, 5 + t))
-            tt(at(v("SN", 0, wide), v("RL16")), v("RVB"), v("CT3", S * (t - 1), S * t), add)
+            act(v("RVB"), at(v("SN", 0, wide), v("HT%d" % (t - 1))))
+            tt(at(v("SN", 0, wide), v("HT%d" % (t - 1))), v("RVB"), v("RVD"), add)
 
     for t in range(T_):
         lanes(t)
@@ -863,12 +939,11 @@ def rank_program(g, core, T, topo):
         if t:
             returned(t)
         adopt(t)
-        if t < 3:
-            sending(t)
         changes(t)
-    dma("y", ("xo", 0, W, T.xo[:]), v("X", 0, W), 4.5)
-    dma("s", ("fo", 0, W, T.fo[:]), v("F1", 0, W, p=(0, 128, 16)), 2.5)
-    dma("s", ("f2o", 0, W, T.f2o[:]), v("F2", 0, W, p=(0, 128, 16)), 2.5)
+    a = W - S
+    dma("y", ("xo", 0, a, T.xo[:, 0:a]), v("X", 0, a), 4.0)
+    dma("s", ("fo", 0, a, T.fo[:, 0:a]), v("F1", 0, a, p=(0, 128, 16)), 2.5)
+    dma("s", ("f2o", 0, a, T.f2o[:, 0:a]), v("F2", 0, a, p=(0, 128, 16)), 2.5)
 
     if not ORDER:
         ORDER.extend(plan(ops))

@@ -11,15 +11,15 @@ KS = 8192.0
 PO = 2048.0
 ROUND = 1.5 * 2 ** 23
 LW = L + 16
-NV = {"A0": 40, "A1": 40, "A2": 40, "AB": 40}
+NVT = ((40, 44, 44, 0), (36, 40, 44, 40), (36, 40, 44, 40), (40, 40, 44, 44))
 BANK = {"A0": ("k0",), "A1": ("k1",), "A2": ("k7",), "AB": ("k2",)}
 CH = ((0, 64), (64, 192))
-SLOW = ()
-YS = (4, 4, 4, 3)
+SLOW = ("A2",)
+YS = (6, 6, 6, 4)
 
 
 def HALVES(n):
-    return ((0, 28), (28, n))
+    return ((0, 28), (28, n)) if n < 48 else ((0, 20), (20, 36), (36, n))
 
 
 TURN = Q // 16
@@ -49,19 +49,19 @@ def _b(kind, dtype, **kw):
 _b("sbuf", "float32", SN=WT, F1=W + L, F2=W + L, H=L + 16, P0=L, S0=L, S1=L, UD=L, SA=L, YW=L, RMOD=384, DIAG=L, D15=L, DTH=S, OF=128, I3=384,
    R16=1, PBF=2, M0=1, E0=1, MK=16, TR4=48, TRM=12, TRN=12, LANB=12, LANE=L, CT3=192, ZER=128, RST=64, CB=128, CT=128, NBS=12,
    U=12, NU=12, UP=12, CA=12, CC=12, BASE=12, W1=12, W2=12, D1=12, T1=12, NF=12, BS0=384, SCB=384,
-   Z4=48, Z5=48, ZT=24, SY=L, MS=L, VT=L, VH=L, RZ=4, RVB=S, RVD=S, GENM=12, LB3=12, LBT=12, RS3=12, MTC=8,
+   Z4=48, Z5=48, ZT=24, SY=L, MS=L, VT=L, VH=L, RZ=4, RVB=S, RVD=S, GENM=12, LB3=16, LBT=16, RS3=16, GO2=4, GO3=4, MTC=8,
    TMC=S, RWC=S, NR16=1, NR17=1, NLS=4, CTS=128, AA=128, AB=128, XJ=L)
 for _n in PARTS:
     _b("sbuf", "float32", **{"MM" + _n: 64, "DD" + _n: 64, "EE" + _n: 64, "SF" + _n: 64})
     _b("sbuf", "float16", **{"RR" + _n: 64})
     _b("sbuf", "bfloat16", **{"XT" + _n: 128, "XR" + _n: 1024, "UU" + _n: 1024})
     _b("sbuf", "uint16", **{"IX" + _n: 64, "LL" + _n: 4})
-_b("sbuf", "float16", SWH=512, ONESH=128, DX=384, YR=384, PICK=2048, FAS=RW, GNS=RW, RRS=RW, YP=12, NFL=12,
-   POR=128, ONR=384, TMP=L, RWH=L, RWP=L, RWQ=L, TMH=S, HW=S)
+_b("sbuf", "float16", SWH=512, ONESH=128, DX=384, YR=384, PICK=2048, FAS=RW, GNS=RW, RRS=RW, YP=12, SH=12, NFL=12, IDH=128, LIFT=12, LIFB=4,
+   POR=128, ONR=384, TMP=L, RWH=L, RWP=L, RWQ=L, TMH=S, HW=S, TMI=128, RWI=128, TMG=S, RWG=S)
 _b("sbuf", "bfloat16", X=WT, GN=W, RM=W + L, ANE=M, SELP=16, SEL=2048, SELD=2048, R2=128, SEV=12, EY=1056, WONE=128, REP=1024, ONES=L, ONESB=128, NONESB=128, TRI=128, TIMO=128,
-   SLR=128, ZEH=L, JL=4 * L, XJB=L, XS=L, IDB=128, NIDB=128, IDK=128, NIDK=128, ID16=128, IDHALF=128, QRT=128, QRZ=128, TMPB=128, WC=1, RS0=384,
+   SLR=128, ZEH=L, JL=4 * L, XJB=L, XS=L, IDB=128, NIDB=128, IDK=128, IDS=128, NIDS=128, KSR=128, ID16=128, IDHALF=128, QRT=128, QRZ=128, TMPB=128, WC=1, RS0=384,
    OK=128, OH=L, NOH=L, VAL=L, GG=L, CUM=L, JK=12 * 128, BT=512, FLG=L, BR=L, EQ0=L, EQ1=L, A0N=L, NE0=L, UR=L, ED=384, EQ=2112, NFR=L, FR=L, FRS=L,
-   AY=L, EMY=L, SR=L, SRS=L, EQS=L, FD=S, XN=S)
+   AY=L, EMY=L, SR=L, SRS=L, EQS=L, FD=S, XN=S, TMR=S, RWR=S)
 _b("sbuf", "int32", SNI=M, FAI=RW, GNI=RW, PI=1, PI2=1, CI=4, CI2=4)
 _b("sbuf", "uint16", BL=12, HL=12, IDX=8, P0L=12, P1L=12, SA16=L, YL=12, SL=12, L4=48, LI=4, RL16=4, BF16=4)
 _b("psum", "float32", k0=512, k1=512, k2=512, k3=512, k4=512, k5=512, k6=512, k7=512)
@@ -73,7 +73,7 @@ for _t in range(3):
 
 _b("sbuf", "bfloat16", me3=LW, AX=2 * S)
 MSGS = [("e", 0), ("s", 0), ("e", 1), ("r", 1), ("s", 1), ("e", 2), ("r", 2), ("s", 2), ("r", 3)]
-SEMAPHORES = ["qv", "qs", "qt", "qg", "lo"] + ["d%d" % i for i in range(24)] + ["x%s%d" % m for m in MSGS] + ["a%s%d" % m for m in MSGS]
+SEMAPHORES = ["qv", "qs", "qt", "qg", "lo"] + ["d%d" % i for i in range(40)] + ["x%s%d" % m for m in MSGS] + ["a%s%d" % m for m in MSGS]
 
 
 def goal(T, rank, kind, t):
@@ -107,10 +107,10 @@ def hand_on(g, core, T, topo):
         g.wait_ge(T.sem.lo, n)
 
 
-HOP, CY, GA, SC = 0.2, 0.00097, 1.56, 3.8
+HOP, CY, GA, SC = 0.27, 0.001, 1.56, 3.8
 
 
-FAR = {"e0": 28.0, "e1": 26.0, "e2": 26.0, "s0": 9.5, "r1": 9.5, "s1": 5.5, "r2": 5.5, "s2": 9.5, "r3": 9.5}
+FAR = {"e0": 28.0, "e1": 26.0, "e2": 26.0, "s0": 9.0, "r1": 9.0, "s1": 5.0, "r2": 5.0, "s2": 9.0, "r3": 9.0}
 LEAD = {"A0": 4.0, "A1": 2.0, "A2": 0.1, "AB": 2.1}
 ROWS = ("FLG", "BR", "TMP", "H", "RWH", "XL", "P0", "RWP", "RWQ", "EQ0", "S0", "A0N", "NE0", "UR", "S1", "EQ1", "UD", "SA", "SA16")
 
@@ -129,9 +129,10 @@ def lead(x):
     return 0.0
 
 
-PASSES, SHAKE = 900, 0.5
+PASSES, SHAKE = 1500, 0.3
 SPARE = 0.15
 PE = 0.6
+OWN = 0.28
 ENDS = []
 
 
@@ -160,7 +161,7 @@ def plan(ops):
             succ[j].append(i)
 
     def hop(a, b):
-        return 0.0 if ops[a][0] == ops[b][0] == "t" else HOP
+        return 0.0 if ops[a][0] == ops[b][0] == "t" else OWN if ops[a][0] == ops[b][0] else HOP
     banks = [set(x[0] for x in o[3] + o[4] if x[0] in BANKS) for o in ops]
 
     uses = [[(ops[i][0], 0.0)] + [(b, HOP) for b in sorted(banks[i])] for i in range(n)]
@@ -243,30 +244,45 @@ def plan(ops):
     def die():
         dice[0] = (dice[0] * 1103515245 + 12345) % 2 ** 31
         return dice[0] / 2 ** 31
-    for k in range(PASSES):
-        if k >= 3:
-            mid, wide = die() * best[0], 5 + 30 * die()
-            if k % 2:
-                move = {x: 4 * SHAKE * (2 * die() - 1) for x in sorted(set(part))}
-                key = [t + (move[part[i]] + 0.1 * die() if abs(t - mid) < wide else 0.0) for i, t in enumerate(best[1])]
-            else:
-                key = [t + (SHAKE * (2 * die() - 1) if abs(t - mid) < wide else 0.0) for t in best[1]]
-        late = far[k // 8 % len(far)] if k % 8 == 7 and 3 * k > PASSES else None
-        if late is not None:
-            key = best[1]
-            stretch(late, 1.0)
-        at = place(sorted_by(key, pred, succ), pred, False)
+    marks = [i for i in range(n) if ops[i][4][0][0] == "OK"][2:]
+
+    def packed(key, again):
+        at = place(sorted_by(key, pred, succ), pred, False) if again else key
         bk = place(sorted_by([-at[i] - dur[i] for i in range(n)], succ, pred), succ, True)
         at = place(sorted_by([-bk[i] - dur[i] for i in range(n)], pred, succ), pred, False)
-        end = max(at[i] + dur[i] for i in range(n))
-        if late is not None:
-            if end <= best[0] + SPARE:
-                best = (end, at)
+        return max(at[i] + dur[i] for i in range(n)), at
+    for k in range(3):
+        best = packed(key, True)
+        key = best[1]
+    for k in range(PASSES):
+        if k % 16 == 7 and 3 * k > PASSES:
+            late = far[k // 16 % len(far)]
+            stretch(late, 1.0)
+            got = packed(best[1], True)
+            if got[0] <= best[0] + SPARE:
+                best = got
             else:
                 stretch(late, -1.0)
-        elif best is None or end <= best[0] + 0.03:
-            best = (min(end, best[0]) if best else end, at)
-        key = at
+            continue
+        cut = [0.0] + [best[1][i] for i in marks] + [best[0]]
+        rnd = [sum(t >= c for c in cut[1:-1]) for t in best[1]]
+        spot = [(a + die() * (b - a), 4 + 22 * die()) for a, b in zip(cut, cut[1:])]
+        if k % 2:
+            move = [{x: 4 * SHAKE * (2 * die() - 1) for x in sorted(set(part))} for c in spot]
+            key = [t + (move[rnd[i]][part[i]] + 0.1 * die() if abs(t - spot[rnd[i]][0]) < spot[rnd[i]][1] else 0.0) for i, t in enumerate(best[1])]
+        else:
+            key = [t + (SHAKE * (2 * die() - 1) if abs(t - spot[rnd[i]][0]) < spot[rnd[i]][1] else 0.0) for i, t in enumerate(best[1])]
+        got = packed(key, k % 3 == 0)
+        if got[0] <= best[0] + 0.4 * (1 - k / PASSES) * die():
+            best = got
+            continue
+        new = [0.0] + [got[1][i] for i in marks] + [got[0]]
+        won = [new[r + 1] - new[r] < cut[r + 1] - cut[r] - 0.05 for r in range(len(spot))]
+        if any(won):
+            key = [got[1][i] - new[rnd[i]] + cut[rnd[i]] if won[rnd[i]] else t for i, t in enumerate(best[1])]
+            got = packed(key, False)
+            if got[0] <= best[0] + 0.02 + 0.4 * (1 - k / PASSES) * die():
+                best = got
     ENDS.append(round(best[0], 1))
     ENDS.append([dur[i] for i in far])
     loads = [i for i in range(n) if ops[i][1] == "o"]
@@ -287,6 +303,7 @@ def rank_program(g, core, T, topo):
     dsem = [0]
     total = {}
     ops = []
+    NV = {}
     landed = {}
     for kind, t in MSGS:
         src = [c for r, c in enumerate(T.cores) if goal(T, r, kind, t) == core][0]
@@ -482,6 +499,7 @@ def rank_program(g, core, T, topo):
     fill(v("SEL"), 0.0)
     for s in range(16):
         act(v("SEL", s * 128 + s, (s + 1) * 128, 16), v("ONESB", s, 128, 16), scale=SELW)
+    joined(16)
     act(v("NONESB"), v("ONESB"), scale=-1.0)
     pick(v("TRI"), v("ONESB"), [[1, 128]], ge, -1, -1)
     pick(v("TIMO"), v("NONESB"), [[-1, 128]], ge, -1, 1)
@@ -496,10 +514,10 @@ def rank_program(g, core, T, topo):
     for i, base in enumerate((0, 16, -16)):
         pick(v("I3", 128 * i, 128 * (i + 1)), v("OF"), [[-1, 128]], eq, base, 1)
     ID = v("I3", 0, 128)
-    for nm, c in (("IDB", 1.0), ("NIDB", -1.0), ("IDK", float(BK)), ("NIDK", -float(BK)), ("ID16", 16.0), ("IDHALF", 0.5)):
+    for nm, c in (("IDB", 1.0), ("NIDB", -1.0), ("IDK", float(BK)), ("IDS", KS), ("NIDS", -KS), ("ID16", 16.0), ("IDHALF", 0.5)):
         act(v(nm), ID, scale=c)
-    act(v("OF"), ID, scale=-1.0)
-    NID = v("OF")
+    tc(v("IDH"), ID)
+    fill(v("KSR", p=(0, 1)), KS)
     for t in range(T_):
         a = Q * t // 16
         iota(v("BT", 128 * t, 128 * t + NB - a), [[1, NB - a]], a, 0)
@@ -577,7 +595,6 @@ def rank_program(g, core, T, topo):
     for t in range(1, 3):
         ts(v("MTC", t, t + 1), R16, float(t), eq)
         ts(v("CT3", S * (t - 1), S * t), v("CT3", S * (t - 1), S * t), v("MTC", t, t + 1), mul)
-    tc(v("ONESH"), v("ONESB"))
     fill(v("POR", p=(0, 1)), PO)
     fill(v("ONR", p=(0, 1)), 1.0)
     fill(v("QRT", p=(0, 1)), -0.25)
@@ -585,7 +602,7 @@ def rank_program(g, core, T, topo):
     act(v("SCB"), v("RMOD"), AF.Abs, v("NR17"))
     act(v("BS0"), v("SCB"), AF.Relu, PO, -PO)
     fill(v("RS3"), 1.0)
-    fill(v("RS3", 0, 12, 3), 0.0)
+    fill(v("RS3", 0, 16, 4), 0.0)
 
     def listed(res, masked):
         a, b = masked[1:3]
@@ -599,6 +616,7 @@ def rank_program(g, core, T, topo):
         if tag in SLOW:
             for s in range(16):
                 pick(v("XR" + tag, s, 16 * NV[tag], 16), v(src[0], src[1], src[1] + NV[tag]), [[0, NV[tag]]], ge, 0, 0)
+            joined(16)
             return
         for a in range(0, 16 * NV[tag], 384):
             b = min(a + 384, 16 * NV[tag])
@@ -646,15 +664,16 @@ def rank_program(g, core, T, topo):
             mm(KK, v("NONESB"), r("NE0"), False, True)
             act(r("UR"), KK, AF.Relu, 1.0)
             mm(W0, ID, r("S0"), True, False)
-            mm(W0, v("IDK"), r("EQ0"), False, True)
-            mm(WD, NID, r("S0"), True, False)
-            mm(WD, v("NIDK"), r("EQ0"), False, False)
+            mm(W0, v("IDK"), r("EQ0"), False, False)
+            mm(W0, v("IDS"), r("UR"), False, True)
+            act(r("UD"), W0)
+            mm(WD, v("KSR", p=(0, 1)), v("ONES", a, b, p=(0, 1)), True, False)
+            mm(WD, v("NIDS"), r("UR"), False, False)
             act(r("S1"), at(tab, l("P1L")))
             tt(r("EQ1"), at(tab, l("P1L")), r("P0"), eq)
             mm(WD, ID, r("S1"), False, False)
             mm(WD, v("IDK"), r("EQ1"), False, True)
-            tt(r("UD"), WD, r("UR"), mul)
-            tt(r("SA"), W0, r("UD"), add)
+            tt(r("SA"), WD, r("UD"), OP.min)
             tc(r("SA16"), r("SA"))
         for stage in (first, second):
             for a, b in CH:
@@ -666,8 +685,9 @@ def rank_program(g, core, T, topo):
         ts(v("CA"), pw, 64.0, ge)
         tt(v("UP"), v("CA"), v("U"), mul)
         act(v("CA"), v("U"), scale=M - PO)
-        act(v("CC"), v("UP"), scale=float(M))
+        act(v("CC"), v("UP"), scale=M - KS)
         tt(v("CC"), v("CA"), v("CC"), sub)
+        ts(v("LIFT"), v("UP"), -2 * PO, mul, PO, add)
         tt(v("Z5", 0, 12), hw, v("TR4", 0, 12), sub)
         if t < 3:
             act(v("me%d" % t, LW, LW + L), at(v("GN"), v("HL")))
@@ -679,10 +699,10 @@ def rank_program(g, core, T, topo):
             for x, y, n in ((0, TURN, NB - TURN), (NB - TURN, 0, TURN)):
                 act(v("R2", x, x + n), v("CB", y, y + n), AF.Relu, float(L), -1.0)
                 tt(v("AA", x, x + n), v("OK", y, y + n), v("CTS", y, y + n), mul)
-            sixteen(v("k6", 464, 472), "SEL", "R2", 0, 128)
-            ts(v("IDX"), v("k6", 464, 472), -1.0 / (16 * SELW), mul, L - 1.0, add)
+            tt(v("TMI"), v("R2"), v("k3", 0, 128), mul)
+            ts(v("IDX"), listed("RWI", v("TMI")), -1.0, mul, L - 1.0, add)
 
-    def down(tag, idx, son):
+    def down(tag, idx, son, lift=None):
         n, nv, kb = 64, NV[tag], BANK[tag][0]
         u, xr = "UU" + tag, "XR" + tag
         SP = v("k3", 256 + n * PARTS.index(tag), 256 + n * PARTS.index(tag) + n)
@@ -705,16 +725,19 @@ def rank_program(g, core, T, topo):
         scan(dd, kp, v("ZER", 0, n), add, OP.max)
         tt(ee, SP, dd, sub)
         scan(rr, dd, ee, OP.min, OP.max)
+        if lift:
+            mm(v(kb, 0, 4), v("IDH"), lift, True, False)
         for e in range(2):
             for y in range(2):
-                mm(v(kb, e, 4, 2), v("SWH", 128 * (2 * e + y), 128 * (2 * e + y + 1)), v("RR" + tag, 15 + 16 * y, n, 32), y == 0, y == 1)
-        joined(4)
+                mm(v(kb, e, 4, 2), v("SWH", 128 * (2 * e + y), 128 * (2 * e + y + 1)), v("RR" + tag, 15 + 16 * y, n, 32),
+                   y == 0 and not lift, y == 1 and (e == 1 or not lift))
+        joined(5 if lift else 4)
         return v(kb, 0, 4)
 
-    def step(tag):
+    def step(tag, lift=None):
         tc(v("IX" + tag), at(v("SN"), v("LL" + tag)))
         tc(v("SF" + tag), v("IX" + tag))
-        return down(tag, lambda a, b: v("IX" + tag, a, b), v("SF" + tag))
+        return down(tag, lambda a, b: v("IX" + tag, a, b), v("SF" + tag), lift)
 
     def own(t):
         for h in range(3):
@@ -729,14 +752,14 @@ def rank_program(g, core, T, topo):
         tt(v("D1"), v("D1"), v("U"), mul)
         tt(v("D1"), v("D1"), v("W1"), add)
         ts(v("YP"), v("D1"), 1.0, add)
-        last = [step("A%d" % h) for h in range(3)]
+        last = [step("A%d" % h, v("LIFT", 4 * h, 4 * h + 4)) for h in range(3)]
         early(t)
         tt(v("BASE"), v("W2"), v("NU"), mul)
         tt(v("BASE"), v("BASE"), v("CC"), add)
         for h in range(3):
             o, x = 4 * h, last[h]
-            tt(v("T1", o, o + 4), x, v("UP", o, o + 4), mul)
-            tt(v("BS0", L + 16 * o, L + 16 * o + 64, 16), v("T1", o, o + 4), v("BASE", o, o + 4), add)
+            tt(v("SH", o, o + 4), x, v("BASE", o, o + 4), OP.min)
+            tt(v("BS0", L + 16 * o, L + 16 * o + 64, 16), x, v("BASE", o, o + 4), OP.min)
 
     def arrivals(t):
         ls = "AX"
@@ -746,20 +769,27 @@ def rank_program(g, core, T, topo):
         tt(v("TMC"), v("k2", 0, S), v("DIAG", 0, S), mul)
         tc(v("CI"), listed("RWC", v("TMC")))
         numbers("AB", v(ls, 0, S))
-        sixteen(v("k4", 16, 20), "SEL", ls, S, 2 * S)
-        for d in range(3):
-            ts(v("GENM", d, 12, 3), v("k4", 16, 20), (d + 2) * 16 * SELW, eq)
+        tt(v("TMG"), v(ls, S, 2 * S), v("k3", 0, S), mul)
+        gen = listed("RWG", v("TMG"))
+        for d in range(2):
+            ts(v("GENM", d, 12, 3), gen, float(d + 2), eq)
+        joined(2)
+        ts(v("GO2"), gen, 3.0, sub)
+        act(v("GO3"), v("GO2"), AF.Abs)
+        ts(v("LB3", 0, 16, 4), v("GO3"), 1.5, gt, float(M), mul)
+        ts(v("LB3", 3, 16, 4), gen, 4.0, eq, KS, mul)
+        ts(v("LIFB"), gen, 4.0, ne, 2 * PO, mul)
         ts(v("CI2"), v("CI"), 63, OP.bitwise_and)
         tc(v("LLAB"), v("CI2"))
         for e in range(4):
-            x = step("AB")
+            x = step("AB", v("LIFB") if e == 3 else None)
             if e < 3:
                 tc(v("LLAB"), x)
-            if e:
-                act(v("LB3", e - 1, 12, 3), x, bias=-float(M))
-        tt(v("LBT"), v("LB3"), v("GENM"), mul)
-        scan(v("LB3"), v("RS3"), v("LBT"), mul, add)
-        ts(v("BF16"), v("LB3", 2, 12, 3), float(M), add)
+            if 0 < e < 3:
+                tt(v("LB3", e, 16, 4), x, v("GENM", e - 1, 12, 3), mul)
+        scan(v("LBT"), v("RS3"), v("LB3"), mul, add)
+        tt(v("GO2"), x, v("LBT", 3, 16, 4), OP.min)
+        tc(v("BF16"), v("GO2"))
         act(v("mr%d" % t), at(v("X"), v("BF16")))
         ship("r", t, v("mr%d" % t))
 
@@ -803,15 +833,16 @@ def rank_program(g, core, T, topo):
         sp, yp = v("BS0", L, 384, 16), v("BS0", 0, L, 16)
         scan(v("SCB", L, 384), v("RS0", 0, L), v("BS0", L, 384), mul, add)
         mm(SROW, v("POR", p=(0, 1)), v("ONR", 0, L, p=(0, 1)), True, False)
-        tt(v("DX", 0, L), v("SCB", L, 384), DIAGB, mul)
-        mm(SROW, v("ONESH"), v("DX", 0, L), False, True)
+        for r in range(16):
+            mm(v("k1", r, L, 16), v("PICK", 128 * r, 128 * (r + 1)), v("SH"), False, r == 15)
+        joined(17)
         tc(v("YR", L, 384), SROW)
         ts(v("NF"), sp, M - PO, ne, -2 * PO, mul)
         tt(yp, v("YP"), v("NF"), OP.max)
         scan(v("SCB", 0, L), v("RS0", 0, L), v("BS0", 0, L), mul, add)
         ts(v("SL"), sp, PO, add)
+        ts(v("NFR"), SROW, float(M), eq)
         if t < 3:
-            ts(v("NFL"), sp, M - PO, eq)
             sending(t)
         cuts = [(q, sum((11 - j) * 16 for j in range(q)), (11 - q) * 16) for q in range(11)]
         for q, o, n in cuts:
@@ -834,9 +865,6 @@ def rank_program(g, core, T, topo):
             for q, o, n in part:
                 mm(v("k6", L - n, L), v("ONESB"), v("EY", o, o + n), False, False)
             joined(len(part))
-        act(v("MS"), SROW, AF.Identity, float(M), -1.0)
-        act(v("AY"), v("MS"), AF.Abs)
-        act(v("NFR"), v("AY"), AF.Relu, 1.0, -1.0)
         mm(CNT, v("ONESB"), v("NFR"), False, True)
         if t < 3:
             tt(v("VAL"), v("OH"), CNT, gt)
@@ -854,6 +882,7 @@ def rank_program(g, core, T, topo):
         if t < 3:
             tt(v("EQS"), at(v("SN"), v("YL")), v("YR", L, 384), eq)
             mm(v("k7", 0, L), v("TRI"), v("EQS"), True, True)
+            act(v("MS"), SROW, AF.Identity, float(M), -1.0)
             tt(v("k2", 256, 448), v("EQS"), v("k7", 0, L), gt)
             tt(v("VT"), v("k2", 256, 448), v("MS"), mul)
             act(v("VH"), SROW, AF.Identity, v("E0"), v("M0"))
@@ -872,10 +901,7 @@ def rank_program(g, core, T, topo):
 
     def sending(t):
         ms, hr = "ms%d" % t, "HR%d" % t
-        for r in range(16):
-            mm(v("k7", 256 + r, 256 + L, 16), v("PICK", 128 * r, 128 * (r + 1)), v("NFL"), True, True)
-        joined(16)
-        scan(v("CUM"), v("k7", 256, 256 + L), v("ZEH"), add, add)
+        scan(v("CUM"), v("NFR"), v("ZEH"), add, add)
         for q in range(4):
             act(v("JL", L * q, L * q + L), v("CUM"), AF.Sign, v("LANB", q, q + 1), -1.0, v("NLS", q, q + 1))
         ts(v(ms), v("NLS"), 0.5, mul, L / 2, add)
@@ -896,13 +922,14 @@ def rank_program(g, core, T, topo):
         ts(v("FD"), lr, 256.0, lt)
         if t < 3:
             tc(at(v("RM"), v("HT%d" % (t - 1))), v("FD"))
-            sixteen(v("k2", 128, 132), "SEL", "FD", 0, S)
+            tt(v("TMR"), v("FD"), v("k3", 0, S), mul)
+            come = listed("RWR", v("TMR"))
             sixteen(v("k2", 0, NB), "SEL", "RM", 0, W)
             tt(v("RVD"), v("FD"), v("CT3", S * (t - 1), S * t), mul)
             x = TURN * (t + 1)
+            act(v("AA", a // 16 - x, a // 16 - x + 4), come, scale=2.0)
             tt(v("AB", 0, NB - x), v("AA", 0, NB - x), v("k2", x, NB), sub)
             tt(v("AB", NB - x, NB), v("AA", NB - x, NB), v("k2", 0, x), sub)
-            act(v("AB", a // 16 - x, a // 16 - x + 4), v("k2", 128, 132), scale=2.0 / (16 * SELW))
 
     def changes(t):
         wide = W + L
@@ -932,6 +959,7 @@ def rank_program(g, core, T, topo):
             tt(at(v("SN", 0, wide), v("HT%d" % (t - 1))), v("RVB"), v("RVD"), add)
 
     for t in range(T_):
+        NV.update(zip(PARTS, NVT[t]))
         lanes(t)
         if t:
             arrivals(t)

@@ -3,23 +3,29 @@ from concourse.mybir import AluOpType as OP, ActivationFunctionType as AF
 M, W, L, S, T_, Q = 1744, 1952, 192, 64, 4, 560
 NB = W // 16
 RW = M // 16
-BK = 2176
-WT = BK + W + 32
 TB = W
+DEAD = 2344
+BK = 2368
+WT = 2352
+IDB = WT
+WI = IDB + W + 16
 BIG = 512.0
 KS = 8192.0
-PO = 2048.0
+PO = 2040.0
 ROUND = 1.5 * 2 ** 23
 LW = L + 16
-NVT = ((40, 44, 44, 0), (36, 40, 44, 40), (36, 40, 44, 40), (40, 40, 44, 44))
-BANK = {"A0": ("k0",), "A1": ("k1",), "A2": ("k7",), "AB": ("k2",)}
-CH = ((0, 64), (64, 192))
+NVT = (((40,) * 3, (42,) * 3, (44,) * 3, (0,)),) + (((40,) * 3, (40,) * 3, (42,) * 3, (36, 40, 40, 40)),) * 3
+BANK = {"A0": ("k0",), "A1": ("k1",), "A2": ("k7",), "AB": ("k2", "k4")}
+CH = ((0, 64), (64, 128), (128, 192))
+LB = (("k6", "k6", "k5", "k5", "k4"), ("k6", "k6", "k5", "k5", "k4"))
 SLOW = ("A2",)
-YS = (6, 6, 6, 4)
+YS = (0, 0, 0, 0)
+SS = (0, 0, 0, 0)
+PV = 8
 
 
 def HALVES(n):
-    return ((0, 28), (28, n)) if n < 48 else ((0, 20), (20, 36), (36, n))
+    return ((0, 16), (16, 30), (30, n))
 
 
 TURN = Q // 16
@@ -37,7 +43,7 @@ def _b(kind, dtype, **kw):
     for n, w in kw.items():
         if dtype in ("bfloat16", "uint16", "float16"):
             HALF.add(n)
-        if kind == "psum" or n[:2] in ("me", "be", "le", "ms", "bs", "ls", "mr", "br", "lr"):
+        if kind == "psum" or n[:2] in ("me", "be", "le", "ms", "bs", "ls", "mr", "br", "lr", "mf", "bf", "lf", "mg", "bg", "lg"):
             SCRATCH[n] = (kind, [128, w], dtype)
         else:
             p = POOL[dtype]
@@ -46,38 +52,43 @@ def _b(kind, dtype, **kw):
             SCRATCH[p[0]] = (kind, [128, p[1]], dtype)
 
 
-_b("sbuf", "float32", SN=WT, F1=W + L, F2=W + L, H=L + 16, P0=L, S0=L, S1=L, UD=L, SA=L, YW=L, RMOD=384, DIAG=L, D15=L, DTH=S, OF=128, I3=384,
-   R16=1, PBF=2, M0=1, E0=1, MK=16, TR4=48, TRM=12, TRN=12, LANB=12, LANE=L, CT3=192, ZER=128, RST=64, CB=128, CT=128, NBS=12,
-   U=12, NU=12, UP=12, CA=12, CC=12, BASE=12, W1=12, W2=12, D1=12, T1=12, NF=12, BS0=384, SCB=384,
-   Z4=48, Z5=48, ZT=24, SY=L, MS=L, VT=L, VH=L, RZ=4, RVB=S, RVD=S, GENM=12, LB3=16, LBT=16, RS3=16, GO2=4, GO3=4, MTC=8,
+_b("sbuf", "float32", UB=12, SN=WI, F1=W + 2 * L, F2=W + 2 * L, H0=LW, H1=LW, NU=12, S0=L, UD=L, SA=L, YW=384, RMOD=384, DIAG=L, D15=L, DT=L, OF=128, I3=384,
+   R16=1, PBF=2, M0=1, E0=1, MK=16, TR=12, TRP=12, LANB=12, LANE=L, CT0=128, CT3=128, ZER=128, CB=128, CT=128, NBS=12,
+   UY=12, CA=12, W1=12, W2=12, NF=12, NS=12, BS0=384, SCB=384,
+   Z4=48, Z5=48, SY=L, MS=L, VT=L, VH=L, RZ=4, RVB=S, RVD=S, MTC=8,
    TMC=S, RWC=S, NR16=1, NR17=1, NLS=4, CTS=128, AA=128, AB=128, XJ=L)
 for _n in PARTS:
     _b("sbuf", "float32", **{"MM" + _n: 64, "DD" + _n: 64, "EE" + _n: 64, "SF" + _n: 64})
-    _b("sbuf", "float16", **{"RR" + _n: 64})
+    _b("sbuf", "float16", **{"RR" + _n: 64, "RT" + _n: 64})
     _b("sbuf", "bfloat16", **{"XT" + _n: 128, "XR" + _n: 1024, "UU" + _n: 1024})
     _b("sbuf", "uint16", **{"IX" + _n: 64, "LL" + _n: 4})
-_b("sbuf", "float16", SWH=512, ONESH=128, DX=384, YR=384, PICK=2048, FAS=RW, GNS=RW, RRS=RW, YP=12, SH=12, NFL=12, IDH=128, LIFT=12, LIFB=4,
-   POR=128, ONR=384, TMP=L, RWH=L, RWP=L, RWQ=L, TMH=S, HW=S, TMI=128, RWI=128, TMG=S, RWG=S)
-_b("sbuf", "bfloat16", X=WT, GN=W, RM=W + L, ANE=M, SELP=16, SEL=2048, SELD=2048, R2=128, SEV=12, EY=1056, WONE=128, REP=1024, ONES=L, ONESB=128, NONESB=128, TRI=128, TIMO=128,
-   SLR=128, ZEH=L, JL=4 * L, XJB=L, XS=L, IDB=128, NIDB=128, IDK=128, IDS=128, NIDS=128, KSR=128, ID16=128, IDHALF=128, QRT=128, QRZ=128, TMPB=128, WC=1, RS0=384,
-   OK=128, OH=L, NOH=L, VAL=L, GG=L, CUM=L, JK=12 * 128, BT=512, FLG=L, BR=L, EQ0=L, EQ1=L, A0N=L, NE0=L, UR=L, ED=384, EQ=2112, NFR=L, FR=L, FRS=L,
-   AY=L, EMY=L, SR=L, SRS=L, EQS=L, FD=S, XN=S, TMR=S, RWR=S)
+_b("sbuf", "float16", S1=L, TMQ=L, YR=384, FAS=RW, RRS=RW, YP=12,
+   POR=128, ONR=384, TMP=L, RWH=L, RWP=L, RWQ=L, TMH=S, HW=S, TMI=128, RWI=128, TMG=S, RWG=S, FR=L, FRS=L)
+_b("sbuf", "bfloat16", X=WT, GN=W, RM=W + 2 * S, ANE=M, SWH=512, PICK=2048, WSEL=144, GN1=M, GNS=RW, LIFT=12, LIFB=12, SEL=144, SELD=144, R2=128, WONE=128, REP=1024, ONES=L, ONESB=128, NONESB=128, ONESK=128, NONESK=128,
+   TRI=128, TIMO=128, SLR=128, ZEH=L, JL=4 * L, XJB=L, XS=L, IDB=128, NIDB=128, IDK=128, IDD=128, FST=128, KSR=128, KS1=128, ID16=128, IDHALF=128, QRT=128, TMPB=128,
+   WC=1, RS0=384, OK=128, OH=L, NOH=L, VAL=L, GG=L, CUM=L, JK=12 * 128, BT=512, FLG=L, BR=L, EQ0=L, EQ1=L, A0N=L, NE0=L, UR=L, ED=384, EQ=2112, NFR=L,
+   AY=L, EMY=L, EQS=L, FD=S, XN=S, TMR=S, RWR=S)
 _b("sbuf", "int32", SNI=M, FAI=RW, GNI=RW, PI=1, PI2=1, CI=4, CI2=4)
-_b("sbuf", "uint16", BL=12, HL=12, IDX=8, P0L=12, P1L=12, SA16=L, YL=12, SL=12, L4=48, LI=4, RL16=4, BF16=4)
+_b("sbuf", "uint16", BL=12, HL=12, IDX=8, P0L=12, P1L=12, SA16=L, YL=12, SL=12, L40=48, L41=48, BF16=4)
 _b("psum", "float32", k0=512, k1=512, k2=512, k3=512, k4=512, k5=512, k6=512, k7=512)
 for _t in range(3):
     _b("sbuf", "uint16", **{"ms%d" % _t: 4, "bs%d" % _t: 4, "ls%d" % _t: 4})
-    _b("sbuf", "bfloat16", **{"me%d" % _t: 2 * LW, "be%d" % _t: 2 * LW, "le%d" % _t: 2 * LW, "mr%d" % (_t + 1): S, "br%d" % (_t + 1): S, "lr%d" % (_t + 1): S})
+    _w = 2 * LW if _t else LW
+    _b("sbuf", "bfloat16", **{"me%d" % _t: _w, "be%d" % _t: _w, "le%d" % _t: _w, "mr%d" % (_t + 1): S, "br%d" % (_t + 1): S, "lr%d" % (_t + 1): S})
     _b("sbuf", "float32", **{"HR%d" % _t: S})
     _b("sbuf", "uint16", **{"HT%d" % _t: 4})
 
-_b("sbuf", "bfloat16", me3=LW, AX=2 * S)
-MSGS = [("e", 0), ("s", 0), ("e", 1), ("r", 1), ("s", 1), ("e", 2), ("r", 2), ("s", 2), ("r", 3)]
+_b("sbuf", "bfloat16", me3=LW, AX=2 * S, AYI=L, AYB=S, mf1=S, bf1=S, lf1=S, mf2=S, bf2=S, lf2=S, lf3=S, mg0=LW, bg0=LW, lg0=LW)
+MSGS = [("e", 0), ("g", 0), ("s", 0), ("e", 1), ("f", 1), ("r", 1), ("s", 1), ("e", 2), ("f", 2), ("r", 2), ("s", 2), ("r", 3)]
 SEMAPHORES = ["qv", "qs", "qt", "qg", "lo"] + ["d%d" % i for i in range(40)] + ["x%s%d" % m for m in MSGS] + ["a%s%d" % m for m in MSGS]
 
 
 def goal(T, rank, kind, t):
-    return T.cores[(rank + 1 + t) % 4] if kind != "r" else T.cores[(rank - t) % 4]
+    return T.cores[(rank + 1 + t) % 4] if kind in "egs" else T.cores[(rank - t) % 4]
+
+
+def ages(side, t, n=LW):
+    return (side + "e%d" % t, LW, LW + n) if t else (side + "g0", 0, n)
 
 
 def via(topo, src, dst):
@@ -88,10 +99,18 @@ def via(topo, src, dst):
     return (near + c)[0]
 
 
-def send(g, topo, src, dst, out, in_, rsem, lsem):
+def engines(topo, src, dst, k):
+    e = topo.engines(src, dst)
+    if k in ("e0", "g0") and dst in topo.cores_of(src):
+        return e[:len(e) // 2] if k == "e0" else e[len(e) // 2:]
+    return e
+
+
+def send(g, topo, src, dst, k, out, in_, rsem, lsem):
     rid, pid = topo.addr(dst, src)
-    g.remote_dma(out, in_, rsem, lsem, pid, rid, topo.mask(src, dst))
-    return len(topo.engines(src, dst))
+    e = engines(topo, src, dst, k)
+    g.remote_dma(out, in_, rsem, lsem, pid, rid, sum(1 << x for x in e))
+    return len(e)
 
 
 def hand_on(g, core, T, topo):
@@ -101,18 +120,18 @@ def hand_on(g, core, T, topo):
             dst = goal(T, r, kind, t)
             if via(topo, T.cores[r], dst) == core:
                 k = "%s%d" % (kind, t)
-                g.wait_ge(T.sem["x" + k], len(topo.engines(T.cores[r], core)))
-                n += send(g, topo, core, dst, T["l" + k][:], T["b" + k][:], T.sem["a" + k], T.sem.lo)
+                g.wait_ge(T.sem["x" + k], len(engines(topo, T.cores[r], core, k)))
+                n += send(g, topo, core, dst, k, T["l" + k][:], T["b" + k][:], T.sem["a" + k], T.sem.lo)
     if n:
         g.wait_ge(T.sem.lo, n)
 
 
-HOP, CY, GA, SC = 0.27, 0.001, 1.56, 3.8
+HOP, CY, GA, SC = 0.34, 0.001, 1.56, 3.8
 
 
-FAR = {"e0": 28.0, "e1": 26.0, "e2": 26.0, "s0": 9.0, "r1": 9.0, "s1": 5.0, "r2": 5.0, "s2": 9.0, "r3": 9.0}
+FAR = {"e0": 30.0, "g0": 16.0, "e1": 20.0, "e2": 20.0, "s0": 9.0, "r1": 9.0, "s1": 5.0, "r2": 5.0, "s2": 9.0, "r3": 11.0, "f1": 9.0, "f2": 5.0}
 LEAD = {"A0": 4.0, "A1": 2.0, "A2": 0.1, "AB": 2.1}
-ROWS = ("FLG", "BR", "TMP", "H", "RWH", "XL", "P0", "RWP", "RWQ", "EQ0", "S0", "A0N", "NE0", "UR", "S1", "EQ1", "UD", "SA", "SA16")
+ROWS = ("FLG", "BR", "TMP", "H0", "H1", "RWH", "XL", "P0", "RWP", "RWQ", "EQ0", "S0", "A0N", "NE0", "UR", "S1", "EQ1", "UD", "SA", "SA16", "TMQ")
 
 
 def lead(x):
@@ -124,15 +143,15 @@ def lead(x):
     if nm in ("BL", "HL", "P0L", "P1L", "NBS"):
         return LEAD[PARTS[lo // 4]]
     for p in PARTS:
-        if nm in BANK[p]:
+        if nm == BANK[p][0]:
             return LEAD[p]
     return 0.0
 
 
-PASSES, SHAKE = 1500, 0.3
+PASSES, SHAKE = 2800, 0.3
 SPARE = 0.15
-PE = 0.6
-OWN = 0.28
+PE = 0.65
+OWN = 0.34
 ENDS = []
 
 
@@ -145,10 +164,23 @@ def plan(ops):
             pred[i].update(j for lo2, hi2, j in wr.get(nm, ()) if lo < hi2 and lo2 < hi)
         for nm, lo, hi in writes:
             pred[i].update(j for lo2, hi2, j in rd.get(nm, ()) if lo < hi2 and lo2 < hi)
-            if e == "t":
-                if nm in tlast:
-                    pred[i].add(tlast[nm])
-                tlast[nm] = i
+        if e == "t":
+            nm = writes[0][0]
+            shut, whole, inside = tlast.get(nm, ([], [], []))
+            if kind[1:] == "[]":
+                pred[i].update(shut)
+                tlast[nm] = (shut, whole + [i], [])
+            elif kind[1:] == "[":
+                pred[i].update(shut + whole)
+                tlast[nm] = ([], [], [i])
+            elif kind[1:] == "]":
+                pred[i].update(inside)
+                tlast[nm] = ([i], [], [])
+            else:
+                pred[i].add(inside[0])
+                inside.append(i)
+            if kind[1:] in ("", "]"):
+                pred[i].difference_update(inside[1:-1] if kind[1:] == "" else ())
         for nm, lo, hi in writes:
             wr[nm] = [x for x in wr.get(nm, ()) if not (lo <= x[0] and x[1] <= hi)] + [(lo, hi, i)]
             rd[nm] = [x for x in rd.get(nm, ()) if not (lo <= x[0] and x[1] <= hi)]
@@ -167,7 +199,7 @@ def plan(ops):
     uses = [[(ops[i][0], 0.0)] + [(b, HOP) for b in sorted(banks[i])] for i in range(n)]
     dur = [o[6] for o in ops]
     lag = [[[(j, dur[j] + hop(i, j)) for j in sorted(x[i])] for i in range(n)] for x in (pred, succ)]
-    far = [i for i in range(n) if ops[i][1] == "r" and ops[i][4][0][0][:2] != "le"]
+    far = [i for i in range(n) if ops[i][1] == "r" and ops[i][4][0][0][:2] not in ("le", "lg")]
 
     def stretch(i, d):
         dur[i] += d
@@ -175,63 +207,66 @@ def plan(ops):
             for j in y[i]:
                 lag[x][j] = [(k, t + d if k == i else t) for k, t in lag[x][j]]
 
-    def first(l, t, k):
-        a, b = 0, len(l)
-        while a < b:
-            m = (a + b) // 2
-            if l[m][k] <= t:
-                a = m + 1
-            else:
-                b = m
-        return a
+    what = [(o[0], o[5], uses[i], len(uses[i]) > 1) for i, o in enumerate(ops)]
 
     def place(seq, before, back):
         at, gaps = [0.0] * n, lag[back]
-        busy = {r: [] for r in list("vstgy") + list(BANKS)}
+        busy = {r: [(-9.0, -9.0, "")] for r in list("vstgy") + list(BANKS)}
         for i in seq:
-            e, us = ops[i][0], ops[i][5]
+            e, us, use, many = what[i]
             s = 0.0
             for j, d in gaps[i]:
-                if at[j] + d > s:
-                    s = at[j] + d
+                d += at[j]
+                if d > s:
+                    s = d
             off = dur[i] - us if back else 0.0
             s += off
+            if not many:
+                l = busy[e]
+                k = len(l)
+                while l[k - 1][1] > s + 1e-9:
+                    k -= 1
+                m = len(l)
+                while k < m and l[k][0] < s + us:
+                    s = l[k][1]
+                    k += 1
+                l.insert(k, (s, s + us, e))
+                at[i] = s - off
+                continue
             moved = True
             while moved:
                 moved = False
-                for r, pad in uses[i]:
+                for r, pad in use:
                     l = busy[r]
-                    k = len(l)
-                    while k and l[k - 1][1] + pad > s + 1e-9:
+                    k = m = len(l)
+                    lim = s + 1e-9 - pad
+                    while l[k - 1][1] > lim:
                         k -= 1
-                    for k in range(k, len(l)):
+                    while k < m:
                         x, y, e2 = l[k]
                         if x >= s + us + pad:
                             break
                         if (not pad or e2 != e) and y + pad > s + 1e-9:
                             s = y + pad
-                            moved = len(uses[i]) > 1
+                            moved = True
+                        k += 1
             at[i] = s - off
-            for r, pad in uses[i]:
+            for r, pad in use:
                 l = busy[r]
                 k = len(l)
-                while k and l[k - 1][0] > s:
+                while l[k - 1][0] > s:
                     k -= 1
                 l.insert(k, (s, s + us, e))
         return at
 
-    def sorted_by(key, before, after):
-        left = [len(p) for p in before]
-        free = sorted((key[i], i) for i in range(n) if not left[i])
-        seq = []
-        while free:
-            i = free.pop(0)[1]
-            seq.append(i)
-            for j in after[i]:
-                left[j] -= 1
-                if not left[j]:
-                    free.insert(first(free, key[j], 0), (key[j], j))
-        return seq
+    def sorted_by(key, before, order):
+        key = list(key)
+        for i in order:
+            for j in before[i]:
+                if key[j] >= key[i]:
+                    key[i] = key[j] + 1e-7
+        return sorted(order, key=lambda i: key[i])
+    up, down = range(n), range(n - 1, -1, -1)
     rest = [0.0] * n
     for i in range(n - 1, -1, -1):
         rest[i] = ops[i][6] + max([hop(i, j) + rest[j] for j in succ[i]], default=0.0)
@@ -247,10 +282,13 @@ def plan(ops):
     marks = [i for i in range(n) if ops[i][4][0][0] == "OK"][2:]
 
     def packed(key, again):
-        at = place(sorted_by(key, pred, succ), pred, False) if again else key
-        bk = place(sorted_by([-at[i] - dur[i] for i in range(n)], succ, pred), succ, True)
-        at = place(sorted_by([-bk[i] - dur[i] for i in range(n)], pred, succ), pred, False)
-        return max(at[i] + dur[i] for i in range(n)), at
+        if again:
+            at = place(sorted_by(key, pred, up), pred, False)
+            bk = place(sorted(up, key=lambda i: -at[i] - dur[i]), succ, True)
+        else:
+            bk = place(sorted_by([-key[i] - dur[i] for i in up], succ, down), succ, True)
+        at = place(sorted(up, key=lambda i: -bk[i] - dur[i]), pred, False)
+        return max(at[i] + dur[i] for i in up), at
     for k in range(3):
         best = packed(key, True)
         key = best[1]
@@ -285,8 +323,9 @@ def plan(ops):
                 best = got
     ENDS.append(round(best[0], 1))
     ENDS.append([dur[i] for i in far])
+    ENDS.append(best[1])
     loads = [i for i in range(n) if ops[i][1] == "o"]
-    return loads + [i for i in sorted_by(best[1], pred, succ) if ops[i][1] != "o"]
+    return loads + [i for i in sorted_by(best[1], pred, up) if ops[i][1] != "o"]
 
 
 def rank_program(g, core, T, topo):
@@ -362,8 +401,11 @@ def rank_program(g, core, T, topo):
         if kind in "do":
             sem = "d%d" % dsem[0]
             dsem[0] += 1
-            call().then_inc(T.sem[sem], 16)
-            note(e, sem, 16, reads, writes)
+            made = call()
+            made = made if isinstance(made, list) else [made]
+            for x in made:
+                x.then_inc(T.sem[sem], 16)
+            note(e, sem, 16 * len(made), reads, writes)
         else:
             sem = "q" + e
             count[sem] += 1
@@ -390,7 +432,8 @@ def rank_program(g, core, T, topo):
         def call():
             return [o[2]() for o in part][-1]
         us = sum(o[5] for o in part)
-        ops.append((part[0][0], "c", call, sum((o[3] for o in part), []), sum((o[4] for o in part), []), us, us))
+        kind = "c" + "[" * ("[" in part[0][1]) + "]" * ("]" in part[-1][1])
+        ops.append((part[0][0], kind, call, sum((o[3] for o in part), []), sum((o[4] for o in part), []), us, us))
 
     def size(x):
         return x[3].shape[1] if len(x) == 4 else 16 * x[1][3].shape[1]
@@ -458,7 +501,7 @@ def rank_program(g, core, T, topo):
 
     def mm(out, lhsT, rhs, start, stop):
         emit("t", lambda: g.tensor.matmul(ap(out), ap(lhsT), ap(rhs), start, stop), [lhsT, rhs], [out],
-             CY * max(min(64, size(lhsT)), size(out)) * (PE if two(lhsT) else 4 * PE))
+             CY * max(min(64, size(lhsT)), size(out)) * (PE if two(lhsT) else 4 * PE), "c" + "[" * start + "]" * stop)
 
     def iota(out, pattern, base, cm, after=None):
         us = 0.15 + 2 * CY * size(out)
@@ -481,7 +524,7 @@ def rank_program(g, core, T, topo):
         dma("y", v("SNI", j * C4, (j + 1) * C4), ("sn", j * C4, (j + 1) * C4, T.sn[:, j * C4:(j + 1) * C4]), 3.5 + 1.1 * j, turns)
     dma("s", v("FAI"), ("fa", 0, M, T.fa[:]), 3.5, turns)
     dma("y", v("X", 0, M), ("x", 0, M, T.x[:]), 8.5, turns)
-    dma("y", v("WC"), ("w", 0, 1, T.w[:]), 9.0, turns)
+    dma("y", v("WC"), ("w", 0, 1, T.w[:]), 25.0, turns)
 
     R16 = v("R16")
     DIAGB = v("k3", 0, L)
@@ -495,11 +538,14 @@ def rank_program(g, core, T, topo):
     tc(R16, v("PI2"))
     ts(v("MK"), v("RMOD", 0, 16), R16, eq)
     for m in range(16):
-        ts(v("PICK", 128 * m, 128 * (m + 1)), v("ONESB"), v("MK", m, m + 1), mul)
-    fill(v("SEL"), 0.0)
-    for s in range(16):
-        act(v("SEL", s * 128 + s, (s + 1) * 128, 16), v("ONESB", s, 128, 16), scale=SELW)
-    joined(16)
+        if m < PV:
+            ts(v("PICK", 128 * m, 128 * (m + 1)), v("ONESB"), v("MK", m, m + 1), mul)
+        else:
+            act(v("PICK", 128 * m, 128 * (m + 1)), v("ONESB"), scale=v("MK", m, m + 1))
+    for nm in ("SEL", "SELD"):
+        fill(v(nm), 0.0)
+        act(v(nm, 15, 143, 16), v("ONESB", 0, 128, 16), scale=SELW)
+    act(v("SELD", 16, 144, 16), v("ONESB", 0, 128, 16), scale=-SELW)
     act(v("NONESB"), v("ONESB"), scale=-1.0)
     pick(v("TRI"), v("ONESB"), [[1, 128]], ge, -1, -1)
     pick(v("TIMO"), v("NONESB"), [[-1, 128]], ge, -1, 1)
@@ -514,10 +560,14 @@ def rank_program(g, core, T, topo):
     for i, base in enumerate((0, 16, -16)):
         pick(v("I3", 128 * i, 128 * (i + 1)), v("OF"), [[-1, 128]], eq, base, 1)
     ID = v("I3", 0, 128)
-    for nm, c in (("IDB", 1.0), ("NIDB", -1.0), ("IDK", float(BK)), ("IDS", KS), ("NIDS", -KS), ("ID16", 16.0), ("IDHALF", 0.5)):
+    for nm, c in (("IDB", 1.0), ("NIDB", -1.0), ("IDK", float(BK)), ("IDD", float(DEAD - M)), ("ID16", 16.0), ("IDHALF", 0.5)):
         act(v(nm), ID, scale=c)
-    tc(v("IDH"), ID)
-    fill(v("KSR", p=(0, 1)), KS)
+    act(v("ONESK"), v("ONESB"), scale=KS)
+    act(v("NONESK"), v("ONESB"), scale=-KS)
+    fill(v("KSR", p=(0, 1)), 16 * KS)
+    fill(v("KS1", p=(0, 1)), KS)
+    tt(v("TMPB"), v("TRI"), v("IDB"), sub)
+    act(v("FST"), v("TMPB"), scale=KS)
     for t in range(T_):
         a = Q * t // 16
         iota(v("BT", 128 * t, 128 * t + NB - a), [[1, NB - a]], a, 0)
@@ -530,10 +580,11 @@ def rank_program(g, core, T, topo):
     ts(v("RRS"), v("GNI"), 2, ge, float(M + 1), mul)
     ts(v("RRS"), v("RRS"), -1.0, add)
 
-    def sixteen(out, sel, src, a, b):
+    def sixteen(out, sel, src, a, b, run=16):
         for r in range(16):
-            mm(out, v(sel, 128 * r, 128 * (r + 1)), v(src, a + r, b, 16), r == 0, r == 15)
-        joined(16)
+            mm(out, v(sel, 15 - r, 143 - r), v(src, a + r, b, 16), r == 0, r == 15)
+            if r % run == run - 1:
+                joined(run)
 
     def spread(src, j, k):
         for m in range(4 * j, 4 * j + 4):
@@ -554,7 +605,7 @@ def rank_program(g, core, T, topo):
     act(DIAGB, v("D15"), AF.Relu, 1.0, -1.0)
     act(v("RS0"), v("RMOD"), AF.Sign)
     fill(v("F1", M, 1760), float(M + 1))
-    act(v("F1", 1760, W + L), v("RMOD"), scale=0.0)
+    act(v("F1", 1760, W), v("RMOD", 0, L), scale=0.0)
     fill(v("X", M, WT), BIG)
     ts(v("PI2"), v("PI"), 4, OP.logical_shift_right, 1, OP.bitwise_and)
     tc(v("PBF", 1, 2), v("PI2"))
@@ -562,47 +613,44 @@ def rank_program(g, core, T, topo):
     for e in range(2):
         for y in range(2):
             i = 0 if e == y else 1 if y else 2
-            ts(v("SWH", 128 * (2 * e + y), 128 * (2 * e + y + 1)), v("I3", 128 * i, 128 * (i + 1)), v("PBF", e, e + 1), mul)
+            act(v("SWH", 128 * (2 * e + y), 128 * (2 * e + y + 1)), v("I3", 128 * i, 128 * (i + 1)), scale=v("PBF", e, e + 1))
     fill(v("SLR", p=(0, 1)), KS)
     fill(v("SLR", 0, 128, 16, p=(0, 1)), -float(2 ** 32))
-    for j in range(4):
-        a = 512 * j
-        mm(v("k7"), v("IDB"), v("SEL", a, a + 512), True, False)
-        mm(v("k7", 0 if j else 1, 512), v("NIDB"), v("SEL", a - 1 if j else 0, a + 511), False, True)
-        act(v("SELD", a, a + 512), v("k7"))
-    iota(v("REP", p=(0, 64)), [[-1, 64], [0, 16]], 0, 1, v("I3"))
-    ts(v("REP", p=(0, 64)), v("REP", p=(0, 64)), 0.0, eq)
-    iota(v("TR4"), [[0, 4], [16, 12]], TB, 0)
-    iota(v("CT3"), [[1, 192]], 1760 - M, 0)
+    iota(v("REP", p=(0, 64)), [[0, 1024]], 1, 0, v("I3"))
+    pick(v("REP", p=(0, 64)), v("REP", p=(0, 64)), [[-1, 64], [0, 16]], eq, 0, 1)
+    iota(v("CT0"), [[1, 128]], 1760 - M, 0)
     for nm in ("AA", "AB", "R2"):
         fill(v(nm, NB, 128), 0.0)
     fill(v("ZEH"), 0.0)
-    fill(v("H", L, LW), float(M))
+    for h in ("H0", "H1"):
+        fill(v(h, L, LW), float(M))
     for t in range(3):
         act(v("me%d" % t, L, LW), v("ONES", 0, 16))
-        act(v("me%d" % t, LW + L, 2 * LW), v("ONES", 0, 16), scale=0.0)
-    fill(v("QRZ", p=(0, 1)), 0.0)
-    ts(v("TR4"), v("TR4"), R16, add)
-    ts(v("TRM"), v("TR4", 0, 12), -PO, add)
-    ts(v("TRN"), v("TR4", 0, 12), 1 - PO, add)
-    for j in range(4):
-        act(v("GN", j * C4, (j + 1) * C4), spread("GNS", j, ("k2", "k5")[j % 2]))
-    fill(v("GN", M, W), 0.0)
-    dma("y", v("F2"), v("F1"), 5.0)
-    iota(v("RM"), [[0, W + L]], 0, 0, v("REP"))
+        nm, a, b = ages("m", t)
+        act(v(nm, a + L, b), v("ONES", 0, 16), scale=7.0)
+    act(v("TR"), v("LANB"), bias=TB - 1.0, scale=2.0)
+    act(v("TRP"), v("LANB"), bias=TB - 1.0 - PO, scale=2.0)
+    act(v("DT"), v("LANE"), bias=TB + PO / 15, scale=2.0)
+    tt(v("DT"), v("DT"), DIAGB, mul)
+    act(v("DT"), v("DT"), bias=-PO / 15)
+    dma("s", v("GN1", p=(0, 128, 16)), v("GNS"), 3.0)
+    emit("y", lambda: [g.sync.dma_start(ap(v("GN", 0, M, p=(r, 128, 16))), ap(v("GN1", p=(0, 128, 16)))) for r in range(16)],
+         [v("GN1"), v("X", 0, M)], [v("GN", 0, M)], 1.2, "d", 9.0)
+    fill(v("GN", M, W), 7.0)
+    emit("y", lambda: g.sync.dma_start(ap(v("F2", 0, W)), ap(v("F1", 0, W))), [v("F1", 0, W), v("GN", 0, M)], [v("F2", 0, W)], 0.07, "d", 8.0)
+    iota(v("RM", 0, W), [[0, W]], 0, 0, v("REP"))
+    iota(v("SN", IDB, IDB + W), [[1, W]], 0, 0, v("REP"))
+    fill(v("SN", IDB + W, WI), float(M))
     ts(v("M0"), R16, 0.0, eq)
     ts(v("E0"), R16, 0.0, ne, float(M), mul)
     for t in range(1, 3):
-        ts(v("MTC", t, t + 1), R16, float(t), eq)
-        ts(v("CT3", S * (t - 1), S * t), v("CT3", S * (t - 1), S * t), v("MTC", t, t + 1), mul)
+        act(v("CT3", S * (t - 1), S * t), v("CT0", S * (t - 1), S * t), scale=v("MK", t, t + 1))
     fill(v("POR", p=(0, 1)), PO)
     fill(v("ONR", p=(0, 1)), 1.0)
     fill(v("QRT", p=(0, 1)), -0.25)
     ts(v("WONE"), v("ONESB"), v("WC"), mul)
     act(v("SCB"), v("RMOD"), AF.Abs, v("NR17"))
     act(v("BS0"), v("SCB"), AF.Relu, PO, -PO)
-    fill(v("RS3"), 1.0)
-    fill(v("RS3", 0, 16, 4), 0.0)
 
     def listed(res, masked):
         a, b = masked[1:3]
@@ -610,16 +658,16 @@ def rank_program(g, core, T, topo):
         return v(res, a + 15, b, 16)
 
     def numbers(tag, src):
-        k = BANK[tag][0]
+        k, nv = BANK[tag][0], max(NV[tag])
         mm(v(k, 128, 256, p=(0, 64)), src, v("IDB"), True, True)
         act(v("XT" + tag, p=(0, 64)), v(k, 128, 256, p=(0, 64)))
-        if tag in SLOW:
+        if tag in SLOW and src[0] != "me0":
             for s in range(16):
-                pick(v("XR" + tag, s, 16 * NV[tag], 16), v(src[0], src[1], src[1] + NV[tag]), [[0, NV[tag]]], ge, 0, 0)
+                pick(v("XR" + tag, s, 16 * nv, 16), v(src[0], src[1], src[1] + nv), [[0, nv]], ge, 0, 0)
             joined(16)
             return
-        for a in range(0, 16 * NV[tag], 384):
-            b = min(a + 384, 16 * NV[tag])
+        for a in range(0, 16 * nv, 384):
+            b = min(a + 384, 16 * nv)
             mm(v(k, 128, 128 + b - a), v("XT" + tag, p=(0, 64)), v("REP", a, b, p=(0, 64)), True, True)
             act(v("XR" + tag, a, b), v(k, 128, 128 + b - a))
 
@@ -632,244 +680,250 @@ def rank_program(g, core, T, topo):
         for q in range(12):
             act(v("JK", 128 * q, 128 * q + NB), v("CB", 0, NB), AF.Sign, v("LANB", q, q + 1), -1.0, v("NBS", q, q + 1))
         F = v("F1" if t % 2 == 0 else "F2", 0, W)
-        tab = v("SN")
+        tab, H = v("SN", 0, WT), "H%d" % (t % 2)
 
         def first(a, b):
             r, l = (lambda n: v(n, a, b)), (lambda n: v(n, a // 16, b // 16))
             ts(l("BL"), l("NBS"), 0.5, mul, NB / 2, add)
             tt(r("FLG"), at(v("CT"), l("BL")), r("LANE"), le)
             act(r("BR"), at(v("BT", 128 * t, 128 * t + 128), l("BL")))
-            mm(r("k6"), v("ID16"), r("BR"), True, False)
-            mm(r("k6"), v("ONESB"), r("FLG"), False, True)
-            tt(r("TMP"), r("k6"), r("DIAG"), mul)
-            act(r("H"), r("k6"))
+            kh = r(LB[a > 0][0])
+            mm(kh, v("ID16"), r("BR"), True, False)
+            mm(kh, v("ONESB"), r("FLG"), False, True)
+            tt(r("TMP"), kh, r("DIAG"), mul)
+            act(r(H), kh)
             tc(l("HL"), listed("RWH", r("TMP")))
             tt(r("TMP"), at(F, l("HL")), r("DIAG"), mul)
             act(r("me%d" % t), at(v("X"), l("HL")))
-            act(r("P0"), at(F, l("HL")))
+            mm(r(LB[a > 0][4]), v("ONESB"), r("TMP"), True, True)
             tc(l("P0L"), listed("RWP", r("TMP")))
             for h in range(a // 64, b // 64):
                 numbers("A%d" % h, v("me%d" % t, 64 * h, 64 * h + 64))
 
         def second(a, b):
             r, l = (lambda n: v(n, a, b)), (lambda n: v(n, a // 16, b // 16))
-            tt(r("TMP"), at(F, l("P0L")), r("DIAG"), mul)
-            tc(l("P1L"), listed("RWQ", r("TMP")))
-            tt(r("EQ0"), at(tab, l("P0L")), r("H"), eq)
+            tt(r("TMQ"), at(F, l("P0L")), r("DIAG"), mul)
+            tc(l("P1L"), listed("RWQ", r("TMQ")))
             act(r("S0"), at(tab, l("P0L")))
+            kh, kk, k0, kd, kp = LB[a > 0]
+            tt(r("EQ0"), r("S0"), r(kh), eq)
             act(r("A0N"), r("S0"), AF.Abs, -float(M))
-            act(r("NE0"), r("A0N"), AF.Sign)
-            KK, W0, WD = v("k6", L + a, L + b), r("k5"), v("k5", L + a, L + b)
+            act(r("NE0"), r("A0N"), AF.Relu, 1.0, -1.0)
+            KK, W0, WD = v(kk, L + a, L + b), r(k0), v(kd, L + a, L + b)
+            mm(W0, v("IDK"), r("EQ0"), True, False)
+            mm(W0, v("IDD"), r("NE0"), False, True)
+            tt(r("UD"), r("S0"), W0, add)
             mm(KK, v("ONESB"), r("EQ0"), True, False)
-            mm(KK, v("NONESB"), r("NE0"), False, True)
-            act(r("UR"), KK, AF.Relu, 1.0)
-            mm(W0, ID, r("S0"), True, False)
-            mm(W0, v("IDK"), r("EQ0"), False, False)
-            mm(W0, v("IDS"), r("UR"), False, True)
-            act(r("UD"), W0)
+            mm(KK, v("ONESB"), r("NE0"), False, True)
+            act(r("UR"), KK, AF.Relu, -15.0)
             mm(WD, v("KSR", p=(0, 1)), v("ONES", a, b, p=(0, 1)), True, False)
-            mm(WD, v("NIDS"), r("UR"), False, False)
-            act(r("S1"), at(tab, l("P1L")))
-            tt(r("EQ1"), at(tab, l("P1L")), r("P0"), eq)
-            mm(WD, ID, r("S1"), False, False)
+            mm(WD, v("NONESK"), r("EQ0"), False, False)
+            mm(WD, v("NONESK"), r("NE0"), False, False)
+            tc(r("S1"), at(tab, l("P1L")))
+            tt(r("EQ1"), r("S1"), r(kp), eq)
+            mm(WD, v("IDB"), r("S1"), False, False)
             mm(WD, v("IDK"), r("EQ1"), False, True)
             tt(r("SA"), WD, r("UD"), OP.min)
-            tc(r("SA16"), r("SA"))
+            ts(r("SA16"), r("SA"), float(DEAD), OP.min)
         for stage in (first, second):
             for a, b in CH:
                 stage(a, b)
         hw, pw = v("RWH", 15, L, 16), v("RWP", 15, L, 16)
         sixteen(v("k6", 448, 460), "SEL", "UR", 0, L)
-        act(v("U"), v("k6", 448, 460), scale=1.0 / (16 * SELW))
-        act(v("NU"), v("U"), AF.Identity, 1.0, -1.0)
-        ts(v("CA"), pw, 64.0, ge)
-        tt(v("UP"), v("CA"), v("U"), mul)
-        act(v("CA"), v("U"), scale=M - PO)
-        act(v("CC"), v("UP"), scale=M - KS)
-        tt(v("CC"), v("CA"), v("CC"), sub)
-        ts(v("LIFT"), v("UP"), -2 * PO, mul, PO, add)
-        tt(v("Z5", 0, 12), hw, v("TR4", 0, 12), sub)
+        act(v("NU"), v("k6", 448, 460), bias=float(IDB), scale=-IDB / (16 * SELW))
+        act(v("UY"), v("k6", 448, 460), bias=-PO, scale=DEAD / (16 * SELW))
+        act(v("UB"), v("k6", 448, 460), bias=float(IDB), scale=(KS - IDB) / (16 * SELW))
+        ts(v("CA"), pw, 64.0, lt, KS, mul)
+        tt(v("CA"), v("CA"), v("NU"), OP.max)
+        tt(v("LIFT"), v("CA"), v("UB"), OP.min)
+        act(v("NF"), v("LIFT"), bias=KS + M - PO, scale=-1.0)
         if t < 3:
-            act(v("me%d" % t, LW, LW + L), at(v("GN"), v("HL")))
-            ship("e", t, v("me%d" % t))
+            ts(v("Z5", 24, 36), hw, -PO, add)
+            act(v(*ages("m", t, L)), at(v("GN"), v("HL")))
+            if t:
+                ship("e", t, v("me%d" % t))
+            else:
+                ship("e", t, v("me0"), [v("TRI"), v("BT"), v("CT0"), v("SN", IDB, IDB + W)])
+                ship("g", t, v("mg0"))
             mm(v("k5", 0, L), v("ONESB"), v("FLG"), True, True)
             ts(v("OH"), v("k5", 0, L), R16, eq)
             act(v("NOH"), v("OH"), AF.Identity, 1.0, -1.0)
-            act(v("CTS", 0, NB), v("CT", 0, NB), scale=1.0 / (L + 0.5))
+            act(v("CTS", 0, NB), v("CT", 0, NB), scale=-1.0 / (L + 0.5))
             for x, y, n in ((0, TURN, NB - TURN), (NB - TURN, 0, TURN)):
                 act(v("R2", x, x + n), v("CB", y, y + n), AF.Relu, float(L), -1.0)
                 tt(v("AA", x, x + n), v("OK", y, y + n), v("CTS", y, y + n), mul)
             tt(v("TMI"), v("R2"), v("k3", 0, 128), mul)
             ts(v("IDX"), listed("RWI", v("TMI")), -1.0, mul, L - 1.0, add)
 
-    def down(tag, idx, son, lift=None):
-        n, nv, kb = 64, NV[tag], BANK[tag][0]
+    def down(tag, e, idx, son, lift=(), row=None):
+        n, nv, kb = 64, NV[tag][e], BANK[tag][0]
         u, xr = "UU" + tag, "XR" + tag
         SP = v("k3", 256 + n * PARTS.index(tag), 256 + n * PARTS.index(tag) + n)
         turn(SP, son)
-        us, dif = v(u, 16 * nv, 16 * n), v(kb, n, n + 16 * (n - nv))
-        mm(dif, v("XT" + tag, p=(0, 64)), v("REP", 16 * nv, 16 * n, p=(0, 64)), True, False)
-        act(us, at(v("X"), idx(nv, n)))
-        mm(dif, v("NIDB"), us, False, True)
+        mid = (nv + n) // 4 * 2
+        cuts = [(kb, nv, n)] if n - nv <= 32 else [(kb, nv, mid), (BANK[tag][1], mid, n)]
+        for k, a, b in cuts:
+            us, dif = v(u, 16 * a, 16 * b), v(k, 512 - 16 * (b - a), 512)
+            mm(dif, v("XT" + tag, p=(0, 64)), v("REP", 16 * a, 16 * b, p=(0, 64)), True, False)
+            act(us, at(v("X"), idx(a, b)))
+            mm(dif, v("NIDB"), us, False, True)
         for a, b in HALVES(nv):
             ux = v(u, 16 * a, 16 * b)
             tt(ux, at(v("X"), idx(a, b)), v(xr, 16 * a, 16 * b), sub)
             act(ux, ux, AF.Abs)
-        act(us, dif, AF.Abs)
+        for k, a, b in cuts:
+            act(v(u, 16 * a, 16 * b), v(k, 512 - 16 * (b - a), 512), AF.Abs)
         mm(v(kb, 0, n), v("SLR", p=(0, 1)), v("ONES", 0, n, p=(0, 1)), True, False)
         for s in range(16):
-            mm(v(kb, 0, n), v("SELD", 128 * s, 128 * (s + 1)), v(u, s, 16 * n, 16), False, s == 15)
+            mm(v(kb, 0, n), v("SELD", 15 - s, 143 - s), v(u, s, 16 * n, 16), False, s == 15)
         joined(17)
         kp, dd, ee, rr = [v(x + tag) for x in ("MM", "DD", "EE", "RR")]
         turn(kp, v(kb, 0, n))
         scan(dd, kp, v("ZER", 0, n), add, OP.max)
         tt(ee, SP, dd, sub)
         scan(rr, dd, ee, OP.min, OP.max)
-        if lift:
-            mm(v(kb, 0, 4), v("IDH"), lift, True, False)
+        if row:
+            turn(v("RT" + tag), rr)
+            mm(row, v("PICK", 128 * 15, 128 * 16), v("RT" + tag), True, True)
+        for j, x in enumerate(lift):
+            mm(v(kb, 0, 4), v("IDB"), x, j == 0, False)
         for e in range(2):
             for y in range(2):
                 mm(v(kb, e, 4, 2), v("SWH", 128 * (2 * e + y), 128 * (2 * e + y + 1)), v("RR" + tag, 15 + 16 * y, n, 32),
                    y == 0 and not lift, y == 1 and (e == 1 or not lift))
-        joined(5 if lift else 4)
+        joined(4 + len(lift))
         return v(kb, 0, 4)
 
-    def step(tag, lift=None):
-        tc(v("IX" + tag), at(v("SN"), v("LL" + tag)))
+    def step(tag, e, lift=(), row=None):
+        tc(v("IX" + tag), at(v("SN", 0, WT if e < 2 else WI), v("LL" + tag)))
         tc(v("SF" + tag), v("IX" + tag))
-        return down(tag, lambda a, b: v("IX" + tag, a, b), v("SF" + tag), lift)
+        return down(tag, e, lambda a, b: v("IX" + tag, a, b), v("SF" + tag), lift, row)
+
+    def barren(tile, places, out):
+        act(tile, at(v("SN"), places), AF.Abs, -float(M))
+        mm(out, v("ONESB"), tile, True, True)
 
     def own(t):
         for h in range(3):
             tag, o, lo = "A%d" % h, 4 * h, 64 * h
-            x = down(tag, lambda a, b: v("SA16", lo + a, lo + b), v("SA", lo, lo + 64))
-            tc(v("LL" + tag), x)
+            x = down(tag, 0, lambda a, b: v("SA16", lo + a, lo + b), v("SA", lo, lo + 64))
+            ts(v("LL" + tag), x, float(DEAD), OP.min)
             act(v("W1", o, o + 4), x, bias=-PO)
-            x = step(tag)
-            tc(v("LL" + tag), x)
+            x = step(tag, 1, [v("LIFT", o, o + 4)])
+            ts(v("LL" + tag), x, float(IDB + W), OP.min)
             act(v("W2", o, o + 4), x, bias=-PO)
-        tt(v("D1"), v("W2"), v("W1"), sub)
-        tt(v("D1"), v("D1"), v("U"), mul)
-        tt(v("D1"), v("D1"), v("W1"), add)
-        ts(v("YP"), v("D1"), 1.0, add)
-        last = [step("A%d" % h, v("LIFT", 4 * h, 4 * h + 4)) for h in range(3)]
+            if t < 3:
+                barren(v("AYI", lo, lo + 64), v("LL" + tag), v("k4", 320 + lo, 384 + lo))
+        if t < 3:
+            act(v("NFR"), v("k4", 320, 512), AF.Relu, 1.0, -1.0)
+            sending(t)
+        tt(v("W1"), v("W1"), v("UY"), OP.max)
+        tt(v("W1"), v("W1"), v("NF"), OP.min)
+        tt(v("YP"), v("W1"), v("W2"), OP.min)
+        tt(v("BS0", 0, L, 16), v("W1"), v("W2"), OP.min)
         early(t)
-        tt(v("BASE"), v("W2"), v("NU"), mul)
-        tt(v("BASE"), v("BASE"), v("CC"), add)
         for h in range(3):
-            o, x = 4 * h, last[h]
-            tt(v("SH", o, o + 4), x, v("BASE", o, o + 4), OP.min)
-            tt(v("BS0", L + 16 * o, L + 16 * o + 64, 16), x, v("BASE", o, o + 4), OP.min)
+            a = 64 * h
+            x = step("A%d" % h, 2, (), v("k4", 64 + a, 128 + a))
+            act(v("BS0", L + a, L + a + 64, 16), x, bias=-PO)
+            if 16 * SS[t] + 16 < a + 64:
+                lo = max(a, 16 * SS[t] + 16)
+                tc(v("YR", L + lo, L + a + 64), v("k4", 64 + lo, 128 + a))
+            if SS[t]:
+                act(v("YW", L + a, L + a + 64), v("k4", 64 + a, 128 + a), bias=-PO)
 
     def arrivals(t):
         ls = "AX"
         act(v(ls, 0, S), at(v("le%d" % (t - 1), 0, LW), v("ls%d" % (t - 1))))
-        act(v(ls, S, 2 * S), at(v("le%d" % (t - 1), LW, 2 * LW), v("ls%d" % (t - 1))))
+        act(v(ls, S, 2 * S), at(v(*ages("l", t - 1)), v("ls%d" % (t - 1))))
         mm(v("k2", 0, S), v("WONE"), v(ls, 0, S), True, True)
         tt(v("TMC"), v("k2", 0, S), v("DIAG", 0, S), mul)
         tc(v("CI"), listed("RWC", v("TMC")))
         numbers("AB", v(ls, 0, S))
         tt(v("TMG"), v(ls, S, 2 * S), v("k3", 0, S), mul)
         gen = listed("RWG", v("TMG"))
-        for d in range(2):
-            ts(v("GENM", d, 12, 3), gen, float(d + 2), eq)
-        joined(2)
-        ts(v("GO2"), gen, 3.0, sub)
-        act(v("GO3"), v("GO2"), AF.Abs)
-        ts(v("LB3", 0, 16, 4), v("GO3"), 1.5, gt, float(M), mul)
-        ts(v("LB3", 3, 16, 4), gen, 4.0, eq, KS, mul)
-        ts(v("LIFB"), gen, 4.0, ne, 2 * PO, mul)
+        ts(v("LIFB", 0, 4), gen, 4.5, gt, float(BK), mul)
+        ts(v("LIFB", 4, 8), gen, 2.5, lt, float(IDB), mul)
+        ts(v("LIFB", 8, 12), gen, 3.5, lt, float(IDB), mul)
         ts(v("CI2"), v("CI"), 63, OP.bitwise_and)
         tc(v("LLAB"), v("CI2"))
         for e in range(4):
-            x = step("AB", v("LIFB") if e == 3 else None)
-            if e < 3:
-                tc(v("LLAB"), x)
-            if 0 < e < 3:
-                tt(v("LB3", e, 16, 4), x, v("GENM", e - 1, 12, 3), mul)
-        scan(v("LBT"), v("RS3"), v("LB3"), mul, add)
-        tt(v("GO2"), x, v("LBT", 3, 16, 4), OP.min)
-        tc(v("BF16"), v("GO2"))
+            x = step("AB", e, [v("LIFB", 4 * e, 4 * e + 4)] if e < 3 else ())
+            ts(v("LLAB" if e < 3 else "BF16"), x, float(WI - 1 if e else DEAD), OP.min)
+            if e == 2 and t < 3:
+                barren(v("AYB"), v("LLAB"), v("k4", 256, 320))
+                act(v("mf%d" % t), v("k4", 256, 320), AF.Sign)
+                ship("f", t, v("mf%d" % t))
         act(v("mr%d" % t), at(v("X"), v("BF16")))
         ship("r", t, v("mr%d" % t))
 
     sent = [0]
 
-    def ship(kind, t, src):
+    def ship(kind, t, src, after=()):
         k = "%s%d" % (kind, t)
         dst = goal(T, rank, kind, t)
         mid = via(topo, core, dst)
 
         def call():
             if mid is None:
-                sent[0] += send(g, topo, core, dst, T["l" + k][:], src[3], T.sem["a" + k], T.sem.lo)
+                sent[0] += send(g, topo, core, dst, k, T["l" + k][:], src[3], T.sem["a" + k], T.sem.lo)
             else:
-                sent[0] += send(g, topo, core, mid, T["b" + k][:], src[3], T.sem["x" + k], T.sem.lo)
-        emit("g", call, [src], [v("l" + k)], 1.0, "r", FAR[k])
+                sent[0] += send(g, topo, core, mid, k, T["b" + k][:], src[3], T.sem["x" + k], T.sem.lo)
+        emit("g", call, [src] + list(after), [v("l" + k)], 8.0 if k == "e0" else 1.0, "r", FAR[k])
 
-    YROW, SROW, CNT = v("k5", 0, L), v("k1", 0, L), v("k6", 0, L)
+    YROW, SROW, CNT = v("k5", 0, L), v("k4", 64, 64 + L), v("k6", 0, L)
+
+    def alike(lo, whole, wide, last):
+        scan(v("SCB", lo, lo + L), v("RS0", 0, L), v("BS0", lo, lo + L), mul, add)
+        tt(v("ED", lo, lo + L), v("SCB", lo, lo + L), whole, eq)
+        mm(CNT, v("ONESK"), v("ED", lo, lo + L), False, False)
+        cuts = [(q, 1056 * (lo // L) + sum((11 - j) * 16 for j in range(q)), (11 - q) * 16) for q in range(11)]
+        for q, o, n in cuts[wide:]:
+            ts(v("EQ", o, o + n), v("YR", lo + L - n, lo + L), PO, sub, v("BS0", lo + 16 * q, lo + 16 * q + 1), eq)
+            mm(v("k6", L - n, L), v("ONESK"), v("EQ", o, o + n), False, last and q == 10 and not wide)
+        parts = [x for x in (cuts[:min(wide, 2)], cuts[2:min(wide, 5)], cuts[5:wide]) if x]
+        for part in parts:
+            for q, o, n in part:
+                act(v("EQ", o, o + n), v("YW", lo + L - n, lo + L), AF.Abs, v("BS0", lo + 16 * q, lo + 16 * q + 1), -1.0)
+            a, b = part[0][1], part[-1][1] + part[-1][2]
+            act(v("EQ", a, b), v("EQ", a, b), AF.Relu, 1.0, -1.0)
+            for q, o, n in part:
+                mm(v("k6", L - n, L), v("ONESK"), v("EQ", o, o + n), False, last and q == wide - 1)
+            joined(len(part))
 
     def early(t):
+        yp, sons = v("BS0", 0, L, 16), v("k4", 32, 44)
         mm(YROW, v("POR", p=(0, 1)), v("ONR", 0, L, p=(0, 1)), True, False)
         for r in range(16):
             mm(v("k5", r, L, 16), v("PICK", 128 * r, 128 * (r + 1)), v("YP"), False, r == 15)
         joined(17)
-        if YS[t] < 11:
-            tc(v("YR", 16 * YS[t] + 16, L), v("k5", 16 * YS[t] + 16, L))
-        act(v("YW"), YROW, bias=-PO)
-        ts(v("YL"), v("YP"), PO - 1, add)
-        act(v("SY"), at(v("SN"), v("YL")))
+        tc(v("YR", 16 * YS[t] + 16, L), v("k5", 16 * YS[t] + 16, L))
+        if YS[t]:
+            act(v("YW", 0, L), YROW, bias=-PO)
+        ts(v("YL"), v("YP"), PO, add)
+        act(v("SY"), at(v("SN", 0, WT), v("YL")))
         act(v("AY"), v("SY"), AF.Abs, -float(M))
         act(v("EMY"), v("AY"), AF.Sign)
-        sixteen(v("k4", 32, 44), "SEL", "EMY", 0, L)
-        sev = v("SEV")
-        ts(sev, v("k4", 32, 44), 1.5 * SELW, gt)
+        if t == 3:
+            mm(v("k5", L, 2 * L), v("ONESB"), v("AY"), True, True)
+            act(v("NFR"), v("k5", L, 2 * L), AF.Relu, 1.0, -1.0)
+        mm(CNT, v("ONESK"), v("NFR"), True, False)
         if t < 3:
-            tt(v("ZT", 0, 12), v("YP"), v("TRN"), sub)
-            tt(v("Z5", 24, 36), v("ZT", 0, 12), sev, mul)
-        mm(CNT, v("QRZ", p=(0, 1)), v("ONES", 0, L, p=(0, 1)), True, False)
+            mm(CNT, v("NIDB"), v("OH"), False, False)
+        sixteen(sons, "SEL", "EMY", 0, L)
+        ts(v("NS"), sons, 1.5 * SELW, gt, -KS, mul)
+        tt(v("NS"), v("NS"), v("TRP"), add)
+        if t < 3:
+            tt(v("Z5", 36, 48), yp, v("NS"), OP.max)
+        alike(0, YROW, YS[t], False)
 
     def adopt(t):
-        sp, yp = v("BS0", L, 384, 16), v("BS0", 0, L, 16)
-        scan(v("SCB", L, 384), v("RS0", 0, L), v("BS0", L, 384), mul, add)
-        mm(SROW, v("POR", p=(0, 1)), v("ONR", 0, L, p=(0, 1)), True, False)
-        for r in range(16):
-            mm(v("k1", r, L, 16), v("PICK", 128 * r, 128 * (r + 1)), v("SH"), False, r == 15)
-        joined(17)
-        tc(v("YR", L, 384), SROW)
-        ts(v("NF"), sp, M - PO, ne, -2 * PO, mul)
-        tt(yp, v("YP"), v("NF"), OP.max)
-        scan(v("SCB", 0, L), v("RS0", 0, L), v("BS0", 0, L), mul, add)
+        sp, L4 = v("BS0", L, 384, 16), "L4%d" % (t % 2)
         ts(v("SL"), sp, PO, add)
-        ts(v("NFR"), SROW, float(M), eq)
+        alike(L, SROW, SS[t], True)
         if t < 3:
-            sending(t)
-        cuts = [(q, sum((11 - j) * 16 for j in range(q)), (11 - q) * 16) for q in range(11)]
-        for q, o, n in cuts:
-            ts(v("EQ", o, o + n), v("YR", 2 * L - n, 2 * L), PO, sub, v("BS0", L + 16 * q, L + 16 * q + 1), eq)
-            mm(v("k6", L - n, L), v("ONESB"), v("EQ", o, o + n), False, False)
-        for lo, whole in ((0, YROW), (L, SROW)):
-            tt(v("ED", lo, lo + L), v("SCB", lo, lo + L), whole, eq)
-            mm(CNT, v("ONESB"), v("ED", lo, lo + L), False, False)
-        ys = YS[t]
-        for q, o, n in cuts[ys:]:
-            ts(v("EY", o, o + n), v("YR", L - n, L), PO, sub, v("BS0", 16 * q, 16 * q + 1), eq)
-            mm(v("k6", L - n, L), v("ONESB"), v("EY", o, o + n), False, False)
-        for part in (cuts[:min(ys, 2)], cuts[2:min(ys, 5)], cuts[5:ys]):
-            if not part:
-                continue
-            for q, o, n in part:
-                act(v("EY", o, o + n), v("YW", L - n, L), AF.Abs, v("BS0", 16 * q, 16 * q + 1), -1.0)
-            a, b = part[0][1], part[-1][1] + part[-1][2]
-            act(v("EY", a, b), v("EY", a, b), AF.Relu, 1.0, -1.0)
-            for q, o, n in part:
-                mm(v("k6", L - n, L), v("ONESB"), v("EY", o, o + n), False, False)
-            joined(len(part))
-        mm(CNT, v("ONESB"), v("NFR"), False, True)
-        if t < 3:
-            tt(v("VAL"), v("OH"), CNT, gt)
-            scan(v("GG"), v("NOH"), v("VAL"), mul, add)
-            tt(v("OK"), at(v("GG"), v("IDX")), v("AB" if t else "AA"), lt)
+            scan(v("GG"), v("NOH"), CNT, mul, OP.min)
+            tt(v("OK"), at(v("GG"), v("IDX")), v("AB" if t else "AA"), gt)
         act(v("XS"), at(v("X"), v("SL")))
         XG = v("k0", 0, L)
         mm(XG, v("QRT", p=(0, 1)), v("ONES", 0, L, p=(0, 1)), True, False)
@@ -877,27 +931,20 @@ def rank_program(g, core, T, topo):
         mm(XG, v("IDHALF"), v("XS"), False, True)
         act(v("XJ"), XG, bias=ROUND)
         act(v("XJB"), v("XJ"), bias=-ROUND)
-        tt(v("Z5", 12, 24), sp, v("TRM"), sub)
-        tt(v("Z5", 36, 48), v("Z5", 12, 24), v("SEV"), mul)
+        tt(v("Z5", 12, 24), sp, v("NS"), OP.max)
         if t < 3:
-            tt(v("EQS"), at(v("SN"), v("YL")), v("YR", L, 384), eq)
-            mm(v("k7", 0, L), v("TRI"), v("EQS"), True, True)
-            act(v("MS"), SROW, AF.Identity, float(M), -1.0)
-            tt(v("k2", 256, 448), v("EQS"), v("k7", 0, L), gt)
-            tt(v("VT"), v("k2", 256, 448), v("MS"), mul)
+            tt(v("EQS"), v("SY"), SROW, eq)
+            mm(v("k7", 0, L), v("KS1", p=(0, 1)), v("ONES", 0, L, p=(0, 1)), True, False)
+            mm(v("k7", 0, L), v("FST"), v("EQS"), False, True)
+            tt(v("VT"), v("SY"), v("k7", 0, L), OP.min)
+            act(v("MS"), v("k7", 0, L), AF.Relu, float(M), -1.0)
             act(v("VH"), SROW, AF.Identity, v("E0"), v("M0"))
-        tt(v("FR"), v("DIAG"), CNT, gt)
-        go = listed("FRS", v("FR"))
-        keep = range(4) if t < 3 else (1, 3)
-        for j in keep:
-            tt(v("Z4", 12 * j, 12 * j + 12), v("Z5", 12 * j, 12 * j + 12), go, mul)
-        if t < 3:
-            tt(v("Z4"), v("Z4"), v("TR4"), add)
-            tc(v("L4"), v("Z4"))
-        else:
-            for j in keep:
-                tt(v("Z4", 12 * j, 12 * j + 12), v("Z4", 12 * j, 12 * j + 12), v("TR4", 0, 12), add)
-                tc(v("L4", 12 * j, 12 * j + 12), v("Z4", 12 * j, 12 * j + 12))
+        tt(v("FR"), v("DT"), CNT, OP.min)
+        spare = listed("FRS", v("FR"))
+        n = 4 if t < 3 else 2
+        for j in range(n):
+            tt(v("Z4", 12 * j, 12 * j + 12), v("Z5", 12 * j, 12 * j + 12) if j else sp, spare, OP.max)
+        ts(v(L4, 0, 12 * n), v("Z4", 0, 12 * n), PO, add)
 
     def sending(t):
         ms, hr = "ms%d" % t, "HR%d" % t
@@ -906,54 +953,56 @@ def rank_program(g, core, T, topo):
             act(v("JL", L * q, L * q + L), v("CUM"), AF.Sign, v("LANB", q, q + 1), -1.0, v("NLS", q, q + 1))
         ts(v(ms), v("NLS"), 0.5, mul, L / 2, add)
         ship("s", t, v(ms))
-        act(v(hr), at(v("H"), v(ms)))
+        act(v(hr), at(v("H%d" % (t % 2)), v(ms)))
         if t < 2:
             tt(v("TMH"), v(hr), v("k3", 0, S), mul)
             hw = listed("HW", v("TMH"))
             ts(v("RZ"), hw, float(M), eq)
-            tt(v("RZ"), v("RZ"), v("TR4", 0, 4), mul)
+            tt(v("RZ"), v("RZ"), v("TR", 0, 4), mul)
             tt(v("RZ"), v("RZ"), hw, OP.max)
             tc(v("HT%d" % t), v("RZ"))
         if t == 0:
-            act(v("GN", 1760, 1760 + S), at(v("me0", LW, 2 * LW), v(ms)), AF.Identity, 1.0)
+            act(v("GN", 1760, 1760 + S), at(v("mg0"), v(ms)), AF.Identity, 1.0)
 
     def returned(t):
-        lr, a = v("lr%d" % t), 1760 + S * (t - 1)
-        ts(v("FD"), lr, 256.0, lt)
-        if t < 3:
-            tc(at(v("RM"), v("HT%d" % (t - 1))), v("FD"))
-            tt(v("TMR"), v("FD"), v("k3", 0, S), mul)
+        a = 1760 + S * (t - 1)
+        if t == 3:
+            ts(v("lf3"), v("lr3"), 256.0, lt)
+        else:
+            fd = v("lf%d" % t)
+            tc(at(v("RM"), v("HT%d" % (t - 1))), fd)
+            tt(v("TMR"), fd, v("k3", 0, S), mul)
             come = listed("RWR", v("TMR"))
-            sixteen(v("k2", 0, NB), "SEL", "RM", 0, W)
-            tt(v("RVD"), v("FD"), v("CT3", S * (t - 1), S * t), mul)
+            sixteen(v("k5", 384, 384 + NB), "SEL", "RM", 0, W, 4)
+            tt(v("RVD"), fd, v("CT3", S * (t - 1), S * t), mul)
             x = TURN * (t + 1)
-            act(v("AA", a // 16 - x, a // 16 - x + 4), come, scale=2.0)
-            tt(v("AB", 0, NB - x), v("AA", 0, NB - x), v("k2", x, NB), sub)
-            tt(v("AB", NB - x, NB), v("AA", NB - x, NB), v("k2", 0, x), sub)
+            act(v("AA", a // 16 - x, a // 16 - x + 4), come, scale=-2.0)
+            tt(v("AB", 0, NB - x), v("AA", 0, NB - x), v("k5", 384 + x, 384 + NB), add)
+            tt(v("AB", NB - x, NB), v("AA", NB - x, NB), v("k5", 384, 384 + x), add)
 
     def changes(t):
-        wide = W + L
+        wide, H, L4 = W + 2 * L, v("H%d" % (t % 2), 0, L), "L4%d" % (t % 2)
         if t:
-            lr, a, hr = v("lr%d" % t), 1760 + S * (t - 1), v("HR%d" % (t - 1))
+            lr, a, hr, fd = v("lr%d" % t), 1760 + S * (t - 1), v("HR%d" % (t - 1)), v("lf%d" % t)
             if t < 3:
-                tt(v("X", a, a + S), lr, v("FD"), mul)
-                tt(v("F1", a, a + S), hr, v("FD"), mul)
-                tt(v("F2", a, a + S), hr, v("FD"), mul)
+                tt(v("X", a, a + S), lr, fd, mul)
+                tt(v("F1", a, a + S), hr, fd, mul)
+                tt(v("F2", a, a + S), hr, fd, mul)
             else:
-                tt(v("XN"), lr, v("FD"), mul)
-                tt(v("RVB"), hr, v("FD"), mul)
+                tt(v("XN"), lr, fd, mul)
+                tt(v("RVB"), hr, fd, mul)
                 dma("y", ("xo", a, W, T.xo[:, a:W]), v("XN"), 2.5)
                 dma("y", ("fo", a, W, T.fo[:, a:W]), v("RVB", p=(0, 128, 16)), 2.2)
                 dma("y", ("f2o", a, W, T.f2o[:, a:W]), v("RVB", p=(0, 128, 16)), 2.2)
         if t == 3:
             for f in ("X", "F1", "F2"):
                 fill(v(f, M, 1760), 0.0)
-        tc(at(v("X", 0, wide), v("L4", 12, 24)), v("XJB"))
-        tc(at(v("F2"), v("L4", 12, 24)), v("H", 0, L))
-        tc(at(v("F1"), v("L4", 36, 48)), v("H", 0, L))
+        tc(at(v("X", 0, wide), v(L4, 0, 12)), v("XJB"))
+        tc(at(v("F2"), v(L4, 0, 12)), H)
+        tc(at(v("F1"), v(L4, 12, 24)), H)
         if t < 3:
-            tc(at(v("SN", 0, wide), v("L4", 0, 12)), v("VH"))
-            tt(at(v("SN", 0, wide), v("L4", 24, 36)), v("SY"), v("VT"), add)
+            tc(at(v("SN", 0, wide), v(L4, 24, 36)), v("VH"))
+            tt(at(v("SN", 0, wide), v(L4, 36, 48)), v("VT"), v("MS"), add)
         if 0 < t < 3:
             act(v("RVB"), at(v("SN", 0, wide), v("HT%d" % (t - 1))))
             tt(at(v("SN", 0, wide), v("HT%d" % (t - 1))), v("RVB"), v("RVD"), add)

@@ -3,29 +3,41 @@ from concourse.mybir import AluOpType as OP, ActivationFunctionType as AF
 M, W, L, S, T_, Q = 1744, 1952, 192, 64, 4, 560
 NB = W // 16
 RW = M // 16
-TB = W
-DEAD = 2344
-BK = 2368
-WT = 2352
+NEW = 32
+A = NEW + W - M - 16
+E = A + M
+WP = NEW + W
+NOB, NOS = 8, 16
+TB = WP
+WT = TB + 2 * L
+BK = WT
 IDB = WT
-WI = IDB + W + 16
+WI = IDB + WP
 BIG = 512.0
 KS = 8192.0
 PO = 2040.0
 ROUND = 1.5 * 2 ** 23
+RAISE = 2.0 ** 17
 LW = L + 16
-NVT = (((40,) * 3, (42,) * 3, (44,) * 3, (0,)),) + (((40,) * 3, (40,) * 3, (42,) * 3, (36, 40, 40, 40)),) * 3
+NVT = (((40,) * 3, (40,) * 3, (40,) * 3, (0,)),) + (((42, 40, 38),) * 3 + ((42, 40, 40, 40),),) * 3
 BANK = {"A0": ("k0",), "A1": ("k1",), "A2": ("k7",), "AB": ("k2", "k4")}
-CH = ((0, 64), (64, 128), (128, 192))
-LB = (("k6", "k6", "k5", "k5", "k4"), ("k6", "k6", "k5", "k5", "k4"))
-SLOW = ("A2",)
-YS = (0, 0, 0, 0)
-SS = (0, 0, 0, 0)
+CH = ((128, 192), (0, 128))
+SLOW = ("A0",)
+PTURN = ()
+TBANK = ""
+ONV = {"PR": 1, "QR": 1, "S0": 0, "SY": 0, "XJ": 0, "F1": 0, "F2": 0, "SNH": 0, "SNY": 1, "KP": 1, "XG": 1, "UR": 1, "NS": 1}
+YS, SEED, MORE, XB, TRUE = 11, 1, 170, 0, 1
+LOWS = ()
+BARKEY = ()
+EARLYC = 0
+AHEAD = 0
+SENDFIRST = ()
+PLAIN = ()
 PV = 8
 
 
 def HALVES(n):
-    return ((0, 16), (16, 30), (30, n))
+    return ((0, 14), (14, 28), (28, n))
 
 
 TURN = Q // 16
@@ -34,15 +46,19 @@ PARTS = ("A0", "A1", "A2", "AB")
 SCRATCH = {}
 PLACE = {}
 HALF = set()
+LISTS = set()
 BANKS = set("k%d" % i for i in range(8))
 POOL = {"float32": ["poolf", 0], "float16": ["poole", 0], "bfloat16": ["poolh", 0], "int32": ["pooli", 0], "uint16": ["poolu", 0]}
 ORDER = []
+EITHER, SWAP = {}, set()
 
 
 def _b(kind, dtype, **kw):
     for n, w in kw.items():
         if dtype in ("bfloat16", "uint16", "float16"):
             HALF.add(n)
+        if dtype == "uint16":
+            LISTS.add(n)
         if kind == "psum" or n[:2] in ("me", "be", "le", "ms", "bs", "ls", "mr", "br", "lr", "mf", "bf", "lf", "mg", "bg", "lg"):
             SCRATCH[n] = (kind, [128, w], dtype)
         else:
@@ -52,23 +68,23 @@ def _b(kind, dtype, **kw):
             SCRATCH[p[0]] = (kind, [128, p[1]], dtype)
 
 
-_b("sbuf", "float32", UB=12, SN=WI, F1=W + 2 * L, F2=W + 2 * L, H0=LW, H1=LW, NU=12, S0=L, UD=L, SA=L, YW=384, RMOD=384, DIAG=L, D15=L, DT=L, OF=128, I3=384,
+_b("sbuf", "float32", SN=WI, F1=WT, F2=WT, H0=LW, H1=LW, S0=L, UD=L, SA=L, RMOD=384, DIAG=L, D15=L, DT=L, OF=128, I3=384,
    R16=1, PBF=2, M0=1, E0=1, MK=16, TR=12, TRP=12, LANB=12, LANE=L, CT0=128, CT3=128, ZER=128, CB=128, CT=128, NBS=12,
-   UY=12, CA=12, W1=12, W2=12, NF=12, NS=12, BS0=384, SCB=384,
-   Z4=48, Z5=48, SY=L, MS=L, VT=L, VH=L, RZ=4, RVB=S, RVD=S, MTC=8,
-   TMC=S, RWC=S, NR16=1, NR17=1, NLS=4, CTS=128, AA=128, AB=128, XJ=L)
+   W1=12, W2=12, NS=12, BS0=384, SCB=384,
+   Z4=48, Z5=48, SY=L, SYR=L, VT=L, VH=L, RZ=4, RVB=S, RVD=S, RVF=S, HRM=S, CAP=L, TOP=L, UP=16, PR=L, QR=L, RWH=L, RWP=L, RWQ=L, RT=12,
+   RWC=S, CRW=S, RWG=S, RWR=S, HW=S, RWI=128, R2=128, ZT=L, CF=256, CR=256, NR16=1, NR17=1, NLS=4, CTS=128, AA=128, AB=128, XJ=L)
 for _n in PARTS:
     _b("sbuf", "float32", **{"MM" + _n: 64, "DD" + _n: 64, "EE" + _n: 64, "SF" + _n: 64})
-    _b("sbuf", "float16", **{"RR" + _n: 64, "RT" + _n: 64})
+    _b("sbuf", "float16", **{"RR" + _n: 64, "RT" + _n: 64, "SH" + _n: 64})
     _b("sbuf", "bfloat16", **{"XT" + _n: 128, "XR" + _n: 1024, "UU" + _n: 1024})
-    _b("sbuf", "uint16", **{"IX" + _n: 64, "LL" + _n: 4})
-_b("sbuf", "float16", S1=L, TMQ=L, YR=384, FAS=RW, RRS=RW, YP=12,
-   POR=128, ONR=384, TMP=L, RWH=L, RWP=L, RWQ=L, TMH=S, HW=S, TMI=128, RWI=128, TMG=S, RWG=S, FR=L, FRS=L)
-_b("sbuf", "bfloat16", X=WT, GN=W, RM=W + 2 * S, ANE=M, SWH=512, PICK=2048, WSEL=144, GN1=M, GNS=RW, LIFT=12, LIFB=12, SEL=144, SELD=144, R2=128, WONE=128, REP=1024, ONES=L, ONESB=128, NONESB=128, ONESK=128, NONESK=128,
-   TRI=128, TIMO=128, SLR=128, ZEH=L, JL=4 * L, XJB=L, XS=L, IDB=128, NIDB=128, IDK=128, IDD=128, FST=128, KSR=128, KS1=128, ID16=128, IDHALF=128, QRT=128, TMPB=128,
-   WC=1, RS0=384, OK=128, OH=L, NOH=L, VAL=L, GG=L, CUM=L, JK=12 * 128, BT=512, FLG=L, BR=L, EQ0=L, EQ1=L, A0N=L, NE0=L, UR=L, ED=384, EQ=2112, NFR=L,
-   AY=L, EMY=L, EQS=L, FD=S, XN=S, TMR=S, RWR=S)
-_b("sbuf", "int32", SNI=M, FAI=RW, GNI=RW, PI=1, PI2=1, CI=4, CI2=4)
+    _b("sbuf", "uint16", **{"IX" + _n: 64})
+_b("sbuf", "uint16", LLAB=4, LL0=12, LL1=12)
+_b("sbuf", "float16", SAH=L, PH=L, S1=L, YR=384, FAS=RW, RRS=RW, YP=12, POR=128, EKS=128, ONR=384, FR=L, FRS=L)
+_b("sbuf", "bfloat16", X=WT, GN=WP, RM=WP + 2 * S, ANE=M, SWH=512, PICK=2048, GN1=M, GNS=RW, NU=12, CA=12, LIFB=12, SEL=144, SELD=144, WONE=128, REP=1024, ONES=256, ONESB=128, NONESB=128, ONESK=128, NONESK=128,
+   TRI=128, TIMO=128, SLR=128, ZEH=L, JL=4 * L, XJB=L, XS=L, IDB=128, NIDB=128, IDK=128, IDW=128, FST=128, RUP=128, RDN=128, ID16=128, IDHALF=128, QRT=128, TMPB=128,
+   WC=1, RS0=384, OK=128, NOH=L, GG=LW, CUM=L, JK=12 * 128, BT=512, FLG=L, BR=L, EQ0=L, EQ1=L, SG0=L, UR=L, ED=384, EQ=2112, NFR=L,
+   EMY=L, EQS=L, XN=S, SGB=256, OFFD=L, LOW=160, EL=160, SELN=144, UN=1024, IDL=128, NLR=128, PEN=128)
+_b("sbuf", "int32", SNI=M, FAI=RW, GNI=RW, PI=1, PI2=1, CI=LW, CI2=LW)
 _b("sbuf", "uint16", BL=12, HL=12, IDX=8, P0L=12, P1L=12, SA16=L, YL=12, SL=12, L40=48, L41=48, BF16=4)
 _b("psum", "float32", k0=512, k1=512, k2=512, k3=512, k4=512, k5=512, k6=512, k7=512)
 for _t in range(3):
@@ -78,8 +94,8 @@ for _t in range(3):
     _b("sbuf", "float32", **{"HR%d" % _t: S})
     _b("sbuf", "uint16", **{"HT%d" % _t: 4})
 
-_b("sbuf", "bfloat16", me3=LW, AX=2 * S, AYI=L, AYB=S, mf1=S, bf1=S, lf1=S, mf2=S, bf2=S, lf2=S, lf3=S, mg0=LW, bg0=LW, lg0=LW)
-MSGS = [("e", 0), ("g", 0), ("s", 0), ("e", 1), ("f", 1), ("r", 1), ("s", 1), ("e", 2), ("f", 2), ("r", 2), ("s", 2), ("r", 3)]
+_b("sbuf", "bfloat16", me3=LW, AX=2 * S, AYI=L, AYB=S, mf1=S, bf1=S, lf1=S, mf2=S, bf2=S, lf2=S, mf3=S, bf3=S, lf3=S, mg0=LW, bg0=LW, lg0=LW)
+MSGS = [("e", 0), ("g", 0), ("s", 0), ("e", 1), ("f", 1), ("r", 1), ("s", 1), ("e", 2), ("f", 2), ("s", 2), ("r", 2), ("f", 3), ("r", 3)]
 SEMAPHORES = ["qv", "qs", "qt", "qg", "lo"] + ["d%d" % i for i in range(40)] + ["x%s%d" % m for m in MSGS] + ["a%s%d" % m for m in MSGS]
 
 
@@ -129,9 +145,9 @@ def hand_on(g, core, T, topo):
 HOP, CY, GA, SC = 0.34, 0.001, 1.56, 3.8
 
 
-FAR = {"e0": 30.0, "g0": 16.0, "e1": 20.0, "e2": 20.0, "s0": 9.0, "r1": 9.0, "s1": 5.0, "r2": 5.0, "s2": 9.0, "r3": 11.0, "f1": 9.0, "f2": 5.0}
-LEAD = {"A0": 4.0, "A1": 2.0, "A2": 0.1, "AB": 2.1}
-ROWS = ("FLG", "BR", "TMP", "H0", "H1", "RWH", "XL", "P0", "RWP", "RWQ", "EQ0", "S0", "A0N", "NE0", "UR", "S1", "EQ1", "UD", "SA", "SA16", "TMQ")
+FAR = {"e0": 28.0, "g0": 16.0, "e1": 20.0, "e2": 20.0, "s0": 8.0, "r1": 8.0, "s1": 4.5, "r2": 4.5, "s2": 8.0, "r3": 8.0, "f1": 8.0, "f2": 4.5, "f3": 9.0}
+LEAD = {"A0": 0.1, "A1": 2.0, "A2": 4.0, "AB": 2.1}
+ROWS = ("FLG", "BR", "H0", "H1", "RWH", "PH", "SAH", "QR", "RWP", "RWQ", "EQ0", "S0", "SG0", "UR", "S1", "EQ1", "UD", "SA", "SA16")
 
 
 def lead(x):
@@ -148,8 +164,8 @@ def lead(x):
     return 0.0
 
 
-PASSES, SHAKE = 2800, 0.3
-SPARE = 0.15
+PASSES, SHAKE = 600, 0.3
+SPARE = 0.0
 PE = 0.65
 OWN = 0.34
 ENDS = []
@@ -159,7 +175,7 @@ def plan(ops):
     n = len(ops)
     pred = [set() for _ in ops]
     wr, rd, tlast = {}, {}, {}
-    for i, (e, kind, call, reads, writes, us, dur) in enumerate(ops):
+    for i, (e, kind, call, reads, writes, us, dur, listed) in enumerate(ops):
         for nm, lo, hi in reads + writes:
             pred[i].update(j for lo2, hi2, j in wr.get(nm, ()) if lo < hi2 and lo2 < hi)
         for nm, lo, hi in writes:
@@ -199,7 +215,7 @@ def plan(ops):
     uses = [[(ops[i][0], 0.0)] + [(b, HOP) for b in sorted(banks[i])] for i in range(n)]
     dur = [o[6] for o in ops]
     lag = [[[(j, dur[j] + hop(i, j)) for j in sorted(x[i])] for i in range(n)] for x in (pred, succ)]
-    far = [i for i in range(n) if ops[i][1] == "r" and ops[i][4][0][0][:2] not in ("le", "lg")]
+    far = [i for i in range(n) if ops[i][1] == "r" and ops[i][4][0][0][:2] not in ("le", "lg") and ops[i][4][0][0][2] != "3"]
 
     def stretch(i, d):
         dur[i] += d
@@ -274,7 +290,7 @@ def plan(ops):
     key = [-rest[i] - part[i] for i in range(n)]
     best = None
     ENDS.append(round(max(rest), 1))
-    dice = [1]
+    dice = [SEED]
 
     def die():
         dice[0] = (dice[0] * 1103515245 + 12345) % 2 ** 31
@@ -288,7 +304,15 @@ def plan(ops):
         else:
             bk = place(sorted_by([-key[i] - dur[i] for i in up], succ, down), succ, True)
         at = place(sorted(up, key=lambda i: -bk[i] - dur[i]), pred, False)
-        return max(at[i] + dur[i] for i in up), at
+        if not TRUE:
+            return max(at[i] + dur[i] for i in up), at, [at[i] for i in marks]
+        seq = sorted(up, key=lambda i: at[i])
+        for run in play[2]:
+            play[3](run, seq, [0.0] * 5, [(-1, 0.0)] * 8)
+        k = len(play[2])
+        return sum(max(run[5][i] + run[1][i] for i in ends) for run in play[2]) / k, at, [sum(run[5][i] for run in play[2]) / k for i in marks]
+    play = player(ops, pred, succ)
+    ends = [i for i in up if not succ[i]]
     for k in range(3):
         best = packed(key, True)
         key = best[1]
@@ -302,7 +326,7 @@ def plan(ops):
             else:
                 stretch(late, -1.0)
             continue
-        cut = [0.0] + [best[1][i] for i in marks] + [best[0]]
+        cut = [0.0] + [best[1][i] for i in marks] + [max(best[1]) + 3.0]
         rnd = [sum(t >= c for c in cut[1:-1]) for t in best[1]]
         spot = [(a + die() * (b - a), 4 + 22 * die()) for a, b in zip(cut, cut[1:])]
         if k % 2:
@@ -314,8 +338,9 @@ def plan(ops):
         if got[0] <= best[0] + 0.4 * (1 - k / PASSES) * die():
             best = got
             continue
-        new = [0.0] + [got[1][i] for i in marks] + [got[0]]
-        won = [new[r + 1] - new[r] < cut[r + 1] - cut[r] - 0.05 for r in range(len(spot))]
+        new, old = [0.0] + got[2] + [got[0]], [0.0] + best[2] + [best[0]]
+        won = [new[r + 1] - new[r] < old[r + 1] - old[r] - 0.05 for r in range(len(spot))]
+        new = [0.0] + [got[1][i] for i in marks]
         if any(won):
             key = [got[1][i] - new[rnd[i]] + cut[rnd[i]] if won[rnd[i]] else t for i, t in enumerate(best[1])]
             got = packed(key, False)
@@ -325,7 +350,205 @@ def plan(ops):
     ENDS.append([dur[i] for i in far])
     ENDS.append(best[1])
     loads = [i for i in range(n) if ops[i][1] == "o"]
-    return loads + [i for i in sorted_by(best[1], pred, up) if ops[i][1] != "o"]
+    return polish(ops, pred, succ, loads + [i for i in sorted_by(best[1], pred, up) if ops[i][1] != "o"], len(loads), die, play)
+
+
+PACES = ((1.0, 1.0, 0.9, 0.34, 1.1), (1.15, 1.15, 0.9, 0.28, 1.25))
+SWEEPS, SPAN, TRIES, HEAT, BIAS, SOFT = 50, 44, 56, 0.1, 1, 0.04
+
+
+def player(ops, pred, succ):
+    n = len(ops)
+    qu = ["vstgy".index(o[0]) for o in ops]
+    bk = [sorted(set(int(x[0][1]) for x in o[3] + o[4] if x[0] in BANKS)) for o in ops]
+    runs = []
+    for c, ga, pe, hop, far in PACES:
+        us = [o[5] * (c * pe if o[0] == "t" else c * ga if o[7] else c) if o[1][0] == "c" else o[5] for o in ops]
+        dur = [us[i] if o[1][0] == "c" else o[6] * (far if o[1] == "r" else 1.0) for i, o in enumerate(ops)]
+        before = [[(j, dur[j] + (0.0 if qu[i] == qu[j] == 2 else hop)) for j in pred[i]] for i in range(n)]
+        after = [[(j, dur[i] + (0.0 if qu[i] == qu[j] == 2 else hop)) for j in succ[i]] for i in range(n)]
+        runs.append((us, dur, before, after, hop, [0.0] * n, [0.0] * n))
+
+    def forward(run, part, free, held):
+        us, dur, before, after, hop, at, rest = run
+        for i in part:
+            q = qu[i]
+            s = free[q]
+            for j, d in before[i]:
+                d += at[j]
+                if d > s:
+                    s = d
+            b = bk[i]
+            if b:
+                for k in b:
+                    who, d = held[k]
+                    if who != q and d > s:
+                        s = d
+                d = s + us[i] + hop
+                for k in b:
+                    held[k] = (q, d)
+            at[i] = s
+            free[q] = s + us[i]
+    return qu, bk, runs, forward
+
+
+def polish(ops, pred, succ, seq, fixed, die, play):
+    n = len(ops)
+    qu, bk, runs, forward = play
+    spare = [{i: x * run[0][i] / ops[i][5] for i, x in EITHER.items()} for run in runs]
+
+    def turned(i):
+        qu[i] = 1 - qu[i]
+        for run, x in zip(runs, spare):
+            run[0][i], x[i] = x[i], run[0][i]
+
+    def backward(run):
+        us, dur, before, after, hop, at, rest = run
+        nq, nb = [-1] * 5, [-1] * 8
+        for i in reversed(seq):
+            r = dur[i]
+            for j, d in after[i]:
+                d += rest[j]
+                if d > r:
+                    r = d
+            q = qu[i]
+            if nq[q] >= 0 and us[i] + rest[nq[q]] > r:
+                r = us[i] + rest[nq[q]]
+            nq[q] = i
+            for k in bk[i]:
+                j = nb[k]
+                if j >= 0 and qu[j] != q and us[i] + hop + rest[j] > r:
+                    r = us[i] + hop + rest[j]
+                nb[k] = i
+            rest[i] = r
+    best = None
+    for sweep in range(SWEEPS + MORE + 1):
+        for run in runs:
+            forward(run, seq, [0.0] * 5, [(-1, 0.0)] * 8)
+        length = sum(max(run[5][i] + run[1][i] for i in seq) for run in runs)
+        if best is None or length < best[0]:
+            best = (length, list(seq), list(qu))
+        if sweep == SWEEPS + MORE:
+            break
+        at = runs[0][5]
+        seq[fixed:] = sorted(seq[fixed:], key=lambda i: at[i])
+        for run in runs:
+            backward(run)
+        whole = [max(run[6]) for run in runs]
+        heat = HEAT * (1.0 - sweep / SWEEPS if sweep < SWEEPS else 0.5 * (SWEEPS + MORE - sweep) / MORE)
+        state = [([0.0] * 5, [(-1, 0.0)] * 8) for run in runs]
+        a = fixed + int(die() * SPAN / 2)
+        for run, (free, held) in zip(runs, state):
+            forward(run, seq[:a], free, held)
+        while a < n - 2:
+            b = min(n, a + SPAN)
+            part = seq[a:b]
+            inside = set(part)
+            nq, nb, left = [-1] * 5, [-1] * 8, 13
+            for k in range(b, min(n, b + 400)):
+                i = seq[k]
+                if nq[qu[i]] < 0:
+                    nq[qu[i]] = i
+                for x in bk[i]:
+                    if nb[x] < 0:
+                        nb[x] = i
+            outs = [{i: max([run[1][i]] + [d + run[6][j] for j, d in run[3][i] if j not in inside]) for i in part} for run in runs]
+
+            marks = [[(list(free), list(held), 0.0)] for free, held in state]
+
+            def noted(p, lo):
+                for run, mark, out in zip(runs, marks, outs):
+                    del mark[lo // 4 + 1:]
+                    for k in range(lo // 4 * 4, len(p), 4):
+                        f, h, m = mark[-1]
+                        f, h = list(f), list(h)
+                        forward(run, p[k:k + 4], f, h)
+                        mark.append((f, h, max([m] + [run[5][i] + out[i] for i in p[k:k + 4]])))
+
+            def worth(p, lo):
+                total, tail = 0.0, p[lo // 4 * 4:]
+                for run, mark, out in zip(runs, marks, outs):
+                    f, h, m = mark[lo // 4]
+                    f, h = list(f), list(h)
+                    forward(run, tail, f, h)
+                    at, rest = run[5], run[6]
+                    for i in tail:
+                        d = out[i] + at[i]
+                        if d > m:
+                            m = d
+                    soft = 0.0
+                    for q in range(5):
+                        if nq[q] >= 0:
+                            d = f[q] + rest[nq[q]]
+                            if d > m:
+                                m = d
+                            if q < 3:
+                                soft += f[q]
+                    for k in range(8):
+                        j = nb[k]
+                        if j >= 0 and qu[j] != h[k][0] and h[k][1] + rest[j] > m:
+                            m = h[k][1] + rest[j]
+                    total += m + SOFT * soft
+                return total
+            noted(part, 0)
+            now = worth(part, 0)
+            kept = [{i: run[5][i] for i in part} for run in runs]
+            slack = {i: min(w - run[5][i] - run[6][i] for run, w in zip(runs, whole)) for i in part}
+            for k in range(TRIES):
+                x, y = int(die() * len(part)), int(die() * len(part))
+                step = 1 if die() < 0.5 else -1
+                if BIAS and (slack[part[x]] - slack[part[y]]) * step < 0:
+                    x = y
+                i = part[x]
+                if i in EITHER and die() < 0.3:
+                    turned(i)
+                    w = worth(part, x)
+                    if w <= now + heat * die():
+                        now = w
+                        noted(part, x)
+                        for run, keep in zip(runs, kept):
+                            for j in part[x // 4 * 4:]:
+                                keep[j] = run[5][j]
+                    else:
+                        turned(i)
+                        for run, keep in zip(runs, kept):
+                            at = run[5]
+                            for j in part[x // 4 * 4:]:
+                                at[j] = keep[j]
+                    continue
+                block = succ[i] if step > 0 else pred[i]
+                y, past = x, 1 + int(die() * die() * 4)
+                while past:
+                    y += step
+                    if y < 0 or y >= len(part) or part[y] in block:
+                        break
+                    if qu[part[y]] == qu[i]:
+                        past -= 1
+                if past:
+                    continue
+                p = part[:x] + part[x + 1:]
+                p.insert(y, i)
+                lo = min(x, y)
+                w = worth(p, lo)
+                if w <= now + heat * die():
+                    part, now = p, w
+                    noted(p, lo)
+                    for run, keep in zip(runs, kept):
+                        for j in p[lo // 4 * 4:]:
+                            keep[j] = run[5][j]
+                else:
+                    for run, keep in zip(runs, kept):
+                        at = run[5]
+                        for j in p[lo // 4 * 4:]:
+                            at[j] = keep[j]
+            seq[a:b] = part
+            c = a + SPAN // 2
+            for run, (free, held) in zip(runs, state):
+                forward(run, seq[a:c], free, held)
+            a = c
+    ENDS.append(round(best[0], 1))
+    SWAP.update(i for i in EITHER if "vstgy"[best[2][i]] != ops[i][0])
+    return best[1]
 
 
 def rank_program(g, core, T, topo):
@@ -389,7 +612,7 @@ def rank_program(g, core, T, topo):
         for n, lo, hi in reads:
             rd.setdefault(n, {})[(e, lo, hi)] = (sem, val)
 
-    def issue(e, kind, call, reads, writes, us, dur):
+    def issue(e, kind, call, reads, writes, us, dur, listed):
         if kind == "r":
             need(e, reads, [])
             call()
@@ -423,7 +646,8 @@ def rank_program(g, core, T, topo):
         return x if x is None or isinstance(x, (int, float)) else x[3] if len(x) == 4 else x[2]
 
     def emit(e, call, reads, writes, us, kind="c", dur=None):
-        ops.append((e, kind, call, flat(reads), flat(writes), us, us if dur is None else dur))
+        reads, writes = flat(reads), flat(writes)
+        ops.append((e, kind, call, reads, writes, us, us if dur is None else dur, us > 0.14 and any(x[0] in LISTS for x in reads)))
 
     def joined(n):
         part = ops[-n:]
@@ -433,7 +657,7 @@ def rank_program(g, core, T, topo):
             return [o[2]() for o in part][-1]
         us = sum(o[5] for o in part)
         kind = "c" + "[" * ("[" in part[0][1]) + "]" * ("]" in part[-1][1])
-        ops.append((part[0][0], kind, call, sum((o[3] for o in part), []), sum((o[4] for o in part), []), us, us))
+        ops.append((part[0][0], kind, call, sum((o[3] for o in part), []), sum((o[4] for o in part), []), us, us, False))
 
     def size(x):
         return x[3].shape[1] if len(x) == 4 else 16 * x[1][3].shape[1]
@@ -477,7 +701,7 @@ def rank_program(g, core, T, topo):
             vec(lambda: g.vector.tensor_scalar(ap(out), ap(a), ap(s1), ap(s2), op0, op1), out, [a, s1, s2], rate)
 
     def scan(out, d0, d1, op0, op1, init=0.0):
-        vec(lambda: g.vector.tensor_tensor_scan(ap(out), ap(d0), ap(d1), init, op0, op1), out, [d0, d1], 0.5 if two(out, d0, d1) else 1)
+        vec(lambda: g.vector.tensor_tensor_scan(ap(out), ap(d0), ap(d1), ap(init), op0, op1), out, [d0, d1, init], 0.5 if two(out, d0, d1) else 1)
 
     def turn(out, in_):
         vec(lambda: g.vector.transpose(ap(out), ap(in_)), out, [in_], 1)
@@ -485,8 +709,13 @@ def rank_program(g, core, T, topo):
     def fill(out, c):
         emit("v", lambda: g.vector.memset(ap(out), c), [], [out], CY * max(64, size(out) * (0.5 if two(out) else 1)))
 
-    def act(out, in_, func=AF.Copy, bias=0.0, scale=1.0, acc=None):
+    def scal(out, in_, func=AF.Copy, bias=0.0, scale=1.0, acc=None):
+        if len(out) == 3:
+            emit("s", lambda: g.scalar.activation(ap(out), ap(in_), AF.Silu), [in_, out[1]], [out[0]], 0.065 + SC * CY * size(out))
+            return
         us = 0.065 + GA * CY * size(out) if len(in_) == 3 else CY * max(64, size(out))
+        if func == AF.Silu:
+            us += 1.3
         kw = {}
         if bias != 0.0:
             kw["bias"] = ap(bias)
@@ -498,6 +727,25 @@ def rank_program(g, core, T, topo):
             kw["accum_out"] = ap(acc)
             us += 0.02
         emit("s", lambda: g.scalar.activation(ap(out), ap(in_), func, **kw), [in_, bias, scale], [out, acc], us)
+
+    other = {}
+
+    def either(first, second):
+        second()
+        x = ops.pop()
+        first()
+        other[len(ops) - 1] = x
+        EITHER[len(ops) - 1] = x[5]
+
+    def act(out, in_, func=AF.Copy, bias=0.0, scale=1.0, acc=None, on="s"):
+        s = lambda: scal(out, in_, func, bias, scale, acc)
+        if func not in (AF.Copy, AF.Identity):
+            return s()
+        w = (lambda: tc(out, in_)) if scale == 1.0 and bias == 0.0 else lambda: ts(out, in_, scale, OP.mult, bias, OP.add)
+        either(*((s, w) if on == "s" else (w, s)))
+
+    def under(out, in_, c, func, bias):
+        either(lambda: scal(out, in_, func, bias, -1.0), lambda: ts(out, in_, c, OP.is_lt))
 
     def mm(out, lhsT, rhs, start, stop):
         emit("t", lambda: g.tensor.matmul(ap(out), ap(lhsT), ap(rhs), start, stop), [lhsT, rhs], [out],
@@ -522,12 +770,11 @@ def rank_program(g, core, T, topo):
     dma("s", v("GNI"), ("gn", 0, M, T.gn[:]), 2.2, turns)
     for j in range(4):
         dma("y", v("SNI", j * C4, (j + 1) * C4), ("sn", j * C4, (j + 1) * C4, T.sn[:, j * C4:(j + 1) * C4]), 3.5 + 1.1 * j, turns)
-    dma("s", v("FAI"), ("fa", 0, M, T.fa[:]), 3.5, turns)
-    dma("y", v("X", 0, M), ("x", 0, M, T.x[:]), 8.5, turns)
+    dma("y", v("FAI"), ("fa", 0, M, T.fa[:]), 7.2, turns)
+    dma("y", v("X", A, E), ("x", 0, M, T.x[:]), 9.0, turns)
     dma("y", v("WC"), ("w", 0, 1, T.w[:]), 25.0, turns)
 
     R16 = v("R16")
-    DIAGB = v("k3", 0, L)
     iota(v("PI"), [[1, 1]], 0, 1)
     fill(v("ONES"), 1.0)
     fill(v("OF"), 1.0)
@@ -538,44 +785,57 @@ def rank_program(g, core, T, topo):
     tc(R16, v("PI2"))
     ts(v("MK"), v("RMOD", 0, 16), R16, eq)
     for m in range(16):
-        if m < PV:
-            ts(v("PICK", 128 * m, 128 * (m + 1)), v("ONESB"), v("MK", m, m + 1), mul)
-        else:
-            act(v("PICK", 128 * m, 128 * (m + 1)), v("ONESB"), scale=v("MK", m, m + 1))
+        act(v("PICK", 128 * m, 128 * (m + 1)), v("ONESB"), scale=v("MK", m, m + 1), on="v" if m < PV else "s")
     for nm in ("SEL", "SELD"):
         fill(v(nm), 0.0)
         act(v(nm, 15, 143, 16), v("ONESB", 0, 128, 16), scale=SELW)
     act(v("SELD", 16, 144, 16), v("ONESB", 0, 128, 16), scale=-SELW)
+    if LOWS:
+        act(v("SELN"), v("SELD"), scale=-2.0)
     act(v("NONESB"), v("ONESB"), scale=-1.0)
     pick(v("TRI"), v("ONESB"), [[1, 128]], ge, -1, -1)
-    pick(v("TIMO"), v("NONESB"), [[-1, 128]], ge, -1, 1)
+    pick(v("TIMO"), v("ONESB"), [[-1, 128]], ge, -1, 1)
     ts(v("NR16"), R16, -1.0, mul)
     ts(v("NR17"), R16, -1.0, mul, -1.0, add)
     fill(v("ZER"), 0.0)
-    fill(v("CT", NB, 128), 9999.0)
+    fill(v("CT", NB, 128), -9999.0)
     fill(v("OK", RW, 128), 0.0)
     iota(v("LANB"), [[16, 12]], 0, 0)
     ts(v("LANB"), v("LANB"), R16, add, 0.5, add)
-    iota(v("LANE"), [[1, L]], 0, 0)
+    iota(v("LANE"), [[-1, L]], 0, 0)
     for i, base in enumerate((0, 16, -16)):
         pick(v("I3", 128 * i, 128 * (i + 1)), v("OF"), [[-1, 128]], eq, base, 1)
     ID = v("I3", 0, 128)
-    for nm, c in (("IDB", 1.0), ("NIDB", -1.0), ("IDK", float(BK)), ("IDD", float(DEAD - M)), ("ID16", 16.0), ("IDHALF", 0.5)):
+    for nm, c in (("IDB", 1.0), ("NIDB", -1.0), ("IDK", float(BK)), ("ID16", 16.0), ("IDHALF", 0.5), ("IDW", W / 2), ("IDL", float(L))):
         act(v(nm), ID, scale=c)
     act(v("ONESK"), v("ONESB"), scale=KS)
     act(v("NONESK"), v("ONESB"), scale=-KS)
-    fill(v("KSR", p=(0, 1)), 16 * KS)
-    fill(v("KS1", p=(0, 1)), KS)
+    fill(v("RUP", p=(0, 1)), ROUND)
+    fill(v("RDN", p=(0, 1)), -ROUND)
+    fill(v("EKS", p=(0, 1)), E - KS)
+    if BARKEY:
+        pick(v("PEN"), v("ONES", 0, 128), [[-1, 128]], eq, 1, 1)
+        tt(v("PEN"), v("IDB"), v("PEN"), sub)
+        act(v("PEN"), v("PEN"), scale=2.0 ** 31)
     tt(v("TMPB"), v("TRI"), v("IDB"), sub)
-    act(v("FST"), v("TMPB"), scale=KS)
+    act(v("FST"), v("TMPB"), scale=-KS)
     for t in range(T_):
-        a = Q * t // 16
-        iota(v("BT", 128 * t, 128 * t + NB - a), [[1, NB - a]], a, 0)
-        if a:
-            iota(v("BT", 128 * t + NB - a, 128 * t + NB), [[1, a]], 0, 0)
-        iota(v("BT", 128 * t + NB, 128 * t + 128), [[0, 128 - NB]], RW, 0)
-    iota(v("SN", M, WT), [[0, WT - M]], M, 0, v("I3"))
-    fill(v("SN", M + 1, M + 2), float(M + 2))
+        a = (Q * t + A - NEW) // 16
+        iota(v("BT", 128 * t, 128 * t + NB - a), [[1, NB - a]], NEW // 16 + a, 0)
+        iota(v("BT", 128 * t + NB - a, 128 * t + NB), [[1, a]], NEW // 16, 0)
+        iota(v("BT", 128 * t + NB, 128 * t + 128), [[0, 128 - NB]], E // 16, 0)
+    iota(v("SN", E, WT), [[0, WT - E]], E, 0, v("I3"))
+    iota(v("SN", 0, A), [[0, A]], E, 0, v("I3"))
+    fill(v("SN", NOB, NOB + 1), float(NOS))
+    ts(v("CAP"), v("RMOD", 0, L), R16, gt, RAISE + 2.0 ** 25, mul)
+    act(v("CAP"), v("CAP"), bias=-2.0 ** 25)
+    ups = {}
+
+    def up(c, k=1.0):
+        if (c, k) not in ups:
+            ups[(c, k)] = v("UP", len(ups), len(ups) + 1)
+            act(ups[(c, k)], R16, bias=c + 15 * k * RAISE, scale=-k * RAISE)
+        return ups[(c, k)]
 
     ts(v("RRS"), v("GNI"), 2, ge, float(M + 1), mul)
     ts(v("RRS"), v("RRS"), -1.0, add)
@@ -598,15 +858,19 @@ def rank_program(g, core, T, topo):
     tc(v("FAS"), v("FAI"))
     tc(v("GNS"), v("GNI"))
     for j in range(4):
-        act(v("F1", j * C4, (j + 1) * C4), spread("FAS", j, ("k2", "k5")[j % 2]))
-        tc(v("SN", j * C4, (j + 1) * C4), v("SNI", j * C4, (j + 1) * C4))
+        act(v("F1", A + j * C4, A + (j + 1) * C4), spread("FAS", j, ("k2", "k5")[j % 2]), bias=float(A))
+        ts(v("SN", A + j * C4, A + (j + 1) * C4), v("SNI", j * C4, (j + 1) * C4), float(A), add)
     act(v("D15"), v("RMOD", 0, L), AF.Abs, v("NR16"))
     act(v("DIAG"), v("D15"), AF.Relu, 1.0, -1.0)
-    act(DIAGB, v("D15"), AF.Relu, 1.0, -1.0)
+    act(v("OFFD"), v("D15"), AF.Sign)
+    fill(v("LOW"), 0.0)
+    for a in (0, 64, 112, 144):
+        ts(v("LOW", a, a + 16), v("RMOD", 0, 16), R16, le)
     act(v("RS0"), v("RMOD"), AF.Sign)
-    fill(v("F1", M, 1760), float(M + 1))
-    act(v("F1", 1760, W), v("RMOD", 0, L), scale=0.0)
-    fill(v("X", M, WT), BIG)
+    fill(v("F1", E, WP), float(NOB))
+    act(v("F1", 0, A), v("ONES", 0, A), AF.Silu, scale=float(A))
+    fill(v("X", E, WT), BIG)
+    fill(v("X", 0, A), BIG)
     ts(v("PI2"), v("PI"), 4, OP.logical_shift_right, 1, OP.bitwise_and)
     tc(v("PBF", 1, 2), v("PI2"))
     ts(v("PBF", 0, 1), v("PBF", 1, 2), -1.0, mul, 1.0, add)
@@ -618,31 +882,38 @@ def rank_program(g, core, T, topo):
     fill(v("SLR", 0, 128, 16, p=(0, 1)), -float(2 ** 32))
     iota(v("REP", p=(0, 64)), [[0, 1024]], 1, 0, v("I3"))
     pick(v("REP", p=(0, 64)), v("REP", p=(0, 64)), [[-1, 64], [0, 16]], eq, 0, 1)
-    iota(v("CT0"), [[1, 128]], 1760 - M, 0)
-    for nm in ("AA", "AB", "R2"):
+    iota(v("CT0"), [[1, 128]], NEW - E, 0)
+    for nm in ("AA", "AB"):
         fill(v(nm, NB, 128), 0.0)
     fill(v("ZEH"), 0.0)
     for h in ("H0", "H1"):
-        fill(v(h, L, LW), float(M))
+        fill(v(h, L, LW), float(E))
     for t in range(3):
         act(v("me%d" % t, L, LW), v("ONES", 0, 16))
         nm, a, b = ages("m", t)
         act(v(nm, a + L, b), v("ONES", 0, 16), scale=7.0)
     act(v("TR"), v("LANB"), bias=TB - 1.0, scale=2.0)
     act(v("TRP"), v("LANB"), bias=TB - 1.0 - PO, scale=2.0)
-    act(v("DT"), v("LANE"), bias=TB + PO / 15, scale=2.0)
-    tt(v("DT"), v("DT"), DIAGB, mul)
-    act(v("DT"), v("DT"), bias=-PO / 15)
+    act(v("DT"), v("LANE"), bias=TB - PO + 16 * L, scale=-2.0)
+    tt(v("DT"), v("DT"), v("DIAG"), mul)
+    act(v("DT"), v("DT"), bias=-float(L))
+    fill(v("NLR", p=(0, 1)), -float(L))
+    fill(v("GG", 0, 1), 0.0)
+    fill(v("CB", NB, 128), 0.0)
+    act(v("TOP"), v("LANE"), scale=0.0)
+    act(v("TOP", 0, L, 16), v("TR"))
     dma("s", v("GN1", p=(0, 128, 16)), v("GNS"), 3.0)
-    emit("y", lambda: [g.sync.dma_start(ap(v("GN", 0, M, p=(r, 128, 16))), ap(v("GN1", p=(0, 128, 16)))) for r in range(16)],
-         [v("GN1"), v("X", 0, M)], [v("GN", 0, M)], 1.2, "d", 9.0)
-    fill(v("GN", M, W), 7.0)
-    emit("y", lambda: g.sync.dma_start(ap(v("F2", 0, W)), ap(v("F1", 0, W))), [v("F1", 0, W), v("GN", 0, M)], [v("F2", 0, W)], 0.07, "d", 8.0)
-    iota(v("RM", 0, W), [[0, W]], 0, 0, v("REP"))
-    iota(v("SN", IDB, IDB + W), [[1, W]], 0, 0, v("REP"))
-    fill(v("SN", IDB + W, WI), float(M))
+    emit("y", lambda: [g.sync.dma_start(ap(v("GN", A, E, p=(r, 128, 16))), ap(v("GN1", p=(0, 128, 16)))) for r in range(16)],
+         [v("GN1"), v("X", A, E)], [v("GN", A, E)], 1.2, "d", 9.0)
+    fill(v("GN", E, WP), 7.0)
+    fill(v("GN", 0, A), 7.0)
+    emit("y", lambda: g.sync.dma_start(ap(v("F2", 0, WP)), ap(v("F1", 0, WP))), [v("F1", 0, WP), v("GN", A, E)], [v("F2", 0, WP)], 0.07, "d", 8.0)
+    for nm, z in (("xo", v("ZEH", 0, 16)), ("fo", v("ZER", 0, 16, p=(0, 128, 16))), ("f2o", v("ZER", 0, 16, p=(0, 128, 16)))):
+        emit("y", lambda nm=nm, z=z: g.sync.dma_start(T[nm][:, M:M + 16], ap(z)), [z, v("F2", 0, WP)], [(nm, M, M + 16, None)], 0.07, "d", 3.0)
+    iota(v("RM", NEW, WP), [[0, W]], 0, 0, v("REP"))
+    iota(v("SN", IDB, WI), [[1, WP]], 0, 0, v("REP"))
     ts(v("M0"), R16, 0.0, eq)
-    ts(v("E0"), R16, 0.0, ne, float(M), mul)
+    ts(v("E0"), R16, 0.0, ne, float(E), mul)
     for t in range(1, 3):
         act(v("CT3", S * (t - 1), S * t), v("CT0", S * (t - 1), S * t), scale=v("MK", t, t + 1))
     fill(v("POR", p=(0, 1)), PO)
@@ -652,10 +923,24 @@ def rank_program(g, core, T, topo):
     act(v("SCB"), v("RMOD"), AF.Abs, v("NR17"))
     act(v("BS0"), v("SCB"), AF.Relu, PO, -PO)
 
-    def listed(res, masked):
-        a, b = masked[1:3]
-        scan(v(res, a, b), v("RS0", a, b), masked, mul, add)
+    def listed(res, row, a=0):
+        b = a + size(row)
+        scan(v(res, a, b), v("CAP", a, b), row, add, OP.max)
         return v(res, a + 15, b, 16)
+
+    def over(name):
+        return 0.0 if ONV[name] else ROUND
+
+    def whole(out, src):
+        if ONV[out[0]]:
+            ts(out, src, ROUND, add, -ROUND, add)
+        else:
+            act(out, src, bias=ROUND)
+
+    def unwound(a, b, out, first=()):
+        for j, (l, r) in enumerate(first):
+            mm(out, l, r, j == 0, False)
+        mm(out, v("IDW"), v("SGB", a, b), not first, True)
 
     def numbers(tag, src):
         k, nv = BANK[tag][0], max(NV[tag])
@@ -666,6 +951,7 @@ def rank_program(g, core, T, topo):
                 pick(v("XR" + tag, s, 16 * nv, 16), v(src[0], src[1], src[1] + nv), [[0, nv]], ge, 0, 0)
             joined(16)
             return
+        k = BANK[tag][XB]
         for a in range(0, 16 * nv, 384):
             b = min(a + 384, 16 * nv)
             mm(v(k, 128, 128 + b - a), v("XT" + tag, p=(0, 64)), v("REP", a, b, p=(0, 64)), True, True)
@@ -676,107 +962,164 @@ def rank_program(g, core, T, topo):
         mm(v("k6", 128, 128 + NB), v("ONESB"), ok, True, True)
         mm(v("k6", 256, 256 + NB), v("TIMO"), ok, True, True)
         scan(v("CB", 0, NB), v("k6", 128, 128 + NB), v("ZER", 0, NB), add, add)
-        tt(v("CT", 0, NB), v("k6", 256, 256 + NB), v("CB", 0, NB), add)
+        tt(v("CT", 0, NB), v("k6", 256, 256 + NB), v("CB", 0, NB), sub)
         for q in range(12):
             act(v("JK", 128 * q, 128 * q + NB), v("CB", 0, NB), AF.Sign, v("LANB", q, q + 1), -1.0, v("NBS", q, q + 1))
-        F = v("F1" if t % 2 == 0 else "F2", 0, W)
+        F = v("F1" if t % 2 == 0 else "F2", 0, WP)
         tab, H = v("SN", 0, WT), "H%d" % (t % 2)
 
         def first(a, b):
             r, l = (lambda n: v(n, a, b)), (lambda n: v(n, a // 16, b // 16))
             ts(l("BL"), l("NBS"), 0.5, mul, NB / 2, add)
-            tt(r("FLG"), at(v("CT"), l("BL")), r("LANE"), le)
+            tt(r("FLG"), at(v("CT"), l("BL")), r("LANE"), ge)
             act(r("BR"), at(v("BT", 128 * t, 128 * t + 128), l("BL")))
-            kh = r(LB[a > 0][0])
-            mm(kh, v("ID16"), r("BR"), True, False)
+            kh = r("k6")
+            if over("S0"):
+                mm(kh, v("RUP", p=(0, 1)), v("ONES", a, b, p=(0, 1)), True, False)
+            mm(kh, v("ID16"), r("BR"), not over("S0"), False)
             mm(kh, v("ONESB"), r("FLG"), False, True)
-            tt(r("TMP"), kh, r("DIAG"), mul)
-            act(r(H), kh)
-            tc(l("HL"), listed("RWH", r("TMP")))
-            tt(r("TMP"), at(F, l("HL")), r("DIAG"), mul)
+            ts(l("HL"), listed("RWH", kh, a), up(over("S0")), sub)
+            if t < 3:
+                act(r(H), kh, bias=-over("S0"))
+            else:
+                act(r("SGB"), r("BR"), AF.Sign, A / 16 - 0.5, -1.0)
+                unwound(a, b, v("k4", 320 + a, 320 + b), [(v("ID16"), r("BR")), (v("ONESB"), r("FLG"))])
+                act(r(H), v("k4", 320 + a, 320 + b), bias=W / 2 - A)
+            ts(r("PH"), at(F, l("HL")), ROUND, add, -ROUND, add)
             act(r("me%d" % t), at(v("X"), l("HL")))
-            mm(r(LB[a > 0][4]), v("ONESB"), r("TMP"), True, True)
-            tc(l("P0L"), listed("RWP", r("TMP")))
+            ts(l("P0L"), listed("RWP", r("PH"), a), up(0.0), sub)
             for h in range(a // 64, b // 64):
                 numbers("A%d" % h, v("me%d" % t, 64 * h, 64 * h + 64))
 
         def second(a, b):
             r, l = (lambda n: v(n, a, b)), (lambda n: v(n, a // 16, b // 16))
-            tt(r("TMQ"), at(F, l("P0L")), r("DIAG"), mul)
-            tc(l("P1L"), listed("RWQ", r("TMQ")))
-            act(r("S0"), at(tab, l("P0L")))
-            kh, kk, k0, kd, kp = LB[a > 0]
-            tt(r("EQ0"), r("S0"), r(kh), eq)
-            act(r("A0N"), r("S0"), AF.Abs, -float(M))
-            act(r("NE0"), r("A0N"), AF.Relu, 1.0, -1.0)
-            KK, W0, WD = v(kk, L + a, L + b), r(k0), v(kd, L + a, L + b)
-            mm(W0, v("IDK"), r("EQ0"), True, False)
-            mm(W0, v("IDD"), r("NE0"), False, True)
-            tt(r("UD"), r("S0"), W0, add)
-            mm(KK, v("ONESB"), r("EQ0"), True, False)
-            mm(KK, v("ONESB"), r("NE0"), False, True)
-            act(r("UR"), KK, AF.Relu, -15.0)
-            mm(WD, v("KSR", p=(0, 1)), v("ONES", a, b, p=(0, 1)), True, False)
-            mm(WD, v("NONESK"), r("EQ0"), False, False)
-            mm(WD, v("NONESK"), r("NE0"), False, False)
-            tc(r("S1"), at(tab, l("P1L")))
-            tt(r("EQ1"), r("S1"), r(kp), eq)
+            whole(r("QR"), at(F, l("P0L")))
+            ts(l("P1L"), listed("RWQ", r("QR"), a), up(over("QR")), sub)
+            whole(r("S0"), at(tab, l("P0L")))
+            tt(r("EQ0"), r("S0"), r("k6"), eq)
+            under(r("SG0"), r("S0"), over("S0") + E, AF.Sign, over("S0") + E)
+            KK, W0, WD = v("k6", L + a, L + b), r("k5"), v("k5", L + a, L + b)
+            if over("S0"):
+                mm(W0, v("RDN", p=(0, 1)), v("ONES", a, b, p=(0, 1)), True, False)
+            mm(W0, v("IDK"), r("EQ0"), not over("S0"), True)
+            late = a in BARKEY
+            ud = v("k3", 256 + a, 256 + b) if late else r("UD")
+            tt(ud, r("S0"), W0, add)
+            mm(KK, v("ONESB"), r("SG0"), True, False)
+            mm(KK, v("NONESB"), r("EQ0"), False, True)
+            if not ONV["UR"]:
+                act(r("UR"), KK, AF.Relu, 1.0, -1.0)
+            mm(WD, v("ONESK"), r("SG0"), True, False)
+            mm(WD, v("NONESK"), r("EQ0"), False, late)
+            if late:
+                act(r("UD"), WD)
+                tt(r("QR"), at(tab, l("P1L")), r("UD"), add)
+                tt(r("SA"), r("QR"), ud, OP.min)
+                ts(r("SA16"), r("SA"), float(E), OP.min, 0.25, add)
+                tc(r("SAH"), r("SA16"))
+                mm(r("k4"), v("ONESK"), r("SG0"), True, False)
+                mm(r("k4"), v("NONESK"), r("EQ0"), False, False)
+                mm(r("k4"), v("IDB"), r("PH"), False, True)
+                tt(r("EQ1"), r("SAH"), r("k4"), eq)
+                mm(v("k4", 192, 256), v("IDB"), r("SAH"), True, False)
+                mm(v("k4", 192, 256), v("IDK"), r("EQ1"), False, True)
+                return
+            ts(r("S1"), at(tab, l("P1L")), ROUND, add, -ROUND, add)
+            tt(r("EQ1"), r("S1"), r("PH"), eq)
             mm(WD, v("IDB"), r("S1"), False, False)
             mm(WD, v("IDK"), r("EQ1"), False, True)
-            tt(r("SA"), WD, r("UD"), OP.min)
-            ts(r("SA16"), r("SA"), float(DEAD), OP.min)
+            sa = r("SAH" if ("A0", 0) in PTURN else "SA")
+            tt(sa, WD, r("UD"), OP.min)
+            ts(r("SA16"), sa, float(E), OP.min)
         for stage in (first, second):
             for a, b in CH:
                 stage(a, b)
         hw, pw = v("RWH", 15, L, 16), v("RWP", 15, L, 16)
-        sixteen(v("k6", 448, 460), "SEL", "UR", 0, L)
-        act(v("NU"), v("k6", 448, 460), bias=float(IDB), scale=-IDB / (16 * SELW))
-        act(v("UY"), v("k6", 448, 460), bias=-PO, scale=DEAD / (16 * SELW))
-        act(v("UB"), v("k6", 448, 460), bias=float(IDB), scale=(KS - IDB) / (16 * SELW))
-        ts(v("CA"), pw, 64.0, lt, KS, mul)
-        tt(v("CA"), v("CA"), v("NU"), OP.max)
-        tt(v("LIFT"), v("CA"), v("UB"), OP.min)
-        act(v("NF"), v("LIFT"), bias=KS + M - PO, scale=-1.0)
+        if ONV["UR"]:
+            ts(v("NU"), listed("ZT", v("k6", L, 2 * L)), up(0.5), gt, float(IDB), mul)
+        else:
+            sixteen(v("k6", 448, 460), "SEL", "UR", 0, L)
+            act(v("NU"), v("k6", 448, 460), bias=float(IDB), scale=-IDB / (16 * SELW))
+        act(v("RT"), pw, AF.Abs, up(-over("PR") - A - 31, -1.0))
+        tt(v("RT"), v("RT"), v("NU"), add)
+        ts(v("CA"), v("RT"), 32.5, lt, KS, mul)
+        if t == 3:
+            cleaned()
         if t < 3:
-            ts(v("Z5", 24, 36), hw, -PO, add)
+            ts(v("Z5", 24, 36), hw, up(over("S0") + PO), sub)
             act(v(*ages("m", t, L)), at(v("GN"), v("HL")))
             if t:
                 ship("e", t, v("me%d" % t))
             else:
-                ship("e", t, v("me0"), [v("TRI"), v("BT"), v("CT0"), v("SN", IDB, IDB + W)])
+                ship("e", t, v("me0"), [v("TRI"), v("BT"), v("CT0"), v("SN", IDB, WI)])
                 ship("g", t, v("mg0"))
             mm(v("k5", 0, L), v("ONESB"), v("FLG"), True, True)
-            ts(v("OH"), v("k5", 0, L), R16, eq)
-            act(v("NOH"), v("OH"), AF.Identity, 1.0, -1.0)
-            act(v("CTS", 0, NB), v("CT", 0, NB), scale=-1.0 / (L + 0.5))
+            ts(v("NOH"), v("k5", 0, L), R16, ne)
             for x, y, n in ((0, TURN, NB - TURN), (NB - TURN, 0, TURN)):
-                act(v("R2", x, x + n), v("CB", y, y + n), AF.Relu, float(L), -1.0)
-                tt(v("AA", x, x + n), v("OK", y, y + n), v("CTS", y, y + n), mul)
-            tt(v("TMI"), v("R2"), v("k3", 0, 128), mul)
-            ts(v("IDX"), listed("RWI", v("TMI")), -1.0, mul, L - 1.0, add)
+                tt(v("AA", x, x + n), v("OK", y, y + n), v("CT", y, y + n), mul)
+            x = NB - TURN
+            scan(v("RWI", 0, x), v("CAP", 0, x), v("CB", TURN, NB), add, OP.max)
+            scan(v("RWI", x, 128), v("CAP", x, 128), v("CB", 0, 128 - x), add, OP.max, v("RWI", x - 1, x))
+            ts(v("IDX"), v("RWI", 15, 128, 16), up(0.0), sub, float(L), OP.min)
 
-    def down(tag, e, idx, son, lift=(), row=None):
+    def cleaned():
+        rows = [v(f, NEW, WP, p=(0, 128, 16)) for f in ("F1", "F2")]
+        for j in range(2):
+            dma("y", v("CF", NB * j, NB * j + NB), rows[j], 3.0)
+        cf, cr, k = v("CF", 0, 2 * NB), v("CR", 0, 2 * NB), v("k6", L, L + 2 * NB)
+        act(cr, cf, bias=ROUND + W / 2 - A)
+        act(v("SGB", 0, 2 * NB), cf, AF.Sign, A - 0.5, -1.0)
+        unwound(0, 2 * NB, k, [(v("RDN", p=(0, 1)), v("ONES", 0, 2 * NB, p=(0, 1)))])
+        tt(cf, cr, k, add)
+        for j in range(2):
+            dma("y", rows[j], v("CF", NB * j, NB * j + NB), 3.0)
+
+    def down(tag, e, idx, son, lift=(), row=None, bar=None):
         n, nv, kb = 64, NV[tag][e], BANK[tag][0]
         u, xr = "UU" + tag, "XR" + tag
-        SP = v("k3", 256 + n * PARTS.index(tag), 256 + n * PARTS.index(tag) + n)
-        turn(SP, son)
+        kt, o = ("k3", n * PARTS.index(tag)) if TBANK or (tag, e) not in PTURN else (kb, 64)
+        SP = v(kt, o, o + n)
+        if (tag, e) in PTURN:
+            for a in range(0, 128, 32):
+                for b in range(0, n, 32):
+                    mm(v(kt, o + b, o + b + 32, p=(a, a + 32)), v(son[0], son[1] + b, son[1] + b + 32, p=(a, a + 32)),
+                       v("IDB", a, a + 32, p=(a, a + 32)), True, True)
+            joined(n // 8)
+        else:
+            turn(SP, son)
         mid = (nv + n) // 4 * 2
         cuts = [(kb, nv, n)] if n - nv <= 32 else [(kb, nv, mid), (BANK[tag][1], mid, n)]
+        plain = (tag, e) in PLAIN
+        if plain:
+            cuts = [(kb, nv, n)] + [(BANK[tag][1], a, b) for a, b in HALVES(nv)]
         for k, a, b in cuts:
             us, dif = v(u, 16 * a, 16 * b), v(k, 512 - 16 * (b - a), 512)
             mm(dif, v("XT" + tag, p=(0, 64)), v("REP", 16 * a, 16 * b, p=(0, 64)), True, False)
-            act(us, at(v("X"), idx(a, b)))
+            (tc if a < nv else act)(us, at(v("X"), idx(a, b)))
+            if (tag, e) in SENDFIRST and NV["t"] < 3:
+                ops[-1][3].append(("NLS", 0, 4))
             mm(dif, v("NIDB"), us, False, True)
-        for a, b in HALVES(nv):
+            if a < nv:
+                act(us, dif, AF.Abs)
+        low = (tag, e) in LOWS
+        for a, b in () if plain else HALVES(nv):
             ux = v(u, 16 * a, 16 * b)
             tt(ux, at(v("X"), idx(a, b)), v(xr, 16 * a, 16 * b), sub)
-            act(ux, ux, AF.Abs)
+            if low:
+                ts(v("UN", 16 * a, 16 * b), ux, 0.0, OP.min)
+            else:
+                act(ux, ux, AF.Abs)
         for k, a, b in cuts:
-            act(v(u, 16 * a, 16 * b), v(k, 512 - 16 * (b - a), 512), AF.Abs)
+            if a >= nv:
+                act(v(u, 16 * a, 16 * b), v(k, 512 - 16 * (b - a), 512), AF.Abs)
         mm(v(kb, 0, n), v("SLR", p=(0, 1)), v("ONES", 0, n, p=(0, 1)), True, False)
+        if bar:
+            mm(v(kb, 0, n), v("PEN"), bar, False, False)
+        for s in range(16 * low):
+            mm(v(kb, 0, nv), v("SELN", 15 - s, 143 - s), v("UN", s, 16 * nv, 16), False, False)
         for s in range(16):
             mm(v(kb, 0, n), v("SELD", 15 - s, 143 - s), v(u, s, 16 * n, 16), False, s == 15)
-        joined(17)
+        joined(16 + 16 * low if EARLYC else 17 + 16 * low + bool(bar))
         kp, dd, ee, rr = [v(x + tag) for x in ("MM", "DD", "EE", "RR")]
         turn(kp, v(kb, 0, n))
         scan(dd, kp, v("ZER", 0, n), add, OP.max)
@@ -794,67 +1137,95 @@ def rank_program(g, core, T, topo):
         joined(4 + len(lift))
         return v(kb, 0, 4)
 
-    def step(tag, e, lift=(), row=None):
-        tc(v("IX" + tag), at(v("SN", 0, WT if e < 2 else WI), v("LL" + tag)))
-        tc(v("SF" + tag), v("IX" + tag))
-        return down(tag, e, lambda a, b: v("IX" + tag, a, b), v("SF" + tag), lift, row)
+    def sons(tag, e, places):
+        sf = v(("SH" if (tag, e) in PTURN else "SF") + tag)
+        ts(v("IX" + tag), at(v("SN", 0, WT if e < 2 else WI), places), ROUND, add, -ROUND, add)
+        tc(sf, v("IX" + tag))
+        return sf
 
-    def barren(tile, places, out):
-        act(tile, at(v("SN"), places), AF.Abs, -float(M))
+    def step(tag, e, places, lift=(), row=None):
+        sf = sons(tag, e, places) if places else v("SF" + tag)
+        return down(tag, e, lambda a, b: v("IX" + tag, a, b), sf, lift, row)
+
+    def barren(tile, src, out):
+        act(tile, src, AF.Sign, E - 0.5, -1.0)
         mm(out, v("ONESB"), tile, True, True)
 
     def own(t):
-        for h in range(3):
+        for h in (2, 1, 0):
             tag, o, lo = "A%d" % h, 4 * h, 64 * h
-            x = down(tag, 0, lambda a, b: v("SA16", lo + a, lo + b), v("SA", lo, lo + 64))
-            ts(v("LL" + tag), x, float(DEAD), OP.min)
-            act(v("W1", o, o + 4), x, bias=-PO)
-            x = step(tag, 1, [v("LIFT", o, o + 4)])
-            ts(v("LL" + tag), x, float(IDB + W), OP.min)
-            act(v("W2", o, o + 4), x, bias=-PO)
+            late = any(a <= lo < b for a, b in CH if a in BARKEY)
+            x = down(tag, 0, lambda a, b: v("SA16", lo + a, lo + b), v("k4", 192, 256) if late else v("SAH" if (tag, 0) in PTURN else "SA", lo, lo + 64),
+                     bar=v("EQ1", lo, lo + 64) if late else None)
+            ts(v("LL0", o, o + 4), x, float(E), OP.min)
+            x = step(tag, 1, v("LL0", o, o + 4), [v("NU", o, o + 4), v("CA", o, o + 4)])
+            ts(v("LL1", o, o + 4), x, float(IDB + E), OP.min)
+            sf = sons(tag, 2, v("LL1", o, o + 4))
             if t < 3:
-                barren(v("AYI", lo, lo + 64), v("LL" + tag), v("k4", 320 + lo, 384 + lo))
+                barren(v("AYI", lo, lo + 64), sf if h else at(v("SN"), v("LL1", o, o + 4)), v("k4", 320 + lo, 384 + lo))
         if t < 3:
-            act(v("NFR"), v("k4", 320, 512), AF.Relu, 1.0, -1.0)
+            under(v("NFR"), v("k4", 320, 512), -15.5, AF.Relu, -15.0)
             sending(t)
-        tt(v("W1"), v("W1"), v("UY"), OP.max)
-        tt(v("W1"), v("W1"), v("NF"), OP.min)
+        ts(v("W1"), v("LL0"), IDB - PO, add)
+        tt(v("W1"), v("W1"), v("NU"), sub)
+        ts(v("W2"), v("LL1"), -PO, add)
         tt(v("YP"), v("W1"), v("W2"), OP.min)
-        tt(v("BS0", 0, L, 16), v("W1"), v("W2"), OP.min)
+        ts(v("BS0", 0, L, 16), v("YP"), E - PO, OP.min)
+        ts(v("YL"), v("YP"), PO, add, float(E), OP.min)
         early(t)
-        for h in range(3):
-            a = 64 * h
-            x = step("A%d" % h, 2, (), v("k4", 64 + a, 128 + a))
-            act(v("BS0", L + a, L + a + 64, 16), x, bias=-PO)
-            if 16 * SS[t] + 16 < a + 64:
-                lo = max(a, 16 * SS[t] + 16)
-                tc(v("YR", L + lo, L + a + 64), v("k4", 64 + lo, 128 + a))
-            if SS[t]:
-                act(v("YW", L + a, L + a + 64), v("k4", 64 + a, 128 + a), bias=-PO)
+        for h in (2, 1, 0):
+            a, srow = 64 * h, v("k4", 64 + 64 * h, 128 + 64 * h)
+            x = step("A%d" % h, 2, None, (), srow)
+            if t == 3:
+                mm(v("k6", a, a + 64), v("PICK", 128 * 15, 128 * 16), v("RTA%d" % h), False, False)
+            if h or t < 3:
+                act(v("BS0", L + a, L + a + 64, 16), x, bias=-PO)
+            ts(v("SL", 4 * h, 4 * h + 4), x, float(E), OP.min)
+            if h:
+                tc(v("YR", L + a, L + a + 64), srow)
+                inside(L + a, L + a + 64, srow)
+            else:
+                lowest(x)
+            xg = v(BANK["A%d" % h][0], 128, 192)
+            act(v("XS", a, a + 64), at(v("X"), v("SL", 4 * h, 4 * h + 4)))
+            mm(xg, v("QRT", p=(0, 1)), v("ONES", 0, 64, p=(0, 1)), True, False)
+            mm(xg, v("IDHALF"), v("me%d" % t, a, a + 64), False, False)
+            mm(xg, v("IDHALF"), v("XS", a, a + 64), False, True)
+            if ONV["XJ"] or t == 3 and not h:
+                ts(v("XJB", a, a + 64), xg, ROUND, add, -ROUND, add)
+            else:
+                act(v("XJ", a, a + 64), xg, bias=ROUND)
+                act(v("XJB", a, a + 64), v("XJ", a, a + 64), bias=-ROUND)
 
     def arrivals(t):
         ls = "AX"
         act(v(ls, 0, S), at(v("le%d" % (t - 1), 0, LW), v("ls%d" % (t - 1))))
         act(v(ls, S, 2 * S), at(v(*ages("l", t - 1)), v("ls%d" % (t - 1))))
-        mm(v("k2", 0, S), v("WONE"), v(ls, 0, S), True, True)
-        tt(v("TMC"), v("k2", 0, S), v("DIAG", 0, S), mul)
-        tc(v("CI"), listed("RWC", v("TMC")))
+        if AHEAD:
+            mm(v("k2", 0, LW), v("WONE"), v("le%d" % (t - 1), 0, LW), True, True)
+            tc(v("CI"), v("k2", 0, LW))
+            ts(v("CI2"), v("CI"), 63, OP.bitwise_and)
+            ts(v("CRW"), at(v("CI2"), v("ls%d" % (t - 1))), float(A), add)
+            ts(v("LLAB"), listed("RWC", v("CRW")), up(0.0), sub)
+        else:
+            mm(v("k2", 0, S), v("WONE"), v(ls, 0, S), True, True)
+            ts(v("CI", 0, 4), listed("RWC", v("k2", 0, S)), up(0.0), sub)
+            ts(v("CI2", 0, 4), v("CI", 0, 4), 63, OP.bitwise_and)
+            ts(v("LLAB"), v("CI2", 0, 4), float(A), add)
         numbers("AB", v(ls, 0, S))
-        tt(v("TMG"), v(ls, S, 2 * S), v("k3", 0, S), mul)
-        gen = listed("RWG", v("TMG"))
-        ts(v("LIFB", 0, 4), gen, 4.5, gt, float(BK), mul)
-        ts(v("LIFB", 4, 8), gen, 2.5, lt, float(IDB), mul)
-        ts(v("LIFB", 8, 12), gen, 3.5, lt, float(IDB), mul)
-        ts(v("CI2"), v("CI"), 63, OP.bitwise_and)
-        tc(v("LLAB"), v("CI2"))
+        gen = listed("RWG", v(ls, S, 2 * S))
+        ts(v("LIFB", 0, 4), gen, up(4.5), gt, float(BK), mul)
+        ts(v("LIFB", 4, 8), gen, up(2.5), lt, float(IDB), mul)
+        ts(v("LIFB", 8, 12), gen, up(3.5), lt, float(IDB), mul)
         for e in range(4):
-            x = step("AB", e, [v("LIFB", 4 * e, 4 * e + 4)] if e < 3 else ())
-            ts(v("LLAB" if e < 3 else "BF16"), x, float(WI - 1 if e else DEAD), OP.min)
-            if e == 2 and t < 3:
-                barren(v("AYB"), v("LLAB"), v("k4", 256, 320))
-                act(v("mf%d" % t), v("k4", 256, 320), AF.Sign)
+            x = step("AB", e, v("LLAB") if e < 3 else None, [v("LIFB", 4 * e, 4 * e + 4)] if e < 3 else ())
+            ts(v("LLAB" if e < 3 else "BF16"), x, float(IDB + E if e else E), OP.min)
+            if e == 2:
+                sons("AB", 3, v("LLAB"))
+                barren(v("AYB"), at(v("SN"), v("LLAB")), v("k4", 256, 320))
+                act(v("mf%d" % t), v("k4", 256, 320), AF.Sign, 16.0)
                 ship("f", t, v("mf%d" % t))
-        act(v("mr%d" % t), at(v("X"), v("BF16")))
+        tt(v("mr%d" % t), at(v("X"), v("BF16")), v("mf%d" % t), mul)
         ship("r", t, v("mr%d" % t))
 
     sent = [0]
@@ -873,23 +1244,38 @@ def rank_program(g, core, T, topo):
 
     YROW, SROW, CNT = v("k5", 0, L), v("k4", 64, 64 + L), v("k6", 0, L)
 
-    def alike(lo, whole, wide, last):
-        scan(v("SCB", lo, lo + L), v("RS0", 0, L), v("BS0", lo, lo + L), mul, add)
-        tt(v("ED", lo, lo + L), v("SCB", lo, lo + L), whole, eq)
-        mm(CNT, v("ONESK"), v("ED", lo, lo + L), False, False)
-        cuts = [(q, 1056 * (lo // L) + sum((11 - j) * 16 for j in range(q)), (11 - q) * 16) for q in range(11)]
-        for q, o, n in cuts[wide:]:
+    def inside(a, b, row):
+        scan(v("SCB", a, b), v("RS0", a, b), v("BS0", a, b), mul, add)
+        tt(v("ED", a, b), v("SCB", a, b), row, eq)
+        mm(v("k6", a % L, a % L + b - a), v("ONESK"), v("ED", a, b), False, False)
+
+    def alike(lo, last):
+        cuts = [(q, sum((11 - j) * 16 for j in range(q)), (11 - q) * 16) for q in range(11 if last else YS, 11)]
+        if cuts:
+            act(v("W2"), v("BS0", 0, L, 16), bias=PO)
+            for q, o, n in cuts:
+                act(v("EQ", o, o + n), v("k5", L - n, L), AF.Abs, v("W2", q, q + 1), -1.0)
+            act(v("EQ", cuts[0][1], 1056), v("EQ", cuts[0][1], 1056), AF.Relu, 1.0, -1.0)
+            for q, o, n in cuts:
+                mm(v("k6", L - n, L), v("ONESK"), v("EQ", o, o + n), False, False)
+            joined(len(cuts))
+        for q in range(10 - len(cuts), 3 if last else -1, -1):
+            o, n = 1056 * (lo // L) + sum((11 - j) * 16 for j in range(q)), (11 - q) * 16
             ts(v("EQ", o, o + n), v("YR", lo + L - n, lo + L), PO, sub, v("BS0", lo + 16 * q, lo + 16 * q + 1), eq)
-            mm(v("k6", L - n, L), v("ONESK"), v("EQ", o, o + n), False, last and q == 10 and not wide)
-        parts = [x for x in (cuts[:min(wide, 2)], cuts[2:min(wide, 5)], cuts[5:wide]) if x]
-        for part in parts:
-            for q, o, n in part:
-                act(v("EQ", o, o + n), v("YW", lo + L - n, lo + L), AF.Abs, v("BS0", lo + 16 * q, lo + 16 * q + 1), -1.0)
-            a, b = part[0][1], part[-1][1] + part[-1][2]
-            act(v("EQ", a, b), v("EQ", a, b), AF.Relu, 1.0, -1.0)
-            for q, o, n in part:
-                mm(v("k6", L - n, L), v("ONESK"), v("EQ", o, o + n), False, last and q == wide - 1)
-            joined(len(part))
+            mm(v("k6", L - n, L), v("ONESK"), v("EQ", o, o + n), False, last and q == 4)
+
+    def lowest(x):
+        k, cuts = BANK["A0"][0], ((0, 64), (64, 112), (112, 144), (144, 160))
+        mm(v(k, 192, 352), v("IDK"), v("LOW"), True, False)
+        for q, (a, b) in enumerate(cuts):
+            mm(v(k, 192 + a, 192 + b), v("PICK", 128 * 15, 128 * 16), v("RTA0", 16 * q, 64), False, q == 3)
+        joined(5)
+        for q, (a, b) in enumerate(cuts):
+            o = 1056 + 128 * q
+            ts(v("EQ", o, o + 128), v("YR", L + 64, 2 * L), v(k, q, q + 1), eq)
+            mm(v("k6", 64, L), v("ONESK"), v("EQ", o, o + 128), False, False)
+            ts(v("EL", a, b), v(k, 192 + a, 192 + b), v(k, q, q + 1), eq)
+            mm(v("k6", 16 * q, 64), v("ONESK"), v("EL", a, b), False, False)
 
     def early(t):
         yp, sons = v("BS0", 0, L, 16), v("k4", 32, 44)
@@ -897,54 +1283,59 @@ def rank_program(g, core, T, topo):
         for r in range(16):
             mm(v("k5", r, L, 16), v("PICK", 128 * r, 128 * (r + 1)), v("YP"), False, r == 15)
         joined(17)
-        tc(v("YR", 16 * YS[t] + 16, L), v("k5", 16 * YS[t] + 16, L))
-        if YS[t]:
-            act(v("YW", 0, L), YROW, bias=-PO)
-        ts(v("YL"), v("YP"), PO, add)
-        act(v("SY"), at(v("SN", 0, WT), v("YL")))
-        act(v("AY"), v("SY"), AF.Abs, -float(M))
-        act(v("EMY"), v("AY"), AF.Sign)
-        if t == 3:
-            mm(v("k5", L, 2 * L), v("ONESB"), v("AY"), True, True)
-            act(v("NFR"), v("k5", L, 2 * L), AF.Relu, 1.0, -1.0)
+        tc(v("YR", 16, L), v("k5", 16, L))
+        if t < 3:
+            if ONV["SY"]:
+                whole(v("SY"), at(v("SN", 0, WT), v("YL")))
+            else:
+                act(v("SYR"), at(v("SN", 0, WT), v("YL")), bias=ROUND)
+                act(v("SY"), v("SYR"), bias=-ROUND)
+            act(v("EMY"), v("SY"), AF.Sign, E - 0.5, -1.0)
+        else:
+            barren(v("EMY"), at(v("SN", 0, WT), v("YL")), v("k5", L, 2 * L))
+            under(v("NFR"), v("k5", L, 2 * L), -15.5, AF.Relu, -15.0)
         mm(CNT, v("ONESK"), v("NFR"), True, False)
         if t < 3:
-            mm(CNT, v("NIDB"), v("OH"), False, False)
-        sixteen(sons, "SEL", "EMY", 0, L)
-        ts(v("NS"), sons, 1.5 * SELW, gt, -KS, mul)
-        tt(v("NS"), v("NS"), v("TRP"), add)
+            mm(CNT, v("NLR", p=(0, 1)), v("ONES", 0, L, p=(0, 1)), False, False)
+            mm(CNT, v("IDL"), v("NOH"), False, False)
+        else:
+            mm(CNT, v("IDK"), v("OFFD"), False, False)
+        if ONV["NS"]:
+            if t < 3:
+                mm(v("k5", L, 2 * L), v("ONESB"), v("EMY"), True, True)
+            ts(v("NS"), listed("PR", v("k5", L, 2 * L)), up(-13.0), gt, -KS, mul)
+        else:
+            sixteen(sons, "SEL", "EMY", 0, L)
+            ts(v("NS"), sons, -13 * SELW, gt, -KS, mul)
+        tt(v("NS"), v("NS"), v("TRP" if t < 3 else "TR"), add)
         if t < 3:
             tt(v("Z5", 36, 48), yp, v("NS"), OP.max)
-        alike(0, YROW, YS[t], False)
+        inside(0, L, YROW)
+        alike(0, False)
 
     def adopt(t):
         sp, L4 = v("BS0", L, 384, 16), "L4%d" % (t % 2)
-        ts(v("SL"), sp, PO, add)
-        alike(L, SROW, SS[t], True)
-        if t < 3:
-            scan(v("GG"), v("NOH"), CNT, mul, OP.min)
-            tt(v("OK"), at(v("GG"), v("IDX")), v("AB" if t else "AA"), gt)
-        act(v("XS"), at(v("X"), v("SL")))
-        XG = v("k0", 0, L)
-        mm(XG, v("QRT", p=(0, 1)), v("ONES", 0, L, p=(0, 1)), True, False)
-        mm(XG, v("IDHALF"), v("me%d" % t, 0, L), False, False)
-        mm(XG, v("IDHALF"), v("XS"), False, True)
-        act(v("XJ"), XG, bias=ROUND)
-        act(v("XJB"), v("XJ"), bias=-ROUND)
+        alike(L, True)
+        if t == 3:
+            scan(v("ZT"), v("TOP"), CNT, OP.max, OP.min)
+            tc(v(L4, 0, 12), v("ZT", 15, L, 16))
+            tt(v("Z4", 0, 12), v("ZT", 15, L, 16), v("NS"), OP.max)
+            tc(v(L4, 12, 24), v("Z4", 0, 12))
+            return
+        scan(v("GG", 1, L + 1), v("NOH"), CNT, mul, OP.min)
+        tt(v("OK"), at(v("GG", 0, L + 1), v("IDX")), v("AB" if t else "AA"), gt)
         tt(v("Z5", 12, 24), sp, v("NS"), OP.max)
-        if t < 3:
-            tt(v("EQS"), v("SY"), SROW, eq)
-            mm(v("k7", 0, L), v("KS1", p=(0, 1)), v("ONES", 0, L, p=(0, 1)), True, False)
-            mm(v("k7", 0, L), v("FST"), v("EQS"), False, True)
-            tt(v("VT"), v("SY"), v("k7", 0, L), OP.min)
-            act(v("MS"), v("k7", 0, L), AF.Relu, float(M), -1.0)
-            act(v("VH"), SROW, AF.Identity, v("E0"), v("M0"))
+        tt(v("EQS"), v("SY"), SROW, eq)
+        mm(v("k7", 0, L), v("EKS", p=(0, 1)), v("ONR", 0, L, p=(0, 1)), True, False)
+        mm(v("k7", 0, L), v("FST"), v("EQS"), False, True)
+        tt(v("VT"), v("SY"), v("k7", 0, L), OP.max)
+        act(v("VH"), SROW, AF.Identity, v("E0"), v("M0"))
         tt(v("FR"), v("DT"), CNT, OP.min)
-        spare = listed("FRS", v("FR"))
-        n = 4 if t < 3 else 2
-        for j in range(n):
+        scan(v("FRS"), v("RS0", 0, L), v("FR"), mul, add)
+        spare = v("FRS", 15, L, 16)
+        for j in range(4):
             tt(v("Z4", 12 * j, 12 * j + 12), v("Z5", 12 * j, 12 * j + 12) if j else sp, spare, OP.max)
-        ts(v(L4, 0, 12 * n), v("Z4", 0, 12 * n), PO, add)
+        ts(v(L4), v("Z4"), PO, add)
 
     def sending(t):
         ms, hr = "ms%d" % t, "HR%d" % t
@@ -955,60 +1346,62 @@ def rank_program(g, core, T, topo):
         ship("s", t, v(ms))
         act(v(hr), at(v("H%d" % (t % 2)), v(ms)))
         if t < 2:
-            tt(v("TMH"), v(hr), v("k3", 0, S), mul)
-            hw = listed("HW", v("TMH"))
-            ts(v("RZ"), hw, float(M), eq)
-            tt(v("RZ"), v("RZ"), v("TR", 0, 4), mul)
-            tt(v("RZ"), v("RZ"), hw, OP.max)
+            hw = listed("HW", v(hr))
+            ts(v("RZ"), hw, up(E), eq, KS, mul)
+            tt(v("RZ"), v("RZ"), hw, add)
+            ts(v("RZ"), v("RZ"), up(0.0), sub)
+            tt(v("RZ"), v("RZ"), v("TR", 0, 4), OP.min)
             tc(v("HT%d" % t), v("RZ"))
+        else:
+            act(v("SGB", 0, S), v(hr), AF.Sign, A - 0.5, -1.0)
+            unwound(0, S, v("k2", 64, 64 + S))
+            act(v("HRM"), v(hr), bias=W / 2 - A)
+            tt(v(hr), v("HRM"), v("k2", 64, 64 + S), add)
         if t == 0:
-            act(v("GN", 1760, 1760 + S), at(v("mg0"), v(ms)), AF.Identity, 1.0)
+            act(v("GN", NEW, NEW + S), at(v("mg0"), v(ms)), AF.Identity, 1.0)
 
     def returned(t):
-        a = 1760 + S * (t - 1)
-        if t == 3:
-            ts(v("lf3"), v("lr3"), 256.0, lt)
-        else:
+        if t < 3:
             fd = v("lf%d" % t)
             tc(at(v("RM"), v("HT%d" % (t - 1))), fd)
-            tt(v("TMR"), fd, v("k3", 0, S), mul)
-            come = listed("RWR", v("TMR"))
-            sixteen(v("k5", 384, 384 + NB), "SEL", "RM", 0, W, 4)
+            come = listed("RWR", fd)
+            sixteen(v("k5", 384, 384 + NB), "SEL", "RM", NEW, WP, 4)
             tt(v("RVD"), fd, v("CT3", S * (t - 1), S * t), mul)
-            x = TURN * (t + 1)
-            act(v("AA", a // 16 - x, a // 16 - x + 4), come, scale=-2.0)
+            x = TURN * (t + 1) + (A - NEW) // 16
+            a = NB - x + S * (t - 1) // 16
+            act(v("AA", a, a + 4), come, AF.Identity, up(0.0, 256.0), -256.0)
             tt(v("AB", 0, NB - x), v("AA", 0, NB - x), v("k5", 384 + x, 384 + NB), add)
             tt(v("AB", NB - x, NB), v("AA", NB - x, NB), v("k5", 384, 384 + x), add)
 
     def changes(t):
-        wide, H, L4 = W + 2 * L, v("H%d" % (t % 2), 0, L), "L4%d" % (t % 2)
+        H, L4, tab = v("H%d" % (t % 2), 0, L), "L4%d" % (t % 2), v("SN", 0, WT)
+        tc(at(v("X"), v(L4, 0, 12)), v("XJB"))
         if t:
-            lr, a, hr, fd = v("lr%d" % t), 1760 + S * (t - 1), v("HR%d" % (t - 1)), v("lf%d" % t)
+            lr, a, hr, fd = v("lr%d" % t), NEW + S * (t - 1), v("HR%d" % (t - 1)), v("lf%d" % t)
             if t < 3:
-                tt(v("X", a, a + S), lr, fd, mul)
-                tt(v("F1", a, a + S), hr, fd, mul)
-                tt(v("F2", a, a + S), hr, fd, mul)
+                act(v("X", a, a + S), lr, on="v")
+                act(v("HRM"), hr, bias=-float(A))
+                tt(v("RVF"), v("HRM"), fd, mul)
+                for f in ("F1", "F2"):
+                    act(v(f, a, a + S), v("RVF"), bias=float(A))
             else:
-                tt(v("XN"), lr, fd, mul)
+                a = W - S
                 tt(v("RVB"), hr, fd, mul)
-                dma("y", ("xo", a, W, T.xo[:, a:W]), v("XN"), 2.5)
                 dma("y", ("fo", a, W, T.fo[:, a:W]), v("RVB", p=(0, 128, 16)), 2.2)
                 dma("y", ("f2o", a, W, T.f2o[:, a:W]), v("RVB", p=(0, 128, 16)), 2.2)
-        if t == 3:
-            for f in ("X", "F1", "F2"):
-                fill(v(f, M, 1760), 0.0)
-        tc(at(v("X", 0, wide), v(L4, 0, 12)), v("XJB"))
-        tc(at(v("F2"), v(L4, 0, 12)), H)
-        tc(at(v("F1"), v(L4, 12, 24)), H)
+                dma("s", ("xo", a, W, T.xo[:, a:W]), lr, 2.5)
+        put = lambda n: tc if t == 3 else lambda out, in_: act(out, in_, on="v" if ONV[n] else "s")
+        put("F2")(at(v("F2"), v(L4, 0, 12)), H)
+        put("F1")(at(v("F1"), v(L4, 12, 24)), H)
         if t < 3:
-            tc(at(v("SN", 0, wide), v(L4, 24, 36)), v("VH"))
-            tt(at(v("SN", 0, wide), v(L4, 36, 48)), v("VT"), v("MS"), add)
+            put("SNH")(at(tab, v(L4, 24, 36)), v("VH"))
+            put("SNY")(at(tab, v(L4, 36, 48)), v("VT"))
         if 0 < t < 3:
-            act(v("RVB"), at(v("SN", 0, wide), v("HT%d" % (t - 1))))
-            tt(at(v("SN", 0, wide), v("HT%d" % (t - 1))), v("RVB"), v("RVD"), add)
+            act(v("RVB"), at(tab, v("HT%d" % (t - 1))))
+            tt(at(tab, v("HT%d" % (t - 1))), v("RVB"), v("RVD"), add)
 
     for t in range(T_):
-        NV.update(zip(PARTS, NVT[t]))
+        NV.update(zip(PARTS, NVT[t]), t=t)
         lanes(t)
         if t:
             arrivals(t)
@@ -1017,15 +1410,15 @@ def rank_program(g, core, T, topo):
             returned(t)
         adopt(t)
         changes(t)
-    a = W - S
-    dma("y", ("xo", 0, a, T.xo[:, 0:a]), v("X", 0, a), 4.0)
-    dma("s", ("fo", 0, a, T.fo[:, 0:a]), v("F1", 0, a, p=(0, 128, 16)), 2.5)
-    dma("s", ("f2o", 0, a, T.f2o[:, 0:a]), v("F2", 0, a, p=(0, 128, 16)), 2.5)
+    for a, b, c in ((0, M, A), (M + 16, W - S, NEW)):
+        dma("y", ("xo", a, b, T.xo[:, a:b]), v("X", c, c + b - a), 2.5 if a else 4.0)
+        dma("s", ("f2o", a, b, T.f2o[:, a:b]), v("F2", c, c + b - a, p=(0, 128, 16)), 2.5)
+        dma("s", ("fo", a, b, T.fo[:, a:b]), v("F1", c, c + b - a, p=(0, 128, 16)), 2.5)
 
     if not ORDER:
-        ORDER.extend(plan(ops))
+        ORDER.extend(sorted(plan(ops), key=lambda i: ops[i][3][:1] == [("lr3", 0, S)]))
     for i in ORDER:
-        issue(*ops[i])
-    for sem in sorted(total):
+        issue(*(other[i] if i in SWAP else ops[i]))
+    total["lo"] = sent[0]
+    for sem in sorted(total, key=lambda x: int(x[1:]) if x[0] == "d" else -1):
         g.wait_ge(T.sem[sem], total[sem])
-    g.wait_ge(T.sem.lo, sent[0])

from concourse.mybir import AluOpType as OP, ActivationFunctionType as AF

M, W, L, S, T_, Q = 1744, 1952, 192, 64, 4, 560
NB = W // 16
RW = M // 16
NEW = 32
A = NEW + W - M - 16
E = A + M
WP = NEW + W
NOB, NOS = 8, 16
TB = WP
WT = TB + 2 * L
BK = WT
IDB = WT
WI = IDB + WP
BIG = 512.0
KS = 8192.0
PO = 2040.0
ROUND = 1.5 * 2 ** 23
RAISE = 2.0 ** 17
LW = L + 16
NVT = (((40,) * 3, (40,) * 3, (40,) * 3, (0,)),) + (((42, 40, 38),) * 3 + ((42, 40, 40, 40),),) * 3
BANK = {"A0": ("k0",), "A1": ("k1",), "A2": ("k7",), "AB": ("k2", "k4")}
CH = ((128, 192), (0, 128))
SLOW = ("A0",)
PTURN = ()
TBANK = ""
ONV = {"PR": 1, "QR": 1, "S0": 0, "SY": 0, "XJ": 0, "F1": 0, "F2": 0, "SNH": 0, "SNY": 1, "KP": 1, "XG": 1, "UR": 1, "NS": 1}
YS, SEED, MORE, XB, TRUE = 11, 1, 170, 0, 1
LOWS = ()
BARKEY = ()
EARLYC = 0
AHEAD = 0
SENDFIRST = ()
PLAIN = ()
PV = 8


def HALVES(n):
    return ((0, 14), (14, 28), (28, n))


TURN = Q // 16
PARTS = ("A0", "A1", "A2", "AB")

SCRATCH = {}
PLACE = {}
HALF = set()
LISTS = set()
BANKS = set("k%d" % i for i in range(8))
POOL = {"float32": ["poolf", 0], "float16": ["poole", 0], "bfloat16": ["poolh", 0], "int32": ["pooli", 0], "uint16": ["poolu", 0]}
ORDER = []
EITHER, SWAP = {}, set()


def _b(kind, dtype, **kw):
    for n, w in kw.items():
        if dtype in ("bfloat16", "uint16", "float16"):
            HALF.add(n)
        if dtype == "uint16":
            LISTS.add(n)
        if kind == "psum" or n[:2] in ("me", "be", "le", "ms", "bs", "ls", "mr", "br", "lr", "mf", "bf", "lf", "mg", "bg", "lg"):
            SCRATCH[n] = (kind, [128, w], dtype)
        else:
            p = POOL[dtype]
            PLACE[n] = (p[0], p[1], w)
            p[1] += (w + 15) // 16 * 16
            SCRATCH[p[0]] = (kind, [128, p[1]], dtype)


_b("sbuf", "float32", SN=WI, F1=WT, F2=WT, H0=LW, H1=LW, S0=L, UD=L, SA=L, RMOD=384, DIAG=L, D15=L, DT=L, OF=128, I3=384,
   R16=1, PBF=2, M0=1, E0=1, MK=16, TR=12, TRP=12, LANB=12, LANE=L, CT0=128, CT3=128, ZER=128, CB=128, CT=128, NBS=12,
   W1=12, W2=12, NS=12, BS0=384, SCB=384,
   Z4=48, Z5=48, SY=L, SYR=L, VT=L, VH=L, RZ=4, RVB=S, RVD=S, RVF=S, HRM=S, CAP=L, TOP=L, UP=16, PR=L, QR=L, RWH=L, RWP=L, RWQ=L, RT=12,
   RWC=S, CRW=S, RWG=S, RWR=S, HW=S, RWI=128, R2=128, ZT=L, CF=256, CR=256, NR16=1, NR17=1, NLS=4, CTS=128, AA=128, AB=128, XJ=L)
for _n in PARTS:
    _b("sbuf", "float32", **{"MM" + _n: 64, "DD" + _n: 64, "EE" + _n: 64, "SF" + _n: 64})
    _b("sbuf", "float16", **{"RR" + _n: 64, "RT" + _n: 64, "SH" + _n: 64})
    _b("sbuf", "bfloat16", **{"XT" + _n: 128, "XR" + _n: 1024, "UU" + _n: 1024})
    _b("sbuf", "uint16", **{"IX" + _n: 64})
_b("sbuf", "uint16", LLAB=4, LL0=12, LL1=12)
_b("sbuf", "float16", SAH=L, PH=L, S1=L, YR=384, FAS=RW, RRS=RW, YP=12, POR=128, EKS=128, ONR=384, FR=L, FRS=L)
_b("sbuf", "bfloat16", X=WT, GN=WP, RM=WP + 2 * S, ANE=M, SWH=512, PICK=2048, GN1=M, GNS=RW, NU=12, CA=12, LIFB=12, SEL=144, SELD=144, WONE=128, REP=1024, ONES=256, ONESB=128, NONESB=128, ONESK=128, NONESK=128,
   TRI=128, TIMO=128, SLR=128, ZEH=L, JL=4 * L, XJB=L, XS=L, IDB=128, NIDB=128, IDK=128, IDW=128, FST=128, RUP=128, RDN=128, ID16=128, IDHALF=128, QRT=128, TMPB=128,
   WC=1, RS0=384, OK=128, NOH=L, GG=LW, CUM=L, JK=12 * 128, BT=512, FLG=L, BR=L, EQ0=L, EQ1=L, SG0=L, UR=L, ED=384, EQ=2112, NFR=L,
   EMY=L, EQS=L, XN=S, SGB=256, OFFD=L, LOW=160, EL=160, SELN=144, UN=1024, IDL=128, NLR=128, PEN=128)
_b("sbuf", "int32", SNI=M, FAI=RW, GNI=RW, PI=1, PI2=1, CI=LW, CI2=LW)
_b("sbuf", "uint16", BL=12, HL=12, IDX=8, P0L=12, P1L=12, SA16=L, YL=12, SL=12, L40=48, L41=48, BF16=4)
_b("psum", "float32", k0=512, k1=512, k2=512, k3=512, k4=512, k5=512, k6=512, k7=512)
for _t in range(3):
    _b("sbuf", "uint16", **{"ms%d" % _t: 4, "bs%d" % _t: 4, "ls%d" % _t: 4})
    _w = 2 * LW if _t else LW
    _b("sbuf", "bfloat16", **{"me%d" % _t: _w, "be%d" % _t: _w, "le%d" % _t: _w, "mr%d" % (_t + 1): S, "br%d" % (_t + 1): S, "lr%d" % (_t + 1): S})
    _b("sbuf", "float32", **{"HR%d" % _t: S})
    _b("sbuf", "uint16", **{"HT%d" % _t: 4})

_b("sbuf", "bfloat16", me3=LW, AX=2 * S, AYI=L, AYB=S, mf1=S, bf1=S, lf1=S, mf2=S, bf2=S, lf2=S, mf3=S, bf3=S, lf3=S, mg0=LW, bg0=LW, lg0=LW)
MSGS = [("e", 0), ("g", 0), ("s", 0), ("e", 1), ("f", 1), ("r", 1), ("s", 1), ("e", 2), ("f", 2), ("s", 2), ("r", 2), ("f", 3), ("r", 3)]
SEMAPHORES = ["qv", "qs", "qt", "qg", "lo"] + ["d%d" % i for i in range(40)] + ["x%s%d" % m for m in MSGS] + ["a%s%d" % m for m in MSGS]


def goal(T, rank, kind, t):
    return T.cores[(rank + 1 + t) % 4] if kind in "egs" else T.cores[(rank - t) % 4]


def ages(side, t, n=LW):
    return (side + "e%d" % t, LW, LW + n) if t else (side + "g0", 0, n)


def via(topo, src, dst):
    if topo.may_write(src, dst):
        return None
    c = [k for k in topo.cores_of(src) if k != src and topo.may_write(k, dst)]
    near = [k for k in c if topo.die(k) == topo.die(src)]
    return (near + c)[0]


def engines(topo, src, dst, k):
    e = topo.engines(src, dst)
    if k in ("e0", "g0") and dst in topo.cores_of(src):
        return e[:len(e) // 2] if k == "e0" else e[len(e) // 2:]
    return e


def send(g, topo, src, dst, k, out, in_, rsem, lsem):
    rid, pid = topo.addr(dst, src)
    e = engines(topo, src, dst, k)
    g.remote_dma(out, in_, rsem, lsem, pid, rid, sum(1 << x for x in e))
    return len(e)


def hand_on(g, core, T, topo):
    n = 0
    for kind, t in MSGS:
        for r in range(len(T.cores)):
            dst = goal(T, r, kind, t)
            if via(topo, T.cores[r], dst) == core:
                k = "%s%d" % (kind, t)
                g.wait_ge(T.sem["x" + k], len(engines(topo, T.cores[r], core, k)))
                n += send(g, topo, core, dst, k, T["l" + k][:], T["b" + k][:], T.sem["a" + k], T.sem.lo)
    if n:
        g.wait_ge(T.sem.lo, n)


HOP, CY, GA, SC = 0.34, 0.001, 1.56, 3.8


FAR = {"e0": 28.0, "g0": 16.0, "e1": 20.0, "e2": 20.0, "s0": 8.0, "r1": 8.0, "s1": 4.5, "r2": 4.5, "s2": 8.0, "r3": 8.0, "f1": 8.0, "f2": 4.5, "f3": 9.0}
LEAD = {"A0": 0.1, "A1": 2.0, "A2": 4.0, "AB": 2.1}
ROWS = ("FLG", "BR", "H0", "H1", "RWH", "PH", "SAH", "QR", "RWP", "RWQ", "EQ0", "S0", "SG0", "UR", "S1", "EQ1", "UD", "SA", "SA16")


def lead(x):
    nm, lo, hi = x
    if nm[-2:] in LEAD:
        return LEAD[nm[-2:]]
    if nm in ROWS or nm[:2] == "me" and lo < L:
        return LEAD[PARTS[lo // 64]]
    if nm in ("BL", "HL", "P0L", "P1L", "NBS"):
        return LEAD[PARTS[lo // 4]]
    for p in PARTS:
        if nm == BANK[p][0]:
            return LEAD[p]
    return 0.0


PASSES, SHAKE = 600, 0.3
SPARE = 0.0
PE = 0.65
OWN = 0.34
ENDS = []


def plan(ops):
    n = len(ops)
    pred = [set() for _ in ops]
    wr, rd, tlast = {}, {}, {}
    for i, (e, kind, call, reads, writes, us, dur, listed) in enumerate(ops):
        for nm, lo, hi in reads + writes:
            pred[i].update(j for lo2, hi2, j in wr.get(nm, ()) if lo < hi2 and lo2 < hi)
        for nm, lo, hi in writes:
            pred[i].update(j for lo2, hi2, j in rd.get(nm, ()) if lo < hi2 and lo2 < hi)
        if e == "t":
            nm = writes[0][0]
            shut, whole, inside = tlast.get(nm, ([], [], []))
            if kind[1:] == "[]":
                pred[i].update(shut)
                tlast[nm] = (shut, whole + [i], [])
            elif kind[1:] == "[":
                pred[i].update(shut + whole)
                tlast[nm] = ([], [], [i])
            elif kind[1:] == "]":
                pred[i].update(inside)
                tlast[nm] = ([i], [], [])
            else:
                pred[i].add(inside[0])
                inside.append(i)
            if kind[1:] in ("", "]"):
                pred[i].difference_update(inside[1:-1] if kind[1:] == "" else ())
        for nm, lo, hi in writes:
            wr[nm] = [x for x in wr.get(nm, ()) if not (lo <= x[0] and x[1] <= hi)] + [(lo, hi, i)]
            rd[nm] = [x for x in rd.get(nm, ()) if not (lo <= x[0] and x[1] <= hi)]
        for nm, lo, hi in reads:
            rd.setdefault(nm, []).append((lo, hi, i))
        pred[i].discard(i)
    succ = [[] for _ in ops]
    for i in range(n):
        for j in pred[i]:
            succ[j].append(i)

    def hop(a, b):
        return 0.0 if ops[a][0] == ops[b][0] == "t" else OWN if ops[a][0] == ops[b][0] else HOP
    banks = [set(x[0] for x in o[3] + o[4] if x[0] in BANKS) for o in ops]

    uses = [[(ops[i][0], 0.0)] + [(b, HOP) for b in sorted(banks[i])] for i in range(n)]
    dur = [o[6] for o in ops]
    lag = [[[(j, dur[j] + hop(i, j)) for j in sorted(x[i])] for i in range(n)] for x in (pred, succ)]
    far = [i for i in range(n) if ops[i][1] == "r" and ops[i][4][0][0][:2] not in ("le", "lg") and ops[i][4][0][0][2] != "3"]

    def stretch(i, d):
        dur[i] += d
        for x, y in ((0, succ), (1, pred)):
            for j in y[i]:
                lag[x][j] = [(k, t + d if k == i else t) for k, t in lag[x][j]]

    what = [(o[0], o[5], uses[i], len(uses[i]) > 1) for i, o in enumerate(ops)]

    def place(seq, before, back):
        at, gaps = [0.0] * n, lag[back]
        busy = {r: [(-9.0, -9.0, "")] for r in list("vstgy") + list(BANKS)}
        for i in seq:
            e, us, use, many = what[i]
            s = 0.0
            for j, d in gaps[i]:
                d += at[j]
                if d > s:
                    s = d
            off = dur[i] - us if back else 0.0
            s += off
            if not many:
                l = busy[e]
                k = len(l)
                while l[k - 1][1] > s + 1e-9:
                    k -= 1
                m = len(l)
                while k < m and l[k][0] < s + us:
                    s = l[k][1]
                    k += 1
                l.insert(k, (s, s + us, e))
                at[i] = s - off
                continue
            moved = True
            while moved:
                moved = False
                for r, pad in use:
                    l = busy[r]
                    k = m = len(l)
                    lim = s + 1e-9 - pad
                    while l[k - 1][1] > lim:
                        k -= 1
                    while k < m:
                        x, y, e2 = l[k]
                        if x >= s + us + pad:
                            break
                        if (not pad or e2 != e) and y + pad > s + 1e-9:
                            s = y + pad
                            moved = True
                        k += 1
            at[i] = s - off
            for r, pad in use:
                l = busy[r]
                k = len(l)
                while l[k - 1][0] > s:
                    k -= 1
                l.insert(k, (s, s + us, e))
        return at

    def sorted_by(key, before, order):
        key = list(key)
        for i in order:
            for j in before[i]:
                if key[j] >= key[i]:
                    key[i] = key[j] + 1e-7
        return sorted(order, key=lambda i: key[i])
    up, down = range(n), range(n - 1, -1, -1)
    rest = [0.0] * n
    for i in range(n - 1, -1, -1):
        rest[i] = ops[i][6] + max([hop(i, j) + rest[j] for j in succ[i]], default=0.0)
    part = [max(lead(x) for x in ops[i][4]) for i in range(n)]
    key = [-rest[i] - part[i] for i in range(n)]
    best = None
    ENDS.append(round(max(rest), 1))
    dice = [SEED]

    def die():
        dice[0] = (dice[0] * 1103515245 + 12345) % 2 ** 31
        return dice[0] / 2 ** 31
    marks = [i for i in range(n) if ops[i][4][0][0] == "OK"][2:]

    def packed(key, again):
        if again:
            at = place(sorted_by(key, pred, up), pred, False)
            bk = place(sorted(up, key=lambda i: -at[i] - dur[i]), succ, True)
        else:
            bk = place(sorted_by([-key[i] - dur[i] for i in up], succ, down), succ, True)
        at = place(sorted(up, key=lambda i: -bk[i] - dur[i]), pred, False)
        if not TRUE:
            return max(at[i] + dur[i] for i in up), at, [at[i] for i in marks]
        seq = sorted(up, key=lambda i: at[i])
        for run in play[2]:
            play[3](run, seq, [0.0] * 5, [(-1, 0.0)] * 8)
        k = len(play[2])
        return sum(max(run[5][i] + run[1][i] for i in ends) for run in play[2]) / k, at, [sum(run[5][i] for run in play[2]) / k for i in marks]
    play = player(ops, pred, succ)
    ends = [i for i in up if not succ[i]]
    for k in range(3):
        best = packed(key, True)
        key = best[1]
    for k in range(PASSES):
        if k % 16 == 7 and 3 * k > PASSES:
            late = far[k // 16 % len(far)]
            stretch(late, 1.0)
            got = packed(best[1], True)
            if got[0] <= best[0] + SPARE:
                best = got
            else:
                stretch(late, -1.0)
            continue
        cut = [0.0] + [best[1][i] for i in marks] + [max(best[1]) + 3.0]
        rnd = [sum(t >= c for c in cut[1:-1]) for t in best[1]]
        spot = [(a + die() * (b - a), 4 + 22 * die()) for a, b in zip(cut, cut[1:])]
        if k % 2:
            move = [{x: 4 * SHAKE * (2 * die() - 1) for x in sorted(set(part))} for c in spot]
            key = [t + (move[rnd[i]][part[i]] + 0.1 * die() if abs(t - spot[rnd[i]][0]) < spot[rnd[i]][1] else 0.0) for i, t in enumerate(best[1])]
        else:
            key = [t + (SHAKE * (2 * die() - 1) if abs(t - spot[rnd[i]][0]) < spot[rnd[i]][1] else 0.0) for i, t in enumerate(best[1])]
        got = packed(key, k % 3 == 0)
        if got[0] <= best[0] + 0.4 * (1 - k / PASSES) * die():
            best = got
            continue
        new, old = [0.0] + got[2] + [got[0]], [0.0] + best[2] + [best[0]]
        won = [new[r + 1] - new[r] < old[r + 1] - old[r] - 0.05 for r in range(len(spot))]
        new = [0.0] + [got[1][i] for i in marks]
        if any(won):
            key = [got[1][i] - new[rnd[i]] + cut[rnd[i]] if won[rnd[i]] else t for i, t in enumerate(best[1])]
            got = packed(key, False)
            if got[0] <= best[0] + 0.02 + 0.4 * (1 - k / PASSES) * die():
                best = got
    ENDS.append(round(best[0], 1))
    ENDS.append([dur[i] for i in far])
    ENDS.append(best[1])
    loads = [i for i in range(n) if ops[i][1] == "o"]
    return polish(ops, pred, succ, loads + [i for i in sorted_by(best[1], pred, up) if ops[i][1] != "o"], len(loads), die, play)


PACES = ((1.0, 1.0, 0.9, 0.34, 1.1), (1.15, 1.15, 0.9, 0.28, 1.25))
SWEEPS, SPAN, TRIES, HEAT, BIAS, SOFT = 50, 44, 56, 0.1, 1, 0.04


def player(ops, pred, succ):
    n = len(ops)
    qu = ["vstgy".index(o[0]) for o in ops]
    bk = [sorted(set(int(x[0][1]) for x in o[3] + o[4] if x[0] in BANKS)) for o in ops]
    runs = []
    for c, ga, pe, hop, far in PACES:
        us = [o[5] * (c * pe if o[0] == "t" else c * ga if o[7] else c) if o[1][0] == "c" else o[5] for o in ops]
        dur = [us[i] if o[1][0] == "c" else o[6] * (far if o[1] == "r" else 1.0) for i, o in enumerate(ops)]
        before = [[(j, dur[j] + (0.0 if qu[i] == qu[j] == 2 else hop)) for j in pred[i]] for i in range(n)]
        after = [[(j, dur[i] + (0.0 if qu[i] == qu[j] == 2 else hop)) for j in succ[i]] for i in range(n)]
        runs.append((us, dur, before, after, hop, [0.0] * n, [0.0] * n))

    def forward(run, part, free, held):
        us, dur, before, after, hop, at, rest = run
        for i in part:
            q = qu[i]
            s = free[q]
            for j, d in before[i]:
                d += at[j]
                if d > s:
                    s = d
            b = bk[i]
            if b:
                for k in b:
                    who, d = held[k]
                    if who != q and d > s:
                        s = d
                d = s + us[i] + hop
                for k in b:
                    held[k] = (q, d)
            at[i] = s
            free[q] = s + us[i]
    return qu, bk, runs, forward


def polish(ops, pred, succ, seq, fixed, die, play):
    n = len(ops)
    qu, bk, runs, forward = play
    spare = [{i: x * run[0][i] / ops[i][5] for i, x in EITHER.items()} for run in runs]

    def turned(i):
        qu[i] = 1 - qu[i]
        for run, x in zip(runs, spare):
            run[0][i], x[i] = x[i], run[0][i]

    def backward(run):
        us, dur, before, after, hop, at, rest = run
        nq, nb = [-1] * 5, [-1] * 8
        for i in reversed(seq):
            r = dur[i]
            for j, d in after[i]:
                d += rest[j]
                if d > r:
                    r = d
            q = qu[i]
            if nq[q] >= 0 and us[i] + rest[nq[q]] > r:
                r = us[i] + rest[nq[q]]
            nq[q] = i
            for k in bk[i]:
                j = nb[k]
                if j >= 0 and qu[j] != q and us[i] + hop + rest[j] > r:
                    r = us[i] + hop + rest[j]
                nb[k] = i
            rest[i] = r
    best = None
    for sweep in range(SWEEPS + MORE + 1):
        for run in runs:
            forward(run, seq, [0.0] * 5, [(-1, 0.0)] * 8)
        length = sum(max(run[5][i] + run[1][i] for i in seq) for run in runs)
        if best is None or length < best[0]:
            best = (length, list(seq), list(qu))
        if sweep == SWEEPS + MORE:
            break
        at = runs[0][5]
        seq[fixed:] = sorted(seq[fixed:], key=lambda i: at[i])
        for run in runs:
            backward(run)
        whole = [max(run[6]) for run in runs]
        heat = HEAT * (1.0 - sweep / SWEEPS if sweep < SWEEPS else 0.5 * (SWEEPS + MORE - sweep) / MORE)
        state = [([0.0] * 5, [(-1, 0.0)] * 8) for run in runs]
        a = fixed + int(die() * SPAN / 2)
        for run, (free, held) in zip(runs, state):
            forward(run, seq[:a], free, held)
        while a < n - 2:
            b = min(n, a + SPAN)
            part = seq[a:b]
            inside = set(part)
            nq, nb, left = [-1] * 5, [-1] * 8, 13
            for k in range(b, min(n, b + 400)):
                i = seq[k]
                if nq[qu[i]] < 0:
                    nq[qu[i]] = i
                for x in bk[i]:
                    if nb[x] < 0:
                        nb[x] = i
            outs = [{i: max([run[1][i]] + [d + run[6][j] for j, d in run[3][i] if j not in inside]) for i in part} for run in runs]

            marks = [[(list(free), list(held), 0.0)] for free, held in state]

            def noted(p, lo):
                for run, mark, out in zip(runs, marks, outs):
                    del mark[lo // 4 + 1:]
                    for k in range(lo // 4 * 4, len(p), 4):
                        f, h, m = mark[-1]
                        f, h = list(f), list(h)
                        forward(run, p[k:k + 4], f, h)
                        mark.append((f, h, max([m] + [run[5][i] + out[i] for i in p[k:k + 4]])))

            def worth(p, lo):
                total, tail = 0.0, p[lo // 4 * 4:]
                for run, mark, out in zip(runs, marks, outs):
                    f, h, m = mark[lo // 4]
                    f, h = list(f), list(h)
                    forward(run, tail, f, h)
                    at, rest = run[5], run[6]
                    for i in tail:
                        d = out[i] + at[i]
                        if d > m:
                            m = d
                    soft = 0.0
                    for q in range(5):
                        if nq[q] >= 0:
                            d = f[q] + rest[nq[q]]
                            if d > m:
                                m = d
                            if q < 3:
                                soft += f[q]
                    for k in range(8):
                        j = nb[k]
                        if j >= 0 and qu[j] != h[k][0] and h[k][1] + rest[j] > m:
                            m = h[k][1] + rest[j]
                    total += m + SOFT * soft
                return total
            noted(part, 0)
            now = worth(part, 0)
            kept = [{i: run[5][i] for i in part} for run in runs]
            slack = {i: min(w - run[5][i] - run[6][i] for run, w in zip(runs, whole)) for i in part}
            for k in range(TRIES):
                x, y = int(die() * len(part)), int(die() * len(part))
                step = 1 if die() < 0.5 else -1
                if BIAS and (slack[part[x]] - slack[part[y]]) * step < 0:
                    x = y
                i = part[x]
                if i in EITHER and die() < 0.3:
                    turned(i)
                    w = worth(part, x)
                    if w <= now + heat * die():
                        now = w
                        noted(part, x)
                        for run, keep in zip(runs, kept):
                            for j in part[x // 4 * 4:]:
                                keep[j] = run[5][j]
                    else:
                        turned(i)
                        for run, keep in zip(runs, kept):
                            at = run[5]
                            for j in part[x // 4 * 4:]:
                                at[j] = keep[j]
                    continue
                block = succ[i] if step > 0 else pred[i]
                y, past = x, 1 + int(die() * die() * 4)
                while past:
                    y += step
                    if y < 0 or y >= len(part) or part[y] in block:
                        break
                    if qu[part[y]] == qu[i]:
                        past -= 1
                if past:
                    continue
                p = part[:x] + part[x + 1:]
                p.insert(y, i)
                lo = min(x, y)
                w = worth(p, lo)
                if w <= now + heat * die():
                    part, now = p, w
                    noted(p, lo)
                    for run, keep in zip(runs, kept):
                        for j in p[lo // 4 * 4:]:
                            keep[j] = run[5][j]
                else:
                    for run, keep in zip(runs, kept):
                        at = run[5]
                        for j in p[lo // 4 * 4:]:
                            at[j] = keep[j]
            seq[a:b] = part
            c = a + SPAN // 2
            for run, (free, held) in zip(runs, state):
                forward(run, seq[a:c], free, held)
            a = c
    ENDS.append(round(best[0], 1))
    SWAP.update(i for i in EITHER if "vstgy"[best[2][i]] != ops[i][0])
    return best[1]


def rank_program(g, core, T, topo):
    rank = T.rank_of(core)
    if rank is None:
        hand_on(g, core, T, topo)
        return

    queue = {"v": g.vector, "s": g.scalar, "t": g.tensor, "g": g, "y": g.sync}
    count = {"qv": 0, "qs": 0, "qt": 0, "qg": 0}
    known = {e: {} for e in queue}
    clock = {}
    wr, rd = {}, {}
    dsem = [0]
    total = {}
    ops = []
    NV = {}
    landed = {}
    for kind, t in MSGS:
        src = [c for r, c in enumerate(T.cores) if goal(T, r, kind, t) == core][0]
        landed["%s%d" % (kind, t)] = len(topo.engines(via(topo, src, core) or src, core))

    def need(e, reads, writes):
        w = {}

        def want(sem, val):
            if known[e].get(sem, 0) < val and w.get(sem, 0) < val:
                w[sem] = val
        for isw, lst in ((0, reads), (1, writes)):
            for n, lo, hi in lst:
                ps = n in BANKS
                for lo2, hi2, e2, sem, val in wr.get(n, ()):
                    if ps and e2 != e or lo < hi2 and lo2 < hi:
                        if not (e == "t" and e2 == "t" and ps):
                            want(sem, val)
                if isw or ps:
                    for (e2, lo2, hi2), (sem, val) in rd.get(n, {}).items():
                        if ps and e2 != e or (isw and lo < hi2 and lo2 < hi):
                            want(sem, val)
        for sem in sorted(w):
            if known[e].get(sem, 0) >= w[sem]:
                continue
            queue[e].wait_ge(T.sem[sem], w[sem])
            known[e][sem] = w[sem]
            for s2, v2 in clock.get((sem, w[sem]), {}).items():
                if known[e].get(s2, 0) < v2:
                    known[e][s2] = v2

    def note(e, sem, val, reads, writes):
        c = dict(known[e])
        if sem[0] == "q":
            for s2, v2 in clock.get((sem, val - 1), {}).items():
                if c.get(s2, 0) < v2:
                    c[s2] = v2
        c[sem] = val
        clock[(sem, val)] = c
        total[sem] = max(total.get(sem, 0), val)
        for n, lo, hi in writes:
            wr[n] = [x for x in wr.get(n, []) if not (lo <= x[0] and x[1] <= hi)] + [(lo, hi, e, sem, val)]
            rd[n] = {k: x for k, x in rd.get(n, {}).items() if not (lo <= k[1] and k[2] <= hi)}
        for n, lo, hi in reads:
            rd.setdefault(n, {})[(e, lo, hi)] = (sem, val)

    def issue(e, kind, call, reads, writes, us, dur, listed):
        if kind == "r":
            need(e, reads, [])
            call()
            n = writes[0][0]
            wr[n] = [(0, 1 << 20, "remote", "a" + n[1:], landed[n[1:]])]
            total["a" + n[1:]] = landed[n[1:]]
            return
        need(e, reads, writes)
        if kind in "do":
            sem = "d%d" % dsem[0]
            dsem[0] += 1
            made = call()
            made = made if isinstance(made, list) else [made]
            for x in made:
                x.then_inc(T.sem[sem], 16)
            note(e, sem, 16 * len(made), reads, writes)
        else:
            sem = "q" + e
            count[sem] += 1
            call().then_inc(T.sem[sem], 1)
            note(e, sem, count[sem], reads, writes)

    def flat(xs):
        r = []
        for x in xs:
            if x is not None and not isinstance(x, (int, float)):
                r += [x[0:3]] if len(x) == 4 else [x[0][0:3], x[1][0:3]]
        return r

    def ap(x):
        return x if x is None or isinstance(x, (int, float)) else x[3] if len(x) == 4 else x[2]

    def emit(e, call, reads, writes, us, kind="c", dur=None):
        reads, writes = flat(reads), flat(writes)
        ops.append((e, kind, call, reads, writes, us, us if dur is None else dur, us > 0.14 and any(x[0] in LISTS for x in reads)))

    def joined(n):
        part = ops[-n:]
        del ops[-n:]

        def call():
            return [o[2]() for o in part][-1]
        us = sum(o[5] for o in part)
        kind = "c" + "[" * ("[" in part[0][1]) + "]" * ("]" in part[-1][1])
        ops.append((part[0][0], kind, call, sum((o[3] for o in part), []), sum((o[4] for o in part), []), us, us, False))

    def size(x):
        return x[3].shape[1] if len(x) == 4 else 16 * x[1][3].shape[1]

    def two(*xs):
        return all(len(x) == 4 and (x[0] in HALF) for x in xs)

    def dma(e, out, in_, dur, turn=None):
        emit(e, lambda: queue[e].dma_start(ap(out), ap(in_)), [in_], [out], 0.07, "o" if turn else "d", dur)

    def v(name, lo=0, hi=None, st=1, p=None):
        buf, o, w = PLACE[name] if name in PLACE else (name, 0, SCRATCH[name][1][1])
        t = T[buf]
        if hi is None:
            hi = w
        ps = slice(None) if p is None else slice(*p)
        return (name, lo, hi, t[ps, o + lo:o + hi] if st == 1 else t[ps, o + lo:o + hi:st])

    def at(win, off):
        return (win, off, win[3].indirect(off[3]))

    def vec(call, out, ins, rate):
        if len(out) == 3:
            emit("v", call, ins + [out[1]], [out[0]], 0.05 + SC * CY * size(out))
        elif len(ins[0]) == 3:
            emit("v", call, ins, [out], 0.05 + GA * CY * size(out))
        else:
            emit("v", call, ins, [out], CY * max(64, size(out) * rate))

    def tc(out, in_):
        vec(lambda: g.vector.tensor_copy(ap(out), ap(in_)), out, [in_], 0.5 if two(out, in_) else 1)

    def tt(out, a, b, op):
        vec(lambda: g.vector.tensor_tensor(ap(out), ap(a), ap(b), op), out, [a, b], 1 if a[0] in BANKS or b[0] in BANKS else 2)

    def ts(out, a, s1, op0, s2=None, op1=None):
        rate = 0.5 if two(out, a) else 1
        if op1 is None:
            vec(lambda: g.vector.tensor_scalar(ap(out), ap(a), ap(s1), None, op0), out, [a, s1], rate)
        else:
            vec(lambda: g.vector.tensor_scalar(ap(out), ap(a), ap(s1), ap(s2), op0, op1), out, [a, s1, s2], rate)

    def scan(out, d0, d1, op0, op1, init=0.0):
        vec(lambda: g.vector.tensor_tensor_scan(ap(out), ap(d0), ap(d1), ap(init), op0, op1), out, [d0, d1, init], 0.5 if two(out, d0, d1) else 1)

    def turn(out, in_):
        vec(lambda: g.vector.transpose(ap(out), ap(in_)), out, [in_], 1)

    def fill(out, c):
        emit("v", lambda: g.vector.memset(ap(out), c), [], [out], CY * max(64, size(out) * (0.5 if two(out) else 1)))

    def scal(out, in_, func=AF.Copy, bias=0.0, scale=1.0, acc=None):
        if len(out) == 3:
            emit("s", lambda: g.scalar.activation(ap(out), ap(in_), AF.Silu), [in_, out[1]], [out[0]], 0.065 + SC * CY * size(out))
            return
        us = 0.065 + GA * CY * size(out) if len(in_) == 3 else CY * max(64, size(out))
        if func == AF.Silu:
            us += 1.3
        kw = {}
        if bias != 0.0:
            kw["bias"] = ap(bias)
            if func == AF.Copy:
                func = AF.Identity
        if scale != 1.0:
            kw["scale"] = ap(scale)
        if acc is not None:
            kw["accum_out"] = ap(acc)
            us += 0.02
        emit("s", lambda: g.scalar.activation(ap(out), ap(in_), func, **kw), [in_, bias, scale], [out, acc], us)

    other = {}

    def either(first, second):
        second()
        x = ops.pop()
        first()
        other[len(ops) - 1] = x
        EITHER[len(ops) - 1] = x[5]

    def act(out, in_, func=AF.Copy, bias=0.0, scale=1.0, acc=None, on="s"):
        s = lambda: scal(out, in_, func, bias, scale, acc)
        if func not in (AF.Copy, AF.Identity):
            return s()
        w = (lambda: tc(out, in_)) if scale == 1.0 and bias == 0.0 else lambda: ts(out, in_, scale, OP.mult, bias, OP.add)
        either(*((s, w) if on == "s" else (w, s)))

    def under(out, in_, c, func, bias):
        either(lambda: scal(out, in_, func, bias, -1.0), lambda: ts(out, in_, c, OP.is_lt))

    def mm(out, lhsT, rhs, start, stop):
        emit("t", lambda: g.tensor.matmul(ap(out), ap(lhsT), ap(rhs), start, stop), [lhsT, rhs], [out],
             CY * max(min(64, size(lhsT)), size(out)) * (PE if two(lhsT) else 4 * PE), "c" + "[" * start + "]" * stop)

    def iota(out, pattern, base, cm, after=None):
        us = 0.15 + 2 * CY * size(out)
        if out[0] == "PI":
            emit("g", lambda: g.iota(ap(out), pattern, base, cm), [], [out], us)
        else:
            emit("g", lambda: g.iota(ap(out), pattern, base, cm, allow_small_or_imprecise_dtypes=True), [after], [out], us)

    def pick(out, in_, pattern, op, base, cm):
        emit("g", lambda: g.affine_select(ap(out), ap(in_), pattern, op, 0.0, base, cm), [in_], [out], 0.17 + 2 * CY * size(out))

    add, sub, mul, eq, ne = OP.add, OP.subtract, OP.mult, OP.is_equal, OP.not_equal
    ge, gt, lt, le = OP.is_ge, OP.is_gt, OP.is_lt, OP.is_le
    SELW = 16 * KS

    C4 = M // 4
    turns = ("y", 0, 1, None)
    dma("s", v("GNI"), ("gn", 0, M, T.gn[:]), 2.2, turns)
    for j in range(4):
        dma("y", v("SNI", j * C4, (j + 1) * C4), ("sn", j * C4, (j + 1) * C4, T.sn[:, j * C4:(j + 1) * C4]), 3.5 + 1.1 * j, turns)
    dma("y", v("FAI"), ("fa", 0, M, T.fa[:]), 7.2, turns)
    dma("y", v("X", A, E), ("x", 0, M, T.x[:]), 9.0, turns)
    dma("y", v("WC"), ("w", 0, 1, T.w[:]), 25.0, turns)

    R16 = v("R16")
    iota(v("PI"), [[1, 1]], 0, 1)
    fill(v("ONES"), 1.0)
    fill(v("OF"), 1.0)
    pick(v("TMPB"), v("ONES", 0, 128), [[-16, 8], [0, 16]], ge, 0, 1)
    pick(v("ONESB"), v("TMPB"), [[16, 8], [0, 16]], ge, 15, -1)
    iota(v("RMOD"), [[0, 24], [1, 16]], 0, 0)
    ts(v("PI2"), v("PI"), 15, OP.bitwise_and)
    tc(R16, v("PI2"))
    ts(v("MK"), v("RMOD", 0, 16), R16, eq)
    for m in range(16):
        act(v("PICK", 128 * m, 128 * (m + 1)), v("ONESB"), scale=v("MK", m, m + 1), on="v" if m < PV else "s")
    for nm in ("SEL", "SELD"):
        fill(v(nm), 0.0)
        act(v(nm, 15, 143, 16), v("ONESB", 0, 128, 16), scale=SELW)
    act(v("SELD", 16, 144, 16), v("ONESB", 0, 128, 16), scale=-SELW)
    if LOWS:
        act(v("SELN"), v("SELD"), scale=-2.0)
    act(v("NONESB"), v("ONESB"), scale=-1.0)
    pick(v("TRI"), v("ONESB"), [[1, 128]], ge, -1, -1)
    pick(v("TIMO"), v("ONESB"), [[-1, 128]], ge, -1, 1)
    ts(v("NR16"), R16, -1.0, mul)
    ts(v("NR17"), R16, -1.0, mul, -1.0, add)
    fill(v("ZER"), 0.0)
    fill(v("CT", NB, 128), -9999.0)
    fill(v("OK", RW, 128), 0.0)
    iota(v("LANB"), [[16, 12]], 0, 0)
    ts(v("LANB"), v("LANB"), R16, add, 0.5, add)
    iota(v("LANE"), [[-1, L]], 0, 0)
    for i, base in enumerate((0, 16, -16)):
        pick(v("I3", 128 * i, 128 * (i + 1)), v("OF"), [[-1, 128]], eq, base, 1)
    ID = v("I3", 0, 128)
    for nm, c in (("IDB", 1.0), ("NIDB", -1.0), ("IDK", float(BK)), ("ID16", 16.0), ("IDHALF", 0.5), ("IDW", W / 2), ("IDL", float(L))):
        act(v(nm), ID, scale=c)
    act(v("ONESK"), v("ONESB"), scale=KS)
    act(v("NONESK"), v("ONESB"), scale=-KS)
    fill(v("RUP", p=(0, 1)), ROUND)
    fill(v("RDN", p=(0, 1)), -ROUND)
    fill(v("EKS", p=(0, 1)), E - KS)
    if BARKEY:
        pick(v("PEN"), v("ONES", 0, 128), [[-1, 128]], eq, 1, 1)
        tt(v("PEN"), v("IDB"), v("PEN"), sub)
        act(v("PEN"), v("PEN"), scale=2.0 ** 31)
    tt(v("TMPB"), v("TRI"), v("IDB"), sub)
    act(v("FST"), v("TMPB"), scale=-KS)
    for t in range(T_):
        a = (Q * t + A - NEW) // 16
        iota(v("BT", 128 * t, 128 * t + NB - a), [[1, NB - a]], NEW // 16 + a, 0)
        iota(v("BT", 128 * t + NB - a, 128 * t + NB), [[1, a]], NEW // 16, 0)
        iota(v("BT", 128 * t + NB, 128 * t + 128), [[0, 128 - NB]], E // 16, 0)
    iota(v("SN", E, WT), [[0, WT - E]], E, 0, v("I3"))
    iota(v("SN", 0, A), [[0, A]], E, 0, v("I3"))
    fill(v("SN", NOB, NOB + 1), float(NOS))
    ts(v("CAP"), v("RMOD", 0, L), R16, gt, RAISE + 2.0 ** 25, mul)
    act(v("CAP"), v("CAP"), bias=-2.0 ** 25)
    ups = {}

    def up(c, k=1.0):
        if (c, k) not in ups:
            ups[(c, k)] = v("UP", len(ups), len(ups) + 1)
            act(ups[(c, k)], R16, bias=c + 15 * k * RAISE, scale=-k * RAISE)
        return ups[(c, k)]

    ts(v("RRS"), v("GNI"), 2, ge, float(M + 1), mul)
    ts(v("RRS"), v("RRS"), -1.0, add)

    def sixteen(out, sel, src, a, b, run=16):
        for r in range(16):
            mm(out, v(sel, 15 - r, 143 - r), v(src, a + r, b, 16), r == 0, r == 15)
            if r % run == run - 1:
                joined(run)

    def spread(src, j, k):
        for m in range(4 * j, 4 * j + 4):
            mm(v(k, (m % 4) * RW, (m % 4 + 1) * RW), v("PICK", 128 * m, 128 * (m + 1)), v(src), True, True)
        return v(k, 0, C4)
    for j in range(4):
        tt(v("ANE", j * C4, (j + 1) * C4), v("SNI", j * C4, (j + 1) * C4), spread("RRS", j, ("k0", "k1")[j % 2]), ne)
    for a, b in ((0, 54), (54, RW)):
        sixteen(v("k6", a, b), "SEL", "ANE", 16 * a, 16 * b)
    ts(v("OK", 0, RW), v("k6", 0, RW), 0.0, eq)
    tc(v("FAS"), v("FAI"))
    tc(v("GNS"), v("GNI"))
    for j in range(4):
        act(v("F1", A + j * C4, A + (j + 1) * C4), spread("FAS", j, ("k2", "k5")[j % 2]), bias=float(A))
        ts(v("SN", A + j * C4, A + (j + 1) * C4), v("SNI", j * C4, (j + 1) * C4), float(A), add)
    act(v("D15"), v("RMOD", 0, L), AF.Abs, v("NR16"))
    act(v("DIAG"), v("D15"), AF.Relu, 1.0, -1.0)
    act(v("OFFD"), v("D15"), AF.Sign)
    fill(v("LOW"), 0.0)
    for a in (0, 64, 112, 144):
        ts(v("LOW", a, a + 16), v("RMOD", 0, 16), R16, le)
    act(v("RS0"), v("RMOD"), AF.Sign)
    fill(v("F1", E, WP), float(NOB))
    act(v("F1", 0, A), v("ONES", 0, A), AF.Silu, scale=float(A))
    fill(v("X", E, WT), BIG)
    fill(v("X", 0, A), BIG)
    ts(v("PI2"), v("PI"), 4, OP.logical_shift_right, 1, OP.bitwise_and)
    tc(v("PBF", 1, 2), v("PI2"))
    ts(v("PBF", 0, 1), v("PBF", 1, 2), -1.0, mul, 1.0, add)
    for e in range(2):
        for y in range(2):
            i = 0 if e == y else 1 if y else 2
            act(v("SWH", 128 * (2 * e + y), 128 * (2 * e + y + 1)), v("I3", 128 * i, 128 * (i + 1)), scale=v("PBF", e, e + 1))
    fill(v("SLR", p=(0, 1)), KS)
    fill(v("SLR", 0, 128, 16, p=(0, 1)), -float(2 ** 32))
    iota(v("REP", p=(0, 64)), [[0, 1024]], 1, 0, v("I3"))
    pick(v("REP", p=(0, 64)), v("REP", p=(0, 64)), [[-1, 64], [0, 16]], eq, 0, 1)
    iota(v("CT0"), [[1, 128]], NEW - E, 0)
    for nm in ("AA", "AB"):
        fill(v(nm, NB, 128), 0.0)
    fill(v("ZEH"), 0.0)
    for h in ("H0", "H1"):
        fill(v(h, L, LW), float(E))
    for t in range(3):
        act(v("me%d" % t, L, LW), v("ONES", 0, 16))
        nm, a, b = ages("m", t)
        act(v(nm, a + L, b), v("ONES", 0, 16), scale=7.0)
    act(v("TR"), v("LANB"), bias=TB - 1.0, scale=2.0)
    act(v("TRP"), v("LANB"), bias=TB - 1.0 - PO, scale=2.0)
    act(v("DT"), v("LANE"), bias=TB - PO + 16 * L, scale=-2.0)
    tt(v("DT"), v("DT"), v("DIAG"), mul)
    act(v("DT"), v("DT"), bias=-float(L))
    fill(v("NLR", p=(0, 1)), -float(L))
    fill(v("GG", 0, 1), 0.0)
    fill(v("CB", NB, 128), 0.0)
    act(v("TOP"), v("LANE"), scale=0.0)
    act(v("TOP", 0, L, 16), v("TR"))
    dma("s", v("GN1", p=(0, 128, 16)), v("GNS"), 3.0)
    emit("y", lambda: [g.sync.dma_start(ap(v("GN", A, E, p=(r, 128, 16))), ap(v("GN1", p=(0, 128, 16)))) for r in range(16)],
         [v("GN1"), v("X", A, E)], [v("GN", A, E)], 1.2, "d", 9.0)
    fill(v("GN", E, WP), 7.0)
    fill(v("GN", 0, A), 7.0)
    emit("y", lambda: g.sync.dma_start(ap(v("F2", 0, WP)), ap(v("F1", 0, WP))), [v("F1", 0, WP), v("GN", A, E)], [v("F2", 0, WP)], 0.07, "d", 8.0)
    for nm, z in (("xo", v("ZEH", 0, 16)), ("fo", v("ZER", 0, 16, p=(0, 128, 16))), ("f2o", v("ZER", 0, 16, p=(0, 128, 16)))):
        emit("y", lambda nm=nm, z=z: g.sync.dma_start(T[nm][:, M:M + 16], ap(z)), [z, v("F2", 0, WP)], [(nm, M, M + 16, None)], 0.07, "d", 3.0)
    iota(v("RM", NEW, WP), [[0, W]], 0, 0, v("REP"))
    iota(v("SN", IDB, WI), [[1, WP]], 0, 0, v("REP"))
    ts(v("M0"), R16, 0.0, eq)
    ts(v("E0"), R16, 0.0, ne, float(E), mul)
    for t in range(1, 3):
        act(v("CT3", S * (t - 1), S * t), v("CT0", S * (t - 1), S * t), scale=v("MK", t, t + 1))
    fill(v("POR", p=(0, 1)), PO)
    fill(v("ONR", p=(0, 1)), 1.0)
    fill(v("QRT", p=(0, 1)), -0.25)
    ts(v("WONE"), v("ONESB"), v("WC"), mul)
    act(v("SCB"), v("RMOD"), AF.Abs, v("NR17"))
    act(v("BS0"), v("SCB"), AF.Relu, PO, -PO)

    def listed(res, row, a=0):
        b = a + size(row)
        scan(v(res, a, b), v("CAP", a, b), row, add, OP.max)
        return v(res, a + 15, b, 16)

    def over(name):
        return 0.0 if ONV[name] else ROUND

    def whole(out, src):
        if ONV[out[0]]:
            ts(out, src, ROUND, add, -ROUND, add)
        else:
            act(out, src, bias=ROUND)

    def unwound(a, b, out, first=()):
        for j, (l, r) in enumerate(first):
            mm(out, l, r, j == 0, False)
        mm(out, v("IDW"), v("SGB", a, b), not first, True)

    def numbers(tag, src):
        k, nv = BANK[tag][0], max(NV[tag])
        mm(v(k, 128, 256, p=(0, 64)), src, v("IDB"), True, True)
        act(v("XT" + tag, p=(0, 64)), v(k, 128, 256, p=(0, 64)))
        if tag in SLOW and src[0] != "me0":
            for s in range(16):
                pick(v("XR" + tag, s, 16 * nv, 16), v(src[0], src[1], src[1] + nv), [[0, nv]], ge, 0, 0)
            joined(16)
            return
        k = BANK[tag][XB]
        for a in range(0, 16 * nv, 384):
            b = min(a + 384, 16 * nv)
            mm(v(k, 128, 128 + b - a), v("XT" + tag, p=(0, 64)), v("REP", a, b, p=(0, 64)), True, True)
            act(v("XR" + tag, a, b), v(k, 128, 128 + b - a))

    def lanes(t):
        ok = v("OK", 0, NB)
        mm(v("k6", 128, 128 + NB), v("ONESB"), ok, True, True)
        mm(v("k6", 256, 256 + NB), v("TIMO"), ok, True, True)
        scan(v("CB", 0, NB), v("k6", 128, 128 + NB), v("ZER", 0, NB), add, add)
        tt(v("CT", 0, NB), v("k6", 256, 256 + NB), v("CB", 0, NB), sub)
        for q in range(12):
            act(v("JK", 128 * q, 128 * q + NB), v("CB", 0, NB), AF.Sign, v("LANB", q, q + 1), -1.0, v("NBS", q, q + 1))
        F = v("F1" if t % 2 == 0 else "F2", 0, WP)
        tab, H = v("SN", 0, WT), "H%d" % (t % 2)

        def first(a, b):
            r, l = (lambda n: v(n, a, b)), (lambda n: v(n, a // 16, b // 16))
            ts(l("BL"), l("NBS"), 0.5, mul, NB / 2, add)
            tt(r("FLG"), at(v("CT"), l("BL")), r("LANE"), ge)
            act(r("BR"), at(v("BT", 128 * t, 128 * t + 128), l("BL")))
            kh = r("k6")
            if over("S0"):
                mm(kh, v("RUP", p=(0, 1)), v("ONES", a, b, p=(0, 1)), True, False)
            mm(kh, v("ID16"), r("BR"), not over("S0"), False)
            mm(kh, v("ONESB"), r("FLG"), False, True)
            ts(l("HL"), listed("RWH", kh, a), up(over("S0")), sub)
            if t < 3:
                act(r(H), kh, bias=-over("S0"))
            else:
                act(r("SGB"), r("BR"), AF.Sign, A / 16 - 0.5, -1.0)
                unwound(a, b, v("k4", 320 + a, 320 + b), [(v("ID16"), r("BR")), (v("ONESB"), r("FLG"))])
                act(r(H), v("k4", 320 + a, 320 + b), bias=W / 2 - A)
            ts(r("PH"), at(F, l("HL")), ROUND, add, -ROUND, add)
            act(r("me%d" % t), at(v("X"), l("HL")))
            ts(l("P0L"), listed("RWP", r("PH"), a), up(0.0), sub)
            for h in range(a // 64, b // 64):
                numbers("A%d" % h, v("me%d" % t, 64 * h, 64 * h + 64))

        def second(a, b):
            r, l = (lambda n: v(n, a, b)), (lambda n: v(n, a // 16, b // 16))
            whole(r("QR"), at(F, l("P0L")))
            ts(l("P1L"), listed("RWQ", r("QR"), a), up(over("QR")), sub)
            whole(r("S0"), at(tab, l("P0L")))
            tt(r("EQ0"), r("S0"), r("k6"), eq)
            under(r("SG0"), r("S0"), over("S0") + E, AF.Sign, over("S0") + E)
            KK, W0, WD = v("k6", L + a, L + b), r("k5"), v("k5", L + a, L + b)
            if over("S0"):
                mm(W0, v("RDN", p=(0, 1)), v("ONES", a, b, p=(0, 1)), True, False)
            mm(W0, v("IDK"), r("EQ0"), not over("S0"), True)
            late = a in BARKEY
            ud = v("k3", 256 + a, 256 + b) if late else r("UD")
            tt(ud, r("S0"), W0, add)
            mm(KK, v("ONESB"), r("SG0"), True, False)
            mm(KK, v("NONESB"), r("EQ0"), False, True)
            if not ONV["UR"]:
                act(r("UR"), KK, AF.Relu, 1.0, -1.0)
            mm(WD, v("ONESK"), r("SG0"), True, False)
            mm(WD, v("NONESK"), r("EQ0"), False, late)
            if late:
                act(r("UD"), WD)
                tt(r("QR"), at(tab, l("P1L")), r("UD"), add)
                tt(r("SA"), r("QR"), ud, OP.min)
                ts(r("SA16"), r("SA"), float(E), OP.min, 0.25, add)
                tc(r("SAH"), r("SA16"))
                mm(r("k4"), v("ONESK"), r("SG0"), True, False)
                mm(r("k4"), v("NONESK"), r("EQ0"), False, False)
                mm(r("k4"), v("IDB"), r("PH"), False, True)
                tt(r("EQ1"), r("SAH"), r("k4"), eq)
                mm(v("k4", 192, 256), v("IDB"), r("SAH"), True, False)
                mm(v("k4", 192, 256), v("IDK"), r("EQ1"), False, True)
                return
            ts(r("S1"), at(tab, l("P1L")), ROUND, add, -ROUND, add)
            tt(r("EQ1"), r("S1"), r("PH"), eq)
            mm(WD, v("IDB"), r("S1"), False, False)
            mm(WD, v("IDK"), r("EQ1"), False, True)
            sa = r("SAH" if ("A0", 0) in PTURN else "SA")
            tt(sa, WD, r("UD"), OP.min)
            ts(r("SA16"), sa, float(E), OP.min)
        for stage in (first, second):
            for a, b in CH:
                stage(a, b)
        hw, pw = v("RWH", 15, L, 16), v("RWP", 15, L, 16)
        if ONV["UR"]:
            ts(v("NU"), listed("ZT", v("k6", L, 2 * L)), up(0.5), gt, float(IDB), mul)
        else:
            sixteen(v("k6", 448, 460), "SEL", "UR", 0, L)
            act(v("NU"), v("k6", 448, 460), bias=float(IDB), scale=-IDB / (16 * SELW))
        act(v("RT"), pw, AF.Abs, up(-over("PR") - A - 31, -1.0))
        tt(v("RT"), v("RT"), v("NU"), add)
        ts(v("CA"), v("RT"), 32.5, lt, KS, mul)
        if t == 3:
            cleaned()
        if t < 3:
            ts(v("Z5", 24, 36), hw, up(over("S0") + PO), sub)
            act(v(*ages("m", t, L)), at(v("GN"), v("HL")))
            if t:
                ship("e", t, v("me%d" % t))
            else:
                ship("e", t, v("me0"), [v("TRI"), v("BT"), v("CT0"), v("SN", IDB, WI)])
                ship("g", t, v("mg0"))
            mm(v("k5", 0, L), v("ONESB"), v("FLG"), True, True)
            ts(v("NOH"), v("k5", 0, L), R16, ne)
            for x, y, n in ((0, TURN, NB - TURN), (NB - TURN, 0, TURN)):
                tt(v("AA", x, x + n), v("OK", y, y + n), v("CT", y, y + n), mul)
            x = NB - TURN
            scan(v("RWI", 0, x), v("CAP", 0, x), v("CB", TURN, NB), add, OP.max)
            scan(v("RWI", x, 128), v("CAP", x, 128), v("CB", 0, 128 - x), add, OP.max, v("RWI", x - 1, x))
            ts(v("IDX"), v("RWI", 15, 128, 16), up(0.0), sub, float(L), OP.min)

    def cleaned():
        rows = [v(f, NEW, WP, p=(0, 128, 16)) for f in ("F1", "F2")]
        for j in range(2):
            dma("y", v("CF", NB * j, NB * j + NB), rows[j], 3.0)
        cf, cr, k = v("CF", 0, 2 * NB), v("CR", 0, 2 * NB), v("k6", L, L + 2 * NB)
        act(cr, cf, bias=ROUND + W / 2 - A)
        act(v("SGB", 0, 2 * NB), cf, AF.Sign, A - 0.5, -1.0)
        unwound(0, 2 * NB, k, [(v("RDN", p=(0, 1)), v("ONES", 0, 2 * NB, p=(0, 1)))])
        tt(cf, cr, k, add)
        for j in range(2):
            dma("y", rows[j], v("CF", NB * j, NB * j + NB), 3.0)

    def down(tag, e, idx, son, lift=(), row=None, bar=None):
        n, nv, kb = 64, NV[tag][e], BANK[tag][0]
        u, xr = "UU" + tag, "XR" + tag
        kt, o = ("k3", n * PARTS.index(tag)) if TBANK or (tag, e) not in PTURN else (kb, 64)
        SP = v(kt, o, o + n)
        if (tag, e) in PTURN:
            for a in range(0, 128, 32):
                for b in range(0, n, 32):
                    mm(v(kt, o + b, o + b + 32, p=(a, a + 32)), v(son[0], son[1] + b, son[1] + b + 32, p=(a, a + 32)),
                       v("IDB", a, a + 32, p=(a, a + 32)), True, True)
            joined(n // 8)
        else:
            turn(SP, son)
        mid = (nv + n) // 4 * 2
        cuts = [(kb, nv, n)] if n - nv <= 32 else [(kb, nv, mid), (BANK[tag][1], mid, n)]
        plain = (tag, e) in PLAIN
        if plain:
            cuts = [(kb, nv, n)] + [(BANK[tag][1], a, b) for a, b in HALVES(nv)]
        for k, a, b in cuts:
            us, dif = v(u, 16 * a, 16 * b), v(k, 512 - 16 * (b - a), 512)
            mm(dif, v("XT" + tag, p=(0, 64)), v("REP", 16 * a, 16 * b, p=(0, 64)), True, False)
            (tc if a < nv else act)(us, at(v("X"), idx(a, b)))
            if (tag, e) in SENDFIRST and NV["t"] < 3:
                ops[-1][3].append(("NLS", 0, 4))
            mm(dif, v("NIDB"), us, False, True)
            if a < nv:
                act(us, dif, AF.Abs)
        low = (tag, e) in LOWS
        for a, b in () if plain else HALVES(nv):
            ux = v(u, 16 * a, 16 * b)
            tt(ux, at(v("X"), idx(a, b)), v(xr, 16 * a, 16 * b), sub)
            if low:
                ts(v("UN", 16 * a, 16 * b), ux, 0.0, OP.min)
            else:
                act(ux, ux, AF.Abs)
        for k, a, b in cuts:
            if a >= nv:
                act(v(u, 16 * a, 16 * b), v(k, 512 - 16 * (b - a), 512), AF.Abs)
        mm(v(kb, 0, n), v("SLR", p=(0, 1)), v("ONES", 0, n, p=(0, 1)), True, False)
        if bar:
            mm(v(kb, 0, n), v("PEN"), bar, False, False)
        for s in range(16 * low):
            mm(v(kb, 0, nv), v("SELN", 15 - s, 143 - s), v("UN", s, 16 * nv, 16), False, False)
        for s in range(16):
            mm(v(kb, 0, n), v("SELD", 15 - s, 143 - s), v(u, s, 16 * n, 16), False, s == 15)
        joined(16 + 16 * low if EARLYC else 17 + 16 * low + bool(bar))
        kp, dd, ee, rr = [v(x + tag) for x in ("MM", "DD", "EE", "RR")]
        turn(kp, v(kb, 0, n))
        scan(dd, kp, v("ZER", 0, n), add, OP.max)
        tt(ee, SP, dd, sub)
        scan(rr, dd, ee, OP.min, OP.max)
        if row:
            turn(v("RT" + tag), rr)
            mm(row, v("PICK", 128 * 15, 128 * 16), v("RT" + tag), True, True)
        for j, x in enumerate(lift):
            mm(v(kb, 0, 4), v("IDB"), x, j == 0, False)
        for e in range(2):
            for y in range(2):
                mm(v(kb, e, 4, 2), v("SWH", 128 * (2 * e + y), 128 * (2 * e + y + 1)), v("RR" + tag, 15 + 16 * y, n, 32),
                   y == 0 and not lift, y == 1 and (e == 1 or not lift))
        joined(4 + len(lift))
        return v(kb, 0, 4)

    def sons(tag, e, places):
        sf = v(("SH" if (tag, e) in PTURN else "SF") + tag)
        ts(v("IX" + tag), at(v("SN", 0, WT if e < 2 else WI), places), ROUND, add, -ROUND, add)
        tc(sf, v("IX" + tag))
        return sf

    def step(tag, e, places, lift=(), row=None):
        sf = sons(tag, e, places) if places else v("SF" + tag)
        return down(tag, e, lambda a, b: v("IX" + tag, a, b), sf, lift, row)

    def barren(tile, src, out):
        act(tile, src, AF.Sign, E - 0.5, -1.0)
        mm(out, v("ONESB"), tile, True, True)

    def own(t):
        for h in (2, 1, 0):
            tag, o, lo = "A%d" % h, 4 * h, 64 * h
            late = any(a <= lo < b for a, b in CH if a in BARKEY)
            x = down(tag, 0, lambda a, b: v("SA16", lo + a, lo + b), v("k4", 192, 256) if late else v("SAH" if (tag, 0) in PTURN else "SA", lo, lo + 64),
                     bar=v("EQ1", lo, lo + 64) if late else None)
            ts(v("LL0", o, o + 4), x, float(E), OP.min)
            x = step(tag, 1, v("LL0", o, o + 4), [v("NU", o, o + 4), v("CA", o, o + 4)])
            ts(v("LL1", o, o + 4), x, float(IDB + E), OP.min)
            sf = sons(tag, 2, v("LL1", o, o + 4))
            if t < 3:
                barren(v("AYI", lo, lo + 64), sf if h else at(v("SN"), v("LL1", o, o + 4)), v("k4", 320 + lo, 384 + lo))
        if t < 3:
            under(v("NFR"), v("k4", 320, 512), -15.5, AF.Relu, -15.0)
            sending(t)
        ts(v("W1"), v("LL0"), IDB - PO, add)
        tt(v("W1"), v("W1"), v("NU"), sub)
        ts(v("W2"), v("LL1"), -PO, add)
        tt(v("YP"), v("W1"), v("W2"), OP.min)
        ts(v("BS0", 0, L, 16), v("YP"), E - PO, OP.min)
        ts(v("YL"), v("YP"), PO, add, float(E), OP.min)
        early(t)
        for h in (2, 1, 0):
            a, srow = 64 * h, v("k4", 64 + 64 * h, 128 + 64 * h)
            x = step("A%d" % h, 2, None, (), srow)
            if t == 3:
                mm(v("k6", a, a + 64), v("PICK", 128 * 15, 128 * 16), v("RTA%d" % h), False, False)
            if h or t < 3:
                act(v("BS0", L + a, L + a + 64, 16), x, bias=-PO)
            ts(v("SL", 4 * h, 4 * h + 4), x, float(E), OP.min)
            if h:
                tc(v("YR", L + a, L + a + 64), srow)
                inside(L + a, L + a + 64, srow)
            else:
                lowest(x)
            xg = v(BANK["A%d" % h][0], 128, 192)
            act(v("XS", a, a + 64), at(v("X"), v("SL", 4 * h, 4 * h + 4)))
            mm(xg, v("QRT", p=(0, 1)), v("ONES", 0, 64, p=(0, 1)), True, False)
            mm(xg, v("IDHALF"), v("me%d" % t, a, a + 64), False, False)
            mm(xg, v("IDHALF"), v("XS", a, a + 64), False, True)
            if ONV["XJ"] or t == 3 and not h:
                ts(v("XJB", a, a + 64), xg, ROUND, add, -ROUND, add)
            else:
                act(v("XJ", a, a + 64), xg, bias=ROUND)
                act(v("XJB", a, a + 64), v("XJ", a, a + 64), bias=-ROUND)

    def arrivals(t):
        ls = "AX"
        act(v(ls, 0, S), at(v("le%d" % (t - 1), 0, LW), v("ls%d" % (t - 1))))
        act(v(ls, S, 2 * S), at(v(*ages("l", t - 1)), v("ls%d" % (t - 1))))
        if AHEAD:
            mm(v("k2", 0, LW), v("WONE"), v("le%d" % (t - 1), 0, LW), True, True)
            tc(v("CI"), v("k2", 0, LW))
            ts(v("CI2"), v("CI"), 63, OP.bitwise_and)
            ts(v("CRW"), at(v("CI2"), v("ls%d" % (t - 1))), float(A), add)
            ts(v("LLAB"), listed("RWC", v("CRW")), up(0.0), sub)
        else:
            mm(v("k2", 0, S), v("WONE"), v(ls, 0, S), True, True)
            ts(v("CI", 0, 4), listed("RWC", v("k2", 0, S)), up(0.0), sub)
            ts(v("CI2", 0, 4), v("CI", 0, 4), 63, OP.bitwise_and)
            ts(v("LLAB"), v("CI2", 0, 4), float(A), add)
        numbers("AB", v(ls, 0, S))
        gen = listed("RWG", v(ls, S, 2 * S))
        ts(v("LIFB", 0, 4), gen, up(4.5), gt, float(BK), mul)
        ts(v("LIFB", 4, 8), gen, up(2.5), lt, float(IDB), mul)
        ts(v("LIFB", 8, 12), gen, up(3.5), lt, float(IDB), mul)
        for e in range(4):
            x = step("AB", e, v("LLAB") if e < 3 else None, [v("LIFB", 4 * e, 4 * e + 4)] if e < 3 else ())
            ts(v("LLAB" if e < 3 else "BF16"), x, float(IDB + E if e else E), OP.min)
            if e == 2:
                sons("AB", 3, v("LLAB"))
                barren(v("AYB"), at(v("SN"), v("LLAB")), v("k4", 256, 320))
                act(v("mf%d" % t), v("k4", 256, 320), AF.Sign, 16.0)
                ship("f", t, v("mf%d" % t))
        tt(v("mr%d" % t), at(v("X"), v("BF16")), v("mf%d" % t), mul)
        ship("r", t, v("mr%d" % t))

    sent = [0]

    def ship(kind, t, src, after=()):
        k = "%s%d" % (kind, t)
        dst = goal(T, rank, kind, t)
        mid = via(topo, core, dst)

        def call():
            if mid is None:
                sent[0] += send(g, topo, core, dst, k, T["l" + k][:], src[3], T.sem["a" + k], T.sem.lo)
            else:
                sent[0] += send(g, topo, core, mid, k, T["b" + k][:], src[3], T.sem["x" + k], T.sem.lo)
        emit("g", call, [src] + list(after), [v("l" + k)], 8.0 if k == "e0" else 1.0, "r", FAR[k])

    YROW, SROW, CNT = v("k5", 0, L), v("k4", 64, 64 + L), v("k6", 0, L)

    def inside(a, b, row):
        scan(v("SCB", a, b), v("RS0", a, b), v("BS0", a, b), mul, add)
        tt(v("ED", a, b), v("SCB", a, b), row, eq)
        mm(v("k6", a % L, a % L + b - a), v("ONESK"), v("ED", a, b), False, False)

    def alike(lo, last):
        cuts = [(q, sum((11 - j) * 16 for j in range(q)), (11 - q) * 16) for q in range(11 if last else YS, 11)]
        if cuts:
            act(v("W2"), v("BS0", 0, L, 16), bias=PO)
            for q, o, n in cuts:
                act(v("EQ", o, o + n), v("k5", L - n, L), AF.Abs, v("W2", q, q + 1), -1.0)
            act(v("EQ", cuts[0][1], 1056), v("EQ", cuts[0][1], 1056), AF.Relu, 1.0, -1.0)
            for q, o, n in cuts:
                mm(v("k6", L - n, L), v("ONESK"), v("EQ", o, o + n), False, False)
            joined(len(cuts))
        for q in range(10 - len(cuts), 3 if last else -1, -1):
            o, n = 1056 * (lo // L) + sum((11 - j) * 16 for j in range(q)), (11 - q) * 16
            ts(v("EQ", o, o + n), v("YR", lo + L - n, lo + L), PO, sub, v("BS0", lo + 16 * q, lo + 16 * q + 1), eq)
            mm(v("k6", L - n, L), v("ONESK"), v("EQ", o, o + n), False, last and q == 4)

    def lowest(x):
        k, cuts = BANK["A0"][0], ((0, 64), (64, 112), (112, 144), (144, 160))
        mm(v(k, 192, 352), v("IDK"), v("LOW"), True, False)
        for q, (a, b) in enumerate(cuts):
            mm(v(k, 192 + a, 192 + b), v("PICK", 128 * 15, 128 * 16), v("RTA0", 16 * q, 64), False, q == 3)
        joined(5)
        for q, (a, b) in enumerate(cuts):
            o = 1056 + 128 * q
            ts(v("EQ", o, o + 128), v("YR", L + 64, 2 * L), v(k, q, q + 1), eq)
            mm(v("k6", 64, L), v("ONESK"), v("EQ", o, o + 128), False, False)
            ts(v("EL", a, b), v(k, 192 + a, 192 + b), v(k, q, q + 1), eq)
            mm(v("k6", 16 * q, 64), v("ONESK"), v("EL", a, b), False, False)

    def early(t):
        yp, sons = v("BS0", 0, L, 16), v("k4", 32, 44)
        mm(YROW, v("POR", p=(0, 1)), v("ONR", 0, L, p=(0, 1)), True, False)
        for r in range(16):
            mm(v("k5", r, L, 16), v("PICK", 128 * r, 128 * (r + 1)), v("YP"), False, r == 15)
        joined(17)
        tc(v("YR", 16, L), v("k5", 16, L))
        if t < 3:
            if ONV["SY"]:
                whole(v("SY"), at(v("SN", 0, WT), v("YL")))
            else:
                act(v("SYR"), at(v("SN", 0, WT), v("YL")), bias=ROUND)
                act(v("SY"), v("SYR"), bias=-ROUND)
            act(v("EMY"), v("SY"), AF.Sign, E - 0.5, -1.0)
        else:
            barren(v("EMY"), at(v("SN", 0, WT), v("YL")), v("k5", L, 2 * L))
            under(v("NFR"), v("k5", L, 2 * L), -15.5, AF.Relu, -15.0)
        mm(CNT, v("ONESK"), v("NFR"), True, False)
        if t < 3:
            mm(CNT, v("NLR", p=(0, 1)), v("ONES", 0, L, p=(0, 1)), False, False)
            mm(CNT, v("IDL"), v("NOH"), False, False)
        else:
            mm(CNT, v("IDK"), v("OFFD"), False, False)
        if ONV["NS"]:
            if t < 3:
                mm(v("k5", L, 2 * L), v("ONESB"), v("EMY"), True, True)
            ts(v("NS"), listed("PR", v("k5", L, 2 * L)), up(-13.0), gt, -KS, mul)
        else:
            sixteen(sons, "SEL", "EMY", 0, L)
            ts(v("NS"), sons, -13 * SELW, gt, -KS, mul)
        tt(v("NS"), v("NS"), v("TRP" if t < 3 else "TR"), add)
        if t < 3:
            tt(v("Z5", 36, 48), yp, v("NS"), OP.max)
        inside(0, L, YROW)
        alike(0, False)

    def adopt(t):
        sp, L4 = v("BS0", L, 384, 16), "L4%d" % (t % 2)
        alike(L, True)
        if t == 3:
            scan(v("ZT"), v("TOP"), CNT, OP.max, OP.min)
            tc(v(L4, 0, 12), v("ZT", 15, L, 16))
            tt(v("Z4", 0, 12), v("ZT", 15, L, 16), v("NS"), OP.max)
            tc(v(L4, 12, 24), v("Z4", 0, 12))
            return
        scan(v("GG", 1, L + 1), v("NOH"), CNT, mul, OP.min)
        tt(v("OK"), at(v("GG", 0, L + 1), v("IDX")), v("AB" if t else "AA"), gt)
        tt(v("Z5", 12, 24), sp, v("NS"), OP.max)
        tt(v("EQS"), v("SY"), SROW, eq)
        mm(v("k7", 0, L), v("EKS", p=(0, 1)), v("ONR", 0, L, p=(0, 1)), True, False)
        mm(v("k7", 0, L), v("FST"), v("EQS"), False, True)
        tt(v("VT"), v("SY"), v("k7", 0, L), OP.max)
        act(v("VH"), SROW, AF.Identity, v("E0"), v("M0"))
        tt(v("FR"), v("DT"), CNT, OP.min)
        scan(v("FRS"), v("RS0", 0, L), v("FR"), mul, add)
        spare = v("FRS", 15, L, 16)
        for j in range(4):
            tt(v("Z4", 12 * j, 12 * j + 12), v("Z5", 12 * j, 12 * j + 12) if j else sp, spare, OP.max)
        ts(v(L4), v("Z4"), PO, add)

    def sending(t):
        ms, hr = "ms%d" % t, "HR%d" % t
        scan(v("CUM"), v("NFR"), v("ZEH"), add, add)
        for q in range(4):
            act(v("JL", L * q, L * q + L), v("CUM"), AF.Sign, v("LANB", q, q + 1), -1.0, v("NLS", q, q + 1))
        ts(v(ms), v("NLS"), 0.5, mul, L / 2, add)
        ship("s", t, v(ms))
        act(v(hr), at(v("H%d" % (t % 2)), v(ms)))
        if t < 2:
            hw = listed("HW", v(hr))
            ts(v("RZ"), hw, up(E), eq, KS, mul)
            tt(v("RZ"), v("RZ"), hw, add)
            ts(v("RZ"), v("RZ"), up(0.0), sub)
            tt(v("RZ"), v("RZ"), v("TR", 0, 4), OP.min)
            tc(v("HT%d" % t), v("RZ"))
        else:
            act(v("SGB", 0, S), v(hr), AF.Sign, A - 0.5, -1.0)
            unwound(0, S, v("k2", 64, 64 + S))
            act(v("HRM"), v(hr), bias=W / 2 - A)
            tt(v(hr), v("HRM"), v("k2", 64, 64 + S), add)
        if t == 0:
            act(v("GN", NEW, NEW + S), at(v("mg0"), v(ms)), AF.Identity, 1.0)

    def returned(t):
        if t < 3:
            fd = v("lf%d" % t)
            tc(at(v("RM"), v("HT%d" % (t - 1))), fd)
            come = listed("RWR", fd)
            sixteen(v("k5", 384, 384 + NB), "SEL", "RM", NEW, WP, 4)
            tt(v("RVD"), fd, v("CT3", S * (t - 1), S * t), mul)
            x = TURN * (t + 1) + (A - NEW) // 16
            a = NB - x + S * (t - 1) // 16
            act(v("AA", a, a + 4), come, AF.Identity, up(0.0, 256.0), -256.0)
            tt(v("AB", 0, NB - x), v("AA", 0, NB - x), v("k5", 384 + x, 384 + NB), add)
            tt(v("AB", NB - x, NB), v("AA", NB - x, NB), v("k5", 384, 384 + x), add)

    def changes(t):
        H, L4, tab = v("H%d" % (t % 2), 0, L), "L4%d" % (t % 2), v("SN", 0, WT)
        tc(at(v("X"), v(L4, 0, 12)), v("XJB"))
        if t:
            lr, a, hr, fd = v("lr%d" % t), NEW + S * (t - 1), v("HR%d" % (t - 1)), v("lf%d" % t)
            if t < 3:
                act(v("X", a, a + S), lr, on="v")
                act(v("HRM"), hr, bias=-float(A))
                tt(v("RVF"), v("HRM"), fd, mul)
                for f in ("F1", "F2"):
                    act(v(f, a, a + S), v("RVF"), bias=float(A))
            else:
                a = W - S
                tt(v("RVB"), hr, fd, mul)
                dma("y", ("fo", a, W, T.fo[:, a:W]), v("RVB", p=(0, 128, 16)), 2.2)
                dma("y", ("f2o", a, W, T.f2o[:, a:W]), v("RVB", p=(0, 128, 16)), 2.2)
                dma("s", ("xo", a, W, T.xo[:, a:W]), lr, 2.5)
        put = lambda n: tc if t == 3 else lambda out, in_: act(out, in_, on="v" if ONV[n] else "s")
        put("F2")(at(v("F2"), v(L4, 0, 12)), H)
        put("F1")(at(v("F1"), v(L4, 12, 24)), H)
        if t < 3:
            put("SNH")(at(tab, v(L4, 24, 36)), v("VH"))
            put("SNY")(at(tab, v(L4, 36, 48)), v("VT"))
        if 0 < t < 3:
            act(v("RVB"), at(tab, v("HT%d" % (t - 1))))
            tt(at(tab, v("HT%d" % (t - 1))), v("RVB"), v("RVD"), add)

    for t in range(T_):
        NV.update(zip(PARTS, NVT[t]), t=t)
        lanes(t)
        if t:
            arrivals(t)
        own(t)
        if t:
            returned(t)
        adopt(t)
        changes(t)
    for a, b, c in ((0, M, A), (M + 16, W - S, NEW)):
        dma("y", ("xo", a, b, T.xo[:, a:b]), v("X", c, c + b - a), 2.5 if a else 4.0)
        dma("s", ("f2o", a, b, T.f2o[:, a:b]), v("F2", c, c + b - a, p=(0, 128, 16)), 2.5)
        dma("s", ("fo", a, b, T.fo[:, a:b]), v("F1", c, c + b - a, p=(0, 128, 16)), 2.5)

    if not ORDER:
        ORDER.extend(sorted(plan(ops), key=lambda i: ops[i][3][:1] == [("lr3", 0, S)]))
    for i in ORDER:
        issue(*(other[i] if i in SWAP else ops[i]))
    total["lo"] = sent[0]
    for sem in sorted(total, key=lambda x: int(x[1:]) if x[0] == "d" else -1):
        g.wait_ge(T.sem[sem], total[sem])
